import numpy as np, ml_dtypes
CORES = [40,41,42,43,44,45,46,47]
N = 8
import mx_ref
BF = ml_dtypes.bfloat16
def entries(a):
    return np.ascontiguousarray(a.T).reshape(-1)
def table(e):
    return np.ascontiguousarray(np.reshape(e, (-1, 16)).T).astype(np.int32)
def cols(t, e):
    v = np.concatenate([t.reshape(128, -1, 4), np.zeros((128, 1, 4), BF)], axis=1)
    return np.ascontiguousarray(v[:, e]).reshape(128, -1)
def cut(t, i, w=512):
    return t[:, w * i:w * i + w]
def pick(q, e):
    c = np.concatenate([q[0].reshape(128, -1, 4), np.zeros((128, 1, 4), np.uint8)], axis=1); s = np.concatenate([q[1], np.ones((16, 1), np.uint8)], axis=1)
    return (np.ascontiguousarray(c[:, e].reshape(128, -1)), np.ascontiguousarray(s[:, e]))
def join(*qs):
    return (np.concatenate([q[0] for q in qs], axis=1), np.concatenate([q[1] for q in qs], axis=1))
def put(q, e, v):
    c, s = q[0].reshape(128, -1, 4).copy(), q[1].copy(); c[:, e] = v[0].reshape(128, -1, 4); s[:, e] = v[1]
    return (c.reshape(128, -1), s)
def pk(c, s):
    return (np.ascontiguousarray(c), mx_ref.live(s))
def emit(q):
    return q[0], q[1]
def decode(q):
    o = []
    for b in range(4):
        e = np.zeros((128, 128, 4), np.float32); e[np.arange(128), np.arange(128), b] = 1
        o.append(mx_ref.matmul(mx_ref.quantize(e.reshape(128, 512).astype(BF)), q))
    return np.stack(o, axis=2).reshape(128, -1)
def f(rng, *shape):
    return mx_ref.flush((rng.standard_normal(shape, dtype=np.float32) * np.exp2(rng.integers(-2, 3, shape[:-1] + (1,)))).astype(BF))
def wide(rng, *shape, cols=0):
    v = rng.standard_normal(shape, dtype=np.float32) * np.exp2(rng.integers(-12, 13, shape)).astype(np.float32)
    if cols: v *= np.repeat(np.exp2(rng.integers(-cols, cols + 1, shape[:-2] + (1, shape[-1] // 4))) * (rng.random(shape[:-2] + (1, shape[-1] // 4)) > 0.0625), 4, axis=-1).astype(np.float32)
    return mx_ref.flush(v.astype(BF))
P, A, C, E, KP = 256, 16, 16, 8, 4
LC, M = 48, 5
def clean(v):
    v = np.array(v, np.float32)
    v[np.abs(v) < np.float32(2.0 ** -16)] = 0
    return v.astype(BF)
def lists(rng, full=False, own=False):
    out = []
    for r in range(N):
        pool = np.stack([P * q + rng.permutation(P)[:LC] for q in range(N)])
        must = np.zeros(0, int)
        if full: must = rng.permutation(pool[(r + 1 + rng.permutation(N - 1)[:M]) % N].reshape(-1))
        if own: must = P * r + rng.permutation(P)[:A * (C - 4)]
        rows = []
        for i in range(A):
            a = must[i::A]
            b = rng.permutation(np.setdiff1d(pool, a))[:C - a.size]
            rows.append(rng.permutation(np.concatenate([a, b])))
        out.append(table(np.concatenate(rows)))
    return {"cd": np.stack(out)}
def clusters(rng, n, low, high, noise):
    m = f(rng, 128, 4 * n).astype(np.float32).reshape(128, n, 4)
    h = rng.integers(0, n, (N, P))
    tb = np.stack([m[:, h[q]].reshape(128, -1) for q in range(N)]) + noise * f(rng, N, 128, 4 * P).astype(np.float32)
    a = low + (high - low) * rng.random((N, A, n))
    x = np.einsum("png,rin->rpig", m, a).reshape(N, 128, 4 * A) + noise * f(rng, N, 128, 4 * A).astype(np.float32)
    return {"tb": clean(tb), "x": clean(x), "w": f(rng, N, 128, 512)}
def setup_inputs(rng):
    return {**clusters(rng, 8, 0.2, 1.0, 0.5), **lists(rng)}
def setup_inputs_alike(rng):
    return {**clusters(rng, 3, 0.3, 0.7, 0.25), **lists(rng, full=True)}
def setup_inputs_one(rng):
    o, m, n = 0, min(A, LC // KP), P // KP
    kind = rng.permutation(P) % KP
    part = np.arange(128) // (128 // KP)
    tb = f(rng, N, 128, 4 * P).astype(np.float32).reshape(N, 128, P, 4) * np.float32(0.0625)
    tb[o] = (4 + 4 * rng.random((128, P, 4))) * (part[:, None] == kind[None, :])[:, :, None]
    order = np.stack([rng.permutation(np.flatnonzero(kind == k)) for k in range(KP)])
    out = []
    for r in range(N):
        size, at = (A, 0) if r == o else (m, A + m * (r - int(r > o)))
        big = P * o + order[:, (at + np.arange(A) % size) % n]
        pool = rng.permutation(np.concatenate([P * q + rng.permutation(P)[:LC] for q in range(N) if q != o]))
        rest = pool[:A * (C - KP)].reshape(A, C - KP)
        out.append(table(np.concatenate([rng.permutation(v) for v in np.concatenate([big.T, rest], axis=1)])))
    return {"tb": clean(tb.reshape(N, 128, 4 * P)), "x": clean(1 + rng.random((N, 128, 4 * A))), "w": f(rng, N, 128, 512), "cd": np.stack(out)}
def setup_inputs_ties(rng):
    m = clean(f(rng, 128, 12)).astype(np.float32).reshape(128, 3, 4)
    h = rng.integers(0, 3, (N, P))
    i = np.arange(A)
    k = np.where(i // 3 % 2 == 0, 1.0, 2.0)[None, :, None]
    tb = clean(np.stack([m[:, h[q]].reshape(128, -1) for q in range(N)])).reshape(N, 128, P, 4)
    x = clean(np.stack([(m[:, (i + r) % 3] * k).reshape(128, -1) for r in range(N)])).reshape(N, 128, A, 4)
    cd = lists(rng, own=True)["cd"]
    top = np.arange(128) < 64
    x[:, :, A - 2] = np.where(top, 4.0, 1.0).astype(BF)[None, :, None]
    x[:, :, A - 1] = np.where(top, -1.0, -4.0).astype(BF)[None, :, None]
    for r in range(N):
        g = rng.permutation(P)[:C + 1]
        g[:3] = np.sort(g[:3])
        tb[r][:, g[0]] = BF(-0.0)
        tb[r][:, g[1]] = BF(0.0)
        tb[r][:, g[2]] = np.array([1.0, -1.0, 1.0, -1.0]).astype(BF)[None, :]
        tb[r][:, g[3:]] = clean((1 + rng.random((128, C - 2, 4))) * np.where(top, -1.0, 1.0)[:, None, None])
        e = np.array(entries(cd[r])).reshape(A, C)
        e[A - 2] = P * r + rng.permutation(np.delete(g, 1))
        e[A - 1] = P * r + rng.permutation(np.delete(g, 0))
        cd[r] = table(e)
    return {"tb": tb.reshape(N, 128, 4 * P), "x": x.reshape(N, 128, 4 * A), "w": f(rng, N, 128, 512), "cd": cd}
def setup_inputs_shared(rng):
    place = np.stack([rng.permutation(P) for q in range(N)])
    tb = f(rng, N, 128, 4 * P).astype(np.float32).reshape(N, 128, P, 4) * np.float32(0.0625)
    part = np.arange(128) // (128 // KP)
    big = np.zeros((N, KP), int)
    for g in range(N):
        for k in range(KP):
            o = (g + k) % N
            tb[o, :, place[o, k]] = (4 + 4 * rng.random((128, 4))) * (part == k)[:, None]
            big[g, k] = P * o + place[o, k]
    out = []
    for r in range(N):
        pool = np.concatenate([P * q + rng.permutation(place[q, KP:])[:LC - KP] for q in range(N)])
        at = rng.integers(0, r + 1, A)
        at[0], at[A - 1] = 0, r
        out.append(table(np.concatenate([rng.permutation(np.concatenate([big[g], rng.permutation(pool)[:C - KP]])) for g in at])))
    return {"tb": clean(tb.reshape(N, 128, 4 * P)), "x": clean(1 + rng.random((N, 128, 4 * A))), "w": f(rng, N, 128, 512), "cd": np.stack(out)}
def setup_inputs_spread(rng):
    return {"tb": clean(wide(rng, N, 128, 4 * P, cols=6)), "x": clean(wide(rng, N, 128, 4 * A, cols=6)), "w": f(rng, N, 128, 512), **lists(rng)}
def check_inputs(d):
    b = []
    for k, low in (("tb", -16), ("x", -16), ("w", -30)):
        v = np.abs(d[k].astype(np.float32))
        if not (np.isfinite(v).all() and ((v == 0) | (v >= 2.0 ** low) & (v <= 2.0 ** 30)).all()): b.append("a value of " + k)
    for r in range(N):
        e = entries(d["cd"][r])
        if e.min() < 0 or e.max() >= N * P:
            b.append("cd: a number out of range")
            continue
        if any(len(set(v.tolist())) < C for v in e.reshape(A, C)): b.append("cd: a candidate twice at one point")
        n = np.bincount(np.unique(e) // P, minlength=N)
        n[r] = 0
        if n.max() > LC: b.append("cd: too many columns of one other rank")
    return b
def chosen(every, x, cd):
    kept = np.full((N, A, KP), -1)
    for r in range(N):
        e = entries(cd[r])
        t = cols(every, e)
        v = mx_ref.quantize(t)
        points = mx_ref.quantize(cols(x[r], np.concatenate([np.arange(A), np.full(128 - A, -1)])))
        s = mx_ref.matmul(points, v) + np.float32(0)
        g = np.concatenate([mx_ref.matmul(mx_ref.quantize(np.ascontiguousarray(cut(t, j))), v) for j in range(C * A // 128)]) + np.float32(0)
        for i in range(A):
            at = np.arange(C * i, C * i + C)
            best = at[np.lexsort((e[at], -s[i, at]))[:E]]
            mine = []
            for c in best:
                if len(mine) < KP and all(s[i, c] > g[c, k] for k in mine): mine.append(c)
            kept[r, i, :len(mine)] = e[mine]
    return kept
def reference(tb, x, w, cd):
    every = np.concatenate([tb[q] for q in range(N)], axis=1)
    kept = chosen(every, x, cd)
    y = np.zeros((N, 128, KP * A), np.float32)
    oc, osc = np.zeros((N, 128, 4 * P), np.uint8), np.zeros((N, 16, P), np.uint8)
    for r in range(N):
        y[r] = mx_ref.matmul(mx_ref.quantize(w[r]), mx_ref.quantize(cols(every, kept[r].reshape(-1))))
    dx = [decode(mx_ref.quantize(x[r])).reshape(128, A, 4) for r in range(N)]
    half = np.float32(0.5)
    for q in range(N):
        v = mx_ref.quantize(tb[q])
        m = decode(v).reshape(128, P, 4)
        named = np.zeros(P, bool)
        for r in range(N):
            for i in range(A):
                for c in kept[r, i]:
                    j = c - P * q
                    if 0 <= j < P and not named[j]:
                        m[:, j] = m[:, j] * half + dx[r][:, i] * half
                        named[j] = True
        at = np.flatnonzero(named)
        new = mx_ref.quantize(np.ascontiguousarray(m.reshape(128, -1).astype(BF)))
        oc[q], osc[q] = emit(put(v, at, pick(new, at)))
    return {"y": y, "kp": np.ascontiguousarray(kept.transpose(0, 2, 1)).astype(np.float32), "oc": oc, "osc": osc}

@@ -1,0 +1,716 @@
+from concourse.bass import DstId, RemoteDMATransfer
+from concourse.mybir import dt, AluOpType, AxisListType, ActivationFunctionType
+
+NR, P, A, C, E, KP, LC = 8, 256, 16, 16, 8, 4, 48
+WOWN = (NR - 1) * LC
+SH = 16
+DUMP = NR * P + SH
+CLW = DUMP + KP * A
+GW = 16 * (E - 1)
+S0 = P * (NR - 1)
+FW = 48
+PW = NR * A + 16
+ORDER = (1, 4, 2, 5, 3, 6, 7)
+WAVES = ((0, 4), (4, 7))
+
+F, B, I, U = "float32", "bfloat16", "int32", "uint16"
+SB = {
+    "cdi": (16, I), "offl": (16, U), "ones": (64, B), "zz": (288, B), "pres": (4 * (S0 + NR * P), B), "r4": (4 * P, B), "orx": (4 * P, B),
+    "cnt": (P + 32, B), "ind": (2 * P, B), "indc": (2 * P, B), "junk": (P, B), "req": (3, U), "rland": (24, U), "reql": (24, U), "rj": (48, F),
+    "jwb": (2, B), "dumpc": (4, F), "imj": (96, F), "r8": (32, F), "tro": (8, U), "of3": (24, U), "ofx": (32, U),
+    "offs": (16, U), "offp": (16, U), "cf": (96, F), "li": (68, I), "m16": (256, B), "m4": (896, B),
+    "r16": (256, B), "zw": (DUMP, F), "vals": (256, B), "vald": (256, B), "erow": (160, F), "erow2": (256, F),
+    "lf": (32, F), "lt": (32, F), "cm2": (256, B), "rn": (256, B), "oh2": (256, F), "nsz": (256, F), "nz3": (256, F),
+    "offw": (16, U), "lw": (256, B), "lall": (128, B), "la": (128, F), "lsm": (256, F), "lsz": (256, F), "offc": (16, U),
+    "sm": (256, F), "sz": (256, F), "sn": (32, F), "n1": (16, F), "rep": (256, F), "cm": (256, B), "rk": (256, B), "oh": (128, F), "lm": (128, F),
+    "lz": (128, F), "offr": (16, U), "ss": (128, F), "ssz": (128, F), "sr": (16, F), "nm": (128, F), "nz": (128, F), "gb": (896, B),
+    "gs": (912, B), "fb": (192, F), "pp": (40, F), "bo": (20, F), "kh": (32, F), "km": (64, F), "ky": (64, F),
+    "kf": (32, F), "kt": (32, F), "kd": (16, F), "kl0": (4, U), "zrow": (64, F), "dz": (256, F), "dm": (8, F), "kmsg": (4, U),
+    "kland": (32, U), "kc": (32, F), "okl": (16, U), "ysb": (144, F), "yo": (64, F),
+    "xt": (512, B), "wt": (512, B), "tt": (1024, B), "ebm": (520, B), "eb": (520, B), "cl": (2176, B), "ttc": (544, B), "cw": (16, F),
+    "ptd": (4 * PW, B), "tbd": (2 * P, B), "gp": (2 * P, B), "ptl": (16, U), "sel": (32, F), "sell": (16, U), "bb": (1024, B),
+}
+CODES = {"p8": 128, "wq": 128, "tq": 256, "win": 592, "tn": 512, "snd": 336, "cand": 256, "pk": 240, "eq": 512, "pt": 128, "ocq": 256}
+ICOL = {n: i for i, n in enumerate(["pi", "pmi", "ggi", "ogi", "t1i", "t2i", "t3i", "t4i", "t5i", "t6i", "t7i", "t8i"])}
+FCOL = {n: i for i, n in enumerate(["pm", "u1", "u2", "u3", "u4", "thr", "pm8", "th0", "u5", "u6", "isr", "hneg",
+                                    "u7", "u8", "og64", "sb", "acc", "bx", "by", "bz"])}
+
+SCRATCH = {n: ("sbuf", [128, k], d) for n, (k, d) in SB.items()}
+SCRATCH["dl"] = ("dram", [16, 128], B)
+SCRATCH["ic"] = ("sbuf", [128, len(ICOL)], I)
+SCRATCH["fc"] = ("sbuf", [128, len(FCOL)], F)
+for _n, _k in CODES.items():
+    SCRATCH[_n] = ("sbuf", [128, _k], "float8_e4m3fn_x4")
+    SCRATCH[_n + "s"] = ("sbuf", [128, _k], "uint8")
+SCRATCH["ps"] = ("psum", [128, 4096], F)
+
+ROADS = ["ptc", "pts", "req", "cod0", "cod1", "pln0", "pln1", "kept"]
+XS = ["x%d" % i for i in range(128)]
+SEMAPHORES = ["v", "s", "step", "scat", "claim", "prune"] + ["r_" + n for n in ROADS] + ["l_" + n for n in ROADS] + XS
+
+
+def rank_program(g, core, T, topo):
+    r = T.rank_of(core)
+    if r is None:
+        return
+    V, S, Q, M = g.vector, g.scalar, g.sync, g.tensor
+    op, X, fn = AluOpType, AxisListType.X, ActivationFunctionType
+    others = [r ^ m for m in ORDER]
+    wave = [others[a:b] for a, b in WAVES]
+    u8, u32 = dt.uint8, dt.uint32
+
+    free = list(XS)
+    vn, sn_, pn = [0], [0], [0]
+
+    def new():
+        return free.pop(0)
+
+    def v(inst, sig=None):
+        inst.then_inc(T.sem[sig or "v"], 1)
+        if sig is None:
+            vn[0] += 1
+        if sig == "step":
+            pn[0] += 1
+        return sig
+
+    def vw():
+        V.wait_ge(T.sem["v"], vn[0])
+
+    def pw():
+        V.wait_ge(T.sem["step"], pn[0])
+
+    def s(inst, sig=None):
+        inst.then_inc(T.sem[sig or "s"], 1)
+        if sig is None:
+            sn_[0] += 1
+        return sig
+
+    def sw():
+        S.wait_ge(T.sem["s"], sn_[0])
+
+    def on(q, sig, n=1):
+        q.wait_ge(T.sem[sig], n)
+
+    def ic(n):
+        return T.ic[:, ICOL[n]:ICOL[n] + 1]
+
+    def fc(n):
+        return T.fc[:, FCOL[n]:FCOL[n] + 1]
+
+    def ts(o, a, s1, op0, s2=None, op1=None, sig=None):
+        if op1 is None:
+            return v(V.tensor_scalar(o, a, s1, None, op0), sig)
+        return v(V.tensor_scalar(o, a, s1, s2, op0, op1), sig)
+
+    def bits(o, a, s1, op0, s2=None, op1=None):
+        if op1 is None:
+            return v(V.tensor_scalar(o, a, s1, None, op0))
+        return v(V.tensor_scalar(o, a, s1, s2, op0, op1))
+
+    def tt(o, a, b, o_, sig=None):
+        return v(V.tensor_tensor(o, a, b, o_), sig)
+
+    def cp(o, a, sig=None):
+        return v(V.tensor_copy(o, a), sig)
+
+    def fill(o, c, sig=None):
+        return v(V.memset(o, c), sig)
+
+    def scan(o, a, b, o0, o1, sig=None):
+        return v(V.tensor_tensor_scan(o, a, b, 0.0, o0, o1), sig)
+
+    def sums(o, a, sig=None):
+        return scan(o, T.r16[:, 0:o.shape[1]], a, op.mult, op.add, sig)
+
+    def act(o, a, sig=None):
+        return s(S.activation(o, a, fn.Copy), sig)
+
+    def pick_v(o, src, off, sig):
+        V.tensor_copy(o.bitcast(u32), src.bitcast(u32).indirect(off)).then_inc(T.sem[sig], 1)
+
+    def pick_s(o, src, off, sig):
+        S.activation(o, src.indirect(off), fn.Copy).then_inc(T.sem[sig], 1)
+
+    def quant(o, a, b, src, sig):
+        v(V.quantize_mx(T[o][:, a:b], T[o + "s"][:, a:b], src), sig)
+
+    def iota(o, pat, base, cm, sig):
+        g.iota(o, pat, base, cm, allow_small_or_imprecise_dtypes=True).then_inc(T.sem[sig], 1)
+
+    def load(q, o, a, sig):
+        q.dma_start(o, a).then_inc(T.sem[sig], 16)
+
+    def masks(dests, n):
+        near = [q for q in dests if topo.die(T.cores[q]) == topo.die(core)]
+        far = [q for q in dests if q not in near]
+        places = {0: [k for k in range(16 // n) if k % 2 == 0], 1: [k for k in range(16 // n) if k % 2 == 1]}
+        out = {}
+        for side, grp in ((0, near), (1, far)):
+            for q in grp:
+                k = (places[side] or places[1 - side]).pop(0)
+                e = topo.engines(core, T.cores[q])
+                out[q] = sum(1 << e[j] for j in range(k, len(e), len(e) // n))
+        return out
+
+    def send(src, dst, road, dests=others, n=2):
+        tr, mk = [], masks(dests, n)
+        for q in dests:
+            rid, pid = topo.addr(T.cores[q])[:2]
+            tr.append(RemoteDMATransfer(dst_ids=[DstId(rid=rid, pnc=pid)], dma_engine_mask=mk[q], remote_sem=T.sem["r_" + road], src=src(q), dst=dst(q)))
+        g.remote_dma_fused(tr, local_sem=T.sem["l_" + road])
+
+    ids, every = [], topo.mask(core, T.cores[others[0]])
+    for q in others:
+        rid, pid = topo.addr(T.cores[q])[:2]
+        ids.append(DstId(rid=rid, pnc=pid))
+        every &= topo.mask(core, T.cores[q])
+    EV = bin(every).count("1")
+
+    def tell(src, dst, road):
+        g.remote_dma_fused([RemoteDMATransfer(dst_ids=ids, dma_engine_mask=every, remote_sem=T.sem["r_" + road], srcs=[src],
+                                              dsts=[dst(q) for q in others])], local_sem=T.sem["l_" + road])
+
+    ALL = 2 * (NR - 1)
+
+    def seat(a, b):
+        return ORDER.index(a ^ b)
+
+    def spot(q):
+        return LC * ((r - q - 1) % NR)
+
+    row16, jm, jw = T.rj[:, 0:16], T.rj[:, 16:32], T.rj[:, 32:48]
+    dd, ma, mb, bs, lts = [T.cf[:, 16 * k:16 * k + 16] for k in range(5)]
+    nsi, owi = T.li[:, 0:16], T.li[:, 16:32]
+    im64, jm8 = T.imj[:, 0:64], T.imj[:, 64:96]
+    rot, psel, tl = T.tro[:, 2:3], T.tro[:, 4:5], T.tro[:, 0:1]
+    offn, offg, offf, offz = T.of3[:, 0:2], T.of3[:, 4:8], T.of3[:, 16:17], T.of3[:, 18:20]
+    klf, ub = T.kc[:, 0:32], T.pp[:, 16:33]
+
+    x_cd, x_x, x_tb, x_w = new(), new(), new(), new()
+    for k in range(8):
+        load(Q if k < 4 else S, T.cdi[16 * k:16 * k + 16, :], T.cd[:, :], x_cd)
+    load(Q, T.xt[:, 0:64], T.x[:, :], x_x)
+    load(Q, T.tt[:, :], T.tb[:, :], x_tb)
+    load(S, T.wt[:, :], T.w[:, :], x_w)
+
+    x_pi, x_io1, x_io2, x_er2, x_eb, x_ebd, x_r4 = new(), new(), new(), new(), new(), new(), new()
+    g.iota(ic("pi"), [[1, 1]], 0, 1).then_inc(T.sem[x_pi], 1)
+    iota(jm, [[1, 16]], 0, 0, x_io1)
+    iota(row16, [[16, 16]], 0, 0, x_io1)
+    iota(T.r4[:, :], [[0, P], [1, 4]], 0, 0, x_r4)
+    iota(T.erow2[:, :], [[2, 16], [0, 16]], 1 - C, 0, x_er2)
+
+    x_r16, x_m, x_zz, x_isr, x_pr, x_pz = new(), new(), new(), new(), new(), new()
+    fill(T.pres[:, 4 * S0:4 * S0 + 4 * P], 0.0, sig=x_pz)
+    on(V, x_pi)
+    bits(ic("ggi"), ic("pi"), 4, op.arith_shift_right)
+    fill(T.ones[:, :], 1.0, sig="step")
+    fill(T.zz[:, :], 0.0, sig=x_zz)
+    vw()
+    ts(fc("isr"), ic("ggi"), float(r), op.is_equal, sig=x_isr)
+    for k in range(4):
+        ts(T.bo[:, 16 + k:17 + k], ic("ggi"), float(-4 * P), op.mult, float(4 * S0 + k), op.add, sig="step")
+    bits(ic("pmi"), ic("pi"), 15, op.bitwise_and)
+    ts(fc("hneg"), ic("ggi"), float(-P), op.mult, 16.0, op.add)
+    pw()
+
+    x_xt, x_cz = new(), new()
+    on(S, x_pz)
+    on(S, x_isr)
+    own = T.pres[:, 4 * S0:4 * S0 + 4 * P:4]
+    s(S.activation(own, own, fn.Identity, bias=fc("isr")), x_pr)
+    on(S, x_zz)
+    act(T.cnt[:, 0:16], T.zz[:, 0:16], sig=x_cz)
+    act(T.cnt[:, P + 16:P + 32], T.zz[:, 0:16], sig=x_cz)
+    on(S, x_x, 16)
+    act(T.xt[:, 64:128], T.xt[:, 0:64]); sw()
+    act(T.xt[:, 128:256], T.xt[:, 0:128]); sw()
+    act(T.xt[:, 256:512], T.xt[:, 0:256], sig=x_xt)
+
+    on(V, x_cd, 128)
+    for k in range(4):
+        ts(T.offl[:, k:16:4], T.cdi[:, k:16:4], 4.0, op.mult, T.bo[:, 16 + k:17 + k], op.add, sig="step")
+    on(V, x_io1, 2)
+    ts(T.r16[:, 0:16], jm, 0.0, op.is_gt, sig=x_r16)
+    pw()
+    on(V, x_pr)
+    x_p8, x_lt, x_sb = new(), new(), new()
+    for i in range(4):
+        if i:
+            on(V, "scat", i)
+        v(V.tensor_copy(T.pres[:, :].indirect(T.offl[:, 4 * i:4 * i + 4]), T.ones[:, :]), "scat")
+        vw()
+        if i == 0:
+            cp(fc("pm"), ic("pmi"))
+            cp(T.lf[:, 0:16], T.cdi[:, :])
+            cp(T.lf[:, 16:32], T.cdi[:, :])
+        if i == 1:
+            ts(dd, jm, fc("pm"), op.subtract)
+            ts(jw, row16, fc("pm"), op.add)
+            v(V.transpose(T.lt[:, :], T.lf[:, :]), x_lt)
+        if i == 2:
+            ts(T.m16[:, 0:16], dd, 0.0, op.is_equal, sig=x_m)
+            ts(fc("sb"), T.rj[:, 34:35], 0.5, op.add, sig=x_sb)
+            cp(T.jwb[:, :], T.rj[:, 32:34])
+        if i == 3:
+            ts(T.offw[:, :], T.cdi[:, :], fc("hneg"), op.add, P + 16.0, op.min)
+            on(V, x_xt)
+            quant("p8", 0, 128, T.xt[:, :], x_p8)
+    on(V, "scat", 4)
+    on(V, x_r4)
+    scan(T.orx[:, :], T.r4[:, :], T.pres[:, 4 * S0:4 * S0 + 4 * P], op.min, op.max)
+    ts(fc("u5"), ic("pmi"), 16.0, op.mult, 15.0, op.add)
+    vw()
+    x_cnt = scan(T.cnt[:, 16:P + 16], T.orx[:, 3:4 * P:4], T.orx[:, 3:4 * P:4], op.add, op.max, sig=new())
+    ts(T.offp[:, :], row16, 0.0, op.mult, fc("pm"), op.add)
+
+    def rows(t, n, m, sig):
+        while n < m:
+            k = min(n, m - n)
+            act(t[:, n:n + k], t[:, 0:k], sig=sig if n + k == m else None)
+            n += k
+            if n < m:
+                sw()
+    x_r16b, x_m16, x_cm, x_acc, x_cl, x_r8 = new(), new(), new(), new(), new(), new()
+    on(S, x_r16)
+    rows(T.r16, 16, 256, x_r16b)
+    on(S, x_m)
+    rows(T.m16, 16, 256, x_m16)
+    on(S, x_sb)
+    on(S, x_cnt)
+    s(S.activation(T.junk[:, 0:P - 1], T.cnt[:, 16:P + 15], fn.Sign, bias=fc("sb"), scale=-1.0, accum_out=fc("acc")), x_acc)
+    on(S, x_lt)
+    for c in range(C):
+        s(S.activation(T.cm2[:, 16 * c:16 * c + 16], T.lt[:, 0:16], fn.Sign, bias=T.lt[:, c:c + 1], scale=-1.0), x_cm)
+
+    on(V, x_cnt)
+    for k in range(2):
+        ts(T.ind[:, P * k:P * k + P - 1], T.cnt[:, 16:P + 15], T.jwb[:, k:k + 1], op.is_le)
+    vw()
+    for k in range(2):
+        a = slice(P * k, P * k + P - 1)
+        scan(T.indc[:, a], T.ind[:, a], T.ind[:, a], op.add, op.max)
+    ts(T.offs[:, :], row16, 0.0, op.mult, fc("u5"), op.add)
+    vw()
+    x_req = new()
+    cp(T.req[:, 0:2], T.indc[:, P - 2:2 * P - 1:P], sig=x_req)
+    on(V, x_acc)
+    ts(T.req[:, 2:3], fc("acc"), 0.5, op.mult, (P - 1) * 0.5, op.add, sig=x_req)
+
+    on(g, x_p8)
+    send(lambda q: T.p8[:, 0:A].bitcast(u8), lambda q: T.pt[:, A * r:A * r + A].bitcast(u8), "ptc")
+    on(g, x_req, 2)
+    tell(T.req[:, :], lambda q: T.rland[:, 3 * seat(q, r):3 * seat(q, r) + 3], "req")
+    iota(T.erow[:, 0:128], [[1, 8], [0, 16]], 0, 0, x_io2)
+    iota(T.erow[:, 128:160], [[-1, 4], [1, 8]], 0, 0, x_io2)
+    iota(im64, [[0, 4], [1, 16]], 0, 0, x_io2)
+    iota(jm8, [[0, 4], [1, 8]], 0, 0, x_io2)
+
+    x_lv, x_tq, x_h1, x_h2, x_wino, x_tno, x_rl, x_ptown = new(), new(), new(), new(), new(), new(), new(), new()
+    on(V, x_cz, 2)
+    cp(T.lw[:, :], T.cnt[:, :].indirect(T.offw[:, :]), sig=x_lv)
+    on(V, x_lt)
+    ts(nsi, T.lt[:, 0:16], float(-P * (r + 1)), op.add)
+    ts(fc("u2"), ic("pmi"), 16.0, op.mult)
+    bits(ic("ogi"), ic("pi"), 4, op.arith_shift_right, 1, op.bitwise_and)
+    ts(ma, dd, 0.0, op.is_gt)
+    ts(mb, dd, 1.0, op.is_equal, 31.0, op.mult)
+    vw()
+    bits(owi, nsi, 8, op.arith_shift_right, NR - 1, op.bitwise_and)
+    on(V, x_tb, 16)
+    quant("tq", 0, P, T.tt[:, :], x_tq)
+    on(V, x_cm, C)
+    on(V, x_r16)
+    on(V, x_r16b)
+    vw()
+    sums(T.rn[:, :], T.cm2[:, :])
+    ts(bs, owi, float(LC), op.mult, -1.0, op.add)
+    ts(lts, T.lt[:, 0:16], float(SH), op.add)
+    bits(ic("t7i"), ic("pi"), 3, op.arith_shift_right, 1, op.bitwise_and)
+    bits(ic("t8i"), ic("pmi"), 2, op.arith_shift_right)
+    bits(ic("t1i"), ic("pmi"), 1, op.bitwise_and)
+    bits(ic("t4i"), ic("pmi"), 7, op.bitwise_and)
+    x_m4a, x_m4 = tt(T.m4[:, 0:16], ma, mb, op.add, sig=new()), new()
+    on(V, x_er2)
+    vw()
+    tt(T.oh2[:, :], T.rn[:, :].indirect(T.offs[:, 0:16]), T.erow2[:, :], op.is_equal)
+    quant("win", WOWN, WOWN + P, T.tt[:, :], x_wino)
+    vw()
+    tt(T.nsz[:, :], lts.indirect(T.offp[:, 0:16]), T.oh2[:, :], op.mult)
+
+    on(Q, x_p8)
+    load(Q, T.pt[:, A * r:A * r + A].bitcast(u8), T.p8[:, 0:A].bitcast(u8), x_ptown)
+    load(Q, T.pts[:, A * r:A * r + A], T.p8s[:, 0:A], x_ptown)
+    on(Q, x_lv)
+    for k in range(8):
+        load(Q, T.dl[:, 16 * k:16 * k + 16], T.lw[16 * k:16 * k + 1, :], x_h1)
+    for k in range(2):
+        s(S.activation(T.ebm[:, 260 * k:260 * k + 260], T.zz[:, 0:260], fn.Identity, bias=0.5), x_eb)
+    for q_ in (S, Q):
+        on(q_, "r_req", EV * len(others))
+        for k in range(8):
+            if (k < 4) == (q_ is S):
+                load(q_, T.reql[16 * k:16 * k + 16, 0:21], T.rland[16 * r:16 * r + 16, 0:21], x_rl)
+    s(S.activation(T.gs[:, GW * E:GW * E + 16], T.zz[:, 0:16], fn.Identity, bias=100.0), x_r8)
+    s(S.activation(T.fb[:, 64:192], T.zz[:, 0:128], fn.Identity, bias=-1.0), x_r8)
+    act(T.fb[:, FW - 4:FW + 8], T.zz[:, 0:12], sig=x_r8)
+    act(T.pp[:, 0:1], T.zz[:, 0:1], sig=x_r8)
+    act(T.pp[:, 8:9], T.zz[:, 0:1])
+    act(T.cm[:, 255:256], T.zz[:, 0:1], sig=x_r8)
+    on(S, x_io2, 4)
+    s(S.activation(T.r8[:, :], jm8, fn.Sign), x_r8)
+    on(Q, x_h1, 128)
+    for k in range(8):
+        load(Q, T.lall[16 * k:16 * k + 16, :], T.dl[:, :], x_h2)
+
+    x_zw, x_vals, x_og, x_vald, x_kown = new(), new(), new(), new(), new()
+    for q_ in (V, S):
+        on(q_, x_tq)
+        on(q_, x_rl, 128)
+    for w in range(2):
+        x_sndc, x_snds = new(), new()
+        c, d = WAVES[w]
+        pick_v(T.snd[:, LC * c:LC * d], T.tq[:, :], T.reql[:, 3 * c:3 * d], x_sndc)
+        pick_s(T.snds[:, LC * c:LC * d], T.tqs[:, :], T.reql[:, 3 * c:3 * d], x_snds)
+        on(g, x_sndc)
+        send(lambda q: T.snd[:, LC * seat(r, q):LC * seat(r, q) + LC].bitcast(u8), lambda q: T.win[:, spot(q):spot(q) + LC].bitcast(u8), "cod%d" % w, wave[w], 4)
+        on(g, x_snds)
+        send(lambda q: T.snds[:, LC * seat(r, q):LC * seat(r, q) + LC], lambda q: T.wins[:, spot(q):spot(q) + LC], "pln%d" % w, wave[w], 4)
+    send(lambda q: T.p8s[:, 0:A], lambda q: T.pts[:, A * r:A * r + A], "pts")
+    on(g, x_eb, 2)
+    g.affine_select(T.eb[:, 0:516], T.ebm[:, 0:516], [[1, 516]], op.is_equal, 0.0, -3, -4).then_inc(T.sem[x_ebd], 1)
+    iota(T.zw[:, :], [[32, DUMP]], 0, 0, x_zw)
+    iota(T.vals[:, :], [[16, 4], [0, 4], [-1, 16]], 16, 0, x_vals)
+
+    on(S, x_m4a)
+    rows(T.m4, 16, 896, x_m4)
+    on(V, x_h2, 128)
+    tt(T.la[:, 0:64], T.lall[:, 0:64], T.lall[:, 64:128], op.add, sig="step")
+    tt(ic("t2i"), ic("pmi"), ic("ggi"), op.add)
+    tt(ic("t3i"), ic("t7i"), ic("ggi"), op.add)
+    cp(fc("u6"), ic("t4i"))
+    pw()
+    tt(T.la[:, 64:96], T.la[:, 0:32], T.la[:, 32:64], op.add, sig="step")
+    vw()
+    ts(fc("u1"), ic("ogi"), -2.0, op.mult, 1.0, op.add)
+    ts(fc("bz"), ic("ggi"), -1.0, op.mult, 9.0, op.add)
+    tt(fc("by"), ic("t4i"), ic("t7i"), op.subtract)
+    pw()
+    tt(T.la[:, 96:112], T.la[:, 64:80], T.la[:, 80:96], op.add, sig="step")
+    vw()
+    ts(fc("bx"), ic("t3i"), -1.0, op.mult, 15.0, op.add)
+    bits(ic("t5i"), ic("t2i"), 7, op.bitwise_and)
+    cp(ic("t6i"), fc("bz"))
+    pw()
+    tt(T.la[:, 112:128], T.la[:, 96:112], bs, op.add)
+    ts(fc("u3"), ic("t1i"), fc("u1"), op.mult, 272.0, op.mult)
+    ts(fc("u4"), ic("ogi"), 256.0, op.mult, fc("u2"), op.add)
+    vw()
+    tt(T.lsm[:, :], T.la[:, 112:128].indirect(T.offp[:, 0:16]), T.oh2[:, :], op.mult, sig="step")
+    ts(T.li[:, 64:68], T.rj[:, 0:8:2], -1.0 / 16, op.mult, fc("bx"), op.add)
+    ts(fc("by"), fc("by"), 16.0, op.mult)
+    bits(ic("t6i"), ic("t6i"), 7, op.bitwise_and)
+    pw()
+    sums(T.lsz[:, :], T.lsm[:, :])
+    ts(fc("bz"), fc("u6"), -16.0, op.mult, 127.0, op.add)
+    vw()
+    x_offc = cp(T.offc[:, :], T.lsz[:, 15:256:16], sig=new())
+    bits(T.li[:, 64:68], T.li[:, 64:68], 7, op.bitwise_and)
+    ts(T.bo[:, 4:8], T.rj[:, 0:8:2], fc("by"), op.is_ge, 2000.0, op.mult)
+    sums(T.nz3[:, :], T.nsz[:, :])
+    on(V, x_m16)
+
+    x_cc, x_cs, x_s = [new(), new()], [new(), new()], [new(), new()]
+    for w in range(2):
+        on(V, "r_cod%d" % w, 4 * len(wave[w]))
+        on(S, "r_pln%d" % w, 4 * len(wave[w]))
+    for q_ in (V, S):
+        on(q_, x_offc)
+        on(q_, x_wino)
+    on(M, x_p8)
+    for h in range(2):
+        a = slice(128 * h, 128 * h + 128)
+        pick_v(T.cand[:, a], T.win[:, :], T.offc[:, 8 * h:8 * h + 8], x_cc[h])
+        pick_s(T.cands[:, a], T.wins[:, :], T.offc[:, 8 * h:8 * h + 8], x_cs[h])
+        on(M, x_cc[h])
+        on(M, x_cs[h])
+        M.matmul_mx(T.ps[:, 512 * h:512 * h + 128], T.p8[:, :], T.p8s[:, :], T.cand[:, a], T.cands[:, a], True, True).then_inc(T.sem[x_s[h]], 1)
+    vw()
+    ts(T.bo[:, 0:4], T.li[:, 64:68], float(GW), op.mult, fc("bz"), op.add)
+    ts(T.ofx[:, 0:C - 4], T.rj[:, 18:30], fc("pm"), op.add)
+    ts(T.ofx[:, 16:32], row16, 15.0, op.add)
+    ts(fc("th0"), fc("pm"), 14.5, op.is_lt, 15.5, op.mult)
+    ts(fc("u7"), ic("t8i"), -8.0, op.mult, 28.0, op.add)
+    for h in range(2):
+        a = slice(128 * h, 128 * h + 128)
+        on(V, x_s[h])
+        tt(T.sm[:, a], T.ps[:, 512 * h:512 * h + 128], T.m16[:, a], op.mult, sig=None if h else "step")
+    x_n1, x_rep, x_sz = new(), new(), new()
+    pw()
+    sums(T.sz[:, 0:128], T.sm[:, 0:128], sig=x_sz)
+    vw()
+    sums(T.sz[:, 128:256], T.sm[:, 128:256], sig=x_sz)
+    sv = T.sz[:, 15:256:16]
+    on(S, x_sz, 2)
+    s(S.activation(T.n1[:, :], sv, fn.Abs, bias=2.0 ** -115, scale=2.0 ** -24 * 1.0625), x_n1)
+    pick_s(T.rep[:, 0:16 * (C - 4)], T.sz[:, :], T.ofx[:, 18:30], x_rep)
+    on(V, x_sz, 2)
+    cp(T.sn[:, 0:16], sv)
+    on(V, x_r8, 6)
+    ts(T.cm[:, 0:16], sv, T.sz[:, 15:16], op.is_gt)
+    ts(T.cm[:, 240:255], T.sz[:, 15:240:16], T.sz[:, 255:256], op.is_ge)
+    on(V, x_n1)
+    tt(T.sn[:, 16:32], sv, T.n1[:, :], op.add)
+    ts(fc("thr"), fc("th0"), 0.5, op.add)
+    vw()
+    for c in (1, 14):
+        ts(T.cm[:, 16 * c:16 * c + 16], T.sn[:, c:c + 16], T.sn[:, c:c + 1], op.is_gt)
+    on(V, x_rep)
+    tt(T.cm[:, 32:224], T.sn[:, :].indirect(T.ofx[:, 0:C - 4]), T.rep[:, 0:16 * (C - 4)], op.is_gt)
+    vw()
+    sums(T.rk[:, :], T.cm[:, :])
+    ts(rot, ic("t5i"), 16.0, op.mult, 15.0, op.add)
+    tt(T.bo[:, 8:12], T.bo[:, 0:4], T.bo[:, 4:8], op.add)
+    on(V, x_io2, 4)
+    vw()
+    tt(T.oh[:, :], T.rk[:, :].indirect(T.offs[:, 0:8]), T.erow[:, 0:128], op.is_equal); vw()
+    tt(T.lm[:, :], T.lsz[:, :].indirect(T.offs[:, 0:8]), T.oh[:, :], op.mult, sig="step")
+    tt(T.ss[:, :], T.sz[:, :].indirect(T.offs[:, 0:8]), T.oh[:, :], op.mult)
+    pw()
+    sums(T.lz[:, :], T.lm[:, :], sig="step")
+    ts(offn, T.rj[:, 0:2], 0.0, op.mult, fc("u6"), op.add)
+    ts(offg, T.bo[:, 8:12], float(GW * E), op.min)
+    pw()
+    x_offr, x_offs, x_kc, x_ks = new(), new(), [new(), new()], [new(), new()]
+    cp(T.offr[:, 0:8], T.lz[:, 15:128:16], sig=x_offr)
+    cp(T.offr[:, 8:16], T.lz[:, 15:128:16], sig=x_offs)
+    for q_ in (V, S):
+        on(q_, x_offr)
+    on(Q, x_offr)
+    load(Q, T.tn[:, 0:P].bitcast(u8), T.tq[:, :].bitcast(u8), x_tno)
+    load(Q, T.tns[:, 0:P], T.tqs[:, :], x_tno)
+    for k, a, b in ((0, 0, 8), (1, 8, 15)):
+        pick_v(T.pk[:, 16 * a:16 * b], T.win[:, :], T.offr[:, a:b], x_kc[k])
+        pick_s(T.pks[:, 16 * a:16 * b], T.wins[:, :], T.offr[:, a:b], x_ks[k])
+        if k == 0:
+            for q_ in (V, S):
+                on(q_, x_offs)
+    x_g = []
+    for t in range(E):
+        if t < 2:
+            on(M, x_kc[t])
+            on(M, x_ks[t])
+        a = slice(16 * t, 16 * t + 128)
+        x_g.append(new())
+        M.matmul_mx(T.ps[:, 512 * t:512 * t + 128], T.pk[:, a], T.pks[:, a], T.pk[:, 0:128], T.pks[:, 0:128], True, True).then_inc(T.sem[x_g[t]], 1)
+    vw()
+    sums(T.ssz[:, :], T.ss[:, :])
+    ts(fc("og64"), ic("ogi"), 64.0, op.mult, sig=x_og)
+    ts(offf, ic("t6i"), float(GW), op.mult, 15.0, op.add)
+    vw()
+    x_sr = cp(T.sr[:, :], T.ssz[:, :].indirect(rot), sig=new())
+    x_gd = [new(), new(), new()]
+    x_un = [new(), new()]
+    for q_ in (V, S):
+        on(q_, x_sr)
+    for t in range(E):
+        o, a, b = T.gb[:, GW * t:GW * t + GW], T.ps[:, 512 * t:512 * t + GW], T.sr[:, t:t + 1]
+        k = max(t // 2 - 1, 0)
+        if t % 2:
+            on(S, x_g[t])
+            s(S.activation(o, a, fn.Sign, bias=b, scale=-1.0), x_gd[k])
+        else:
+            on(V, x_g[t])
+            ts(o, a, b, op.is_lt, sig=x_gd[k])
+        if t in (3, 5, 7):
+            a = 0 if t == 3 else t - 1
+            on(V, x_m4)
+            on(V, x_gd[k], t + 1 - a)
+            a = slice(GW * a, GW * t + GW)
+            scan(T.gs[:, a], T.m4[:, a], T.gb[:, a], op.mult, op.add)
+    c0 = 32 + SH + P * r
+    act(T.cl[:, c0 - 16:c0 + 272], T.zz[:, 0:288], sig=x_cl)
+    act(T.ptd[:, NR * A:4 * PW:PW], T.zz[:, 0:4], sig=x_un[0])
+    on(S, x_vals)
+    on(S, x_og)
+    s(S.activation(T.vald[:, :], T.vals[:, :], fn.Identity, bias=fc("og64")), x_vald)
+    ts(fc("pm8"), fc("pm"), -8.0, op.add)
+    ts(fc("u8"), ic("ogi"), -16.0, op.mult, fc("pm"), op.add)
+    vw()
+    v(V.tensor_scalar(T.fb[:, FW - 20:FW - 4], T.gs[:, :].indirect(offf), fc("thr"), None, op.is_lt), "prune")
+    v(V.tensor_scalar(T.fb[:, 64:192:2], T.gs[:, :].indirect(offg), fc("thr"), None, op.is_lt), "prune")
+    tt(T.nm[:, :], T.nz3[:, :].indirect(T.offs[:, 0:8]), T.oh[:, :], op.mult)
+
+    def fl(b):
+        return T.fb[:, FW - 4 * b - 1:FW - 4 * b]
+    for b in range(2, E):
+        on(V, "prune", b)
+        e, n = FW - 4 * b, 2 * b + 3
+        scan(T.fb[:, e - n:e], T.fb[:, e + 1:e + 1 + 2 * n:2], T.fb[:, 192 - 18 * b:192 - 18 * b + n], op.subtract, op.max, sig="prune")
+        if b == 2:
+            ts(T.of3[:, 18:19], fc("u6"), 16.0, op.mult, 15.0, op.add)
+        if b == 3:
+            vw()
+            sums(T.nz[:, :], T.nm[:, :])
+        if b == 4:
+            ts(T.of3[:, 19:20], fc("u6"), 16.0, op.mult, 15.0, op.add)
+        if b == 5:
+            ts(T.dumpc[:, :], T.rj[:, 32:36], float(DUMP), op.add)
+    x_pp = new()
+    for b in range(1, E - 1):
+        on(S, "prune", b + 1)
+        sw()
+        s(S.activation(T.pp[:, 8 + b:9 + b], fl(b), fn.Identity, bias=T.pp[:, 7 + b:8 + b]), x_pp if b == E - 2 else None)
+        s(S.activation(T.pp[:, b:b + 1], fl(b), fn.Identity, bias=T.pp[:, 7 + b:8 + b], scale=101.0), x_pp)
+    on(V, "prune", E)
+    on(V, x_pp, E - 1)
+    ts(T.pp[:, 7:8], fl(7), 101.0, op.mult, T.pp[:, 14:15], op.add); vw()
+    tt(T.kh[:, :], T.pp[:, 0:8].indirect(offn), T.erow[:, 128:160], op.is_equal); vw()
+    tt(T.km[:, 0:32], T.nz[:, :].indirect(offz), T.kh[:, :], op.mult); vw()
+    scan(T.km[:, 32:64], T.r8[:, :], T.km[:, 0:32], op.mult, op.add); vw()
+    k1 = T.km[:, 39:64:8]
+    cp(T.kl0[:, :], k1)
+    ts(T.dm[:, 0:4], k1, 32.0, op.mult, fc("pm8"), op.add)
+    ts(T.kd[:, 0:4], k1, 0.0, op.is_equal, 1e9, op.mult)
+    x_zr, x_dz = new(), new()
+    on(V, x_zw)
+    vw()
+    tt(T.zrow[:, :], T.zw[:, :].indirect(T.kl0[:, 0:4]), im64, op.add, sig=x_zr)
+    ts(T.kd[:, 4:8], T.kd[:, 0:4], 7.5, op.max); vw()
+    on(S, x_zr)
+    on(V, x_zr)
+    for k in range(KP):
+        o = T.dz[:, 64 * k:64 * k + 64]
+        if k < 2:
+            ts(o, T.zrow[:, :], T.dm[:, k:k + 1], op.subtract)
+        else:
+            s(S.activation(o, T.zrow[:, :], fn.Identity, bias=T.dm[:, k:k + 1], scale=-1.0), x_dz)
+    vw()
+    for k in range(KP):
+        if k == 2:
+            on(V, x_dz, 2)
+        v(V.tensor_reduce(T.dm[:, 4 + k:5 + k], T.dz[:, 64 * k:64 * k + 64], X, op.min, apply_absolute_value=True))
+    vw()
+    tt(T.kd[:, 8:12], T.dm[:, 4:8], T.kd[:, 4:8], op.is_lt); vw()
+    x_km = new()
+    for k in range(KP):
+        ts(T.kmsg[:, k:k + 1], T.kd[:, 8 + k:9 + k], T.dumpc[:, k:k + 1], op.mult, T.km[:, 39 + 8 * k:40 + 8 * k], op.max, sig=x_km)
+    on(g, x_km, KP)
+    tell(T.kmsg[:, :], lambda q: T.kland[:, 4 * r:4 * r + 4], "kept")
+    on(Q, x_km, KP)
+    load(Q, T.kland[:, 4 * r:4 * r + 4], T.kmsg[:, :], x_kown)
+
+    x_eq, x_wq, x_y, x_ysb, x_yo, x_st = new(), new(), new(), new(), new(), new()
+
+    def tile(b):
+        quant("eq", 128 * b, 128 * b + 128, T.eb[:, 3 - b:515 - b], x_eq)
+    fill(T.kf[:, :], 0.0)
+    ts(psel, fc("u7"), fc("u8"), op.add)
+    ts(tl, fc("u3"), fc("u4"), op.add, 1.0 / 32, op.mult)
+    ts(T.cw[:, 0:8], T.rj[:, 32:40], -128.0, op.add)
+    fill(T.ysb[:, 128:144], 0.0)
+    on(V, x_w, 16)
+    quant("wq", 0, 128, T.wt[:, :], x_wq)
+    on(V, x_ebd)
+    vw()
+    ts(T.kf[:, 0:4], k1, float(-SH), op.add, -1.0, op.max)
+    tt(T.ky[:, 0:32], T.cw[:, 0:8].indirect(offn), T.kh[:, :], op.mult)
+    tile(0)
+    tile(1)
+    vw()
+    x_kt = v(V.transpose(T.kt[0:32, :], T.kf[0:32, :]), new())
+    scan(T.ky[:, 32:64], T.r8[:, :], T.ky[:, 0:32], op.mult, op.add)
+    tile(2)
+    vw()
+    ts(T.of3[:, 8:16:2], T.ky[:, 39:64:8], 128.0, op.add)
+    tile(3)
+    vw()
+    for k in range(3):
+        on(M, x_gd[k], 4 if k == 0 else 2)
+    on(M, x_wq)
+    M.matmul_mx(T.ps[:, 0:128], T.wq[:, :], T.wqs[:, :], T.pk[:, 0:128], T.pks[:, 0:128], True, True).then_inc(T.sem[x_y], 1)
+    x_up, x_ut = [new() for b in range(4)], [new() for b in range(4)]
+    on(S, x_y)
+    act(T.ysb[:, 0:128], T.ps[:, 0:128], sig=x_ysb)
+    on(M, x_eq, 4)
+    on(M, x_tq)
+    on(M, x_ptown, 32)
+    on(M, "r_ptc", ALL)
+    on(M, "r_pts", ALL)
+    for b in range(4):
+        e = slice(128 * b, 128 * b + 128)
+        M.matmul_mx(T.ps[:, 2048 + 512 * b:2176 + 512 * b], T.eq[:, e], T.eqs[:, e], T.pt[:, :], T.pts[:, :], True, True).then_inc(T.sem[x_up[b]], 1)
+        if b == 0:
+            on(M, x_ysb)
+        M.matmul_mx(T.ps[:, 512 * b:512 * b + P], T.eq[:, e], T.eqs[:, e], T.tq[:, :], T.tqs[:, :], True, True).then_inc(T.sem[x_ut[b]], 1)
+        on(S, x_up[b])
+        act(T.ptd[:, PW * b:PW * b + NR * A], T.ps[:, 2048 + 512 * b:2176 + 512 * b], sig=x_un[b] if b < 2 else None)
+        if b < 2:
+            on(S, x_ut[b])
+            act(T.tbd[:, P * b:P * b + P], T.ps[:, 512 * b:512 * b + P], sig=x_un[b])
+    on(Q, x_kt)
+    load(Q, T.kp[:, :], T.kt[0:4, 0:16], x_st)
+    on(Q, x_yo, KP)
+    load(Q, T.y[:, :], T.yo[:, :], x_st)
+
+    on(V, x_vald)
+    on(V, x_cl)
+    on(V, x_kown, 16)
+    on(V, "r_kept", EV * len(others))
+    cp(klf, T.kland[:, :]); vw()
+    cp(T.okl[:, :], klf.indirect(psel)); vw()
+    for i in range(NR // 2):
+        cp(T.cl[:, 32:32 + CLW].indirect(T.okl[:, 4 * i:4 * i + 4]), T.vald[:, 64 * i:64 * i + 64], sig="claim")
+        if i == 0:
+            on(V, x_ysb)
+        v(V.tensor_copy(T.yo[:, i:64:4], T.ysb[:, :].indirect(T.of3[:, 8 + 2 * i:9 + 2 * i])), x_yo)
+        on(V, "claim", i + 1)
+    v(V.transpose(T.ttc[:, 0:256], T.cl[:, c0:c0 + 256]))
+    v(V.transpose(T.ttc[:, 256:544], T.cl[:, c0 - 16:c0 + 272])); vw()
+    tt(ub, T.ttc[:, 0:544:32], T.ttc[:, 16:544:32], op.max); vw()
+    x_new, x_oc, x_os, x_st2, x_gp = new(), [new(), new()], new(), new(), [new(), new()]
+    x_ptl = ts(T.ptl[:, :], ub.indirect(tl), -1.0, op.mult, float(NR * A), op.add, sig=new())
+    sw()
+    on(S, x_un[0], 3)
+    on(S, x_ptl)
+    for b in (2, 3):
+        pick_s(T.gp[:, P * b - 2 * P:P * b - P], T.ptd[:, PW * b:PW * b + PW], T.ptl[:, 0:16], x_gp[b - 2])
+    on(V, x_un[0], 3)
+    on(V, x_ptl)
+    ts(T.sel[:, 0:16], T.ptl[:, :], NR * A - 0.5, op.is_lt, float(P), op.mult)
+    for b in range(4):
+        o = T.bb[:, b:1024:4]
+        if b < 2:
+            if b == 1:
+                on(V, x_un[1], 2)
+            tt(o, T.ptd[:, PW * b:PW * b + PW].indirect(T.ptl[:, 0:16]), T.tbd[:, P * b:P * b + P], op.add)
+        else:
+            on(V, x_ut[b])
+            on(V, x_gp[b - 2])
+            tt(o, T.gp[:, P * b - 2 * P:P * b - P], T.ps[:, 512 * b:512 * b + P], op.add)
+        if b == 0:
+            vw()
+        if b == 1:
+            tt(T.sel[:, 16:32], T.sel[:, 0:16], jw, op.add)
+    vw()
+    quant("tn", P, 2 * P, T.bb[:, :], x_new)
+    x_sel = cp(T.sell[:, :], T.sel[:, 16:32], sig=new())
+    for q_ in (V, S):
+        on(q_, x_tno, 32)
+        on(q_, x_sel)
+        on(q_, x_new)
+    pick_s(T.ocqs[:, :], T.tns[:, :], T.sell[:, 0:16], x_os)
+    for h in range(2):
+        a = slice(128 * h, 128 * h + 128)
+        pick_v(T.ocq[:, a], T.tn[:, :], T.sell[:, 8 * h:8 * h + 8], x_oc[h])
+        on(Q, x_oc[h])
+        load(Q, T.oc[:, 512 * h:512 * h + 512], T.ocq[:, a].bitcast(u8), x_st)
+    on(S, x_os)
+    for k in range(4):
+        load(S, T.osc[4 * k:4 * k + 4, :], T.ocqs[32 * k:32 * k + 4, :], x_st2)
+    on(Q, x_st, 64)
+    on(S, x_st2, 64)
+    on(V, "v", vn[0])
+    on(S, "s", sn_[0])
+    for n in ROADS:
+        on(g, "l_" + n, 4 * len(wave[int(n[-1])]) if n[-1] in "01" else EV if n in ("req", "kept") else ALL)

@@ -4,12 +4,16 @@ from concourse.mybir import dt, AluOpType, AxisListType, ActivationFunctionType
 NR, P, A, C, E, KP, LC = 8, 256, 16, 16, 8, 4, 48
 WOWN = (NR - 1) * LC
 SH = 16
-DUMP = NR * P + SH
-CLW = DUMP + KP * A
+ZW = NR * P + SH
+DL = 4096.0
+DUMP = 7 * 4096
+SHB = DUMP + KP * A
+CLW = KP * A + NR * P + 16
 GW = 16 * (E - 1)
 S0 = P * (NR - 1)
 FW = 48
 PW = NR * A + 16
+R0, R1 = 3, 14
 ORDER = (1, 4, 2, 5, 3, 6, 7)
 WAVES = ((0, 4), (4, 7))
 
@@ -19,21 +23,21 @@ SB = {
     "cnt": (P + 32, B), "ind": (2 * P, B), "indc": (2 * P, B), "junk": (P, B), "req": (3, U), "rland": (24, U), "reql": (24, U), "rj": (48, F),
     "jwb": (2, B), "dumpc": (4, F), "imj": (96, F), "r8": (32, F), "tro": (8, U), "of3": (24, U), "ofx": (32, U),
     "offs": (16, U), "offp": (16, U), "cf": (96, F), "li": (68, I), "m16": (256, B), "m4": (896, B),
-    "r16": (256, B), "zw": (DUMP, F), "vals": (256, B), "vald": (256, B), "erow": (160, F), "erow2": (256, F),
+    "r16": (256, B), "sg": (256, B), "zw": (ZW, F), "vals": (64, B), "vald": (64, B), "erow": (160, F), "erow2": (256, F),
     "lf": (32, F), "lt": (32, F), "cm2": (256, B), "rn": (256, B), "oh2": (256, F), "nsz": (256, F), "nz3": (256, F),
     "offw": (16, U), "lw": (256, B), "lall": (128, B), "la": (128, F), "lsm": (256, F), "lsz": (256, F), "offc": (16, U),
-    "sm": (256, F), "sz": (256, F), "sn": (32, F), "n1": (16, F), "rep": (256, F), "cm": (256, B), "rk": (256, B), "oh": (128, F), "lm": (128, F),
+    "sm": (256, F), "sz": (256, F), "rep": (256, F), "cm": (256, B), "rk": (256, B), "oh": (128, F), "lm": (128, F),
     "lz": (128, F), "offr": (16, U), "ss": (128, F), "ssz": (128, F), "sr": (16, F), "nm": (128, F), "nz": (128, F), "gb": (896, B),
     "gs": (912, B), "fb": (192, F), "pp": (40, F), "bo": (20, F), "kh": (32, F), "km": (64, F), "ky": (64, F),
     "kf": (32, F), "kt": (32, F), "kd": (16, F), "kl0": (4, U), "zrow": (64, F), "dz": (256, F), "dm": (8, F), "kmsg": (4, U),
-    "kland": (32, U), "kc": (32, F), "okl": (16, U), "ysb": (144, F), "yo": (64, F),
-    "xt": (512, B), "wt": (512, B), "tt": (1024, B), "ebm": (520, B), "eb": (520, B), "cl": (2176, B), "ttc": (544, B), "cw": (16, F),
+    "kland": (32, U), "kc": (32, F), "okl": (16, U), "ysb": (144, F), "yo": (64, F), "mx": (80, F),
+    "xt": (512, B), "wt": (512, B), "tt": (1024, B), "ebm": (520, B), "eb": (520, B), "cl": (CLW, B), "ttc": (544, B), "cw": (16, F),
     "ptd": (4 * PW, B), "tbd": (2 * P, B), "gp": (2 * P, B), "ptl": (16, U), "sel": (32, F), "sell": (16, U), "bb": (1024, B),
 }
 CODES = {"p8": 128, "wq": 128, "tq": 256, "win": 592, "tn": 512, "snd": 336, "cand": 256, "pk": 240, "eq": 512, "pt": 128, "ocq": 256}
-ICOL = {n: i for i, n in enumerate(["pi", "pmi", "ggi", "ogi", "t1i", "t2i", "t3i", "t4i", "t5i", "t6i", "t7i", "t8i"])}
+ICOL = {n: i for i, n in enumerate(["pi", "pmi", "ggi", "ogi", "t1i", "t2i", "t3i", "t4i", "t5i", "t6i", "t7i"])}
 FCOL = {n: i for i, n in enumerate(["pm", "u1", "u2", "u3", "u4", "thr", "pm8", "th0", "u5", "u6", "isr", "hneg",
-                                    "u7", "u8", "og64", "sb", "acc", "bx", "by", "bz"])}
+                                    "g4", "c7", "g16", "sb", "acc", "bx", "by", "bz", "n7"])}
 
 SCRATCH = {n: ("sbuf", [128, k], d) for n, (k, d) in SB.items()}
 SCRATCH["dl"] = ("dram", [16, 128], B)
@@ -185,6 +189,7 @@ def rank_program(g, core, T, topo):
     rot, psel, tl = T.tro[:, 2:3], T.tro[:, 4:5], T.tro[:, 0:1]
     offn, offg, offf, offz = T.of3[:, 0:2], T.of3[:, 4:8], T.of3[:, 16:17], T.of3[:, 18:20]
     klf, ub = T.kc[:, 0:32], T.pp[:, 16:33]
+    NM = R1 - R0
 
     x_cd, x_x, x_tb, x_w = new(), new(), new(), new()
     for k in range(8):
@@ -301,12 +306,13 @@ def rank_program(g, core, T, topo):
     send(lambda q: T.p8[:, 0:A].bitcast(u8), lambda q: T.pt[:, A * r:A * r + A].bitcast(u8), "ptc")
     on(g, x_req, 2)
     tell(T.req[:, :], lambda q: T.rland[:, 3 * seat(q, r):3 * seat(q, r) + 3], "req")
-    iota(T.erow[:, 0:128], [[1, 8], [0, 16]], 0, 0, x_io2)
+    iota(T.erow[:, 0:128], [[-1, 8], [-1, 16]], C, 0, x_io2)
     iota(T.erow[:, 128:160], [[-1, 4], [1, 8]], 0, 0, x_io2)
     iota(im64, [[0, 4], [1, 16]], 0, 0, x_io2)
     iota(jm8, [[0, 4], [1, 8]], 0, 0, x_io2)
 
     x_lv, x_tq, x_h1, x_h2, x_wino, x_tno, x_rl, x_ptown = new(), new(), new(), new(), new(), new(), new(), new()
+    x_zw, x_vals, x_og, x_vald, x_kown, x_sg = new(), new(), new(), new(), new(), new()
     on(V, x_cz, 2)
     cp(T.lw[:, :], T.cnt[:, :].indirect(T.offw[:, :]), sig=x_lv)
     on(V, x_lt)
@@ -325,9 +331,9 @@ def rank_program(g, core, T, topo):
     vw()
     sums(T.rn[:, :], T.cm2[:, :])
     ts(bs, owi, float(LC), op.mult, -1.0, op.add)
-    ts(lts, T.lt[:, 0:16], float(SH), op.add)
+    ts(lts, T.lt[:, 0:16], float(SHB), op.add)
     bits(ic("t7i"), ic("pi"), 3, op.arith_shift_right, 1, op.bitwise_and)
-    bits(ic("t8i"), ic("pmi"), 2, op.arith_shift_right)
+    ts(fc("th0"), fc("pm"), 14.5, op.is_lt, 15.5, op.mult)
     bits(ic("t1i"), ic("pmi"), 1, op.bitwise_and)
     bits(ic("t4i"), ic("pmi"), 7, op.bitwise_and)
     x_m4a, x_m4 = tt(T.m4[:, 0:16], ma, mb, op.add, sig=new()), new()
@@ -337,6 +343,10 @@ def rank_program(g, core, T, topo):
     quant("win", WOWN, WOWN + P, T.tt[:, :], x_wino)
     vw()
     tt(T.nsz[:, :], lts.indirect(T.offp[:, 0:16]), T.oh2[:, :], op.mult)
+    ts(T.ofx[:, 0:NM], T.rj[:, R0:R1], fc("u2"), op.min, 15.0, op.add)
+    ts(T.ofx[:, 16:16 + NM], T.rj[:, R0:R1], fc("u2"), op.max, 15.0, op.add)
+    ts(fc("g16"), ic("ggi"), -16.0, op.mult, sig=x_og)
+    ts(fc("pm8"), fc("pm"), DL, op.mult, -DL * (8 + 32 * (SHB - SH)), op.add)
 
     on(Q, x_p8)
     load(Q, T.pt[:, A * r:A * r + A].bitcast(u8), T.p8[:, 0:A].bitcast(u8), x_ptown)
@@ -356,14 +366,12 @@ def rank_program(g, core, T, topo):
     act(T.fb[:, FW - 4:FW + 8], T.zz[:, 0:12], sig=x_r8)
     act(T.pp[:, 0:1], T.zz[:, 0:1], sig=x_r8)
     act(T.pp[:, 8:9], T.zz[:, 0:1])
-    act(T.cm[:, 255:256], T.zz[:, 0:1], sig=x_r8)
     on(S, x_io2, 4)
     s(S.activation(T.r8[:, :], jm8, fn.Sign), x_r8)
     on(Q, x_h1, 128)
     for k in range(8):
         load(Q, T.lall[16 * k:16 * k + 16, :], T.dl[:, :], x_h2)
 
-    x_zw, x_vals, x_og, x_vald, x_kown = new(), new(), new(), new(), new()
     for q_ in (V, S):
         on(q_, x_tq)
         on(q_, x_rl, 128)
@@ -377,10 +385,13 @@ def rank_program(g, core, T, topo):
         on(g, x_snds)
         send(lambda q: T.snds[:, LC * seat(r, q):LC * seat(r, q) + LC], lambda q: T.wins[:, spot(q):spot(q) + LC], "pln%d" % w, wave[w], 4)
     send(lambda q: T.p8s[:, 0:A], lambda q: T.pts[:, A * r:A * r + A], "pts")
+    on(g, x_r16)
+    on(g, x_r16b)
+    g.affine_select(T.sg[:, :], T.r16[:, :], [[1, 16], [-1, 16]], op.not_equal, -1.0, 0, 0).then_inc(T.sem[x_sg], 1)
     on(g, x_eb, 2)
     g.affine_select(T.eb[:, 0:516], T.ebm[:, 0:516], [[1, 516]], op.is_equal, 0.0, -3, -4).then_inc(T.sem[x_ebd], 1)
-    iota(T.zw[:, :], [[32, DUMP]], 0, 0, x_zw)
-    iota(T.vals[:, :], [[16, 4], [0, 4], [-1, 16]], 16, 0, x_vals)
+    iota(T.zw[:, :], [[32, ZW]], 0, 0, x_zw)
+    iota(T.vals[:, :], [[0, 4], [-1, 16]], NR * A, 0, x_vals)
 
     on(S, x_m4a)
     rows(T.m4, 16, 896, x_m4)
@@ -437,49 +448,44 @@ def rank_program(g, core, T, topo):
         M.matmul_mx(T.ps[:, 512 * h:512 * h + 128], T.p8[:, :], T.p8s[:, :], T.cand[:, a], T.cands[:, a], True, True).then_inc(T.sem[x_s[h]], 1)
     vw()
     ts(T.bo[:, 0:4], T.li[:, 64:68], float(GW), op.mult, fc("bz"), op.add)
-    ts(T.ofx[:, 0:C - 4], T.rj[:, 18:30], fc("pm"), op.add)
-    ts(T.ofx[:, 16:32], row16, 15.0, op.add)
-    ts(fc("th0"), fc("pm"), 14.5, op.is_lt, 15.5, op.mult)
-    ts(fc("u7"), ic("t8i"), -8.0, op.mult, 28.0, op.add)
-    for h in range(2):
-        a = slice(128 * h, 128 * h + 128)
-        on(V, x_s[h])
-        tt(T.sm[:, a], T.ps[:, 512 * h:512 * h + 128], T.m16[:, a], op.mult, sig=None if h else "step")
-    x_n1, x_rep, x_sz = new(), new(), new()
+    x_rep, x_sz = new(), new()
+    on(V, x_s[0])
+    tt(T.sm[:, 0:128], T.ps[:, 0:128], T.m16[:, 0:128], op.mult, sig="step")
+    on(V, x_s[1])
+    tt(T.sm[:, 128:256], T.ps[:, 512:640], T.m16[:, 128:256], op.mult)
     pw()
     sums(T.sz[:, 0:128], T.sm[:, 0:128], sig=x_sz)
     vw()
     sums(T.sz[:, 128:256], T.sm[:, 128:256], sig=x_sz)
-    sv = T.sz[:, 15:256:16]
-    on(S, x_sz, 2)
-    s(S.activation(T.n1[:, :], sv, fn.Abs, bias=2.0 ** -115, scale=2.0 ** -24 * 1.0625), x_n1)
-    pick_s(T.rep[:, 0:16 * (C - 4)], T.sz[:, :], T.ofx[:, 18:30], x_rep)
-    on(V, x_sz, 2)
-    cp(T.sn[:, 0:16], sv)
-    on(V, x_r8, 6)
-    ts(T.cm[:, 0:16], sv, T.sz[:, 15:16], op.is_gt)
-    ts(T.cm[:, 240:255], T.sz[:, 15:240:16], T.sz[:, 255:256], op.is_ge)
-    on(V, x_n1)
-    tt(T.sn[:, 16:32], sv, T.n1[:, :], op.add)
-    ts(fc("thr"), fc("th0"), 0.5, op.add)
-    vw()
-    for c in (1, 14):
-        ts(T.cm[:, 16 * c:16 * c + 16], T.sn[:, c:c + 16], T.sn[:, c:c + 1], op.is_gt)
-    on(V, x_rep)
-    tt(T.cm[:, 32:224], T.sn[:, :].indirect(T.ofx[:, 0:C - 4]), T.rep[:, 0:16 * (C - 4)], op.is_gt)
-    vw()
-    sums(T.rk[:, :], T.cm[:, :])
-    ts(rot, ic("t5i"), 16.0, op.mult, 15.0, op.add)
     tt(T.bo[:, 8:12], T.bo[:, 0:4], T.bo[:, 4:8], op.add)
+    on(S, x_sz, 2)
+    pick_s(T.rep[:, 0:16 * NM], T.sz[:, :], T.ofx[:, 16:16 + NM], x_rep)
+    on(V, x_sz, 2)
+    for c in list(range(R0)) + list(range(R1, C)):
+        me = T.sz[:, 16 * c + 15:16 * c + 16]
+        n = c + 1 if c else 0
+        if n:
+            ts(T.cm[:, 16 * c:16 * c + n], T.sz[:, 15:16 * n:16], me, op.is_ge)
+        if n < C:
+            ts(T.cm[:, 16 * c + n:16 * c + 16], T.sz[:, 16 * n + 15:256:16], me, op.is_le)
+    on(V, x_rep)
+    tt(T.cm[:, 16 * R0:16 * R1], T.sz[:, :].indirect(T.ofx[:, 0:NM]), T.rep[:, 0:16 * NM], op.is_ge)
+    on(V, x_r8, 5)
+    on(V, x_sg)
+    vw()
+    scan(T.rk[:, :], T.sg[:, :], T.cm[:, :], op.mult, op.add)
+    ts(rot, ic("t5i"), 16.0, op.mult, 15.0, op.add)
     on(V, x_io2, 4)
     vw()
-    tt(T.oh[:, :], T.rk[:, :].indirect(T.offs[:, 0:8]), T.erow[:, 0:128], op.is_equal); vw()
+    tt(T.oh[:, :], T.rk[:, :].indirect(T.offs[:, 0:8]), T.erow[:, 0:128], op.is_equal)
+    ts(offg, T.bo[:, 8:12], float(GW * E), op.min)
+    vw()
     tt(T.lm[:, :], T.lsz[:, :].indirect(T.offs[:, 0:8]), T.oh[:, :], op.mult, sig="step")
     tt(T.ss[:, :], T.sz[:, :].indirect(T.offs[:, 0:8]), T.oh[:, :], op.mult)
     pw()
     sums(T.lz[:, :], T.lm[:, :], sig="step")
-    ts(offn, T.rj[:, 0:2], 0.0, op.mult, fc("u6"), op.add)
-    ts(offg, T.bo[:, 8:12], float(GW * E), op.min)
+    vw()
+    sums(T.ssz[:, :], T.ss[:, :])
     pw()
     x_offr, x_offs, x_kc, x_ks = new(), new(), [new(), new()], [new(), new()]
     cp(T.offr[:, 0:8], T.lz[:, 15:128:16], sig=x_offr)
@@ -504,11 +510,9 @@ def rank_program(g, core, T, topo):
         x_g.append(new())
         M.matmul_mx(T.ps[:, 512 * t:512 * t + 128], T.pk[:, a], T.pks[:, a], T.pk[:, 0:128], T.pks[:, 0:128], True, True).then_inc(T.sem[x_g[t]], 1)
     vw()
-    sums(T.ssz[:, :], T.ss[:, :])
-    ts(fc("og64"), ic("ogi"), 64.0, op.mult, sig=x_og)
-    ts(offf, ic("t6i"), float(GW), op.mult, 15.0, op.add)
-    vw()
     x_sr = cp(T.sr[:, :], T.ssz[:, :].indirect(rot), sig=new())
+    ts(offf, ic("t6i"), float(GW), op.mult, 15.0, op.add)
+    ts(fc("thr"), fc("th0"), 0.5, op.add)
     x_gd = [new(), new(), new()]
     x_un = [new(), new()]
     for q_ in (V, S):
@@ -528,18 +532,17 @@ def rank_program(g, core, T, topo):
             on(V, x_gd[k], t + 1 - a)
             a = slice(GW * a, GW * t + GW)
             scan(T.gs[:, a], T.m4[:, a], T.gb[:, a], op.mult, op.add)
-    c0 = 32 + SH + P * r
+    c0 = KP * A + P * r
     act(T.cl[:, c0 - 16:c0 + 272], T.zz[:, 0:288], sig=x_cl)
     act(T.ptd[:, NR * A:4 * PW:PW], T.zz[:, 0:4], sig=x_un[0])
     on(S, x_vals)
     on(S, x_og)
-    s(S.activation(T.vald[:, :], T.vals[:, :], fn.Identity, bias=fc("og64")), x_vald)
-    ts(fc("pm8"), fc("pm"), -8.0, op.add)
-    ts(fc("u8"), ic("ogi"), -16.0, op.mult, fc("pm"), op.add)
+    s(S.activation(T.vald[:, :], T.vals[:, :], fn.Identity, bias=fc("g16")), x_vald)
+    ts(offn, T.rj[:, 0:2], 0.0, op.mult, fc("u6"), op.add)
     vw()
     v(V.tensor_scalar(T.fb[:, FW - 20:FW - 4], T.gs[:, :].indirect(offf), fc("thr"), None, op.is_lt), "prune")
     v(V.tensor_scalar(T.fb[:, 64:192:2], T.gs[:, :].indirect(offg), fc("thr"), None, op.is_lt), "prune")
-    tt(T.nm[:, :], T.nz3[:, :].indirect(T.offs[:, 0:8]), T.oh[:, :], op.mult)
+    ts(T.of3[:, 18:19], fc("u6"), 16.0, op.mult, 15.0, op.add)
 
     def fl(b):
         return T.fb[:, FW - 4 * b - 1:FW - 4 * b]
@@ -547,54 +550,59 @@ def rank_program(g, core, T, topo):
         on(V, "prune", b)
         e, n = FW - 4 * b, 2 * b + 3
         scan(T.fb[:, e - n:e], T.fb[:, e + 1:e + 1 + 2 * n:2], T.fb[:, 192 - 18 * b:192 - 18 * b + n], op.subtract, op.max, sig="prune")
-        if b == 2:
-            ts(T.of3[:, 18:19], fc("u6"), 16.0, op.mult, 15.0, op.add)
-        if b == 3:
+        if b in (2, 3):
+            a = slice(64 * b - 128, 64 * b - 64)
+            tt(T.nm[:, a], T.nz3[:, :].indirect(T.offs[:, 4 * b - 8:4 * b - 4]), T.oh[:, a], op.mult)
+        if b == 4:
             vw()
             sums(T.nz[:, :], T.nm[:, :])
-        if b == 4:
-            ts(T.of3[:, 19:20], fc("u6"), 16.0, op.mult, 15.0, op.add)
         if b == 5:
+            ts(T.of3[:, 19:20], fc("u6"), 16.0, op.mult, 15.0, op.add)
+        if b == 6:
+            vw()
+            cp(fc("n7"), T.nz[:, 127:128])
+        if b == 7:
             ts(T.dumpc[:, :], T.rj[:, 32:36], float(DUMP), op.add)
     x_pp = new()
     for b in range(1, E - 1):
         on(S, "prune", b + 1)
         sw()
-        s(S.activation(T.pp[:, 8 + b:9 + b], fl(b), fn.Identity, bias=T.pp[:, 7 + b:8 + b]), x_pp if b == E - 2 else None)
+        last = b == E - 2
+        s(S.activation(T.pp[:, 7:8] if last else T.pp[:, 8 + b:9 + b], fl(b), fn.Identity, bias=T.pp[:, 7 + b:8 + b]), x_pp if last else None)
         s(S.activation(T.pp[:, b:b + 1], fl(b), fn.Identity, bias=T.pp[:, 7 + b:8 + b], scale=101.0), x_pp)
     on(V, "prune", E)
+    vw()
+    ts(T.nz[:, 127:128], fl(7), 0.5, op.is_lt, fc("n7"), op.mult)
     on(V, x_pp, E - 1)
-    ts(T.pp[:, 7:8], fl(7), 101.0, op.mult, T.pp[:, 14:15], op.add); vw()
     tt(T.kh[:, :], T.pp[:, 0:8].indirect(offn), T.erow[:, 128:160], op.is_equal); vw()
     tt(T.km[:, 0:32], T.nz[:, :].indirect(offz), T.kh[:, :], op.mult); vw()
     scan(T.km[:, 32:64], T.r8[:, :], T.km[:, 0:32], op.mult, op.add); vw()
     k1 = T.km[:, 39:64:8]
-    cp(T.kl0[:, :], k1)
-    ts(T.dm[:, 0:4], k1, 32.0, op.mult, fc("pm8"), op.add)
-    ts(T.kd[:, 0:4], k1, 0.0, op.is_equal, 1e9, op.mult)
-    x_zr, x_dz = new(), new()
+    x_zr, x_dz, x_dm = new(), new(), new()
+    ts(T.kl0[:, :], k1, float(SH - SHB), op.add, sig="step")
+    ts(T.dm[:, 0:4], k1, 32.0 * DL, op.mult, fc("pm8"), op.add, sig=x_dm)
     on(V, x_zw)
-    vw()
+    pw()
     tt(T.zrow[:, :], T.zw[:, :].indirect(T.kl0[:, 0:4]), im64, op.add, sig=x_zr)
-    ts(T.kd[:, 4:8], T.kd[:, 0:4], 7.5, op.max); vw()
-    on(S, x_zr)
-    on(V, x_zr)
+    tt(T.kd[:, 0:4], k1, T.dumpc[:, :], op.max)
+    for q_ in (S, V):
+        on(q_, x_dm)
+        on(q_, x_zr)
     for k in range(KP):
         o = T.dz[:, 64 * k:64 * k + 64]
         if k < 2:
-            ts(o, T.zrow[:, :], T.dm[:, k:k + 1], op.subtract)
+            ts(o, T.zrow[:, :], DL, op.mult, T.dm[:, k:k + 1], op.subtract)
         else:
-            s(S.activation(o, T.zrow[:, :], fn.Identity, bias=T.dm[:, k:k + 1], scale=-1.0), x_dz)
+            s(S.activation(o, T.zrow[:, :], fn.Identity, bias=T.dm[:, k:k + 1], scale=-DL), x_dz)
     vw()
     for k in range(KP):
         if k == 2:
             on(V, x_dz, 2)
         v(V.tensor_reduce(T.dm[:, 4 + k:5 + k], T.dz[:, 64 * k:64 * k + 64], X, op.min, apply_absolute_value=True))
     vw()
-    tt(T.kd[:, 8:12], T.dm[:, 4:8], T.kd[:, 4:8], op.is_lt); vw()
     x_km = new()
     for k in range(KP):
-        ts(T.kmsg[:, k:k + 1], T.kd[:, 8 + k:9 + k], T.dumpc[:, k:k + 1], op.mult, T.km[:, 39 + 8 * k:40 + 8 * k], op.max, sig=x_km)
+        ts(T.kmsg[:, k:k + 1], T.dm[:, 4 + k:5 + k], T.dumpc[:, k:k + 1], op.max, T.kd[:, k:k + 1], op.min, sig=x_km)
     on(g, x_km, KP)
     tell(T.kmsg[:, :], lambda q: T.kland[:, 4 * r:4 * r + 4], "kept")
     on(Q, x_km, KP)
@@ -605,20 +613,24 @@ def rank_program(g, core, T, topo):
     def tile(b):
         quant("eq", 128 * b, 128 * b + 128, T.eb[:, 3 - b:515 - b], x_eq)
     fill(T.kf[:, :], 0.0)
-    ts(psel, fc("u7"), fc("u8"), op.add)
+    ts(fc("g4"), ic("ggi"), 4.0, op.mult)
     ts(tl, fc("u3"), fc("u4"), op.add, 1.0 / 32, op.mult)
-    ts(T.cw[:, 0:8], T.rj[:, 32:40], -128.0, op.add)
+    ts(T.cw[:, 0:7], T.rj[:, 32:39], -128.0, op.add)
+    ts(fc("c7"), fc("pm"), -16.0, op.add)
     fill(T.ysb[:, 128:144], 0.0)
     on(V, x_w, 16)
     quant("wq", 0, 128, T.wt[:, :], x_wq)
     on(V, x_ebd)
     vw()
-    ts(T.kf[:, 0:4], k1, float(-SH), op.add, -1.0, op.max)
-    tt(T.ky[:, 0:32], T.cw[:, 0:8].indirect(offn), T.kh[:, :], op.mult)
+    ts(T.kf[:, 0:4], k1, float(-SHB), op.add, -1.0, op.max)
+    ts(T.cw[:, 7:8], fl(7), 0.5, op.is_lt, fc("c7"), op.mult)
+    ts(psel, fc("pm"), KP - 1.0, op.min, fc("g4"), op.add)
     tile(0)
+    vw()
+    tt(T.ky[:, 0:32], T.cw[:, 0:8].indirect(offn), T.kh[:, :], op.mult)
+    x_kt = v(V.transpose(T.kt[0:32, :], T.kf[0:32, :]), new())
     tile(1)
     vw()
-    x_kt = v(V.transpose(T.kt[0:32, :], T.kf[0:32, :]), new())
     scan(T.ky[:, 32:64], T.r8[:, :], T.ky[:, 0:32], op.mult, op.add)
     tile(2)
     vw()
@@ -653,23 +665,33 @@ def rank_program(g, core, T, topo):
     on(Q, x_yo, KP)
     load(Q, T.y[:, :], T.yo[:, :], x_st)
 
+    def ycol(i):
+        v(V.tensor_copy(T.yo[:, i:64:4], T.ysb[:, :].indirect(T.of3[:, 8 + 2 * i:9 + 2 * i])), x_yo)
+    on(V, x_ysb)
+    ycol(0)
+    ycol(1)
     on(V, x_vald)
     on(V, x_cl)
     on(V, x_kown, 16)
     on(V, "r_kept", EV * len(others))
-    cp(klf, T.kland[:, :]); vw()
-    cp(T.okl[:, :], klf.indirect(psel)); vw()
-    for i in range(NR // 2):
-        cp(T.cl[:, 32:32 + CLW].indirect(T.okl[:, 4 * i:4 * i + 4]), T.vald[:, 64 * i:64 * i + 64], sig="claim")
-        if i == 0:
-            on(V, x_ysb)
-        v(V.tensor_copy(T.yo[:, i:64:4], T.ysb[:, :].indirect(T.of3[:, 8 + 2 * i:9 + 2 * i])), x_yo)
-        on(V, "claim", i + 1)
+    ts(klf, T.kland[:, :], float(-DUMP), op.add)
+    ycol(2)
+    vw()
+    cp(T.okl[:, :], klf.indirect(psel))
+    ycol(3)
+    vw()
+    cp(T.cl[:, :].indirect(T.okl[:, 0:KP]), T.vald[:, :], sig="claim")
+    on(V, "claim")
     v(V.transpose(T.ttc[:, 0:256], T.cl[:, c0:c0 + 256]))
     v(V.transpose(T.ttc[:, 256:544], T.cl[:, c0 - 16:c0 + 272])); vw()
-    tt(ub, T.ttc[:, 0:544:32], T.ttc[:, 16:544:32], op.max); vw()
+    tt(T.mx[0:64, 0:34], T.ttc[0:64, 0:544:16], T.ttc[64:128, 0:544:16], op.max); vw()
+    tt(T.mx[0:32, 40:74], T.mx[0:32, 0:34], T.mx[32:64, 0:34], op.max); vw()
+    for k in range(4):
+        tt(T.pp[32 * k:32 * k + 32, 16:33], T.mx[0:32, 40:74:2], T.mx[0:32, 41:74:2], op.max)
+    vw()
     x_new, x_oc, x_os, x_st2, x_gp = new(), [new(), new()], new(), new(), [new(), new()]
     x_ptl = ts(T.ptl[:, :], ub.indirect(tl), -1.0, op.mult, float(NR * A), op.add, sig=new())
+    ts(T.sel[:, 0:16], ub.indirect(tl), 0.5, op.is_gt, float(P), op.mult)
     sw()
     on(S, x_un[0], 3)
     on(S, x_ptl)
@@ -677,23 +699,21 @@ def rank_program(g, core, T, topo):
         pick_s(T.gp[:, P * b - 2 * P:P * b - P], T.ptd[:, PW * b:PW * b + PW], T.ptl[:, 0:16], x_gp[b - 2])
     on(V, x_un[0], 3)
     on(V, x_ptl)
-    ts(T.sel[:, 0:16], T.ptl[:, :], NR * A - 0.5, op.is_lt, float(P), op.mult)
     for b in range(4):
         o = T.bb[:, b:1024:4]
         if b < 2:
             if b == 1:
                 on(V, x_un[1], 2)
-            tt(o, T.ptd[:, PW * b:PW * b + PW].indirect(T.ptl[:, 0:16]), T.tbd[:, P * b:P * b + P], op.add)
+            tt(o, T.ptd[:, PW * b:PW * b + PW].indirect(T.ptl[:, 0:16]), T.tbd[:, P * b:P * b + P], op.add, sig="step")
         else:
             on(V, x_ut[b])
             on(V, x_gp[b - 2])
-            tt(o, T.gp[:, P * b - 2 * P:P * b - P], T.ps[:, 512 * b:512 * b + P], op.add)
-        if b == 0:
-            vw()
-        if b == 1:
-            tt(T.sel[:, 16:32], T.sel[:, 0:16], jw, op.add)
+            tt(o, T.gp[:, P * b - 2 * P:P * b - P], T.ps[:, 512 * b:512 * b + P], op.add, sig="step")
     vw()
+    tt(T.sel[:, 16:32], T.sel[:, 0:16], jw, op.add)
+    pw()
     quant("tn", P, 2 * P, T.bb[:, :], x_new)
+    vw()
     x_sel = cp(T.sell[:, :], T.sel[:, 16:32], sig=new())
     for q_ in (V, S):
         on(q_, x_tno, 32)

@@ -9,38 +9,39 @@ DL = 4096.0
 DUMP = 7 * 4096
 SHB = DUMP + KP * A
 CLW = KP * A + NR * P + 16
-GW = 16 * (E - 1)
 S0 = P * (NR - 1)
 FW = 48
-PW = NR * A + 16
+RO = NR * A + 1
+PW = NR * A + P + 8
 R0, R1 = 3, 14
+BA = 4
 ORDER = (1, 4, 2, 5, 3, 6, 7)
 WAVES = ((0, 4), (4, 7))
 
 F, B, I, U = "float32", "bfloat16", "int32", "uint16"
 SB = {
-    "cdi": (16, I), "offl": (16, U), "ones": (64, B), "zz": (288, B), "pres": (4 * (S0 + NR * P), B), "r4": (4 * P, B), "orx": (4 * P, B),
-    "cnt": (P + 32, B), "ind": (2 * P, B), "indc": (2 * P, B), "junk": (P, B), "req": (3, U), "rland": (24, U), "reql": (24, U), "rj": (48, F),
-    "jwb": (2, B), "dumpc": (4, F), "imj": (96, F), "r8": (32, F), "tro": (8, U), "of3": (24, U), "ofx": (32, U),
-    "offs": (16, U), "offp": (16, U), "cf": (96, F), "li": (68, I), "m16": (256, B), "m4": (896, B),
+    "cdi": (16, I), "offl": (16, U), "ones": (64, B), "zz": (288, B), "pres": (4 * (S0 + NR * P), B), "r4": (2 * P, B), "orx": (4 * P, B),
+    "cnt": (P + 32, B), "ind": (P, B), "indc": (P, B), "junk": (2 * P, B), "req": (3, U), "rland": (24, U), "reql": (24, U), "rj": (32, F),
+    "jwb": (2, B), "dumpc": (4, F), "imj": (96, F), "r8": (32, F), "tro": (8, U), "of3": (8, U), "ofx": (32, U), "ofy": (8, U), "oy": (8, U),
+    "offs": (8, U), "offp": (16, U), "cf": (96, F), "m16": (256, B), "m4": (288, B),
     "r16": (256, B), "sg": (256, B), "zw": (ZW, F), "vals": (64, B), "vald": (64, B), "erow": (160, F), "erow2": (256, F),
-    "lf": (32, F), "lt": (32, F), "cm2": (256, B), "rn": (256, B), "oh2": (256, F), "nsz": (256, F), "nz3": (256, F),
-    "offw": (16, U), "lw": (256, B), "lall": (128, B), "la": (128, F), "lsm": (256, F), "lsz": (256, F), "offc": (16, U),
+    "lf": (32, F), "lt": (32, F), "cm2": (256, B), "rs": (16, F), "ru": (32, F), "rel": (256, F), "fs": (24, F), "oh2": (256, F),
+    "offw": (16, U), "lw": (256, F), "lall": (128, F), "la": (128, F), "lsm": (256, F), "lsz": (256, F), "offc": (16, U),
     "sm": (256, F), "sz": (256, F), "rep": (256, F), "cm": (256, B), "rk": (256, B), "oh": (128, F), "lm": (128, F),
-    "lz": (128, F), "offr": (16, U), "ss": (128, F), "ssz": (128, F), "sr": (16, F), "nm": (128, F), "nz": (128, F), "gb": (896, B),
-    "gs": (912, B), "fb": (192, F), "pp": (40, F), "bo": (20, F), "kh": (32, F), "km": (64, F), "ky": (64, F),
+    "lz": (128, F), "offr": (10, U), "ss": (128, F), "ssz": (128, F), "nm": (128, F), "nz": (128, F), "gb": (512, B),
+    "gs": (512, B), "fb": (64, F), "pp": (40, F), "bo": (4, F), "kh": (32, F), "km": (64, F), "ky": (64, F),
     "kf": (32, F), "kt": (32, F), "kd": (16, F), "kl0": (4, U), "zrow": (64, F), "dz": (256, F), "dm": (8, F), "kmsg": (4, U),
     "kland": (32, U), "kc": (32, F), "okl": (16, U), "ysb": (144, F), "yo": (64, F), "mx": (80, F),
     "xt": (512, B), "wt": (512, B), "tt": (1024, B), "ebm": (520, B), "eb": (520, B), "cl": (CLW, B), "ttc": (544, B), "cw": (16, F),
-    "ptd": (4 * PW, B), "tbd": (2 * P, B), "gp": (2 * P, B), "ptl": (16, U), "sel": (32, F), "sell": (16, U), "bb": (1024, B),
+    "ptd": (4 * PW, F), "tbd": (2 * P, B), "gp": (2 * P, F), "ptl": (16, U), "bb": (1024, B),
 }
-CODES = {"p8": 128, "wq": 128, "tq": 256, "win": 592, "tn": 512, "snd": 336, "cand": 256, "pk": 240, "eq": 512, "pt": 128, "ocq": 256}
-ICOL = {n: i for i, n in enumerate(["pi", "pmi", "ggi", "ogi", "t1i", "t2i", "t3i", "t4i", "t5i", "t6i", "t7i"])}
-FCOL = {n: i for i, n in enumerate(["pm", "u1", "u2", "u3", "u4", "thr", "pm8", "th0", "u5", "u6", "isr", "hneg",
-                                    "g4", "c7", "g16", "sb", "acc", "bx", "by", "bz", "n7"])}
+CODES = {"p8": 128, "wq": 128, "tq": 256, "win": 592, "tn": 256, "snd": 336, "cand": 256, "pk": 144, "eq": 512, "pt": 128}
+ICOL = {n: i for i, n in enumerate(["pi", "pmi", "ggi", "ogi", "t1i", "t4i"])}
+FCOL = {n: i for i, n in enumerate(["pm", "u1", "u2", "u3", "u4", "pm8", "u5", "u6", "isr", "hneg", "kap", "g4", "c7", "g16", "n7",
+                                    "sb1", "sb2", "ac1", "ac2", "b0", "b1", "base", "nbase", "gs0"])}
 
 SCRATCH = {n: ("sbuf", [128, k], d) for n, (k, d) in SB.items()}
-SCRATCH["dl"] = ("dram", [16, 128], B)
+SCRATCH["dl"] = ("dram", [16, 128], F)
 SCRATCH["ic"] = ("sbuf", [128, len(ICOL)], I)
 SCRATCH["fc"] = ("sbuf", [128, len(FCOL)], F)
 for _n, _k in CODES.items():
@@ -77,8 +78,8 @@ def rank_program(g, core, T, topo):
             pn[0] += 1
         return sig
 
-    def vw():
-        V.wait_ge(T.sem["v"], vn[0])
+    def vw(skip=0):
+        V.wait_ge(T.sem["v"], vn[0] - skip)
 
     def pw():
         V.wait_ge(T.sem["step"], pn[0])
@@ -98,18 +99,13 @@ def rank_program(g, core, T, topo):
     def ic(n):
         return T.ic[:, ICOL[n]:ICOL[n] + 1]
 
-    def fc(n):
-        return T.fc[:, FCOL[n]:FCOL[n] + 1]
+    def fc(n, at=slice(0, 128)):
+        return T.fc[at, FCOL[n]:FCOL[n] + 1]
 
     def ts(o, a, s1, op0, s2=None, op1=None, sig=None):
         if op1 is None:
             return v(V.tensor_scalar(o, a, s1, None, op0), sig)
         return v(V.tensor_scalar(o, a, s1, s2, op0, op1), sig)
-
-    def bits(o, a, s1, op0, s2=None, op1=None):
-        if op1 is None:
-            return v(V.tensor_scalar(o, a, s1, None, op0))
-        return v(V.tensor_scalar(o, a, s1, s2, op0, op1))
 
     def tt(o, a, b, o_, sig=None):
         return v(V.tensor_tensor(o, a, b, o_), sig)
@@ -120,14 +116,17 @@ def rank_program(g, core, T, topo):
     def fill(o, c, sig=None):
         return v(V.memset(o, c), sig)
 
-    def scan(o, a, b, o0, o1, sig=None):
-        return v(V.tensor_tensor_scan(o, a, b, 0.0, o0, o1), sig)
+    def scan(o, a, b, o0, o1, sig=None, init=0.0):
+        return v(V.tensor_tensor_scan(o, a, b, init, o0, o1), sig)
 
     def sums(o, a, sig=None):
         return scan(o, T.r16[:, 0:o.shape[1]], a, op.mult, op.add, sig)
 
     def act(o, a, sig=None):
         return s(S.activation(o, a, fn.Copy), sig)
+
+    def lin(o, a, bias, scale=1.0, sig=None):
+        return s(S.activation(o, a, fn.Identity, bias=bias, scale=scale), sig)
 
     def pick_v(o, src, off, sig):
         V.tensor_copy(o.bitcast(u32), src.bitcast(u32).indirect(off)).then_inc(T.sem[sig], 1)
@@ -182,171 +181,200 @@ def rank_program(g, core, T, topo):
     def spot(q):
         return LC * ((r - q - 1) % NR)
 
-    row16, jm, jw = T.rj[:, 0:16], T.rj[:, 16:32], T.rj[:, 32:48]
-    dd, ma, mb, bs, lts = [T.cf[:, 16 * k:16 * k + 16] for k in range(5)]
-    nsi, owi = T.li[:, 0:16], T.li[:, 16:32]
+    row16, jm = T.rj[:, 0:16], T.rj[:, 16:32]
+    dd, ma, mb, lts, crow, dif = [T.cf[:, 16 * k:16 * k + 16] for k in range(6)]
     im64, jm8 = T.imj[:, 0:64], T.imj[:, 64:96]
-    rot, psel, tl = T.tro[:, 2:3], T.tro[:, 4:5], T.tro[:, 0:1]
-    offn, offg, offf, offz = T.of3[:, 0:2], T.of3[:, 4:8], T.of3[:, 16:17], T.of3[:, 18:20]
+    psel, tl = T.tro[:, 4:5], T.tro[:, 0:1]
+    offn, offz = T.of3[:, 0:2], T.of3[:, 2:4]
     klf, ub = T.kc[:, 0:32], T.pp[:, 16:33]
     NM = R1 - R0
+    odd = r % 2
+    me32 = slice(32 * (r // 2), 32 * (r // 2) + 32)
 
     x_cd, x_x, x_tb, x_w = new(), new(), new(), new()
     for k in range(8):
         load(Q if k < 4 else S, T.cdi[16 * k:16 * k + 16, :], T.cd[:, :], x_cd)
     load(Q, T.xt[:, 0:64], T.x[:, :], x_x)
     load(Q, T.tt[:, :], T.tb[:, :], x_tb)
-    load(S, T.wt[:, :], T.w[:, :], x_w)
+    load(Q, T.wt[:, :], T.w[:, :], x_w)
 
-    x_pi, x_io1, x_io2, x_er2, x_eb, x_ebd, x_r4 = new(), new(), new(), new(), new(), new(), new()
+    x_pi, x_io1, x_io2, x_er2, x_eb, x_ebd, x_r4, x_jm = new(), new(), new(), new(), new(), new(), new(), new()
     g.iota(ic("pi"), [[1, 1]], 0, 1).then_inc(T.sem[x_pi], 1)
-    iota(jm, [[1, 16]], 0, 0, x_io1)
+    iota(jm, [[1, 16]], 0, 0, x_jm)
     iota(row16, [[16, 16]], 0, 0, x_io1)
-    iota(T.r4[:, :], [[0, P], [1, 4]], 0, 0, x_r4)
+    iota(T.r4[:, :], [[0, P // 2], [1, 4]], 0, 0, x_r4)
     iota(T.erow2[:, :], [[2, 16], [0, 16]], 1 - C, 0, x_er2)
 
     x_r16, x_m, x_zz, x_isr, x_pr, x_pz = new(), new(), new(), new(), new(), new()
-    fill(T.pres[:, 4 * S0:4 * S0 + 4 * P], 0.0, sig=x_pz)
-    on(V, x_pi)
-    bits(ic("ggi"), ic("pi"), 4, op.arith_shift_right)
-    fill(T.ones[:, :], 1.0, sig="step")
     fill(T.zz[:, :], 0.0, sig=x_zz)
+    on(V, x_pi)
+    ts(ic("ggi"), ic("pi"), 4, op.arith_shift_right)
+    ts(ic("pmi"), ic("pi"), 15, op.bitwise_and)
+    fill(T.pres[:, 4 * S0:4 * S0 + 4 * P], 0.0, sig=x_pz)
     vw()
     ts(fc("isr"), ic("ggi"), float(r), op.is_equal, sig=x_isr)
-    for k in range(4):
-        ts(T.bo[:, 16 + k:17 + k], ic("ggi"), float(-4 * P), op.mult, float(4 * S0 + k), op.add, sig="step")
-    bits(ic("pmi"), ic("pi"), 15, op.bitwise_and)
-    ts(fc("hneg"), ic("ggi"), float(-P), op.mult, 16.0, op.add)
+    ts(fc("gs0"), ic("ggi"), float(-4 * P), op.mult, float(4 * S0), op.add)
+    x_hn = ts(fc("hneg"), ic("ggi"), float(-P), op.mult, 16.0, op.add, sig=new())
+    on(V, x_jm)
+    vw()
+    ts(T.bo[:, :], T.rj[:, 16:20], fc("gs0"), op.add, sig="step")
+    x_pm = cp(fc("pm"), ic("pmi"), sig=new())
     pw()
 
-    x_xt, x_cz = new(), new()
+    x_xt, x_cz, x_dd = new(), new(), new()
+    on(S, x_zz)
+    lin(T.ones[:, :], T.zz[:, 0:64], 1.0, sig=x_pr)
+    for k in range(2):
+        lin(T.ebm[:, 260 * k:260 * k + 260], T.zz[:, 0:260], 0.5, sig=x_eb)
     on(S, x_pz)
     on(S, x_isr)
     own = T.pres[:, 4 * S0:4 * S0 + 4 * P:4]
-    s(S.activation(own, own, fn.Identity, bias=fc("isr")), x_pr)
-    on(S, x_zz)
-    act(T.cnt[:, 0:16], T.zz[:, 0:16], sig=x_cz)
-    act(T.cnt[:, P + 16:P + 32], T.zz[:, 0:16], sig=x_cz)
+    lin(own, own, fc("isr"), sig=x_pr)
     on(S, x_x, 16)
     act(T.xt[:, 64:128], T.xt[:, 0:64]); sw()
     act(T.xt[:, 128:256], T.xt[:, 0:128]); sw()
     act(T.xt[:, 256:512], T.xt[:, 0:256], sig=x_xt)
+    on(S, x_pm)
+    on(S, x_jm)
+    lin(dd, jm, fc("pm"), -1.0, sig=x_dd)
+    act(T.jwb[:, 0:1], fc("pm"), sig=x_dd)
 
     on(V, x_cd, 128)
     for k in range(4):
-        ts(T.offl[:, k:16:4], T.cdi[:, k:16:4], 4.0, op.mult, T.bo[:, 16 + k:17 + k], op.add, sig="step")
-    on(V, x_io1, 2)
-    ts(T.r16[:, 0:16], jm, 0.0, op.is_gt, sig=x_r16)
+        ts(T.offl[:, k:16:4], T.cdi[:, k:16:4], 4.0, op.mult, T.bo[:, k:k + 1], op.add, sig="step")
+    x_p8, x_lt, x_b0 = new(), new(), new()
+    cp(T.lf[:, 0:16], T.cdi[:, :])
     pw()
-    on(V, x_pr)
-    x_p8, x_lt, x_sb = new(), new(), new()
+    on(V, x_pr, 2)
     for i in range(4):
         if i:
             on(V, "scat", i)
         v(V.tensor_copy(T.pres[:, :].indirect(T.offl[:, 4 * i:4 * i + 4]), T.ones[:, :]), "scat")
-        vw()
         if i == 0:
-            cp(fc("pm"), ic("pmi"))
-            cp(T.lf[:, 0:16], T.cdi[:, :])
             cp(T.lf[:, 16:32], T.cdi[:, :])
         if i == 1:
-            ts(dd, jm, fc("pm"), op.subtract)
-            ts(jw, row16, fc("pm"), op.add)
-            v(V.transpose(T.lt[:, :], T.lf[:, :]), x_lt)
-        if i == 2:
-            ts(T.m16[:, 0:16], dd, 0.0, op.is_equal, sig=x_m)
-            ts(fc("sb"), T.rj[:, 34:35], 0.5, op.add, sig=x_sb)
-            cp(T.jwb[:, :], T.rj[:, 32:34])
-        if i == 3:
-            ts(T.offw[:, :], T.cdi[:, :], fc("hneg"), op.add, P + 16.0, op.min)
             on(V, x_xt)
             quant("p8", 0, 128, T.xt[:, :], x_p8)
+        if i == 2:
+            vw()
+            v(V.transpose(T.lt[:, :], T.lf[:, :]), x_lt)
+        if i == 3:
+            ts(fc("b0"), ic("ggi"), float(r), op.is_le, float(LC * NR), op.mult, sig=x_b0)
     on(V, "scat", 4)
     on(V, x_r4)
-    scan(T.orx[:, :], T.r4[:, :], T.pres[:, 4 * S0:4 * S0 + 4 * P], op.min, op.max)
-    ts(fc("u5"), ic("pmi"), 16.0, op.mult, 15.0, op.add)
-    vw()
+    for k in range(2):
+        a = 2 * P * k
+        scan(T.orx[:, a:a + 2 * P], T.r4[:, :], T.pres[:, 4 * S0 + a:4 * S0 + a + 2 * P], op.min, op.max, sig="step")
+    on(V, x_dd, 2)
+    ts(T.m16[:, 0:16], dd, 0.0, op.is_equal, sig=x_m)
+    pw()
     x_cnt = scan(T.cnt[:, 16:P + 16], T.orx[:, 3:4 * P:4], T.orx[:, 3:4 * P:4], op.add, op.max, sig=new())
-    ts(T.offp[:, :], row16, 0.0, op.mult, fc("pm"), op.add)
+    on(V, x_hn)
+    ts(T.offw[:, :], T.cdi[:, :], fc("hneg"), op.add, P + 16.0, op.min)
 
-    def rows(t, n, m, sig):
+    x_r16b, x_m16, x_cm, x_acc, x_cl, x_r8, x_rs, x_u, x_fs, x_k = [new() for k in range(10)]
+    on(S, x_hn)
+    lin(fc("sb1"), fc("pm"), 16.5)
+    lin(fc("sb2"), fc("pm"), 32.5)
+    s(S.activation(T.r16[:, 0:16], jm, fn.Sign), x_r16)
+    lin(fc("u2"), fc("pm"), 0.0, 16.0, sig=x_k)
+    lin(fc("u5"), fc("pm"), 15.0, 16.0, sig=x_k)
+    lin(fc("g16"), fc("hneg"), -1.0, 1.0 / 16)
+    lin(fc("g4"), fc("hneg"), 0.25, -1.0 / 64, sig=x_k)
+
+    def signs(a, b):
+        for c in range(a, b):
+            s(S.activation(T.cm2[:, 16 * c:16 * c + 16], T.lt[:, 0:16], fn.Sign, bias=T.lt[:, c:c + 1], scale=-1.0, accum_out=T.rs[:, c:c + 1]), x_cm)
+
+    def rows(t, n, m, sig, gaps=()):
+        gaps = list(gaps)
         while n < m:
             k = min(n, m - n)
             act(t[:, n:n + k], t[:, 0:k], sig=sig if n + k == m else None)
+            seen = sn_[0]
+            if gaps:
+                gaps.pop(0)()
             n += k
             if n < m:
-                sw()
-    x_r16b, x_m16, x_cm, x_acc, x_cl, x_r8 = new(), new(), new(), new(), new(), new()
-    on(S, x_r16)
-    rows(T.r16, 16, 256, x_r16b)
-    on(S, x_m)
-    rows(T.m16, 16, 256, x_m16)
-    on(S, x_sb)
-    on(S, x_cnt)
-    s(S.activation(T.junk[:, 0:P - 1], T.cnt[:, 16:P + 15], fn.Sign, bias=fc("sb"), scale=-1.0, accum_out=fc("acc")), x_acc)
+                S.wait_ge(T.sem["s"], seen)
     on(S, x_lt)
-    for c in range(C):
-        s(S.activation(T.cm2[:, 16 * c:16 * c + 16], T.lt[:, 0:16], fn.Sign, bias=T.lt[:, c:c + 1], scale=-1.0), x_cm)
+    signs(0, 3)
+    on(S, x_b0)
+    lin(fc("b1"), fc("hneg"), fc("b0"), -LC / P)
+    signs(3, 4)
+    sw()
+    lin(fc("base"), fc("b1"), 16.0 * LC / P - LC * (r + 1), sig=x_k)
+    lin(fc("nbase"), fc("b1"), LC * (r + 1) - 16.0 * LC / P, -1.0)
+    signs(4, 5)
+    sw()
+    lin(T.cnt[:, 0:16], T.zz[:, 0:16], fc("nbase"), sig=x_cz)
+    lin(T.cnt[:, P + 16:P + 32], T.zz[:, 0:16], fc("nbase"), sig=x_cz)
+    signs(5, 7)
+    on(S, x_cnt)
+    for k in (1, 2):
+        s(S.activation(T.junk[:, P * k - P:P * k - 1], T.cnt[:, 16:P + 15], fn.Sign, bias=fc("sb%d" % k), scale=-1.0, accum_out=fc("ac%d" % k)), x_acc)
+    signs(7, C)
+    on(S, x_r16)
+
+    def scaled():
+        on(S, x_cm, C)
+        s(S.activation(T.ru[:, 0:16], T.rs[:, :], fn.Copy, scale=1024.0), x_rs)
+    rows(T.r16, 16, 256, x_r16b, [scaled, lambda: lin(crow, jm, float(2048 * (C - 1) - SHB), -2048.0, sig=x_fs),
+                                  lambda: act(T.fs[:, 16:17], T.zz[:, 0:1], sig=x_fs)])
+
+    def above(a, b):
+        for k in range(a, b):
+            s(S.activation(T.rel[:, 16 * k:16 * k + 16], T.ru[:, 16:32], fn.Relu, bias=float(1024 * (C - 1 - 2 * k)), accum_out=T.fs[:, k:k + 1]), x_fs)
 
     on(V, x_cnt)
-    for k in range(2):
-        ts(T.ind[:, P * k:P * k + P - 1], T.cnt[:, 16:P + 15], T.jwb[:, k:k + 1], op.is_le)
-    vw()
-    for k in range(2):
-        a = slice(P * k, P * k + P - 1)
-        scan(T.indc[:, a], T.ind[:, a], T.ind[:, a], op.add, op.max)
-    ts(T.offs[:, :], row16, 0.0, op.mult, fc("u5"), op.add)
-    vw()
+    on(V, x_io1)
+    on(V, x_pm)
+    ts(T.ind[:, 0:P - 1], T.cnt[:, 16:P + 15], T.jwb[:, 0:1], op.is_le, sig="step")
+    ts(T.offp[:, :], row16, 0.0, op.mult, fc("pm"), op.add)
+    pw()
+    scan(T.indc[:, 0:P - 1], T.ind[:, 0:P - 1], T.ind[:, 0:P - 1], op.add, op.max, sig="step")
+    ts(ma, dd, 0.0, op.is_equal, -128.0, op.mult)
+    pw()
     x_req = new()
-    cp(T.req[:, 0:2], T.indc[:, P - 2:2 * P - 1:P], sig=x_req)
-    on(V, x_acc)
-    ts(T.req[:, 2:3], fc("acc"), 0.5, op.mult, (P - 1) * 0.5, op.add, sig=x_req)
+    cp(T.req[:, 0:1], T.indc[:, P - 2:P - 1], sig=x_req)
+    ts(mb, dd, -1.0, op.is_equal, 10.0, op.mult)
+    on(V, x_acc, 2)
+    ts(T.req[:, 1:3], T.fc[:, FCOL["ac1"]:FCOL["ac1"] + 2], 0.5, op.mult, (P - 1) * 0.5, op.add, sig=x_req)
 
     on(g, x_p8)
     send(lambda q: T.p8[:, 0:A].bitcast(u8), lambda q: T.pt[:, A * r:A * r + A].bitcast(u8), "ptc")
     on(g, x_req, 2)
     tell(T.req[:, :], lambda q: T.rland[:, 3 * seat(q, r):3 * seat(q, r) + 3], "req")
-    iota(T.erow[:, 0:128], [[-1, 8], [-1, 16]], C, 0, x_io2)
-    iota(T.erow[:, 128:160], [[-1, 4], [1, 8]], 0, 0, x_io2)
-    iota(im64, [[0, 4], [1, 16]], 0, 0, x_io2)
-    iota(jm8, [[0, 4], [1, 8]], 0, 0, x_io2)
+    on(g, x_eb, 2)
+    g.affine_select(T.eb[:, 0:516], T.ebm[:, 0:516], [[1, 516]], op.is_equal, 0.0, -3, -4).then_inc(T.sem[x_ebd], 1)
 
-    x_lv, x_tq, x_h1, x_h2, x_wino, x_tno, x_rl, x_ptown = new(), new(), new(), new(), new(), new(), new(), new()
-    x_zw, x_vals, x_og, x_vald, x_kown, x_sg = new(), new(), new(), new(), new(), new()
+    x_lv, x_tq, x_h1, x_h2, x_wino, x_rl, x_ptown = new(), new(), new(), new(), new(), new(), new()
+    x_zw, x_vals, x_vald, x_kown, x_sg, x_eq = new(), new(), new(), new(), new(), new()
     on(V, x_cz, 2)
-    cp(T.lw[:, :], T.cnt[:, :].indirect(T.offw[:, :]), sig=x_lv)
-    on(V, x_lt)
-    ts(nsi, T.lt[:, 0:16], float(-P * (r + 1)), op.add)
-    ts(fc("u2"), ic("pmi"), 16.0, op.mult)
-    bits(ic("ogi"), ic("pi"), 4, op.arith_shift_right, 1, op.bitwise_and)
-    ts(ma, dd, 0.0, op.is_gt)
-    ts(mb, dd, 1.0, op.is_equal, 31.0, op.mult)
+    on(V, x_k, 4)
     vw()
-    bits(owi, nsi, 8, op.arith_shift_right, NR - 1, op.bitwise_and)
+    ts(T.lw[:, :], T.cnt[:, :].indirect(T.offw[:, :]), fc("base"), op.add, sig=x_lv)
     on(V, x_tb, 16)
     quant("tq", 0, P, T.tt[:, :], x_tq)
-    on(V, x_cm, C)
-    on(V, x_r16)
-    on(V, x_r16b)
-    vw()
-    sums(T.rn[:, :], T.cm2[:, :])
-    ts(bs, owi, float(LC), op.mult, -1.0, op.add)
-    ts(lts, T.lt[:, 0:16], float(SHB), op.add)
-    bits(ic("t7i"), ic("pi"), 3, op.arith_shift_right, 1, op.bitwise_and)
-    ts(fc("th0"), fc("pm"), 14.5, op.is_lt, 15.5, op.mult)
-    bits(ic("t1i"), ic("pmi"), 1, op.bitwise_and)
-    bits(ic("t4i"), ic("pmi"), 7, op.bitwise_and)
+    on(V, x_lt)
+    on(V, x_rs)
+    tt(T.ru[:, 16:32], T.ru[:, 0:16], T.lt[:, 0:16], op.add, sig=x_u)
     x_m4a, x_m4 = tt(T.m4[:, 0:16], ma, mb, op.add, sig=new()), new()
+    ts(T.offs[:, :], T.rj[:, 0:8], 0.0, op.mult, fc("u5"), op.add)
     on(V, x_er2)
-    vw()
-    tt(T.oh2[:, :], T.rn[:, :].indirect(T.offs[:, 0:16]), T.erow2[:, :], op.is_equal)
-    quant("win", WOWN, WOWN + P, T.tt[:, :], x_wino)
-    vw()
-    tt(T.nsz[:, :], lts.indirect(T.offp[:, 0:16]), T.oh2[:, :], op.mult)
-    ts(T.ofx[:, 0:NM], T.rj[:, R0:R1], fc("u2"), op.min, 15.0, op.add)
-    ts(T.ofx[:, 16:16 + NM], T.rj[:, R0:R1], fc("u2"), op.max, 15.0, op.add)
-    ts(fc("g16"), ic("ggi"), -16.0, op.mult, sig=x_og)
-    ts(fc("pm8"), fc("pm"), DL, op.mult, -DL * (8 + 32 * (SHB - SH)), op.add)
+    tt(T.oh2[:, :], T.rs[:, :].indirect(T.offp[:, 0:16]), T.erow2[:, :], op.is_equal)
+    ts(ic("t4i"), ic("pmi"), 7, op.bitwise_and)
+    fill(T.offr[:, :], 0)
+    on(V, x_ebd)
+    for b in range(4):
+        quant("eq", 128 * b, 128 * b + 128, T.eb[:, 3 - b:515 - b], x_eq)
+
+    x_ut = [new() for b in range(4)]
+    on(M, x_eq, 4)
+    on(M, x_tq)
+    for b in range(4):
+        e = slice(128 * b, 128 * b + 128)
+        M.matmul_mx(T.ps[:, 2048 + 512 * b:2048 + 512 * b + P], T.eq[:, e], T.eqs[:, e], T.tq[:, :], T.tqs[:, :], True, True).then_inc(T.sem[x_ut[b]], 1)
 
     on(Q, x_p8)
     load(Q, T.pt[:, A * r:A * r + A].bitcast(u8), T.p8[:, 0:A].bitcast(u8), x_ptown)
@@ -354,81 +382,82 @@ def rank_program(g, core, T, topo):
     on(Q, x_lv)
     for k in range(8):
         load(Q, T.dl[:, 16 * k:16 * k + 16], T.lw[16 * k:16 * k + 1, :], x_h1)
-    for k in range(2):
-        s(S.activation(T.ebm[:, 260 * k:260 * k + 260], T.zz[:, 0:260], fn.Identity, bias=0.5), x_eb)
     for q_ in (S, Q):
         on(q_, "r_req", EV * len(others))
         for k in range(8):
             if (k < 4) == (q_ is S):
                 load(q_, T.reql[16 * k:16 * k + 16, 0:21], T.rland[16 * r:16 * r + 16, 0:21], x_rl)
-    s(S.activation(T.gs[:, GW * E:GW * E + 16], T.zz[:, 0:16], fn.Identity, bias=100.0), x_r8)
-    s(S.activation(T.fb[:, 64:192], T.zz[:, 0:128], fn.Identity, bias=-1.0), x_r8)
-    act(T.fb[:, FW - 4:FW + 8], T.zz[:, 0:12], sig=x_r8)
-    act(T.pp[:, 0:1], T.zz[:, 0:1], sig=x_r8)
-    act(T.pp[:, 8:9], T.zz[:, 0:1])
-    on(S, x_io2, 4)
-    s(S.activation(T.r8[:, :], jm8, fn.Sign), x_r8)
+    on(S, x_u)
+    above(0, 8)
     on(Q, x_h1, 128)
     for k in range(8):
         load(Q, T.lall[16 * k:16 * k + 16, :], T.dl[:, :], x_h2)
+    on(Q, x_tq)
+    load(Q, T.win[:, WOWN:WOWN + P].bitcast(u8), T.tq[:, :].bitcast(u8), x_wino)
+    load(Q, T.wins[:, WOWN:WOWN + P], T.tqs[:, :], x_wino)
 
     for q_ in (V, S):
         on(q_, x_tq)
         on(q_, x_rl, 128)
+
+    def codes(w):
+        send(lambda q: T.snd[:, LC * seat(r, q):LC * seat(r, q) + LC].bitcast(u8), lambda q: T.win[:, spot(q):spot(q) + LC].bitcast(u8), "cod%d" % w, wave[w], 4)
+
+    def planes(w):
+        send(lambda q: T.snds[:, LC * seat(r, q):LC * seat(r, q) + LC], lambda q: T.wins[:, spot(q):spot(q) + LC], "pln%d" % w, wave[w], 4)
     for w in range(2):
         x_sndc, x_snds = new(), new()
         c, d = WAVES[w]
         pick_v(T.snd[:, LC * c:LC * d], T.tq[:, :], T.reql[:, 3 * c:3 * d], x_sndc)
         pick_s(T.snds[:, LC * c:LC * d], T.tqs[:, :], T.reql[:, 3 * c:3 * d], x_snds)
-        on(g, x_sndc)
-        send(lambda q: T.snd[:, LC * seat(r, q):LC * seat(r, q) + LC].bitcast(u8), lambda q: T.win[:, spot(q):spot(q) + LC].bitcast(u8), "cod%d" % w, wave[w], 4)
-        on(g, x_snds)
-        send(lambda q: T.snds[:, LC * seat(r, q):LC * seat(r, q) + LC], lambda q: T.wins[:, spot(q):spot(q) + LC], "pln%d" % w, wave[w], 4)
+        for sig, go in ((x_sndc, codes), (x_snds, planes))[::1 - 2 * w]:
+            on(g, sig)
+            go(w)
     send(lambda q: T.p8s[:, 0:A], lambda q: T.pts[:, A * r:A * r + A], "pts")
     on(g, x_r16)
     on(g, x_r16b)
     g.affine_select(T.sg[:, :], T.r16[:, :], [[1, 16], [-1, 16]], op.not_equal, -1.0, 0, 0).then_inc(T.sem[x_sg], 1)
-    on(g, x_eb, 2)
-    g.affine_select(T.eb[:, 0:516], T.ebm[:, 0:516], [[1, 516]], op.is_equal, 0.0, -3, -4).then_inc(T.sem[x_ebd], 1)
-    iota(T.zw[:, :], [[32, ZW]], 0, 0, x_zw)
+    x_io3 = new()
+    c0 = KP * A + P * r
+    iota(T.erow[:, 0:128], [[1, 8], [-1, 16]], C + 1 - E, 0, x_io2)
+    iota(jm8, [[0, 4], [1, 8]], 0, 0, x_io3)
     iota(T.vals[:, :], [[0, 4], [-1, 16]], NR * A, 0, x_vals)
+    iota(T.erow[:, 128:160], [[-1, 4], [1, 8]], 0, 0, x_zw)
+    iota(im64, [[0, 4], [1, 16]], 0, 0, x_zw)
+    iota(T.zw[:, :], [[32, ZW]], 0, 0, x_zw)
+    iota(T.cl[:, c0 - 16:c0 + 272], [[-1, 288]], 15, 0, x_cl)
 
-    on(S, x_m4a)
-    rows(T.m4, 16, 896, x_m4)
+    x_un = [new(), new()]
+    x_rest = new()
+
+    def rest(b):
+        tt(T.ptd[:, PW * b + RO:PW * b + RO + P], T.tt[:, b:1024:4], T.ps[:, 2048 + 512 * b:2048 + 512 * b + P], op.subtract, sig=x_rest)
+    on(S, x_m)
+    rows(T.m16, 16, 256, x_m16, [lambda: above(8, 10), lambda: above(10, 12), lambda: above(12, 14), lambda: above(14, C)])
     on(V, x_h2, 128)
     tt(T.la[:, 0:64], T.lall[:, 0:64], T.lall[:, 64:128], op.add, sig="step")
-    tt(ic("t2i"), ic("pmi"), ic("ggi"), op.add)
-    tt(ic("t3i"), ic("t7i"), ic("ggi"), op.add)
-    cp(fc("u6"), ic("t4i"))
+    ts(T.ofx[:, 0:NM], T.rj[:, R0:R1], fc("u2"), op.min, 15.0, op.add)
     pw()
     tt(T.la[:, 64:96], T.la[:, 0:32], T.la[:, 32:64], op.add, sig="step")
-    vw()
-    ts(fc("u1"), ic("ogi"), -2.0, op.mult, 1.0, op.add)
-    ts(fc("bz"), ic("ggi"), -1.0, op.mult, 9.0, op.add)
-    tt(fc("by"), ic("t4i"), ic("t7i"), op.subtract)
+    ts(T.ofx[:, 16:16 + NM], T.rj[:, R0:R1], fc("u2"), op.max, 15.0, op.add)
     pw()
     tt(T.la[:, 96:112], T.la[:, 64:80], T.la[:, 80:96], op.add, sig="step")
-    vw()
-    ts(fc("bx"), ic("t3i"), -1.0, op.mult, 15.0, op.add)
-    bits(ic("t5i"), ic("t2i"), 7, op.bitwise_and)
-    cp(ic("t6i"), fc("bz"))
+    vw(2)
+    cp(fc("u6"), ic("t4i"))
     pw()
-    tt(T.la[:, 112:128], T.la[:, 96:112], bs, op.add)
-    ts(fc("u3"), ic("t1i"), fc("u1"), op.mult, 272.0, op.mult)
-    ts(fc("u4"), ic("ogi"), 256.0, op.mult, fc("u2"), op.add)
+    tt(T.lsm[:, :], T.la[:, 96:112].indirect(T.offp[:, 0:16]), T.oh2[:, :], op.mult, sig="step")
     vw()
-    tt(T.lsm[:, :], T.la[:, 112:128].indirect(T.offp[:, 0:16]), T.oh2[:, :], op.mult, sig="step")
-    ts(T.li[:, 64:68], T.rj[:, 0:8:2], -1.0 / 16, op.mult, fc("bx"), op.add)
-    ts(fc("by"), fc("by"), 16.0, op.mult)
-    bits(ic("t6i"), ic("t6i"), 7, op.bitwise_and)
+    ts(offn, T.rj[:, 0:2], 0.0, op.mult, fc("u6"), op.add)
     pw()
-    sums(T.lsz[:, :], T.lsm[:, :])
-    ts(fc("bz"), fc("u6"), -16.0, op.mult, 127.0, op.add)
-    vw()
-    x_offc = cp(T.offc[:, :], T.lsz[:, 15:256:16], sig=new())
-    bits(T.li[:, 64:68], T.li[:, 64:68], 7, op.bitwise_and)
-    ts(T.bo[:, 4:8], T.rj[:, 0:8:2], fc("by"), op.is_ge, 2000.0, op.mult)
-    sums(T.nz3[:, :], T.nsz[:, :])
+    on(V, x_r16)
+    on(V, x_r16b)
+    sums(T.lsz[:, :], T.lsm[:, :], sig="step")
+    ts(fc("u1"), fc("u6"), -16.0, op.mult, 127.0, op.add)
+    pw()
+    x_offc = ts(T.offc[:, :], T.lsz[:, 15:256:16], -1.0, op.add, sig=new())
+    on(V, x_ut[3])
+    rest(3)
+    on(V, x_m)
     on(V, x_m16)
 
     x_cc, x_cs, x_s = [new(), new()], [new(), new()], [new(), new()]
@@ -437,7 +466,7 @@ def rank_program(g, core, T, topo):
         on(S, "r_pln%d" % w, 4 * len(wave[w]))
     for q_ in (V, S):
         on(q_, x_offc)
-        on(q_, x_wino)
+        on(q_, x_wino, 32)
     on(M, x_p8)
     for h in range(2):
         a = slice(128 * h, 128 * h + 128)
@@ -446,18 +475,23 @@ def rank_program(g, core, T, topo):
         on(M, x_cc[h])
         on(M, x_cs[h])
         M.matmul_mx(T.ps[:, 512 * h:512 * h + 128], T.p8[:, :], T.p8s[:, :], T.cand[:, a], T.cands[:, a], True, True).then_inc(T.sem[x_s[h]], 1)
-    vw()
-    ts(T.bo[:, 0:4], T.li[:, 64:68], float(GW), op.mult, fc("bz"), op.add)
+    x_td = [new(), new()]
+    on(S, x_ut[0])
+    act(T.tbd[:, 0:P], T.ps[:, 2048:2048 + P], sig=x_td[0])
     x_rep, x_sz = new(), new()
     on(V, x_s[0])
     tt(T.sm[:, 0:128], T.ps[:, 0:128], T.m16[:, 0:128], op.mult, sig="step")
-    on(V, x_s[1])
-    tt(T.sm[:, 128:256], T.ps[:, 512:640], T.m16[:, 128:256], op.mult)
+    on(V, x_fs, C + 2)
+    tt(dif, T.fs[:, 0:16], T.fs[:, 1:17], op.subtract)
     pw()
     sums(T.sz[:, 0:128], T.sm[:, 0:128], sig=x_sz)
+    on(V, x_s[1])
+    tt(T.sm[:, 128:256], T.ps[:, 512:640], T.m16[:, 128:256], op.mult, sig="step")
     vw()
+    tt(lts, dif, crow, op.subtract)
+    pw()
     sums(T.sz[:, 128:256], T.sm[:, 128:256], sig=x_sz)
-    tt(T.bo[:, 8:12], T.bo[:, 0:4], T.bo[:, 4:8], op.add)
+    ts(offz, T.rj[:, 0:2], 0.0, op.mult, fc("u1"), op.add)
     on(S, x_sz, 2)
     pick_s(T.rep[:, 0:16 * NM], T.sz[:, :], T.ofx[:, 16:16 + NM], x_rep)
     on(V, x_sz, 2)
@@ -470,118 +504,136 @@ def rank_program(g, core, T, topo):
             ts(T.cm[:, 16 * c + n:16 * c + 16], T.sz[:, 16 * n + 15:256:16], me, op.is_le)
     on(V, x_rep)
     tt(T.cm[:, 16 * R0:16 * R1], T.sz[:, :].indirect(T.ofx[:, 0:NM]), T.rep[:, 0:16 * NM], op.is_ge)
-    on(V, x_r8, 5)
+    x_kap = new()
+    on(S, x_m4a)
+    rows(T.m4, 16, 288, x_m4, [lambda: act(T.fb[:, FW - 4:FW], T.zz[:, 0:4], sig=x_r8), lambda: lin(T.fb[:, FW:FW + 8], T.zz[:, 0:8], 1.0, sig=x_r8),
+                               lambda: act(T.pp[:, 0:16], T.zz[:, 0:16], sig=x_r8), lambda: lin(fc("kap"), T.cf[:, 31:32], -11.0, -10.0 / 128, sig=x_kap)])
+    on(S, x_io3)
+    s(S.activation(T.r8[:, :], jm8, fn.Sign), x_r8)
+    act(T.gs[:, 160:192], T.zz[:, 0:32], sig=x_r8)
+    act(T.gs[:, 480:512], T.zz[:, 0:32], sig=x_r8)
+    act(T.kf[:, :], T.zz[:, 0:32], sig=x_r8)
+    act(T.ysb[:, 128:144], T.zz[:, 0:16], sig=x_r8)
+    on(S, x_io1)
+    lin(T.cw[:, 0:8], T.rj[:, 1:9], fc("pm"), -1.0, sig=x_r8)
     on(V, x_sg)
     vw()
-    scan(T.rk[:, :], T.sg[:, :], T.cm[:, :], op.mult, op.add)
-    ts(rot, ic("t5i"), 16.0, op.mult, 15.0, op.add)
-    on(V, x_io2, 4)
-    vw()
-    tt(T.oh[:, :], T.rk[:, :].indirect(T.offs[:, 0:8]), T.erow[:, 0:128], op.is_equal)
-    ts(offg, T.bo[:, 8:12], float(GW * E), op.min)
-    vw()
+    scan(T.rk[:, :], T.sg[:, :], T.cm[:, :], op.mult, op.add, sig="step")
+    ts(fc("pm8"), fc("pm"), DL, op.mult, -DL * (8 + 32 * (SHB - SH)), op.add)
+    on(V, x_io2)
+    pw()
+    tt(T.oh[:, :], T.rk[:, :].indirect(T.offs[:, 0:8]), T.erow[:, 0:128], op.is_equal, sig="step")
+    ts(T.dumpc[:, :], T.rj[:, 0:4], fc("pm"), op.add, float(DUMP), op.add)
+    pw()
     tt(T.lm[:, :], T.lsz[:, :].indirect(T.offs[:, 0:8]), T.oh[:, :], op.mult, sig="step")
-    tt(T.ss[:, :], T.sz[:, :].indirect(T.offs[:, 0:8]), T.oh[:, :], op.mult)
+    tt(T.ss[:, 0:64], T.sz[:, :].indirect(T.offs[:, 0:4]), T.oh[:, 0:64], op.mult)
     pw()
     sums(T.lz[:, :], T.lm[:, :], sig="step")
-    vw()
-    sums(T.ssz[:, :], T.ss[:, :])
+    ts(fc("c7"), fc("pm"), -128.0, op.add)
     pw()
-    x_offr, x_offs, x_kc, x_ks = new(), new(), [new(), new()], [new(), new()]
-    cp(T.offr[:, 0:8], T.lz[:, 15:128:16], sig=x_offr)
-    cp(T.offr[:, 8:16], T.lz[:, 15:128:16], sig=x_offs)
+    x_offr, x_kc, x_ks = new(), new(), new()
+    ts(T.offr[:, odd:odd + 8], T.lz[:, 15:128:16], -1.0, op.add, sig=x_offr)
+    tt(T.ss[:, 64:128], T.sz[:, :].indirect(T.offs[:, 4:8]), T.oh[:, 64:128], op.mult)
     for q_ in (V, S):
         on(q_, x_offr)
-    on(Q, x_offr)
-    load(Q, T.tn[:, 0:P].bitcast(u8), T.tq[:, :].bitcast(u8), x_tno)
-    load(Q, T.tns[:, 0:P], T.tqs[:, :], x_tno)
-    for k, a, b in ((0, 0, 8), (1, 8, 15)):
-        pick_v(T.pk[:, 16 * a:16 * b], T.win[:, :], T.offr[:, a:b], x_kc[k])
-        pick_s(T.pks[:, 16 * a:16 * b], T.wins[:, :], T.offr[:, a:b], x_ks[k])
-        if k == 0:
-            for q_ in (V, S):
-                on(q_, x_offs)
-    x_g = []
-    for t in range(E):
-        if t < 2:
-            on(M, x_kc[t])
-            on(M, x_ks[t])
+    pick_v(T.pk[:, :], T.win[:, :], T.offr[:, 0:9], x_kc)
+    pick_s(T.pks[:, :], T.wins[:, :], T.offr[:, 0:9], x_ks)
+    x_g = [new(), new()]
+    best = slice(16 * odd, 16 * odd + 128)
+    on(M, x_kc)
+    on(M, x_ks)
+    for t in range(2):
         a = slice(16 * t, 16 * t + 128)
-        x_g.append(new())
-        M.matmul_mx(T.ps[:, 512 * t:512 * t + 128], T.pk[:, a], T.pks[:, a], T.pk[:, 0:128], T.pks[:, 0:128], True, True).then_inc(T.sem[x_g[t]], 1)
+        M.matmul_mx(T.ps[:, 1024 + 512 * t:1152 + 512 * t], T.pk[:, a], T.pks[:, a], T.pk[:, best], T.pks[:, best], True, True).then_inc(T.sem[x_g[t]], 1)
     vw()
-    x_sr = cp(T.sr[:, :], T.ssz[:, :].indirect(rot), sig=new())
-    ts(offf, ic("t6i"), float(GW), op.mult, 15.0, op.add)
-    ts(fc("thr"), fc("th0"), 0.5, op.add)
-    x_gd = [new(), new(), new()]
-    x_un = [new(), new()]
-    for q_ in (V, S):
-        on(q_, x_sr)
-    for t in range(E):
-        o, a, b = T.gb[:, GW * t:GW * t + GW], T.ps[:, 512 * t:512 * t + GW], T.sr[:, t:t + 1]
-        k = max(t // 2 - 1, 0)
-        if t % 2:
-            on(S, x_g[t])
-            s(S.activation(o, a, fn.Sign, bias=b, scale=-1.0), x_gd[k])
-        else:
-            on(V, x_g[t])
-            ts(o, a, b, op.is_lt, sig=x_gd[k])
-        if t in (3, 5, 7):
-            a = 0 if t == 3 else t - 1
-            on(V, x_m4)
-            on(V, x_gd[k], t + 1 - a)
-            a = slice(GW * a, GW * t + GW)
-            scan(T.gs[:, a], T.m4[:, a], T.gb[:, a], op.mult, op.add)
-    c0 = KP * A + P * r
-    act(T.cl[:, c0 - 16:c0 + 272], T.zz[:, 0:288], sig=x_cl)
-    act(T.ptd[:, NR * A:4 * PW:PW], T.zz[:, 0:4], sig=x_un[0])
+    x_so = sums(T.ssz[:, :], T.ss[:, :], sig=new())
+    tt(T.nm[:, 0:64], lts.indirect(T.offp[:, 0:4]), T.oh[:, 0:64], op.mult)
+    on(S, x_ut[1])
+    act(T.tbd[:, P:2 * P], T.ps[:, 2560:2560 + P], sig=x_td[1])
     on(S, x_vals)
-    on(S, x_og)
-    s(S.activation(T.vald[:, :], T.vals[:, :], fn.Identity, bias=fc("g16")), x_vald)
-    ts(offn, T.rj[:, 0:2], 0.0, op.mult, fc("u6"), op.add)
-    vw()
-    v(V.tensor_scalar(T.fb[:, FW - 20:FW - 4], T.gs[:, :].indirect(offf), fc("thr"), None, op.is_lt), "prune")
-    v(V.tensor_scalar(T.fb[:, 64:192:2], T.gs[:, :].indirect(offg), fc("thr"), None, op.is_lt), "prune")
-    ts(T.of3[:, 18:19], fc("u6"), 16.0, op.mult, 15.0, op.add)
+    lin(T.vald[:, :], T.vals[:, :], fc("g16"), sig=x_vald)
+
+    def start(b):
+        return 8 * b * (b - 1) + (32 if b > BA else 0)
+
+    def pairs(b, sig=None):
+        a = E - 1 - b
+        t = a % 2
+        h = (a + odd - t) // 2
+        at = slice(32 * h, 32 * h + 32)
+        ts(T.gb[me32, start(b):start(b) + 16 * b], T.ps[at, 1152 + 512 * t - 16 * b:1152 + 512 * t], T.ssz[at, 16 * a + 15:16 * a + 16], op.is_ge,
+           fc("kap", at), op.add, sig=sig)
+
+    def keep(a, b, sig):
+        lo, hi = start(a), start(b) + 16 * b
+        scan(T.gs[me32, lo:hi], T.m4[me32, 0:hi - lo], T.gb[me32, lo:hi], op.add, op.max, sig=sig)
 
     def fl(b):
-        return T.fb[:, FW - 4 * b - 1:FW - 4 * b]
-    for b in range(2, E):
-        on(V, "prune", b)
+        return T.fb[me32, FW - 4 * b - 1:FW - 4 * b]
+    x_ga, x_gb, x_gc = new(), new(), new()
+    on(V, x_so)
+    on(V, x_kap)
+    on(V, x_g[0])
+    pairs(1, "step")
+    pairs(3, "step")
+    on(V, x_g[1])
+    pairs(2, "step")
+    pairs(4, "step")
+    pairs(5, x_gc)
+    on(V, x_m4a)
+    on(V, x_m4)
+    on(V, x_r8, 9)
+    pw()
+    keep(1, BA, x_ga)
+    pairs(6, x_gc)
+    vw()
+    on(V, x_ga)
+    for b in range(1, E):
+        if b > 1:
+            on(V, "prune", b - 1)
+        if b == BA + 1:
+            on(V, x_gb)
         e, n = FW - 4 * b, 2 * b + 3
-        scan(T.fb[:, e - n:e], T.fb[:, e + 1:e + 1 + 2 * n:2], T.fb[:, 192 - 18 * b:192 - 18 * b + n], op.subtract, op.max, sig="prune")
-        if b in (2, 3):
-            a = slice(64 * b - 128, 64 * b - 64)
-            tt(T.nm[:, a], T.nz3[:, :].indirect(T.offs[:, 4 * b - 8:4 * b - 4]), T.oh[:, a], op.mult)
-        if b == 4:
+        scan(T.fb[me32, e - n:e], T.fb[me32, e + 1:e + 1 + 2 * n:2], T.gs[me32, start(b) + 15:start(b) + 15 + 8 * n - 7:8], op.subtract, op.max, sig="prune", init=1.0)
+        if b == 1:
+            pairs(7, x_gc)
+        if b in (2, 4):
+            tt(T.nm[:, 32 + 16 * b:64 + 16 * b], lts.indirect(T.offp[:, 2 + b:4 + b]), T.oh[:, 32 + 16 * b:64 + 16 * b], op.mult)
+        if b == 3:
+            on(V, x_gc, 3)
+            keep(BA + 1, E - 1, x_gb)
+        if b == 5:
             vw()
             sums(T.nz[:, :], T.nm[:, :])
-        if b == 5:
-            ts(T.of3[:, 19:20], fc("u6"), 16.0, op.mult, 15.0, op.add)
-        if b == 6:
-            vw()
-            cp(fc("n7"), T.nz[:, 127:128])
         if b == 7:
-            ts(T.dumpc[:, :], T.rj[:, 32:36], float(DUMP), op.add)
+            vw()
+            cp(fc("n7"), T.nz[:, 15:16])
     x_pp = new()
+    on(S, x_r8, 9)
     for b in range(1, E - 1):
-        on(S, "prune", b + 1)
+        on(S, "prune", b)
         sw()
         last = b == E - 2
-        s(S.activation(T.pp[:, 7:8] if last else T.pp[:, 8 + b:9 + b], fl(b), fn.Identity, bias=T.pp[:, 7 + b:8 + b]), x_pp if last else None)
-        s(S.activation(T.pp[:, b:b + 1], fl(b), fn.Identity, bias=T.pp[:, 7 + b:8 + b], scale=101.0), x_pp)
-    on(V, "prune", E)
+        lin(T.pp[me32, 7:8] if last else T.pp[me32, 8 + b:9 + b], fl(b), T.pp[me32, 7 + b:8 + b], sig=x_pp if last else None)
+        lin(T.pp[me32, b:b + 1], fl(b), T.pp[me32, 7 + b:8 + b], 101.0, sig=x_pp)
+    on(V, "prune", E - 1)
     vw()
-    ts(T.nz[:, 127:128], fl(7), 0.5, op.is_lt, fc("n7"), op.mult)
+    ts(T.nz[me32, 15:16], fl(7), 0.5, op.is_lt, fc("n7", me32), op.mult, sig="step")
     on(V, x_pp, E - 1)
-    tt(T.kh[:, :], T.pp[:, 0:8].indirect(offn), T.erow[:, 128:160], op.is_equal); vw()
-    tt(T.km[:, 0:32], T.nz[:, :].indirect(offz), T.kh[:, :], op.mult); vw()
-    scan(T.km[:, 32:64], T.r8[:, :], T.km[:, 0:32], op.mult, op.add); vw()
+    on(V, x_zw, 3)
+    tt(T.kh[:, :], T.pp[:, 0:8].indirect(offn), T.erow[:, 128:160], op.is_equal, sig="step")
+    ts(psel, fc("pm"), KP - 1.0, op.min, fc("g4"), op.add)
+    pw()
+    tt(T.km[:, 0:32], T.nz[:, :].indirect(offz), T.kh[:, :], op.mult, sig="step")
+    ts(T.cw[me32, 7:8], fl(7), 0.5, op.is_lt, fc("c7", me32), op.mult)
+    pw()
+    scan(T.km[:, 32:64], T.r8[:, :], T.km[:, 0:32], op.mult, op.add, sig="step")
+    fill(T.ofy[:, :], 0)
+    pw()
     k1 = T.km[:, 39:64:8]
     x_zr, x_dz, x_dm = new(), new(), new()
     ts(T.kl0[:, :], k1, float(SH - SHB), op.add, sig="step")
     ts(T.dm[:, 0:4], k1, 32.0 * DL, op.mult, fc("pm8"), op.add, sig=x_dm)
-    on(V, x_zw)
     pw()
     tt(T.zrow[:, :], T.zw[:, :].indirect(T.kl0[:, 0:4]), im64, op.add, sig=x_zr)
     tt(T.kd[:, 0:4], k1, T.dumpc[:, :], op.max)
@@ -591,15 +643,18 @@ def rank_program(g, core, T, topo):
     for k in range(KP):
         o = T.dz[:, 64 * k:64 * k + 64]
         if k < 2:
-            ts(o, T.zrow[:, :], DL, op.mult, T.dm[:, k:k + 1], op.subtract)
+            ts(o, T.zrow[:, :], DL, op.mult, T.dm[:, k:k + 1], op.subtract, sig="step")
         else:
-            s(S.activation(o, T.zrow[:, :], fn.Identity, bias=T.dm[:, k:k + 1], scale=-DL), x_dz)
-    vw()
+            lin(o, T.zrow[:, :], T.dm[:, k:k + 1], -DL, sig=x_dz)
+    ts(T.kf[:, 0:4], k1, float(-SHB), op.add, -1.0, op.max)
+    pw()
     for k in range(KP):
         if k == 2:
             on(V, x_dz, 2)
-        v(V.tensor_reduce(T.dm[:, 4 + k:5 + k], T.dz[:, 64 * k:64 * k + 64], X, op.min, apply_absolute_value=True))
+        v(V.tensor_reduce(T.dm[:, 4 + k:5 + k], T.dz[:, 64 * k:64 * k + 64], X, op.min, apply_absolute_value=True), "step")
     vw()
+    x_kt = v(V.transpose(T.kt[me32, :], T.kf[me32, :]), new())
+    pw()
     x_km = new()
     for k in range(KP):
         ts(T.kmsg[:, k:k + 1], T.dm[:, 4 + k:5 + k], T.dumpc[:, k:k + 1], op.max, T.kd[:, k:k + 1], op.min, sig=x_km)
@@ -608,79 +663,67 @@ def rank_program(g, core, T, topo):
     on(Q, x_km, KP)
     load(Q, T.kland[:, 4 * r:4 * r + 4], T.kmsg[:, :], x_kown)
 
-    x_eq, x_wq, x_y, x_ysb, x_yo, x_st = new(), new(), new(), new(), new(), new()
-
-    def tile(b):
-        quant("eq", 128 * b, 128 * b + 128, T.eb[:, 3 - b:515 - b], x_eq)
-    fill(T.kf[:, :], 0.0)
-    ts(fc("g4"), ic("ggi"), 4.0, op.mult)
-    ts(tl, fc("u3"), fc("u4"), op.add, 1.0 / 32, op.mult)
-    ts(T.cw[:, 0:7], T.rj[:, 32:39], -128.0, op.add)
-    ts(fc("c7"), fc("pm"), -16.0, op.add)
-    fill(T.ysb[:, 128:144], 0.0)
+    x_wq, x_y, x_ysb, x_yo, x_st, x_oy, x_oyd = new(), new(), new(), new(), new(), new(), new()
+    tt(T.ky[:, 0:32], T.cw[:, 0:8].indirect(offn), T.kh[:, :], op.mult, sig="step")
     on(V, x_w, 16)
     quant("wq", 0, 128, T.wt[:, :], x_wq)
-    on(V, x_ebd)
+    pw()
+    scan(T.ky[:, 32:64], T.r8[:, :], T.ky[:, 0:32], op.mult, op.add, sig="step")
+    on(V, x_ut[2])
+    rest(2)
+    pw()
+    ts(T.ofy[:, 0:8:2], T.ky[:, 39:64:8], 128.0, op.add, sig=x_oy)
+    ts(ic("ogi"), ic("pi"), 4, op.arith_shift_right, 1, op.bitwise_and)
+    ts(ic("t1i"), ic("pmi"), 1, op.bitwise_and)
+    on(V, x_td[0])
+    rest(0)
     vw()
-    ts(T.kf[:, 0:4], k1, float(-SHB), op.add, -1.0, op.max)
-    ts(T.cw[:, 7:8], fl(7), 0.5, op.is_lt, fc("c7"), op.mult)
-    ts(psel, fc("pm"), KP - 1.0, op.min, fc("g4"), op.add)
-    tile(0)
-    vw()
-    tt(T.ky[:, 0:32], T.cw[:, 0:8].indirect(offn), T.kh[:, :], op.mult)
-    x_kt = v(V.transpose(T.kt[0:32, :], T.kf[0:32, :]), new())
-    tile(1)
-    vw()
-    scan(T.ky[:, 32:64], T.r8[:, :], T.ky[:, 0:32], op.mult, op.add)
-    tile(2)
-    vw()
-    ts(T.of3[:, 8:16:2], T.ky[:, 39:64:8], 128.0, op.add)
-    tile(3)
-    vw()
-    for k in range(3):
-        on(M, x_gd[k], 4 if k == 0 else 2)
-    on(M, x_wq)
-    M.matmul_mx(T.ps[:, 0:128], T.wq[:, :], T.wqs[:, :], T.pk[:, 0:128], T.pks[:, 0:128], True, True).then_inc(T.sem[x_y], 1)
-    x_up, x_ut = [new() for b in range(4)], [new() for b in range(4)]
-    on(S, x_y)
-    act(T.ysb[:, 0:128], T.ps[:, 0:128], sig=x_ysb)
-    on(M, x_eq, 4)
-    on(M, x_tq)
+    ts(fc("u1"), ic("ogi"), -2.0, op.mult, 1.0, op.add)
+    on(V, x_td[1])
+    rest(1)
+    on(Q, x_oy)
+    for k in range(8):
+        load(Q, T.oy[16 * k:16 * k + 16, :], T.ofy[16 * r:16 * r + 16, :], x_oyd)
+    on(M, x_sz, 2)
+    on(M, x_gb)
+    on(M, x_ga)
     on(M, x_ptown, 32)
     on(M, "r_ptc", ALL)
     on(M, "r_pts", ALL)
+    x_up = [new() for b in range(4)]
     for b in range(4):
         e = slice(128 * b, 128 * b + 128)
-        M.matmul_mx(T.ps[:, 2048 + 512 * b:2176 + 512 * b], T.eq[:, e], T.eqs[:, e], T.pt[:, :], T.pts[:, :], True, True).then_inc(T.sem[x_up[b]], 1)
-        if b == 0:
-            on(M, x_ysb)
-        M.matmul_mx(T.ps[:, 512 * b:512 * b + P], T.eq[:, e], T.eqs[:, e], T.tq[:, :], T.tqs[:, :], True, True).then_inc(T.sem[x_ut[b]], 1)
+        M.matmul_mx(T.ps[:, 512 * b:512 * b + 128], T.eq[:, e], T.eqs[:, e], T.pt[:, :], T.pts[:, :], True, True).then_inc(T.sem[x_up[b]], 1)
         on(S, x_up[b])
-        act(T.ptd[:, PW * b:PW * b + NR * A], T.ps[:, 2048 + 512 * b:2176 + 512 * b], sig=x_un[b] if b < 2 else None)
-        if b < 2:
-            on(S, x_ut[b])
-            act(T.tbd[:, P * b:P * b + P], T.ps[:, 512 * b:512 * b + P], sig=x_un[b])
+        act(T.ptd[:, PW * b:PW * b + NR * A], T.ps[:, 512 * b:512 * b + 128], sig=x_un[min(b, 1)])
+    on(M, x_un[0])
+    on(M, x_wq)
+    M.matmul_mx(T.ps[:, 0:128], T.wq[:, :], T.wqs[:, :], T.pk[:, best], T.pks[:, best], True, True).then_inc(T.sem[x_y], 1)
+    on(S, x_y)
+    act(T.ysb[:, 0:128], T.ps[:, 0:128], sig=x_ysb)
+    on(S, x_ysb)
+    on(S, x_oyd, 128)
+    for i in range(KP):
+        pick_s(T.yo[:, i:64:4], T.ysb[:, :], T.oy[:, 2 * i:2 * i + 1], x_yo)
     on(Q, x_kt)
-    load(Q, T.kp[:, :], T.kt[0:4, 0:16], x_st)
+    load(Q, T.kp[:, :], T.kt[me32.start:me32.start + 4, 16 * odd:16 * odd + 16], x_st)
     on(Q, x_yo, KP)
     load(Q, T.y[:, :], T.yo[:, :], x_st)
 
-    def ycol(i):
-        v(V.tensor_copy(T.yo[:, i:64:4], T.ysb[:, :].indirect(T.of3[:, 8 + 2 * i:9 + 2 * i])), x_yo)
-    on(V, x_ysb)
-    ycol(0)
-    ycol(1)
     on(V, x_vald)
     on(V, x_cl)
     on(V, x_kown, 16)
     on(V, "r_kept", EV * len(others))
-    ts(klf, T.kland[:, :], float(-DUMP), op.add)
-    ycol(2)
+    ts(klf, T.kland[:, :], float(-DUMP), op.add, sig="step")
     vw()
-    cp(T.okl[:, :], klf.indirect(psel))
-    ycol(3)
-    vw()
+    ts(fc("u3"), ic("t1i"), fc("u1"), op.mult, 272.0, op.mult)
+    pw()
+    cp(T.okl[:, :], klf.indirect(psel), sig="step")
+    ts(fc("u4"), ic("ogi"), 256.0, op.mult, fc("u2"), op.add)
+    pw()
     cp(T.cl[:, :].indirect(T.okl[:, 0:KP]), T.vald[:, :], sig="claim")
+    vw()
+    ts(tl, fc("u3"), fc("u4"), op.add, 1.0 / 32, op.mult)
     on(V, "claim")
     v(V.transpose(T.ttc[:, 0:256], T.cl[:, c0:c0 + 256]))
     v(V.transpose(T.ttc[:, 256:544], T.cl[:, c0 - 16:c0 + 272])); vw()
@@ -689,47 +732,32 @@ def rank_program(g, core, T, topo):
     for k in range(4):
         tt(T.pp[32 * k:32 * k + 32, 16:33], T.mx[0:32, 40:74:2], T.mx[0:32, 41:74:2], op.max)
     vw()
-    x_new, x_oc, x_os, x_st2, x_gp = new(), [new(), new()], new(), new(), [new(), new()]
+    x_new, x_st2, x_gp = [new(), new()], new(), [new(), new()]
     x_ptl = ts(T.ptl[:, :], ub.indirect(tl), -1.0, op.mult, float(NR * A), op.add, sig=new())
-    ts(T.sel[:, 0:16], ub.indirect(tl), 0.5, op.is_gt, float(P), op.mult)
-    sw()
-    on(S, x_un[0], 3)
-    on(S, x_ptl)
+    for q_ in (V, S):
+        on(q_, x_un[0])
+        on(q_, x_un[1], 3)
+        on(q_, x_rest, 4)
+        on(q_, x_ptl)
     for b in (2, 3):
         pick_s(T.gp[:, P * b - 2 * P:P * b - P], T.ptd[:, PW * b:PW * b + PW], T.ptl[:, 0:16], x_gp[b - 2])
-    on(V, x_un[0], 3)
-    on(V, x_ptl)
     for b in range(4):
         o = T.bb[:, b:1024:4]
         if b < 2:
-            if b == 1:
-                on(V, x_un[1], 2)
             tt(o, T.ptd[:, PW * b:PW * b + PW].indirect(T.ptl[:, 0:16]), T.tbd[:, P * b:P * b + P], op.add, sig="step")
         else:
-            on(V, x_ut[b])
             on(V, x_gp[b - 2])
-            tt(o, T.gp[:, P * b - 2 * P:P * b - P], T.ps[:, 512 * b:512 * b + P], op.add, sig="step")
-    vw()
-    tt(T.sel[:, 16:32], T.sel[:, 0:16], jw, op.add)
+            tt(o, T.gp[:, P * b - 2 * P:P * b - P], T.ps[:, 2048 + 512 * b:2048 + 512 * b + P], op.add, sig="step")
     pw()
-    quant("tn", P, 2 * P, T.bb[:, :], x_new)
-    vw()
-    x_sel = cp(T.sell[:, :], T.sel[:, 16:32], sig=new())
-    for q_ in (V, S):
-        on(q_, x_tno, 32)
-        on(q_, x_sel)
-        on(q_, x_new)
-    pick_s(T.ocqs[:, :], T.tns[:, :], T.sell[:, 0:16], x_os)
     for h in range(2):
-        a = slice(128 * h, 128 * h + 128)
-        pick_v(T.ocq[:, a], T.tn[:, :], T.sell[:, 8 * h:8 * h + 8], x_oc[h])
-        on(Q, x_oc[h])
-        load(Q, T.oc[:, 512 * h:512 * h + 512], T.ocq[:, a].bitcast(u8), x_st)
-    on(S, x_os)
+        quant("tn", 128 * h, 128 * h + 128, T.bb[:, 512 * h:512 * h + 512], x_new[h])
+        on(Q, x_new[h])
+        load(Q, T.oc[:, 512 * h:512 * h + 512], T.tn[:, 128 * h:128 * h + 128].bitcast(u8), x_st)
+        on(S, x_new[h])
     for k in range(4):
-        load(S, T.osc[4 * k:4 * k + 4, :], T.ocqs[32 * k:32 * k + 4, :], x_st2)
-    on(Q, x_st, 64)
-    on(S, x_st2, 64)
+        load(S if k < 3 else Q, T.osc[4 * k:4 * k + 4, :], T.tns[32 * k:32 * k + 4, :], x_st2 if k < 3 else x_st)
+    on(Q, x_st, 80)
+    on(S, x_st2, 48)
     on(V, "v", vn[0])
     on(S, "s", sn_[0])
     for n in ROADS:

@@ -13,32 +13,35 @@ S0 = P * (NR - 1)
 FW = 48
 RO = NR * A + 1
 PW = NR * A + P + 8
-R0, R1 = 3, 14
+R0, R1 = 2, 14
 BA = 4
+UP = 4096.0
+HI = 2048.0
 ORDER = (1, 4, 2, 5, 3, 6, 7)
-WAVES = ((0, 4), (4, 7))
+WAVES = (slice(0, 4), slice(4, 7))
 
 F, B, I, U = "float32", "bfloat16", "int32", "uint16"
 SB = {
-    "cdi": (16, I), "offl": (16, U), "ones": (64, B), "zz": (288, B), "pres": (4 * (S0 + NR * P), B), "r4": (2 * P, B), "orx": (4 * P, B),
-    "cnt": (P + 32, B), "ind": (P, B), "indc": (P, B), "junk": (2 * P, B), "req": (3, U), "rland": (24, U), "reql": (24, U), "rj": (32, F),
-    "jwb": (2, B), "dumpc": (4, F), "imj": (96, F), "r8": (32, F), "tro": (8, U), "of3": (8, U), "ofx": (32, U), "ofy": (8, U), "oy": (8, U),
-    "offs": (8, U), "offp": (16, U), "cf": (96, F), "m16": (256, B), "m4": (288, B),
-    "r16": (256, B), "sg": (256, B), "zw": (ZW, F), "vals": (64, B), "vald": (64, B), "erow": (160, F), "erow2": (256, F),
-    "lf": (32, F), "lt": (32, F), "cm2": (256, B), "rs": (16, F), "ru": (32, F), "rel": (256, F), "fs": (24, F), "oh2": (256, F),
-    "offw": (16, U), "lw": (256, F), "lall": (128, F), "la": (128, F), "lsm": (256, F), "lsz": (256, F), "offc": (16, U),
-    "sm": (256, F), "sz": (256, F), "rep": (256, F), "cm": (256, B), "rk": (256, B), "oh": (128, F), "lm": (128, F),
-    "lz": (128, F), "offr": (10, U), "ss": (128, F), "ssz": (128, F), "nm": (128, F), "nz": (128, F), "gb": (512, B),
+    "cdi": (16, I), "offl": (16, U), "ones": (64, B), "pres": (4 * (S0 + NR * P), B), "r4": (2 * P, B), "orx": (4 * P, B),
+    "cnt": (P + 32, B), "ind": (P, B), "indc": (P, B), "junk": (2 * P, B), "req": (3, B), "rland": (32, B), "rt1": (32, B), "rt2": (32, B),
+    "reql": (24, U), "rj": (32, F),
+    "jwb": (2, B), "dumpc": (4, F), "imj": (96, F), "r8": (64, F), "tro": (8, U), "of3": (8, U), "ofx": (32, U), "ofy": (8, U), "oy": (8, U),
+    "offs": (16, U), "offp": (16, U), "cf": (48, F), "m16": (256, B), "m4": (288, B), "m4a": (16, B),
+    "r16": (256, B), "sg": (256, B), "zw": (ZW, F), "vals": (64, B), "vald": (64, B), "erow": (160, F), "n256": (256, B),
+    "lf": (32, F), "lt": (32, F), "cm2": (256, B), "rs": (48, F), "oh2": (256, F), "rel": (256, F), "offj": (16, U), "mn": (128, B),
+    "offw": (16, U), "lw": (256, F), "lall": (256, F), "la": (256, F), "lb": (256, F), "offg": (16, U), "lsm": (256, F), "lsz": (256, F), "offc": (16, U),
+    "sm": (256, F), "sz": (256, F), "rep": (256, F), "cm": (256, B), "rk": (256, B), "oh": (128, B), "dec": (128, B), "p16": (32, B),
+    "lz": (128, B), "offr": (12, U), "ss": (128, F), "ssz": (128, F), "nm": (128, F), "nz": (128, F), "gb": (512, B),
     "gs": (512, B), "fb": (64, F), "pp": (40, F), "bo": (4, F), "kh": (32, F), "km": (64, F), "ky": (64, F),
-    "kf": (32, F), "kt": (32, F), "kd": (16, F), "kl0": (4, U), "zrow": (64, F), "dz": (256, F), "dm": (8, F), "kmsg": (4, U),
-    "kland": (32, U), "kc": (32, F), "okl": (16, U), "ysb": (144, F), "yo": (64, F), "mx": (80, F),
-    "xt": (512, B), "wt": (512, B), "tt": (1024, B), "ebm": (520, B), "eb": (520, B), "cl": (CLW, B), "ttc": (544, B), "cw": (16, F),
+    "kf": (32, F), "kt": (32, F), "kd": (16, F), "kl0": (4, U), "zrow": (64, F), "dz": (64, F), "dm": (8, F), "kmsg": (4, U),
+    "kland": (32, U), "kc": (96, F), "okl": (16, U), "ysb": (144, F), "yo": (64, F), "mx": (80, F),
+    "xz": (512, B), "wt": (512, B), "tt": (1024, B), "eb": (520, B), "cl": (CLW, B), "ttc": (544, B),
     "ptd": (4 * PW, F), "tbd": (2 * P, B), "gp": (2 * P, F), "ptl": (16, U), "bb": (1024, B),
 }
-CODES = {"p8": 128, "wq": 128, "tq": 256, "win": 592, "tn": 256, "snd": 336, "cand": 256, "pk": 144, "eq": 512, "pt": 128}
+CODES = {"p1": 128, "p8": 128, "wq": 128, "tq": 256, "win": 592, "tn": 256, "snd": 336, "cand": 256, "pk": 160, "eq": 512, "pt": 128}
 ICOL = {n: i for i, n in enumerate(["pi", "pmi", "ggi", "ogi", "t1i", "t4i"])}
-FCOL = {n: i for i, n in enumerate(["pm", "u1", "u2", "u3", "u4", "pm8", "u5", "u6", "isr", "hneg", "kap", "g4", "c7", "g16", "n7",
-                                    "sb1", "sb2", "ac1", "ac2", "b0", "b1", "base", "nbase", "gs0"])}
+FCOL = {n: i for i, n in enumerate(["pm", "u1", "u2", "u3", "u4", "pm8", "u5", "u6", "isr", "hneg", "kap", "g4", "c7", "g16",
+                                    "sb1", "sb2", "ac1", "ac2", "b0", "nbase", "c6", "kn", "v1", "v3", "v4", "pmh", "gs0"])}
 
 SCRATCH = {n: ("sbuf", [128, k], d) for n, (k, d) in SB.items()}
 SCRATCH["dl"] = ("dram", [16, 128], F)
@@ -49,8 +52,8 @@ for _n, _k in CODES.items():
     SCRATCH[_n + "s"] = ("sbuf", [128, _k], "uint8")
 SCRATCH["ps"] = ("psum", [128, 4096], F)
 
-ROADS = ["ptc", "pts", "req", "cod0", "cod1", "pln0", "pln1", "kept"]
-XS = ["x%d" % i for i in range(128)]
+ROADS = ["ptc", "pts", "req", "cod", "pln", "kept"]
+XS = ["x%d" % i for i in range(132)]
 SEMAPHORES = ["v", "s", "step", "scat", "claim", "prune"] + ["r_" + n for n in ROADS] + ["l_" + n for n in ROADS] + XS
 
 
@@ -61,7 +64,6 @@ def rank_program(g, core, T, topo):
     V, S, Q, M = g.vector, g.scalar, g.sync, g.tensor
     op, X, fn = AluOpType, AxisListType.X, ActivationFunctionType
     others = [r ^ m for m in ORDER]
-    wave = [others[a:b] for a, b in WAVES]
     u8, u32 = dt.uint8, dt.uint32
 
     free = list(XS)
@@ -155,7 +157,7 @@ def rank_program(g, core, T, topo):
                 out[q] = sum(1 << e[j] for j in range(k, len(e), len(e) // n))
         return out
 
-    def send(src, dst, road, dests=others, n=2):
+    def send(src, dst, road, dests, n):
         tr, mk = [], masks(dests, n)
         for q in dests:
             rid, pid = topo.addr(T.cores[q])[:2]
@@ -173,7 +175,7 @@ def rank_program(g, core, T, topo):
         g.remote_dma_fused([RemoteDMATransfer(dst_ids=ids, dma_engine_mask=every, remote_sem=T.sem["r_" + road], srcs=[src],
                                               dsts=[dst(q) for q in others])], local_sem=T.sem["l_" + road])
 
-    ALL = 2 * (NR - 1)
+    ALL = 2 * len(others)
 
     def seat(a, b):
         return ORDER.index(a ^ b)
@@ -182,7 +184,7 @@ def rank_program(g, core, T, topo):
         return LC * ((r - q - 1) % NR)
 
     row16, jm = T.rj[:, 0:16], T.rj[:, 16:32]
-    dd, ma, mb, lts, crow, dif = [T.cf[:, 16 * k:16 * k + 16] for k in range(6)]
+    dd, lts, dif = [T.cf[:, 16 * k:16 * k + 16] for k in range(3)]
     im64, jm8 = T.imj[:, 0:64], T.imj[:, 64:96]
     psel, tl = T.tro[:, 4:5], T.tro[:, 0:1]
     offn, offz = T.of3[:, 0:2], T.of3[:, 2:4]
@@ -191,230 +193,232 @@ def rank_program(g, core, T, topo):
     odd = r % 2
     me32 = slice(32 * (r // 2), 32 * (r // 2) + 32)
 
+    def zeros(n):
+        return T.xz[:, 64:64 + n]
+
     x_cd, x_x, x_tb, x_w = new(), new(), new(), new()
     for k in range(8):
         load(Q if k < 4 else S, T.cdi[16 * k:16 * k + 16, :], T.cd[:, :], x_cd)
-    load(Q, T.xt[:, 0:64], T.x[:, :], x_x)
+    load(Q, T.xz[:, 0:64], T.x[:, :], x_x)
     load(Q, T.tt[:, :], T.tb[:, :], x_tb)
     load(Q, T.wt[:, :], T.w[:, :], x_w)
 
-    x_pi, x_io1, x_io2, x_er2, x_eb, x_ebd, x_r4, x_jm = new(), new(), new(), new(), new(), new(), new(), new()
+    x_pi, x_io1, x_io2, x_er2, x_ebd, x_r4, x_jm = new(), new(), new(), new(), new(), new(), new()
     g.iota(ic("pi"), [[1, 1]], 0, 1).then_inc(T.sem[x_pi], 1)
     iota(jm, [[1, 16]], 0, 0, x_jm)
-    iota(row16, [[16, 16]], 0, 0, x_io1)
     iota(T.r4[:, :], [[0, P // 2], [1, 4]], 0, 0, x_r4)
-    iota(T.erow2[:, :], [[2, 16], [0, 16]], 1 - C, 0, x_er2)
+    iota(row16, [[16, 16]], 0, 0, x_io1)
 
-    x_r16, x_m, x_zz, x_isr, x_pr, x_pz = new(), new(), new(), new(), new(), new()
-    fill(T.zz[:, :], 0.0, sig=x_zz)
+    x_m, x_zz, x_pr, x_hn, x_gs, x_b1, x_p1, x_pm = new(), new(), new(), new(), new(), new(), new(), new()
+    fill(T.xz[:, 64:512], 0.0, sig=x_zz)
     on(V, x_pi)
     ts(ic("ggi"), ic("pi"), 4, op.arith_shift_right)
+    fill(T.pres[:, 4 * S0:4 * S0 + 4 * P:4], 0.0, sig="step")
+    vw()
+    x_is = ts(fc("isr"), ic("ggi"), float(r), op.is_equal, sig=new())
+    ts(fc("gs0"), ic("ggi"), float(-4 * P), op.mult, float(4 * S0), op.add, sig=x_gs)
     ts(ic("pmi"), ic("pi"), 15, op.bitwise_and)
-    fill(T.pres[:, 4 * S0:4 * S0 + 4 * P], 0.0, sig=x_pz)
-    vw()
-    ts(fc("isr"), ic("ggi"), float(r), op.is_equal, sig=x_isr)
-    ts(fc("gs0"), ic("ggi"), float(-4 * P), op.mult, float(4 * S0), op.add)
-    x_hn = ts(fc("hneg"), ic("ggi"), float(-P), op.mult, 16.0, op.add, sig=new())
+    fill(T.pres[:, 4 * S0 + 1:4 * S0 + 4 * P:4], 0.0, sig="step")
     on(V, x_jm)
-    vw()
+    on(V, x_gs)
     ts(T.bo[:, :], T.rj[:, 16:20], fc("gs0"), op.add, sig="step")
-    x_pm = cp(fc("pm"), ic("pmi"), sig=new())
+    vw()
+    cp(fc("pm"), ic("pmi"), sig=x_pm)
     pw()
 
-    x_xt, x_cz, x_dd = new(), new(), new()
+    x_cz, x_dd, x_b0 = new(), new(), new()
     on(S, x_zz)
-    lin(T.ones[:, :], T.zz[:, 0:64], 1.0, sig=x_pr)
-    for k in range(2):
-        lin(T.ebm[:, 260 * k:260 * k + 260], T.zz[:, 0:260], 0.5, sig=x_eb)
-    on(S, x_pz)
-    on(S, x_isr)
-    own = T.pres[:, 4 * S0:4 * S0 + 4 * P:4]
-    lin(own, own, fc("isr"), sig=x_pr)
-    on(S, x_x, 16)
-    act(T.xt[:, 64:128], T.xt[:, 0:64]); sw()
-    act(T.xt[:, 128:256], T.xt[:, 0:128]); sw()
-    act(T.xt[:, 256:512], T.xt[:, 0:256], sig=x_xt)
+    act(T.pres[:, 4 * S0 + 2:4 * S0 + 4 * P:4], zeros(P), sig=x_pr)
+    on(S, x_is)
+    lin(T.pres[:, 4 * S0 + 3:4 * S0 + 4 * P:4], zeros(P), fc("isr"), sig=x_pr)
+    lin(T.ones[:, :], zeros(64), 1.0, sig=x_pr)
     on(S, x_pm)
-    on(S, x_jm)
-    lin(dd, jm, fc("pm"), -1.0, sig=x_dd)
+    lin(fc("pmh"), fc("pm"), 0.5)
     act(T.jwb[:, 0:1], fc("pm"), sig=x_dd)
+    lin(fc("sb1"), fc("pm"), 16.5)
+    sw()
+    on(S, x_jm)
+    lin(dd, jm, fc("pmh"), -1.0, sig=x_dd)
+    lin(fc("sb2"), fc("pm"), 32.5)
+    x_u2, x_k2 = new(), new()
+    lin(fc("u2"), fc("pm"), 0.0, 16.0, sig=x_u2)
+    lin(fc("u5"), fc("pm"), 15.0, 16.0, sig=x_k2)
+    x_r16b, x_r8, x_r9, x_lz = new(), new(), new(), new()
+    lin(T.r16[:, :], zeros(P), 1.0)
+    lin(T.fb[:, :], zeros(64), 1.0)
+    sw()
+    act(T.r16[:, 0:256:16], zeros(16), sig=x_r16b)
+    act(T.fb[:, FW - 3:FW:2], zeros(2), sig=x_r8)
 
     on(V, x_cd, 128)
     for k in range(4):
         ts(T.offl[:, k:16:4], T.cdi[:, k:16:4], 4.0, op.mult, T.bo[:, k:k + 1], op.add, sig="step")
-    x_p8, x_lt, x_b0 = new(), new(), new()
-    cp(T.lf[:, 0:16], T.cdi[:, :])
+    x_p8, x_p8s, x_lt = new(), new(), new()
+    on(V, x_x, 16)
+    on(V, x_zz)
+    quant("p1", 0, 128, T.xz[:, :], x_p1)
     pw()
-    on(V, x_pr, 2)
+    on(V, x_pr, 3)
     for i in range(4):
         if i:
             on(V, "scat", i)
         v(V.tensor_copy(T.pres[:, :].indirect(T.offl[:, 4 * i:4 * i + 4]), T.ones[:, :]), "scat")
-        if i == 0:
-            cp(T.lf[:, 16:32], T.cdi[:, :])
-        if i == 1:
-            on(V, x_xt)
-            quant("p8", 0, 128, T.xt[:, :], x_p8)
+        if i < 2:
+            cp(T.lf[:, 16 * i:16 * i + 16], T.cdi[:, :])
         if i == 2:
             vw()
             v(V.transpose(T.lt[:, :], T.lf[:, :]), x_lt)
         if i == 3:
-            ts(fc("b0"), ic("ggi"), float(r), op.is_le, float(LC * NR), op.mult, sig=x_b0)
+            ts(fc("b0"), ic("ggi"), float(r), op.is_gt, float(LC * NR), op.mult, sig=x_b1)
     on(V, "scat", 4)
     on(V, x_r4)
     for k in range(2):
         a = 2 * P * k
         scan(T.orx[:, a:a + 2 * P], T.r4[:, :], T.pres[:, 4 * S0 + a:4 * S0 + a + 2 * P], op.min, op.max, sig="step")
-    on(V, x_dd, 2)
-    ts(T.m16[:, 0:16], dd, 0.0, op.is_equal, sig=x_m)
+    ts(fc("hneg"), ic("ggi"), float(-P), op.mult, 16.0, op.add, sig=x_hn)
     pw()
     x_cnt = scan(T.cnt[:, 16:P + 16], T.orx[:, 3:4 * P:4], T.orx[:, 3:4 * P:4], op.add, op.max, sig=new())
-    on(V, x_hn)
-    ts(T.offw[:, :], T.cdi[:, :], fc("hneg"), op.add, P + 16.0, op.min)
+    fill(T.offr[:, :], 0)
 
-    x_r16b, x_m16, x_cm, x_acc, x_cl, x_r8, x_rs, x_u, x_fs, x_k = [new() for k in range(10)]
-    on(S, x_hn)
-    lin(fc("sb1"), fc("pm"), 16.5)
-    lin(fc("sb2"), fc("pm"), 32.5)
-    s(S.activation(T.r16[:, 0:16], jm, fn.Sign), x_r16)
-    lin(fc("u2"), fc("pm"), 0.0, 16.0, sig=x_k)
-    lin(fc("u5"), fc("pm"), 15.0, 16.0, sig=x_k)
-    lin(fc("g16"), fc("hneg"), -1.0, 1.0 / 16)
-    lin(fc("g4"), fc("hneg"), 0.25, -1.0 / 64, sig=x_k)
+    x_m16, x_cm, x_acc, x_cl, x_rs, x_op = [new() for k in range(6)]
 
     def signs(a, b):
         for c in range(a, b):
             s(S.activation(T.cm2[:, 16 * c:16 * c + 16], T.lt[:, 0:16], fn.Sign, bias=T.lt[:, c:c + 1], scale=-1.0, accum_out=T.rs[:, c:c + 1]), x_cm)
 
-    def rows(t, n, m, sig, gaps=()):
-        gaps = list(gaps)
-        while n < m:
-            k = min(n, m - n)
-            act(t[:, n:n + k], t[:, 0:k], sig=sig if n + k == m else None)
-            seen = sn_[0]
-            if gaps:
-                gaps.pop(0)()
-            n += k
-            if n < m:
-                S.wait_ge(T.sem["s"], seen)
     on(S, x_lt)
-    signs(0, 3)
+    signs(0, 2)
+    on(S, x_gs)
+    on(S, x_b1)
+    lin(fc("nbase"), fc("gs0"), fc("b0"), LC / (4.0 * P), sig=x_b0)
+    signs(2, 3)
     on(S, x_b0)
-    lin(fc("b1"), fc("hneg"), fc("b0"), -LC / P)
-    signs(3, 4)
+    lin(T.cnt[:, 0:16], zeros(16), fc("nbase"), sig=x_cz)
+    lin(T.cnt[:, P + 16:P + 32], zeros(16), fc("nbase"), sig=x_cz)
+    signs(3, 5)
     sw()
-    lin(fc("base"), fc("b1"), 16.0 * LC / P - LC * (r + 1), sig=x_k)
-    lin(fc("nbase"), fc("b1"), LC * (r + 1) - 16.0 * LC / P, -1.0)
-    signs(4, 5)
-    sw()
-    lin(T.cnt[:, 0:16], T.zz[:, 0:16], fc("nbase"), sig=x_cz)
-    lin(T.cnt[:, P + 16:P + 32], T.zz[:, 0:16], fc("nbase"), sig=x_cz)
-    signs(5, 7)
     on(S, x_cnt)
     for k in (1, 2):
         s(S.activation(T.junk[:, P * k - P:P * k - 1], T.cnt[:, 16:P + 15], fn.Sign, bias=fc("sb%d" % k), scale=-1.0, accum_out=fc("ac%d" % k)), x_acc)
-    signs(7, C)
-    on(S, x_r16)
-
-    def scaled():
-        on(S, x_cm, C)
-        s(S.activation(T.ru[:, 0:16], T.rs[:, :], fn.Copy, scale=1024.0), x_rs)
-    rows(T.r16, 16, 256, x_r16b, [scaled, lambda: lin(crow, jm, float(2048 * (C - 1) - SHB), -2048.0, sig=x_fs),
-                                  lambda: act(T.fs[:, 16:17], T.zz[:, 0:1], sig=x_fs)])
-
-    def above(a, b):
-        for k in range(a, b):
-            s(S.activation(T.rel[:, 16 * k:16 * k + 16], T.ru[:, 16:32], fn.Relu, bias=float(1024 * (C - 1 - 2 * k)), accum_out=T.fs[:, k:k + 1]), x_fs)
+    signs(5, C)
+    on(S, x_cm, C)
+    lin(T.rs[:, 16:32], T.rs[:, 0:16], 8.0 * (C - 1) + 1, 8.0, sig=x_rs)
 
     on(V, x_cnt)
     on(V, x_io1)
     on(V, x_pm)
+    on(V, x_dd, 2)
     ts(T.ind[:, 0:P - 1], T.cnt[:, 16:P + 15], T.jwb[:, 0:1], op.is_le, sig="step")
-    ts(T.offp[:, :], row16, 0.0, op.mult, fc("pm"), op.add)
+    ts(T.offp[:, :], row16, 0.0, op.mult, fc("pm"), op.add, sig=x_op)
     pw()
     scan(T.indc[:, 0:P - 1], T.ind[:, 0:P - 1], T.ind[:, 0:P - 1], op.add, op.max, sig="step")
-    ts(ma, dd, 0.0, op.is_equal, -128.0, op.mult)
+    ts(T.p16[:, 16:32], dd, 0.5, op.is_equal, sig=x_m)
     pw()
     x_req = new()
     cp(T.req[:, 0:1], T.indc[:, P - 2:P - 1], sig=x_req)
-    ts(mb, dd, -1.0, op.is_equal, 10.0, op.mult)
+    on(V, x_hn)
+    ts(T.offw[:, :], T.cdi[:, :], fc("hneg"), op.add, P + 16.0, op.min)
     on(V, x_acc, 2)
     ts(T.req[:, 1:3], T.fc[:, FCOL["ac1"]:FCOL["ac1"] + 2], 0.5, op.mult, (P - 1) * 0.5, op.add, sig=x_req)
 
-    on(g, x_p8)
-    send(lambda q: T.p8[:, 0:A].bitcast(u8), lambda q: T.pt[:, A * r:A * r + A].bitcast(u8), "ptc")
+    def halves(k):
+        g.affine_select(T.eb[:, 258 * k:258 * k + 258], zeros(258), [[1, 258]], op.not_equal, 0.5, 258 * k - 3, -4).then_inc(T.sem[x_ebd], 1)
+    on(g, x_p1)
+    send(lambda q: T.p1[:, 0:A].bitcast(u8), lambda q: T.pt[:, A * r:A * r + A].bitcast(u8), "ptc", others, 2)
+    on(g, x_zz)
+    halves(0)
     on(g, x_req, 2)
     tell(T.req[:, :], lambda q: T.rland[:, 3 * seat(q, r):3 * seat(q, r) + 3], "req")
-    on(g, x_eb, 2)
-    g.affine_select(T.eb[:, 0:516], T.ebm[:, 0:516], [[1, 516]], op.is_equal, 0.0, -3, -4).then_inc(T.sem[x_ebd], 1)
+    halves(1)
+    iota(T.n256[:, :], [[1, P]], 1, 0, x_er2)
 
-    x_lv, x_tq, x_h1, x_h2, x_wino, x_rl, x_ptown = new(), new(), new(), new(), new(), new(), new()
-    x_zw, x_vals, x_vald, x_kown, x_sg, x_eq = new(), new(), new(), new(), new(), new()
+    x_lv, x_tq, x_h1, x_h2, x_wino, x_rl, x_ptown, x_rz = new(), new(), new(), new(), new(), new(), new(), new()
+    x_zw, x_vals, x_vald, x_kown, x_sg, x_eq = new(), new(), new(), new(), new(), [new(), new()]
     on(V, x_cz, 2)
-    on(V, x_k, 4)
+    on(V, x_b0)
+    on(V, x_jm)
+    on(V, x_op)
     vw()
-    ts(T.lw[:, :], T.cnt[:, :].indirect(T.offw[:, :]), fc("base"), op.add, sig=x_lv)
+    ts(T.lw[:, :], T.cnt[:, :].indirect(T.offw[:, :]), fc("nbase"), op.subtract, UP, op.mult, sig=x_lv)
     on(V, x_tb, 16)
     quant("tq", 0, P, T.tt[:, :], x_tq)
-    on(V, x_lt)
-    on(V, x_rs)
-    tt(T.ru[:, 16:32], T.ru[:, 0:16], T.lt[:, 0:16], op.add, sig=x_u)
-    x_m4a, x_m4 = tt(T.m4[:, 0:16], ma, mb, op.add, sig=new()), new()
-    ts(T.offs[:, :], T.rj[:, 0:8], 0.0, op.mult, fc("u5"), op.add)
-    on(V, x_er2)
-    tt(T.oh2[:, :], T.rs[:, :].indirect(T.offp[:, 0:16]), T.erow2[:, :], op.is_equal)
-    ts(ic("t4i"), ic("pmi"), 7, op.bitwise_and)
-    fill(T.offr[:, :], 0)
-    on(V, x_ebd)
-    for b in range(4):
-        quant("eq", 128 * b, 128 * b + 128, T.eb[:, 3 - b:515 - b], x_eq)
+
+    def tile(b):
+        quant("eq", 128 * b, 128 * b + 128, T.eb[:, 3 - b:515 - b], x_eq[b // 2])
+    on(V, x_u2)
+    x_og = ts(T.offg[:, :], jm, fc("u2"), op.add, sig=new())
+    on(V, x_p1)
+    pick_v(T.p8[:, :], T.p1[:, :], T.offp[:, 0:8], x_p8)
+    on(V, x_ebd, 2)
+    for b in range(3):
+        tile(b)
+    on(V, x_rz, 16)
+    on(V, "r_req", EV * len(others))
+    v(V.transpose(T.rt1[me32, :], T.rland[me32, :]), "step")
+    x_m4a, x_m4 = ts(T.m4a[:, 0:16], dd, -128.0, op.mult, 2.0, op.min, sig=new()), new()
+    pw()
+    cp(T.rt1[me32, 16 - 16 * odd:32 - 16 * odd], T.rt1[me32, 16 * odd:16 * odd + 16], sig="step")
+    on(V, x_k2)
+    ts(T.offs[:, :], row16, 0.0, op.mult, fc("u5"), op.add)
+    pw()
+    v(V.transpose(T.rt2[me32, :], T.rt1[me32, :]), "step")
+    ts(ic("t4i"), ic("pi"), 7, op.bitwise_and)
+    pw()
+    for k in range(4):
+        cp(T.reql[32 * k:32 * k + 32, 0:21], T.rt2[me32, 0:21], sig=x_rl)
+    ts(ic("ogi"), ic("pi"), 4, op.arith_shift_right, 1, op.bitwise_and)
 
     x_ut = [new() for b in range(4)]
-    on(M, x_eq, 4)
-    on(M, x_tq)
-    for b in range(4):
-        e = slice(128 * b, 128 * b + 128)
-        M.matmul_mx(T.ps[:, 2048 + 512 * b:2048 + 512 * b + P], T.eq[:, e], T.eqs[:, e], T.tq[:, :], T.tqs[:, :], True, True).then_inc(T.sem[x_ut[b]], 1)
 
-    on(Q, x_p8)
-    load(Q, T.pt[:, A * r:A * r + A].bitcast(u8), T.p8[:, 0:A].bitcast(u8), x_ptown)
-    load(Q, T.pts[:, A * r:A * r + A], T.p8s[:, 0:A], x_ptown)
+    def half(b):
+        e = slice(128 * b, 128 * b + 128)
+        on(M, x_eq[b // 2], 2)
+        M.matmul_mx(T.ps[:, 2048 + 512 * b:2048 + 512 * b + P], T.eq[:, e], T.eqs[:, e], T.tq[:, :], T.tqs[:, :], True, True).then_inc(T.sem[x_ut[b]], 1)
+    on(M, x_tq)
+    half(0)
+    half(1)
+
+    on(Q, x_zz)
+    load(Q, T.rland[:, 21:32], zeros(11), x_rz)
+    on(Q, x_p1)
+    load(Q, T.pt[:, A * r:A * r + A].bitcast(u8), T.p1[:, 0:A].bitcast(u8), x_ptown)
+    load(Q, T.pts[:, A * r:A * r + A], T.p1s[:, 0:A], x_ptown)
     on(Q, x_lv)
     for k in range(8):
         load(Q, T.dl[:, 16 * k:16 * k + 16], T.lw[16 * k:16 * k + 1, :], x_h1)
-    for q_ in (S, Q):
-        on(q_, "r_req", EV * len(others))
-        for k in range(8):
-            if (k < 4) == (q_ is S):
-                load(q_, T.reql[16 * k:16 * k + 16, 0:21], T.rland[16 * r:16 * r + 16, 0:21], x_rl)
-    on(S, x_u)
-    above(0, 8)
-    on(Q, x_h1, 128)
+    x_d8, x_kz = new(), new()
+    act(T.lall[:, 128:144], T.lt[:, 0:16], sig=x_lz)
+    act(T.lall[:, 144:256], zeros(112), sig=x_lz)
+    act(T.pp[:, 0:16], zeros(16), sig=x_r9)
+    on(S, x_op)
+    on(S, x_p1)
+    pick_s(T.p8s[:, :], T.p1s[:, :], T.offp[:, 0:8], x_p8s)
+    for q_ in (Q, S):
+        on(q_, x_h1, 128)
     for k in range(8):
-        load(Q, T.lall[16 * k:16 * k + 16, :], T.dl[:, :], x_h2)
+        load(Q if k < 4 else S, T.lall[16 * k:16 * k + 16, 0:128], T.dl[:, :], x_h2)
     on(Q, x_tq)
     load(Q, T.win[:, WOWN:WOWN + P].bitcast(u8), T.tq[:, :].bitcast(u8), x_wino)
     load(Q, T.wins[:, WOWN:WOWN + P], T.tqs[:, :], x_wino)
 
     for q_ in (V, S):
         on(q_, x_tq)
-        on(q_, x_rl, 128)
+        on(q_, x_rl, 4)
 
     def codes(w):
-        send(lambda q: T.snd[:, LC * seat(r, q):LC * seat(r, q) + LC].bitcast(u8), lambda q: T.win[:, spot(q):spot(q) + LC].bitcast(u8), "cod%d" % w, wave[w], 4)
+        send(lambda q: T.snd[:, LC * seat(r, q):LC * seat(r, q) + LC].bitcast(u8), lambda q: T.win[:, spot(q):spot(q) + LC].bitcast(u8), "cod", others[WAVES[w]], 4)
 
     def planes(w):
-        send(lambda q: T.snds[:, LC * seat(r, q):LC * seat(r, q) + LC], lambda q: T.wins[:, spot(q):spot(q) + LC], "pln%d" % w, wave[w], 4)
+        send(lambda q: T.snds[:, LC * seat(r, q):LC * seat(r, q) + LC], lambda q: T.wins[:, spot(q):spot(q) + LC], "pln", others[WAVES[w]], 4)
     for w in range(2):
         x_sndc, x_snds = new(), new()
-        c, d = WAVES[w]
+        c, d = WAVES[w].start, WAVES[w].stop
         pick_v(T.snd[:, LC * c:LC * d], T.tq[:, :], T.reql[:, 3 * c:3 * d], x_sndc)
         pick_s(T.snds[:, LC * c:LC * d], T.tqs[:, :], T.reql[:, 3 * c:3 * d], x_snds)
         for sig, go in ((x_sndc, codes), (x_snds, planes))[::1 - 2 * w]:
             on(g, sig)
             go(w)
-    send(lambda q: T.p8s[:, 0:A], lambda q: T.pts[:, A * r:A * r + A], "pts")
-    on(g, x_r16)
+    send(lambda q: T.p1s[:, 0:A], lambda q: T.pts[:, A * r:A * r + A], "pts", others, 2)
     on(g, x_r16b)
     g.affine_select(T.sg[:, :], T.r16[:, :], [[1, 16], [-1, 16]], op.not_equal, -1.0, 0, 0).then_inc(T.sem[x_sg], 1)
     x_io3 = new()
@@ -422,52 +426,60 @@ def rank_program(g, core, T, topo):
     iota(T.erow[:, 0:128], [[1, 8], [-1, 16]], C + 1 - E, 0, x_io2)
     iota(jm8, [[0, 4], [1, 8]], 0, 0, x_io3)
     iota(T.vals[:, :], [[0, 4], [-1, 16]], NR * A, 0, x_vals)
-    iota(T.erow[:, 128:160], [[-1, 4], [1, 8]], 0, 0, x_zw)
+    iota(T.erow[:, 128:160], [[-1, 4], [-1, 8]], E - 1, 0, x_zw)
     iota(im64, [[0, 4], [1, 16]], 0, 0, x_zw)
     iota(T.zw[:, :], [[32, ZW]], 0, 0, x_zw)
     iota(T.cl[:, c0 - 16:c0 + 272], [[-1, 288]], 15, 0, x_cl)
 
-    x_un = [new(), new()]
+    x_un, x_oj, x_ox = [new(), new()], new(), new()
     x_rest = new()
 
     def rest(b):
         tt(T.ptd[:, PW * b + RO:PW * b + RO + P], T.tt[:, b:1024:4], T.ps[:, 2048 + 512 * b:2048 + 512 * b + P], op.subtract, sig=x_rest)
+    x_kap, x_dec, x_mn, x_td, x_la = new(), new(), new(), [new(), new()], new()
+    on(S, x_og)
+    on(S, x_lz, 2)
+    on(S, x_h2, 128)
+    pick_s(T.la[:, :], T.lall[:, :], T.offg[:, :], x_la)
     on(S, x_m)
-    rows(T.m16, 16, 256, x_m16, [lambda: above(8, 10), lambda: above(10, 12), lambda: above(12, 14), lambda: above(14, C)])
-    on(V, x_h2, 128)
-    tt(T.la[:, 0:64], T.lall[:, 0:64], T.lall[:, 64:128], op.add, sig="step")
-    ts(T.ofx[:, 0:NM], T.rj[:, R0:R1], fc("u2"), op.min, 15.0, op.add)
+    pick_s(T.m16[:, :], T.p16[:, 16:32], T.offp[:, 0:16], x_m16)
+    on(V, x_rs)
+    tt(T.rs[:, 32:48], T.rs[:, 16:32], jm, op.add, sig="step")
+    on(V, x_ut[0])
+    rest(0)
+    on(V, x_er2)
     pw()
-    tt(T.la[:, 64:96], T.la[:, 0:32], T.la[:, 32:64], op.add, sig="step")
-    ts(T.ofx[:, 16:16 + NM], T.rj[:, R0:R1], fc("u2"), op.max, 15.0, op.add)
-    pw()
-    tt(T.la[:, 96:112], T.la[:, 64:80], T.la[:, 80:96], op.add, sig="step")
-    vw(2)
-    cp(fc("u6"), ic("t4i"))
-    pw()
-    tt(T.lsm[:, :], T.la[:, 96:112].indirect(T.offp[:, 0:16]), T.oh2[:, :], op.mult, sig="step")
-    vw()
-    ts(offn, T.rj[:, 0:2], 0.0, op.mult, fc("u6"), op.add)
-    pw()
-    on(V, x_r16)
+    tt(T.oh2[:, :], T.rs[:, 32:48].indirect(T.offp[:, 0:16]), T.n256[:, :], op.is_equal)
+    on(S, x_rest)
+    act(T.tbd[:, 0:P], T.ps[:, 2048:2048 + P], sig=x_td[0])
+    on(S, x_r16b)
+    lin(T.dec[:, :], T.r16[:, 0:128], -4.0, 4.0 - 1.0 / 32, sig=x_dec)
     on(V, x_r16b)
-    sums(T.lsz[:, :], T.lsm[:, :], sig="step")
-    ts(fc("u1"), fc("u6"), -16.0, op.mult, 127.0, op.add)
+    on(V, x_la)
+    sums(T.lb[:, :], T.la[:, :], sig="step")
+    ts(T.ofx[:, 0:NM], T.rj[:, R0:R1], fc("u2"), op.min, 15.0, op.add, sig=x_ox)
+    vw()
     pw()
-    x_offc = ts(T.offc[:, :], T.lsz[:, 15:256:16], -1.0, op.add, sig=new())
-    on(V, x_ut[3])
-    rest(3)
-    on(V, x_m)
+    tt(T.lsm[:, :], T.lb[:, :].indirect(T.offs[:, 0:16]), T.oh2[:, :], op.mult, sig="step")
+    tile(3)
+    pw()
+    sums(T.lsz[:, :], T.lsm[:, :], sig="step")
+    ts(T.ofx[:, 16:16 + NM], T.rj[:, R0:R1], fc("u2"), op.max, 15.0, op.add, sig=x_ox)
+    pw()
+    x_offc = ts(T.offc[:, :], T.lsz[:, 15:256:16], 1.0 / UP, op.mult, -1.0 + LC * (2 * NR - 2 - r), op.add, sig=new())
+    cp(fc("u6"), ic("t4i"))
+    on(V, x_ut[1])
+    rest(1)
     on(V, x_m16)
 
     x_cc, x_cs, x_s = [new(), new()], [new(), new()], [new(), new()]
-    for w in range(2):
-        on(V, "r_cod%d" % w, 4 * len(wave[w]))
-        on(S, "r_pln%d" % w, 4 * len(wave[w]))
+    on(V, "r_cod", 2 * ALL)
+    on(S, "r_pln", 2 * ALL)
     for q_ in (V, S):
         on(q_, x_offc)
         on(q_, x_wino, 32)
     on(M, x_p8)
+    on(M, x_p8s)
     for h in range(2):
         a = slice(128 * h, 128 * h + 128)
         pick_v(T.cand[:, a], T.win[:, :], T.offc[:, 8 * h:8 * h + 8], x_cc[h])
@@ -475,23 +487,25 @@ def rank_program(g, core, T, topo):
         on(M, x_cc[h])
         on(M, x_cs[h])
         M.matmul_mx(T.ps[:, 512 * h:512 * h + 128], T.p8[:, :], T.p8s[:, :], T.cand[:, a], T.cands[:, a], True, True).then_inc(T.sem[x_s[h]], 1)
-    x_td = [new(), new()]
-    on(S, x_ut[0])
-    act(T.tbd[:, 0:P], T.ps[:, 2048:2048 + P], sig=x_td[0])
+    on(S, x_m4a)
+    pick_s(T.m4[:, 0:256], T.m4a[:, :], T.offp[:, 0:16], x_m4)
+    lin(fc("kap"), fc("pm"), -31.0, 2.0, sig=x_kap)
+    act(T.gs[:, 160:192], zeros(32), sig=x_r8)
+    lin(fc("kn"), fc("pm"), -30 * HI, 2 * HI, sig=x_mn)
     x_rep, x_sz = new(), new()
     on(V, x_s[0])
     tt(T.sm[:, 0:128], T.ps[:, 0:128], T.m16[:, 0:128], op.mult, sig="step")
-    on(V, x_fs, C + 2)
-    tt(dif, T.fs[:, 0:16], T.fs[:, 1:17], op.subtract)
-    pw()
-    sums(T.sz[:, 0:128], T.sm[:, 0:128], sig=x_sz)
+    cp(T.offj[:, :], jm, sig=x_oj)
     on(V, x_s[1])
-    tt(T.sm[:, 128:256], T.ps[:, 512:640], T.m16[:, 128:256], op.mult, sig="step")
-    vw()
-    tt(lts, dif, crow, op.subtract)
+    x_sm = tt(T.sm[:, 128:256], T.ps[:, 512:640], T.m16[:, 128:256], op.mult, sig=new())
     pw()
+    vw()
+    sums(T.sz[:, 0:128], T.sm[:, 0:128], sig=x_sz)
+    on(V, x_sm)
     sums(T.sz[:, 128:256], T.sm[:, 128:256], sig=x_sz)
-    ts(offz, T.rj[:, 0:2], 0.0, op.mult, fc("u1"), op.add)
+    x_df = ts(dif, T.offc[:, :], -UP, op.mult, SHB - UP * (1 - LC * (2 * NR - 2 - r)), op.add, sig=new())
+    for q_ in (V, S):
+        on(q_, x_ox, 2)
     on(S, x_sz, 2)
     pick_s(T.rep[:, 0:16 * NM], T.sz[:, :], T.ofx[:, 16:16 + NM], x_rep)
     on(V, x_sz, 2)
@@ -504,54 +518,68 @@ def rank_program(g, core, T, topo):
             ts(T.cm[:, 16 * c + n:16 * c + 16], T.sz[:, 16 * n + 15:256:16], me, op.is_le)
     on(V, x_rep)
     tt(T.cm[:, 16 * R0:16 * R1], T.sz[:, :].indirect(T.ofx[:, 0:NM]), T.rep[:, 0:16 * NM], op.is_ge)
-    x_kap = new()
-    on(S, x_m4a)
-    rows(T.m4, 16, 288, x_m4, [lambda: act(T.fb[:, FW - 4:FW], T.zz[:, 0:4], sig=x_r8), lambda: lin(T.fb[:, FW:FW + 8], T.zz[:, 0:8], 1.0, sig=x_r8),
-                               lambda: act(T.pp[:, 0:16], T.zz[:, 0:16], sig=x_r8), lambda: lin(fc("kap"), T.cf[:, 31:32], -11.0, -10.0 / 128, sig=x_kap)])
-    on(S, x_io3)
-    s(S.activation(T.r8[:, :], jm8, fn.Sign), x_r8)
-    act(T.gs[:, 160:192], T.zz[:, 0:32], sig=x_r8)
-    act(T.gs[:, 480:512], T.zz[:, 0:32], sig=x_r8)
-    act(T.kf[:, :], T.zz[:, 0:32], sig=x_r8)
-    act(T.ysb[:, 128:144], T.zz[:, 0:16], sig=x_r8)
-    on(S, x_io1)
-    lin(T.cw[:, 0:8], T.rj[:, 1:9], fc("pm"), -1.0, sig=x_r8)
+    on(V, x_df)
+    x_lts = tt(lts, T.lsz[:, 15:256:16], dif, op.add, sig=new())
+    x_rn, x_u3 = new(), new()
+    lin(fc("u3"), fc("u6"), 15.0, 16.0, sig=x_u3)
+    lin(fc("c6"), fc("pm"), -272.0, sig=x_u3)
+    act(T.m4[:, 256:272], T.m4a[:, :], sig=x_kap)
+    act(T.m4[:, 272:288], T.m4a[:, :], sig=x_kap)
+    on(S, x_m4)
+    lin(T.mn[:, :], T.m4[:, 0:128], 0.0, HI, sig=x_mn)
+    on(S, x_lts)
+    on(S, x_oj)
+    pick_s(T.rel[:, :], lts, T.offj[:, :], x_rn)
+    on(S, x_hn)
+    lin(fc("g4"), fc("hneg"), 0.25, -1.0 / 64, sig=x_r9)
+    lin(fc("g16"), fc("hneg"), -1.0, 1.0 / 16)
     on(V, x_sg)
     vw()
     scan(T.rk[:, :], T.sg[:, :], T.cm[:, :], op.mult, op.add, sig="step")
-    ts(fc("pm8"), fc("pm"), DL, op.mult, -DL * (8 + 32 * (SHB - SH)), op.add)
+    x_k0 = fill(T.kmsg[:, :], 0, sig=new())
     on(V, x_io2)
     pw()
     tt(T.oh[:, :], T.rk[:, :].indirect(T.offs[:, 0:8]), T.erow[:, 0:128], op.is_equal, sig="step")
-    ts(T.dumpc[:, :], T.rj[:, 0:4], fc("pm"), op.add, float(DUMP), op.add)
+    on(V, x_u3, 2)
+    ts(offz, T.rj[:, 0:2], 0.0, op.mult, fc("u3"), op.add)
+    on(V, x_dec)
     pw()
-    tt(T.lm[:, :], T.lsz[:, :].indirect(T.offs[:, 0:8]), T.oh[:, :], op.mult, sig="step")
+    scan(T.lz[:, :], T.dec[:, :], T.oh[:, :], op.add, op.max, sig="step")
     tt(T.ss[:, 0:64], T.sz[:, :].indirect(T.offs[:, 0:4]), T.oh[:, 0:64], op.mult)
     pw()
-    sums(T.lz[:, :], T.lm[:, :], sig="step")
-    ts(fc("c7"), fc("pm"), -128.0, op.add)
-    pw()
     x_offr, x_kc, x_ks = new(), new(), new()
-    ts(T.offr[:, odd:odd + 8], T.lz[:, 15:128:16], -1.0, op.add, sig=x_offr)
-    tt(T.ss[:, 64:128], T.sz[:, :].indirect(T.offs[:, 4:8]), T.oh[:, 64:128], op.mult)
+    ts(T.offr[:, 2 * odd:2 * odd + 8], T.lz[:, 15:128:16], 512.0, op.mult, fc("c6"), op.add, sig=x_offr)
+    tt(T.ss[:, 64:112], T.sz[:, :].indirect(T.offs[:, 4:7]), T.oh[:, 64:112], op.mult)
     for q_ in (V, S):
         on(q_, x_offr)
-    pick_v(T.pk[:, :], T.win[:, :], T.offr[:, 0:9], x_kc)
-    pick_s(T.pks[:, :], T.wins[:, :], T.offr[:, 0:9], x_ks)
+    for h in range(2):
+        on(V, x_cc[h])
+        on(S, x_cs[h])
+    pick_v(T.pk[:, 0:144 + 16 * odd], T.cand[:, :], T.offr[:, 0:9 + odd], x_kc)
+    pick_s(T.pks[:, 0:144 + 16 * odd], T.cands[:, :], T.offr[:, 0:9 + odd], x_ks)
     x_g = [new(), new()]
-    best = slice(16 * odd, 16 * odd + 128)
+    best = slice(32 * odd, 32 * odd + 128)
     on(M, x_kc)
     on(M, x_ks)
     for t in range(2):
-        a = slice(16 * t, 16 * t + 128)
+        a = slice(16 * (t + odd), 16 * (t + odd) + 128)
         M.matmul_mx(T.ps[:, 1024 + 512 * t:1152 + 512 * t], T.pk[:, a], T.pks[:, a], T.pk[:, best], T.pks[:, best], True, True).then_inc(T.sem[x_g[t]], 1)
+    half(2)
+    half(3)
     vw()
-    x_so = sums(T.ssz[:, :], T.ss[:, :], sig=new())
-    tt(T.nm[:, 0:64], lts.indirect(T.offp[:, 0:4]), T.oh[:, 0:64], op.mult)
-    on(S, x_ut[1])
-    act(T.tbd[:, P:2 * P], T.ps[:, 2560:2560 + P], sig=x_td[1])
+    x_so = sums(T.ssz[:, 0:112], T.ss[:, 0:112], sig=new())
+    ts(fc("u1"), fc("u6"), -1.0, op.mult, E - 1.0, op.add)
+    x_nm = new()
+    on(S, x_rn)
+    pick_s(T.nm[:, :], T.rel[:, :], T.offr[:, 2 * odd:2 * odd + 8], x_nm)
+    act(T.gs[:, 480:512], zeros(32), sig=x_r9)
+    on(S, x_io3)
+    s(S.activation(T.r8[:, 0:32], jm8, fn.Sign), x_r9)
     on(S, x_vals)
+    sw()
     lin(T.vald[:, :], T.vals[:, :], fc("g16"), sig=x_vald)
+    on(S, x_r9, 4)
+    lin(T.r8[:, 32:64], T.r8[:, 0:32], -4.0, 4.0 - 1.0 / 16, sig=x_d8)
 
     def start(b):
         return 8 * b * (b - 1) + (32 if b > BA else 0)
@@ -567,12 +595,9 @@ def rank_program(g, core, T, topo):
     def keep(a, b, sig):
         lo, hi = start(a), start(b) + 16 * b
         scan(T.gs[me32, lo:hi], T.m4[me32, 0:hi - lo], T.gb[me32, lo:hi], op.add, op.max, sig=sig)
-
-    def fl(b):
-        return T.fb[me32, FW - 4 * b - 1:FW - 4 * b]
     x_ga, x_gb, x_gc = new(), new(), new()
     on(V, x_so)
-    on(V, x_kap)
+    on(V, x_kap, 3)
     on(V, x_g[0])
     pairs(1, "step")
     pairs(3, "step")
@@ -580,9 +605,8 @@ def rank_program(g, core, T, topo):
     pairs(2, "step")
     pairs(4, "step")
     pairs(5, x_gc)
-    on(V, x_m4a)
     on(V, x_m4)
-    on(V, x_r8, 9)
+    on(V, x_r8, 2)
     pw()
     keep(1, BA, x_ga)
     pairs(6, x_gc)
@@ -598,89 +622,107 @@ def rank_program(g, core, T, topo):
         if b == 1:
             pairs(7, x_gc)
         if b in (2, 4):
-            tt(T.nm[:, 32 + 16 * b:64 + 16 * b], lts.indirect(T.offp[:, 2 + b:4 + b]), T.oh[:, 32 + 16 * b:64 + 16 * b], op.mult)
+            a = slice(32 * b - 64, 32 * b)
+            on(V, x_nm)
+            on(V, x_mn, 2)
+            scan(T.nz[:, a], T.mn[:, a], T.nm[:, a], op.add, op.max)
         if b == 3:
             on(V, x_gc, 3)
             keep(BA + 1, E - 1, x_gb)
+            on(V, x_r9, 4)
         if b == 5:
-            vw()
-            sums(T.nz[:, :], T.nm[:, :])
+            ts(offn, T.rj[:, 0:2], 0.0, op.mult, fc("u1"), op.add)
+        if b == 6:
+            vw(1)
+            ts(T.nz[:, 15:128:16], T.nz[:, 15:128:16], fc("kn"), op.add)
         if b == 7:
-            vw()
-            cp(fc("n7"), T.nz[:, 15:16])
+            ts(fc("pm8"), fc("pm"), DL, op.mult, -DL * (8 + 32 * (SHB - SH)), op.add)
     x_pp = new()
-    on(S, x_r8, 9)
     for b in range(1, E - 1):
         on(S, "prune", b)
-        sw()
-        last = b == E - 2
-        lin(T.pp[me32, 7:8] if last else T.pp[me32, 8 + b:9 + b], fl(b), T.pp[me32, 7 + b:8 + b], sig=x_pp if last else None)
-        lin(T.pp[me32, b:b + 1], fl(b), T.pp[me32, 7 + b:8 + b], 101.0, sig=x_pp)
+        s(S.activation(T.kc[me32, 32 + 8 * b:32 + 9 * b], T.fb[me32, FW - 4 * b - 1:FW - 4:4], fn.Identity, accum_out=T.pp[me32, b + 1:b + 2]), x_pp)
+    on(S, x_rest, 2)
+    act(T.tbd[:, P:2 * P], T.ps[:, 2560:2560 + P], sig=x_td[1])
     on(V, "prune", E - 1)
-    vw()
-    ts(T.nz[me32, 15:16], fl(7), 0.5, op.is_lt, fc("n7", me32), op.mult, sig="step")
-    on(V, x_pp, E - 1)
+    vw(1)
+    tt(T.nz[me32, 15:112:16], T.nz[me32, 15:112:16], T.fb[me32, FW - 4 * E + 2:FW - 4:4], op.mult)
+    on(V, x_pp, E - 2)
     on(V, x_zw, 3)
     tt(T.kh[:, :], T.pp[:, 0:8].indirect(offn), T.erow[:, 128:160], op.is_equal, sig="step")
-    ts(psel, fc("pm"), KP - 1.0, op.min, fc("g4"), op.add)
+    ts(T.dumpc[:, :], T.rj[:, 0:4], fc("pm"), op.add, float(DUMP), op.add)
+    vw(1)
     pw()
     tt(T.km[:, 0:32], T.nz[:, :].indirect(offz), T.kh[:, :], op.mult, sig="step")
-    ts(T.cw[me32, 7:8], fl(7), 0.5, op.is_lt, fc("c7", me32), op.mult)
+    ts(psel, fc("pm"), KP - 1.0, op.min, fc("g4"), op.add)
+    vw(1)
     pw()
-    scan(T.km[:, 32:64], T.r8[:, :], T.km[:, 0:32], op.mult, op.add, sig="step")
-    fill(T.ofy[:, :], 0)
+    scan(T.km[:, 32:64], T.r8[:, 0:32], T.km[:, 0:32], op.mult, op.add, sig="step")
+    ts(fc("u4"), fc("u6"), 4.0, op.mult, FW - 4.0 * E + 2, op.add)
     pw()
     k1 = T.km[:, 39:64:8]
     x_zr, x_dz, x_dm = new(), new(), new()
+    blk = [slice(32 * k, 32 * k + 32) for k in range(KP)]
+
+    def bound(k):
+        ts(T.kd[blk[k], 0:1], T.km[me32, 39 + 8 * k:40 + 8 * k], T.dumpc[me32, k:k + 1], op.max)
     ts(T.kl0[:, :], k1, float(SH - SHB), op.add, sig="step")
     ts(T.dm[:, 0:4], k1, 32.0 * DL, op.mult, fc("pm8"), op.add, sig=x_dm)
     pw()
     tt(T.zrow[:, :], T.zw[:, :].indirect(T.kl0[:, 0:4]), im64, op.add, sig=x_zr)
-    tt(T.kd[:, 0:4], k1, T.dumpc[:, :], op.max)
+    bound(0)
     for q_ in (S, V):
         on(q_, x_dm)
         on(q_, x_zr)
     for k in range(KP):
-        o = T.dz[:, 64 * k:64 * k + 64]
+        o = T.dz[blk[k], :]
         if k < 2:
-            ts(o, T.zrow[:, :], DL, op.mult, T.dm[:, k:k + 1], op.subtract, sig="step")
+            ts(o, T.zrow[me32, :], DL, op.mult, T.dm[me32, k:k + 1], op.subtract, sig="step")
         else:
-            lin(o, T.zrow[:, :], T.dm[:, k:k + 1], -DL, sig=x_dz)
-    ts(T.kf[:, 0:4], k1, float(-SHB), op.add, -1.0, op.max)
+            lin(o, T.zrow[me32, :], T.dm[me32, k:k + 1], -DL, sig=x_dz)
+    bound(1)
+    bound(2)
     pw()
-    for k in range(KP):
-        if k == 2:
-            on(V, x_dz, 2)
-        v(V.tensor_reduce(T.dm[:, 4 + k:5 + k], T.dz[:, 64 * k:64 * k + 64], X, op.min, apply_absolute_value=True), "step")
-    vw()
-    x_kt = v(V.transpose(T.kt[me32, :], T.kf[me32, :]), new())
+    on(V, x_dz, 2)
+    v(V.tensor_reduce(T.dm[:, 4:5], T.dz[:, :], X, op.min, apply_absolute_value=True), "step")
+    bound(3)
+    vw(1)
     pw()
-    x_km = new()
+    on(V, x_k0)
+    x_km, x_kt = new(), new()
     for k in range(KP):
-        ts(T.kmsg[:, k:k + 1], T.dm[:, 4 + k:5 + k], T.dumpc[:, k:k + 1], op.max, T.kd[:, k:k + 1], op.min, sig=x_km)
+        if k == KP - 1:
+            vw()
+        ts(T.kmsg[me32, k:k + 1], T.dm[blk[k], 4:5], T.dumpc[blk[k], k:k + 1], op.max, T.kd[blk[k], 0:1], op.min, sig=x_km)
+    for q_ in (g, Q):
+        on(q_, x_k0)
     on(g, x_km, KP)
     tell(T.kmsg[:, :], lambda q: T.kland[:, 4 * r:4 * r + 4], "kept")
     on(Q, x_km, KP)
     load(Q, T.kland[:, 4 * r:4 * r + 4], T.kmsg[:, :], x_kown)
 
-    x_wq, x_y, x_ysb, x_yo, x_st, x_oy, x_oyd = new(), new(), new(), new(), new(), new(), new()
-    tt(T.ky[:, 0:32], T.cw[:, 0:8].indirect(offn), T.kh[:, :], op.mult, sig="step")
+    x_y, x_ysb, x_yo, x_st, x_oy, x_oyd, x_kf, x_wq = new(), new(), new(), new(), new(), new(), new(), new()
+    act(T.ky[:, 32:40], zeros(8), sig=x_kz)
+    lin(fc("c7"), fc("pm"), -128.0, sig=x_kz)
+    act(T.kf[:, :], zeros(32), sig=x_kf)
+    on(V, x_d8)
+    ts(T.of3[:, 4:6], T.rj[:, 0:2], 0.0, op.mult, fc("u4"), op.add, sig="step")
     on(V, x_w, 16)
     quant("wq", 0, 128, T.wt[:, :], x_wq)
     pw()
-    scan(T.ky[:, 32:64], T.r8[:, :], T.ky[:, 0:32], op.mult, op.add, sig="step")
+    tt(T.km[:, 0:32], T.fb[:, :].indirect(T.of3[:, 4:6]), T.kh[:, :], op.mult, sig="step")
     on(V, x_ut[2])
     rest(2)
     pw()
-    ts(T.ofy[:, 0:8:2], T.ky[:, 39:64:8], 128.0, op.add, sig=x_oy)
-    ts(ic("ogi"), ic("pi"), 4, op.arith_shift_right, 1, op.bitwise_and)
-    ts(ic("t1i"), ic("pmi"), 1, op.bitwise_and)
-    on(V, x_td[0])
-    rest(0)
+    scan(T.ky[:, 0:32], T.r8[:, 32:64], T.km[:, 0:32], op.add, op.max, sig="step")
+    ts(ic("t1i"), ic("pi"), 1, op.bitwise_and)
+    ts(fc("v1"), ic("ogi"), -2.0, op.mult, 1.0, op.add)
+    on(V, x_kz, 2)
+    pw()
+    ts(T.ofy[:, :], T.ky[:, 7:39:4], 256.0, op.mult, fc("c7"), op.add, sig=x_oy)
+    on(V, x_ut[3])
+    rest(3)
     vw()
-    ts(fc("u1"), ic("ogi"), -2.0, op.mult, 1.0, op.add)
-    on(V, x_td[1])
-    rest(1)
+    ts(fc("v3"), ic("t1i"), fc("v1"), op.mult, 272.0, op.mult)
     on(Q, x_oy)
     for k in range(8):
         load(Q, T.oy[16 * k:16 * k + 16, :], T.ofy[16 * r:16 * r + 16, :], x_oyd)
@@ -696,37 +738,39 @@ def rank_program(g, core, T, topo):
         M.matmul_mx(T.ps[:, 512 * b:512 * b + 128], T.eq[:, e], T.eqs[:, e], T.pt[:, :], T.pts[:, :], True, True).then_inc(T.sem[x_up[b]], 1)
         on(S, x_up[b])
         act(T.ptd[:, PW * b:PW * b + NR * A], T.ps[:, 512 * b:512 * b + 128], sig=x_un[min(b, 1)])
+    act(T.ysb[:, 0:16], zeros(16), sig=x_ysb)
     on(M, x_un[0])
     on(M, x_wq)
     M.matmul_mx(T.ps[:, 0:128], T.wq[:, :], T.wqs[:, :], T.pk[:, best], T.pks[:, best], True, True).then_inc(T.sem[x_y], 1)
     on(S, x_y)
-    act(T.ysb[:, 0:128], T.ps[:, 0:128], sig=x_ysb)
-    on(S, x_ysb)
+    act(T.ysb[:, 16:144], T.ps[:, 0:128], sig=x_ysb)
+    on(S, x_ysb, 2)
     on(S, x_oyd, 128)
     for i in range(KP):
         pick_s(T.yo[:, i:64:4], T.ysb[:, :], T.oy[:, 2 * i:2 * i + 1], x_yo)
-    on(Q, x_kt)
-    load(Q, T.kp[:, :], T.kt[me32.start:me32.start + 4, 16 * odd:16 * odd + 16], x_st)
     on(Q, x_yo, KP)
     load(Q, T.y[:, :], T.yo[:, :], x_st)
+    on(Q, x_kt)
+    load(Q, T.kp[:, :], T.kt[me32.start:me32.start + 4, 16 * odd:16 * odd + 16], x_st)
 
     on(V, x_vald)
     on(V, x_cl)
     on(V, x_kown, 16)
     on(V, "r_kept", EV * len(others))
     ts(klf, T.kland[:, :], float(-DUMP), op.add, sig="step")
-    vw()
-    ts(fc("u3"), ic("t1i"), fc("u1"), op.mult, 272.0, op.mult)
+    ts(fc("v4"), ic("ogi"), 256.0, op.mult, fc("u2"), op.add)
     pw()
     cp(T.okl[:, :], klf.indirect(psel), sig="step")
-    ts(fc("u4"), ic("ogi"), 256.0, op.mult, fc("u2"), op.add)
+    on(V, x_kf)
+    ts(T.kf[:, 0:4], k1, float(-SHB), op.add, -1.0, op.max)
     pw()
     cp(T.cl[:, :].indirect(T.okl[:, 0:KP]), T.vald[:, :], sig="claim")
-    vw()
-    ts(tl, fc("u3"), fc("u4"), op.add, 1.0 / 32, op.mult)
+    vw(1)
+    ts(tl, fc("v3"), fc("v4"), op.add, 1.0 / 32, op.mult)
     on(V, "claim")
-    v(V.transpose(T.ttc[:, 0:256], T.cl[:, c0:c0 + 256]))
-    v(V.transpose(T.ttc[:, 256:544], T.cl[:, c0 - 16:c0 + 272])); vw()
+    v(V.transpose(T.ttc[:, 0:256], T.cl[:, c0:c0 + 256]), "step")
+    v(V.transpose(T.ttc[:, 256:544], T.cl[:, c0 - 16:c0 + 272]), "step")
+    pw()
     tt(T.mx[0:64, 0:34], T.ttc[0:64, 0:544:16], T.ttc[64:128, 0:544:16], op.max); vw()
     tt(T.mx[0:32, 40:74], T.mx[0:32, 0:34], T.mx[32:64, 0:34], op.max); vw()
     for k in range(4):
@@ -734,10 +778,13 @@ def rank_program(g, core, T, topo):
     vw()
     x_new, x_st2, x_gp = [new(), new()], new(), [new(), new()]
     x_ptl = ts(T.ptl[:, :], ub.indirect(tl), -1.0, op.mult, float(NR * A), op.add, sig=new())
+    v(V.transpose(T.kt[me32, :], T.kf[me32, :]), x_kt)
     for q_ in (V, S):
         on(q_, x_un[0])
         on(q_, x_un[1], 3)
         on(q_, x_rest, 4)
+        on(q_, x_td[0])
+        on(q_, x_td[1])
         on(q_, x_ptl)
     for b in (2, 3):
         pick_s(T.gp[:, P * b - 2 * P:P * b - P], T.ptd[:, PW * b:PW * b + PW], T.ptl[:, 0:16], x_gp[b - 2])
@@ -761,4 +808,4 @@ def rank_program(g, core, T, topo):
     on(V, "v", vn[0])
     on(S, "s", sn_[0])
     for n in ROADS:
-        on(g, "l_" + n, 4 * len(wave[int(n[-1])]) if n[-1] in "01" else EV if n in ("req", "kept") else ALL)
+        on(g, "l_" + n, 2 * ALL if n in ("cod", "pln") else ALL if n in ("ptc", "pts") else EV)

@@ -9,43 +9,48 @@ DL = 4096.0
 DUMP = 7 * 4096
 SHB = DUMP + KP * A
 CLW = KP * A + NR * P + 16
+RQ = 3 * (P - 2)
 S0 = P * (NR - 1)
 FW = 48
 RO = NR * A + 1
 PW = NR * A + P + 8
-R0, R1 = 2, 14
-BA = 4
-UP = 4096.0
+NQ = 12
+TINY = 2.0 ** -90
 HI = 2048.0
+BITS = 0x7C03
 ORDER = (1, 4, 2, 5, 3, 6, 7)
 WAVES = (slice(0, 4), slice(4, 7))
+
+TAB, NT = {}, 0
+for _n, _k in (("offp", 16), ("offs", 16), ("offg", 16), ("offj", 16), ("offu", 16), ("ofs", 2),
+               ("offz", 2), ("offn", 2), ("offf", 2), ("psel", 2), ("tl", 2)):
+    TAB[_n] = (NT, _k)
+    NT += _k
+N1 = TAB["offz"][0]
 
 F, B, I, U = "float32", "bfloat16", "int32", "uint16"
 SB = {
     "cdi": (16, I), "offl": (16, U), "ones": (64, B), "pres": (4 * (S0 + NR * P), B), "r4": (2 * P, B), "orx": (4 * P, B),
-    "cnt": (P + 32, B), "ind": (P, B), "indc": (P, B), "junk": (2 * P, B), "req": (3, B), "rland": (32, B), "rt1": (32, B), "rt2": (32, B),
-    "reql": (24, U), "rj": (32, F),
-    "jwb": (2, B), "dumpc": (4, F), "imj": (96, F), "r8": (64, F), "tro": (8, U), "of3": (8, U), "ofx": (32, U), "ofy": (8, U), "oy": (8, U),
-    "offs": (16, U), "offp": (16, U), "cf": (48, F), "m16": (256, B), "m4": (288, B), "m4a": (16, B),
-    "r16": (256, B), "sg": (256, B), "zw": (ZW, F), "vals": (64, B), "vald": (64, B), "erow": (160, F), "n256": (256, B),
-    "lf": (32, F), "lt": (32, F), "cm2": (256, B), "rs": (48, F), "oh2": (256, F), "rel": (256, F), "offj": (16, U), "mn": (128, B),
-    "offw": (16, U), "lw": (256, F), "lall": (256, F), "la": (256, F), "lb": (256, F), "offg": (16, U), "lsm": (256, F), "lsz": (256, F), "offc": (16, U),
-    "sm": (256, F), "sz": (256, F), "rep": (256, F), "cm": (256, B), "rk": (256, B), "oh": (128, B), "dec": (128, B), "p16": (32, B),
-    "lz": (128, B), "offr": (12, U), "ss": (128, F), "ssz": (128, F), "nm": (128, F), "nz": (128, F), "gb": (512, B),
-    "gs": (512, B), "fb": (64, F), "pp": (40, F), "bo": (4, F), "kh": (32, F), "km": (64, F), "ky": (64, F),
-    "kf": (32, F), "kt": (32, F), "kd": (16, F), "kl0": (4, U), "zrow": (64, F), "dz": (64, F), "dm": (8, F), "kmsg": (4, U),
-    "kland": (32, U), "kc": (96, F), "okl": (16, U), "ysb": (144, F), "yo": (64, F), "mx": (80, F),
+    "cnt": (P + 32, B), "ind": (2 * P, B), "junk": (P, B), "req": (3 * P, B), "rland": (32, B), "rt1": (64, B), "rt2": (64, B),
+    "reql": (32, U), "rj": (32, F), "ct": (NT, F), "cu": (NT, U), "ic": (24, I),
+    "jwb": (2, B), "dumpc": (4, F), "im64": (64, F), "r8": (32, F), "ofy": (8, U), "oy": (8, U),
+    "cf": (32, F), "m16": (256, B), "m4": (256, B), "m4a": (16, B),
+    "r16": (256, B), "zw": (ZW, F), "vald": (64, B), "erow": (160, F),
+    "lf": (32, F), "lt": (32, F), "thr": (256, B), "rel": (256, F), "mn": (128, B),
+    "offw": (16, U), "lw": (256, F), "lall": (256, F), "la": (256, F), "lb": (256, F), "offc": (16, U),
+    "sm": (256, F), "sz": (256, F), "rep": (256, F), "df": (256, B), "cm": (256, B), "rk": (256, B), "oh": (128, B), "dec": (128, B), "p16": (32, B),
+    "lz": (128, B), "offr": (8, U), "ss": (128, F), "ssz": (128, F), "nm": (128, F), "nz": (128, F), "gb": (576, B),
+    "gs": (576, B), "fb": (64, F), "ub": (24, F), "bo": (4, F), "kh": (32, F), "km": (64, F), "ky": (64, F),
+    "kf": (32, F), "kt": (32, F), "kd": (16, F), "kl0": (4, U), "zrow": (64, F), "dz": (64, F), "dm": (8, F),
+    "kk": (48, U), "kc": (136, F), "okl": (16, U), "ysb": (144, F), "yo": (64, F), "mx": (80, F),
     "xz": (512, B), "wt": (512, B), "tt": (1024, B), "eb": (520, B), "cl": (CLW, B), "ttc": (544, B),
     "ptd": (4 * PW, F), "tbd": (2 * P, B), "gp": (2 * P, F), "ptl": (16, U), "bb": (1024, B),
 }
 CODES = {"p1": 128, "p8": 128, "wq": 128, "tq": 256, "win": 592, "tn": 256, "snd": 336, "cand": 256, "pk": 160, "eq": 512, "pt": 128}
-ICOL = {n: i for i, n in enumerate(["pi", "pmi", "ggi", "ogi", "t1i", "t4i"])}
-FCOL = {n: i for i, n in enumerate(["pm", "u1", "u2", "u3", "u4", "pm8", "u5", "u6", "isr", "hneg", "kap", "g4", "c7", "g16",
-                                    "sb1", "sb2", "ac1", "ac2", "b0", "nbase", "c6", "kn", "v1", "v3", "v4", "pmh", "gs0"])}
+FCOL = {n: i for i, n in enumerate(["pm", "p31", "p7", "p7j", "t1", "u2", "pm8", "isr", "hneg", "kap", "c7", "g16", "dmp",
+                                    "sb1", "ac1", "nbase", "c6", "kn", "knb", "o32", "q1", "q2", "q3", "q4", "q5", "q6", "q7"])}
 
 SCRATCH = {n: ("sbuf", [128, k], d) for n, (k, d) in SB.items()}
-SCRATCH["dl"] = ("dram", [16, 128], F)
-SCRATCH["ic"] = ("sbuf", [128, len(ICOL)], I)
 SCRATCH["fc"] = ("sbuf", [128, len(FCOL)], F)
 for _n, _k in CODES.items():
     SCRATCH[_n] = ("sbuf", [128, _k], "float8_e4m3fn_x4")
@@ -98,11 +103,14 @@ def rank_program(g, core, T, topo):
     def on(q, sig, n=1):
         q.wait_ge(T.sem[sig], n)
 
-    def ic(n):
-        return T.ic[:, ICOL[n]:ICOL[n] + 1]
-
     def fc(n, at=slice(0, 128)):
         return T.fc[at, FCOL[n]:FCOL[n] + 1]
+
+    def ct(n, a=0, b=None):
+        return T.ct[:, TAB[n][0] + a:TAB[n][0] + (TAB[n][1] if b is None else b)]
+
+    def cu(n, a=0, b=None):
+        return T.cu[:, TAB[n][0] + a:TAB[n][0] + (TAB[n][1] if b is None else b)]
 
     def ts(o, a, s1, op0, s2=None, op1=None, sig=None):
         if op1 is None:
@@ -127,8 +135,8 @@ def rank_program(g, core, T, topo):
     def act(o, a, sig=None):
         return s(S.activation(o, a, fn.Copy), sig)
 
-    def lin(o, a, bias, scale=1.0, sig=None):
-        return s(S.activation(o, a, fn.Identity, bias=bias, scale=scale), sig)
+    def lin(o, a, bias, scale=1.0, sig=None, f=fn.Identity):
+        return s(S.activation(o, a, f, bias=bias, scale=scale), sig)
 
     def pick_v(o, src, off, sig):
         V.tensor_copy(o.bitcast(u32), src.bitcast(u32).indirect(off)).then_inc(T.sem[sig], 1)
@@ -141,6 +149,9 @@ def rank_program(g, core, T, topo):
 
     def iota(o, pat, base, cm, sig):
         g.iota(o, pat, base, cm, allow_small_or_imprecise_dtypes=True).then_inc(T.sem[sig], 1)
+
+    def const(o, c, sig):
+        iota(o, [[0, o.shape[1]]], c, 0, sig)
 
     def load(q, o, a, sig):
         q.dma_start(o, a).then_inc(T.sem[sig], 16)
@@ -164,18 +175,23 @@ def rank_program(g, core, T, topo):
             tr.append(RemoteDMATransfer(dst_ids=[DstId(rid=rid, pnc=pid)], dma_engine_mask=mk[q], remote_sem=T.sem["r_" + road], src=src(q), dst=dst(q)))
         g.remote_dma_fused(tr, local_sem=T.sem["l_" + road])
 
-    ids, every = [], topo.mask(core, T.cores[others[0]])
+    every = topo.mask(core, T.cores[others[0]])
     for q in others:
-        rid, pid = topo.addr(T.cores[q])[:2]
-        ids.append(DstId(rid=rid, pnc=pid))
         every &= topo.mask(core, T.cores[q])
     EV = bin(every).count("1")
 
-    def tell(src, dst, road):
+    def tell(src, dst, road, dests=others):
+        ids = [DstId(rid=topo.addr(T.cores[q])[0], pnc=topo.addr(T.cores[q])[1]) for q in dests]
         g.remote_dma_fused([RemoteDMATransfer(dst_ids=ids, dma_engine_mask=every, remote_sem=T.sem["r_" + road], srcs=[src],
-                                              dsts=[dst(q) for q in others])], local_sem=T.sem["l_" + road])
+                                              dsts=[dst(q) for q in dests])], local_sem=T.sem["l_" + road])
 
-    ALL = 2 * len(others)
+    def points(near):
+        tell(T.p1[:, 0:A].bitcast(u8), lambda q: T.pt[:, A * r:A * r + A].bitcast(u8), "ptc",
+             [q for q in others if (topo.die(T.cores[q]) == topo.die(core)) == near])
+
+    WAVE = 4 * len(others)
+    PAIR = 2 * len(others)
+    TOLD = EV * len(others)
 
     def seat(a, b):
         return ORDER.index(a ^ b)
@@ -183,13 +199,10 @@ def rank_program(g, core, T, topo):
     def spot(q):
         return LC * ((r - q - 1) % NR)
 
-    row16, jm = T.rj[:, 0:16], T.rj[:, 16:32]
-    dd, lts, dif = [T.cf[:, 16 * k:16 * k + 16] for k in range(3)]
-    im64, jm8 = T.imj[:, 0:64], T.imj[:, 64:96]
-    psel, tl = T.tro[:, 4:5], T.tro[:, 0:1]
-    offn, offz = T.of3[:, 0:2], T.of3[:, 2:4]
-    klf, ub = T.kc[:, 0:32], T.pp[:, 16:33]
-    NM = R1 - R0
+    row16, jm, r8 = T.rj[:, 0:16], T.rj[:, 16:32], T.r16[:, 0:64:2]
+    kland, kmsg = T.kk[:, 0:32], T.kk[:, 40:44]
+    klf, ub = T.kc[:, 0:32], T.ub[:, 0:17]
+    gs0, p7 = T.bo[:, 0:1], T.fc[:, 2:4]
     odd = r % 2
     me32 = slice(32 * (r // 2), 32 * (r // 2) + 32)
 
@@ -201,283 +214,275 @@ def rank_program(g, core, T, topo):
         load(Q if k < 4 else S, T.cdi[16 * k:16 * k + 16, :], T.cd[:, :], x_cd)
     load(Q, T.xz[:, 0:64], T.x[:, :], x_x)
     load(Q, T.tt[:, :], T.tb[:, :], x_tb)
-    load(Q, T.wt[:, :], T.w[:, :], x_w)
 
-    x_pi, x_io1, x_io2, x_er2, x_ebd, x_r4, x_jm = new(), new(), new(), new(), new(), new(), new()
-    g.iota(ic("pi"), [[1, 1]], 0, 1).then_inc(T.sem[x_pi], 1)
+    x_pi, x_pj2, x_io1, x_io2, x_ebd, x_r4, x_jm, x_pr = [new() for k in range(8)]
+    g.iota(T.ic[:, 0:4], [[1, 4]], 64 * 127, -64).then_inc(T.sem[x_pi], 1)
+    const(T.ones[:, :], 1, x_pr)
+    for a, b, m in ((4, 5, 2048), (5, 6, 1024), (6, 8, 4096), (8, 9, 16384)):
+        g.iota(T.ic[:, a:b], [[0, b - a]], 0, m).then_inc(T.sem[x_pj2], 1)
     iota(jm, [[1, 16]], 0, 0, x_jm)
-    iota(T.r4[:, :], [[0, P // 2], [1, 4]], 0, 0, x_r4)
     iota(row16, [[16, 16]], 0, 0, x_io1)
+    iota(T.r4[:, :], [[0, P // 2], [1, 4]], 0, 0, x_r4)
 
-    x_m, x_zz, x_pr, x_hn, x_gs, x_b1, x_p1, x_pm = new(), new(), new(), new(), new(), new(), new(), new()
+    x_m, x_zz, x_hn, x_gs, x_p1, x_pm = new(), new(), new(), new(), new(), new()
     fill(T.xz[:, 64:512], 0.0, sig=x_zz)
     on(V, x_pi)
-    ts(ic("ggi"), ic("pi"), 4, op.arith_shift_right)
+    ts(T.ic[:, 12:16], T.ic[:, 0:4], BITS, op.bitwise_and)
     fill(T.pres[:, 4 * S0:4 * S0 + 4 * P:4], 0.0, sig="step")
     vw()
-    x_is = ts(fc("isr"), ic("ggi"), float(r), op.is_equal, sig=new())
-    ts(fc("gs0"), ic("ggi"), float(-4 * P), op.mult, float(4 * S0), op.add, sig=x_gs)
-    ts(ic("pmi"), ic("pi"), 15, op.bitwise_and)
-    fill(T.pres[:, 4 * S0 + 1:4 * S0 + 4 * P:4], 0.0, sig="step")
-    on(V, x_jm)
+    cp(T.bo[:, :], T.ic[:, 12:16], sig=x_gs)
     on(V, x_gs)
-    ts(T.bo[:, :], T.rj[:, 16:20], fc("gs0"), op.add, sig="step")
-    vw()
-    cp(fc("pm"), ic("pmi"), sig=x_pm)
-    pw()
+    x_is = ts(fc("isr"), gs0, float(4 * S0 - 4 * P * r), op.is_equal, sig=new())
 
-    x_cz, x_dd, x_b0 = new(), new(), new()
+    x_cz, x_dd, x_b0, x_c1, x_c2 = new(), new(), new(), new(), new()
+    x_r16b, x_r8, x_lz, x_h1, x_lf, x_rt = new(), new(), new(), new(), new(), new()
     on(S, x_zz)
-    act(T.pres[:, 4 * S0 + 2:4 * S0 + 4 * P:4], zeros(P), sig=x_pr)
+    for k in (1, 2):
+        act(T.pres[:, 4 * S0 + k:4 * S0 + 4 * P:4], zeros(P), sig=x_pr)
     on(S, x_is)
     lin(T.pres[:, 4 * S0 + 3:4 * S0 + 4 * P:4], zeros(P), fc("isr"), sig=x_pr)
-    lin(T.ones[:, :], zeros(64), 1.0, sig=x_pr)
-    on(S, x_pm)
-    lin(fc("pmh"), fc("pm"), 0.5)
-    act(T.jwb[:, 0:1], fc("pm"), sig=x_dd)
-    lin(fc("sb1"), fc("pm"), 16.5)
+    lin(fc("q5"), gs0, 4.0 * S0 - 4 * P * r - 2 * P, -1.0, f=fn.Sign)
+    lin(fc("q6"), gs0, LC * NR / 2.0, LC / (4.0 * P))
+    lin(fc("hneg"), gs0, 16.0 - S0, 0.25, sig=x_hn)
+    act(T.lall[:, :], zeros(P), sig=x_lz)
     sw()
+    lin(fc("nbase"), fc("q5"), fc("q6"), LC * NR / 2.0, sig=x_b0)
     on(S, x_jm)
-    lin(dd, jm, fc("pmh"), -1.0, sig=x_dd)
-    lin(fc("sb2"), fc("pm"), 32.5)
-    x_u2, x_k2 = new(), new()
-    lin(fc("u2"), fc("pm"), 0.0, 16.0, sig=x_u2)
-    lin(fc("u5"), fc("pm"), 15.0, 16.0, sig=x_k2)
-    x_r16b, x_r8, x_r9, x_lz = new(), new(), new(), new()
-    lin(T.r16[:, :], zeros(P), 1.0)
-    lin(T.fb[:, :], zeros(64), 1.0)
+    act(ct("offj"), jm, sig=x_c1)
+    on(S, x_b0)
+    lin(T.cnt[:, 0:16], zeros(16), fc("nbase"), sig=x_cz)
+    lin(T.cnt[:, P + 16:P + 32], zeros(16), fc("nbase"), sig=x_cz)
+    on(S, x_io1)
+    lin(ct("offu", 0, 8), T.rj[:, 1:9], 15.0, sig=x_c1)
+    lin(ct("offu", 8, 16), T.rj[:, 0:8], 15.0, sig=x_c1)
+    on(S, x_pm)
+    lin(T.jwb[:, :], T.rj[:, 0:4:2], fc("pm"), sig=x_dd)
+    lin(fc("sb1"), fc("pm"), 16.5)
+    on(S, x_lf)
+    act(T.lf[:, 16:32], T.lf[:, 0:16], sig=x_lf)
+    lin(fc("u2"), fc("pm"), 0.0, 16.0)
+    lin(ct("offp"), zeros(16), fc("pm"))
+    lin(fc("q3"), fc("p31"), 0.0, 4.0)
+    lin(fc("q7"), fc("pm"), 66.0, 128.0)
+    lin(T.cf[:, 0:16], jm, fc("pm"), -1.0, f=fn.Abs)
     sw()
-    act(T.r16[:, 0:256:16], zeros(16), sig=x_r16b)
-    act(T.fb[:, FW - 3:FW:2], zeros(2), sig=x_r8)
+    lin(ct("offg"), jm, fc("u2"), sig=x_c1)
+    lin(ct("offs"), ct("offp"), 15.0, 16.0, sig=x_c1)
+    lin(fc("o32"), fc("pm"), fc("q3"), -1.0)
 
     on(V, x_cd, 128)
     for k in range(4):
         ts(T.offl[:, k:16:4], T.cdi[:, k:16:4], 4.0, op.mult, T.bo[:, k:k + 1], op.add, sig="step")
-    x_p8, x_p8s, x_lt = new(), new(), new()
+    x_p8, x_p8s, x_lt, x_k0 = new(), new(), new(), new()
     on(V, x_x, 16)
     on(V, x_zz)
     quant("p1", 0, 128, T.xz[:, :], x_p1)
     pw()
-    on(V, x_pr, 3)
+    on(V, x_pr, 4)
     for i in range(4):
         if i:
             on(V, "scat", i)
         v(V.tensor_copy(T.pres[:, :].indirect(T.offl[:, 4 * i:4 * i + 4]), T.ones[:, :]), "scat")
-        if i < 2:
-            cp(T.lf[:, 16 * i:16 * i + 16], T.cdi[:, :])
-        if i == 2:
+        if i == 0:
+            on(V, x_pj2, 4)
+            ts(T.ic[:, 16:21], T.ic[:, 4:9], BITS, op.bitwise_and)
+        if i == 1:
             vw()
-            v(V.transpose(T.lt[:, :], T.lf[:, :]), x_lt)
+            ts(T.fc[:, 0:5], T.ic[:, 16:21], 1.0 / 2048, op.mult, sig=x_pm)
+        if i == 2:
+            ts(T.lf[:, 0:16], T.cdi[:, :], float(SHB), op.add, TINY, op.mult, sig=x_lf)
         if i == 3:
-            ts(fc("b0"), ic("ggi"), float(r), op.is_gt, float(LC * NR), op.mult, sig=x_b1)
+            fill(T.kk[:, :], 0, sig=x_k0)
     on(V, "scat", 4)
     on(V, x_r4)
     for k in range(2):
         a = 2 * P * k
         scan(T.orx[:, a:a + 2 * P], T.r4[:, :], T.pres[:, 4 * S0 + a:4 * S0 + a + 2 * P], op.min, op.max, sig="step")
-    ts(fc("hneg"), ic("ggi"), float(-P), op.mult, 16.0, op.add, sig=x_hn)
+    on(V, x_lf, 2)
+    v(V.transpose(T.lt[:, :], T.lf[:, :]), x_lt)
     pw()
     x_cnt = scan(T.cnt[:, 16:P + 16], T.orx[:, 3:4 * P:4], T.orx[:, 3:4 * P:4], op.add, op.max, sig=new())
-    fill(T.offr[:, :], 0)
+    on(V, x_hn)
+    x_ow = ts(T.offw[:, :], T.cdi[:, :], fc("hneg"), op.add, P + 16.0, op.min, sig=new())
 
-    x_m16, x_cm, x_acc, x_cl, x_rs, x_op = [new() for k in range(6)]
-
-    def signs(a, b):
-        for c in range(a, b):
-            s(S.activation(T.cm2[:, 16 * c:16 * c + 16], T.lt[:, 0:16], fn.Sign, bias=T.lt[:, c:c + 1], scale=-1.0, accum_out=T.rs[:, c:c + 1]), x_cm)
-
-    on(S, x_lt)
-    signs(0, 2)
-    on(S, x_gs)
-    on(S, x_b1)
-    lin(fc("nbase"), fc("gs0"), fc("b0"), LC / (4.0 * P), sig=x_b0)
-    signs(2, 3)
-    on(S, x_b0)
-    lin(T.cnt[:, 0:16], zeros(16), fc("nbase"), sig=x_cz)
-    lin(T.cnt[:, P + 16:P + 32], zeros(16), fc("nbase"), sig=x_cz)
-    signs(3, 5)
-    sw()
+    x_m16, x_acc, x_cl, x_op, x_rn, x_th, x_req, x_lv, x_h2, x_m4a = [new() for k in range(10)]
     on(S, x_cnt)
-    for k in (1, 2):
-        s(S.activation(T.junk[:, P * k - P:P * k - 1], T.cnt[:, 16:P + 15], fn.Sign, bias=fc("sb%d" % k), scale=-1.0, accum_out=fc("ac%d" % k)), x_acc)
-    signs(5, C)
-    on(S, x_cm, C)
-    lin(T.rs[:, 16:32], T.rs[:, 0:16], 8.0 * (C - 1) + 1, 8.0, sig=x_rs)
+    s(S.activation(T.junk[:, 0:P - 1], T.cnt[:, 16:P + 15], fn.Sign, bias=fc("sb1"), scale=-1.0, accum_out=fc("ac1")), x_acc)
+    sw()
+    lin(ct("ofs"), T.rj[:, 0:2], fc("o32"), sig=x_c1)
+    on(S, x_acc)
+    lin(T.req[:, RQ + 1:RQ + 2], fc("ac1"), (P - 1) * 0.5, 0.5, sig=x_req)
+    on(S, x_cz, 2)
+    on(S, x_ow)
+    lin(T.lw[:, :], T.cnt[:, :].indirect(T.offw[:, :]), fc("nbase"), -1.0, sig=x_lv)
+    lin(T.p16[:, 16:32], T.cf[:, 0:16], 1.0, -1.0, sig=x_m, f=fn.Relu)
+    lin(T.cf[:, 16:32], jm, fc("q7"), -128.0, f=fn.Relu)
+
+    def rows(q, a, b):
+        for j in range(a, b):
+            k, at = j // 2, me32.start + 16 * (j % 2)
+            load(q, T.lall[at:at + 16, 16 * k:16 * k + 16], T.lw[16 * k:16 * k + 1, :], x_h2)
+    on(S, x_lz)
+    on(S, x_lv)
+    rows(S, NQ, 16)
+    sw()
+    lin(T.m4a[:, :], T.cf[:, 16:32], 2.0, -1.0, sig=x_m4a)
 
     on(V, x_cnt)
-    on(V, x_io1)
-    on(V, x_pm)
-    on(V, x_dd, 2)
-    ts(T.ind[:, 0:P - 1], T.cnt[:, 16:P + 15], T.jwb[:, 0:1], op.is_le, sig="step")
-    ts(T.offp[:, :], row16, 0.0, op.mult, fc("pm"), op.add, sig=x_op)
-    pw()
-    scan(T.indc[:, 0:P - 1], T.ind[:, 0:P - 1], T.ind[:, 0:P - 1], op.add, op.max, sig="step")
-    ts(T.p16[:, 16:32], dd, 0.5, op.is_equal, sig=x_m)
-    pw()
-    x_req = new()
-    cp(T.req[:, 0:1], T.indc[:, P - 2:P - 1], sig=x_req)
-    on(V, x_hn)
-    ts(T.offw[:, :], T.cdi[:, :], fc("hneg"), op.add, P + 16.0, op.min)
-    on(V, x_acc, 2)
-    ts(T.req[:, 1:3], T.fc[:, FCOL["ac1"]:FCOL["ac1"] + 2], 0.5, op.mult, (P - 1) * 0.5, op.add, sig=x_req)
+    on(V, x_dd)
+    x_i = new()
+    for k in range(2):
+        ts(T.ind[:, P * k:P * k + P - 1], T.cnt[:, 16:P + 15], T.jwb[:, k:k + 1], op.is_le, sig=x_i)
+    for k in range(2):
+        on(V, x_i, k + 1)
+        scan(T.req[:, 2 * k:RQ + 3:3], T.ind[:, P * k:P * k + P - 1], T.ind[:, P * k:P * k + P - 1], op.add, op.max, sig=x_req)
 
     def halves(k):
         g.affine_select(T.eb[:, 258 * k:258 * k + 258], zeros(258), [[1, 258]], op.not_equal, 0.5, 258 * k - 3, -4).then_inc(T.sem[x_ebd], 1)
     on(g, x_p1)
-    send(lambda q: T.p1[:, 0:A].bitcast(u8), lambda q: T.pt[:, A * r:A * r + A].bitcast(u8), "ptc", others, 2)
+    points(True)
     on(g, x_zz)
     halves(0)
-    on(g, x_req, 2)
-    tell(T.req[:, :], lambda q: T.rland[:, 3 * seat(q, r):3 * seat(q, r) + 3], "req")
+    on(g, x_req, 3)
+    tell(T.req[:, RQ:RQ + 3], lambda q: T.rland[:, 3 * seat(q, r):3 * seat(q, r) + 3], "req")
+    const(T.rt1[:, 0:16], 0, x_rt)
+    const(T.rt1[:, 48:64], 0, x_rt)
     halves(1)
-    iota(T.n256[:, :], [[1, P]], 1, 0, x_er2)
+    g.affine_select(T.r16[:, :], zeros(P), [[0, 16], [1, 16]], op.is_equal, 1.0, 0, 0).then_inc(T.sem[x_r16b], 1)
 
-    x_lv, x_tq, x_h1, x_h2, x_wino, x_rl, x_ptown, x_rz = new(), new(), new(), new(), new(), new(), new(), new()
-    x_zw, x_vals, x_vald, x_kown, x_sg, x_eq = new(), new(), new(), new(), new(), [new(), new()]
-    on(V, x_cz, 2)
-    on(V, x_b0)
-    on(V, x_jm)
-    on(V, x_op)
-    vw()
-    ts(T.lw[:, :], T.cnt[:, :].indirect(T.offw[:, :]), fc("nbase"), op.subtract, UP, op.mult, sig=x_lv)
+    x_tq, x_wino, x_rl, x_ptown, x_rz = new(), new(), new(), new(), new()
+    x_zw, x_im, x_vald, x_pj, x_m4, x_eq = new(), new(), new(), new(), new(), [new(), new()]
     on(V, x_tb, 16)
     quant("tq", 0, P, T.tt[:, :], x_tq)
+    on(V, x_c1, 6)
+    cp(T.cu[:, 0:N1], T.ct[:, 0:N1], sig=x_op)
+    quant("win", WOWN, WOWN + P, T.tt[:, :], x_wino)
 
     def tile(b):
         quant("eq", 128 * b, 128 * b + 128, T.eb[:, 3 - b:515 - b], x_eq[b // 2])
-    on(V, x_u2)
-    x_og = ts(T.offg[:, :], jm, fc("u2"), op.add, sig=new())
+    on(V, x_op)
     on(V, x_p1)
-    pick_v(T.p8[:, :], T.p1[:, :], T.offp[:, 0:8], x_p8)
-    on(V, x_ebd, 2)
-    for b in range(3):
-        tile(b)
+    pick_v(T.p8[:, :], T.p1[:, :], cu("offp", 0, 8), x_p8)
+    on(V, x_k0)
     on(V, x_rz, 16)
-    on(V, "r_req", EV * len(others))
-    v(V.transpose(T.rt1[me32, :], T.rland[me32, :]), "step")
-    x_m4a, x_m4 = ts(T.m4a[:, 0:16], dd, -128.0, op.mult, 2.0, op.min, sig=new()), new()
-    pw()
-    cp(T.rt1[me32, 16 - 16 * odd:32 - 16 * odd], T.rt1[me32, 16 * odd:16 * odd + 16], sig="step")
-    on(V, x_k2)
-    ts(T.offs[:, :], row16, 0.0, op.mult, fc("u5"), op.add)
-    pw()
-    v(V.transpose(T.rt2[me32, :], T.rt1[me32, :]), "step")
-    ts(ic("t4i"), ic("pi"), 7, op.bitwise_and)
-    pw()
+    on(V, "r_req", TOLD)
     for k in range(4):
-        cp(T.reql[32 * k:32 * k + 32, 0:21], T.rt2[me32, 0:21], sig=x_rl)
-    ts(ic("ogi"), ic("pi"), 4, op.arith_shift_right, 1, op.bitwise_and)
+        v(V.transpose(T.rt1[32 * k:32 * k + 32, 16:48], T.rland[me32, :]), "step")
+    on(V, x_rt, 2)
+    pw()
+    for k in range(2):
+        a = 16 * (odd + 1 - k)
+        v(V.transpose(T.rt2[:, 32 * k:32 * k + 32], T.rt1[:, a:a + 32]), "step")
+    pw()
+    cp(T.reql[:, :], T.rt2[:, :].indirect(cu("ofs")), sig=x_rl)
 
     x_ut = [new() for b in range(4)]
-
-    def half(b):
+    on(M, x_tq)
+    for b in range(4):
         e = slice(128 * b, 128 * b + 128)
         on(M, x_eq[b // 2], 2)
         M.matmul_mx(T.ps[:, 2048 + 512 * b:2048 + 512 * b + P], T.eq[:, e], T.eqs[:, e], T.tq[:, :], T.tqs[:, :], True, True).then_inc(T.sem[x_ut[b]], 1)
-    on(M, x_tq)
-    half(0)
-    half(1)
 
     on(Q, x_zz)
     load(Q, T.rland[:, 21:32], zeros(11), x_rz)
+    on(Q, x_lv)
+    on(Q, x_lz)
+    rows(Q, 0, NQ)
+    on(Q, "l_cod", WAVE)
     on(Q, x_p1)
     load(Q, T.pt[:, A * r:A * r + A].bitcast(u8), T.p1[:, 0:A].bitcast(u8), x_ptown)
     load(Q, T.pts[:, A * r:A * r + A], T.p1s[:, 0:A], x_ptown)
-    on(Q, x_lv)
-    for k in range(8):
-        load(Q, T.dl[:, 16 * k:16 * k + 16], T.lw[16 * k:16 * k + 1, :], x_h1)
+    load(Q, T.wt[:, :], T.w[:, :], x_w)
     x_d8, x_kz = new(), new()
-    act(T.lall[:, 128:144], T.lt[:, 0:16], sig=x_lz)
-    act(T.lall[:, 144:256], zeros(112), sig=x_lz)
-    act(T.pp[:, 0:16], zeros(16), sig=x_r9)
     on(S, x_op)
     on(S, x_p1)
-    pick_s(T.p8s[:, :], T.p1s[:, :], T.offp[:, 0:8], x_p8s)
-    for q_ in (Q, S):
-        on(q_, x_h1, 128)
-    for k in range(8):
-        load(Q if k < 4 else S, T.lall[16 * k:16 * k + 16, 0:128], T.dl[:, :], x_h2)
-    on(Q, x_tq)
-    load(Q, T.win[:, WOWN:WOWN + P].bitcast(u8), T.tq[:, :].bitcast(u8), x_wino)
-    load(Q, T.wins[:, WOWN:WOWN + P], T.tqs[:, :], x_wino)
+    pick_s(T.p8s[:, :], T.p1s[:, :], cu("offp", 0, 8), x_p8s)
+    on(S, x_lt)
+    pick_s(T.rel[:, :], T.lt[:, 0:16], cu("offj"), x_rn)
 
     for q_ in (V, S):
         on(q_, x_tq)
-        on(q_, x_rl, 4)
+        on(q_, x_rl)
 
     def codes(w):
         send(lambda q: T.snd[:, LC * seat(r, q):LC * seat(r, q) + LC].bitcast(u8), lambda q: T.win[:, spot(q):spot(q) + LC].bitcast(u8), "cod", others[WAVES[w]], 4)
-
-    def planes(w):
-        send(lambda q: T.snds[:, LC * seat(r, q):LC * seat(r, q) + LC], lambda q: T.wins[:, spot(q):spot(q) + LC], "pln", others[WAVES[w]], 4)
+    x_sndc, x_snds = new(), new()
     for w in range(2):
-        x_sndc, x_snds = new(), new()
         c, d = WAVES[w].start, WAVES[w].stop
         pick_v(T.snd[:, LC * c:LC * d], T.tq[:, :], T.reql[:, 3 * c:3 * d], x_sndc)
         pick_s(T.snds[:, LC * c:LC * d], T.tqs[:, :], T.reql[:, 3 * c:3 * d], x_snds)
-        for sig, go in ((x_sndc, codes), (x_snds, planes))[::1 - 2 * w]:
-            on(g, sig)
-            go(w)
-    send(lambda q: T.p1s[:, 0:A], lambda q: T.pts[:, A * r:A * r + A], "pts", others, 2)
-    on(g, x_r16b)
-    g.affine_select(T.sg[:, :], T.r16[:, :], [[1, 16], [-1, 16]], op.not_equal, -1.0, 0, 0).then_inc(T.sem[x_sg], 1)
-    x_io3 = new()
+    on(g, x_sndc)
+    codes(0)
+    on(g, x_snds, 2)
+    send(lambda q: T.snds[:, LC * seat(r, q):LC * seat(r, q) + LC], lambda q: T.wins[:, spot(q):spot(q) + LC], "pln", others, 2)
+    on(g, x_sndc, 2)
+    codes(1)
+    x_fb = new()
     c0 = KP * A + P * r
-    iota(T.erow[:, 0:128], [[1, 8], [-1, 16]], C + 1 - E, 0, x_io2)
-    iota(jm8, [[0, 4], [1, 8]], 0, 0, x_io3)
-    iota(T.vals[:, :], [[0, 4], [-1, 16]], NR * A, 0, x_vals)
+    iota(T.erow[:, 0:128], [[-1, 8], [0, 16]], E - 1, 0, x_io2)
+    const(T.fb[:, :], 1, x_fb)
+    const(T.gs[:, 7:576:8], 0, x_r8)
+    const(T.kc[:, 36:64], 0, x_h1)
     iota(T.erow[:, 128:160], [[-1, 4], [-1, 8]], E - 1, 0, x_zw)
-    iota(im64, [[0, 4], [1, 16]], 0, 0, x_zw)
+    iota(T.im64[:, :], [[0, 4], [1, 16]], 0, 0, x_im)
     iota(T.zw[:, :], [[32, ZW]], 0, 0, x_zw)
+    points(False)
+    tell(T.p1s[:, 0:A], lambda q: T.pts[:, A * r:A * r + A], "pts")
     iota(T.cl[:, c0 - 16:c0 + 272], [[-1, 288]], 15, 0, x_cl)
 
-    x_un, x_oj, x_ox = [new(), new()], new(), new()
-    x_rest = new()
+    x_un, x_rest = [new(), new()], new()
+    done = [0, 0]
 
-    def rest(b):
-        tt(T.ptd[:, PW * b + RO:PW * b + RO + P], T.tt[:, b:1024:4], T.ps[:, 2048 + 512 * b:2048 + 512 * b + P], op.subtract, sig=x_rest)
-    x_kap, x_dec, x_mn, x_td, x_la = new(), new(), new(), [new(), new()], new()
-    on(S, x_og)
-    on(S, x_lz, 2)
-    on(S, x_h2, 128)
-    pick_s(T.la[:, :], T.lall[:, :], T.offg[:, :], x_la)
+    def rest(n=1):
+        b, a = divmod(64 * done[0], P)
+        if a == 0:
+            on(V, x_ut[b])
+        done[0] += n
+        done[1] += 1
+        tt(T.ptd[:, PW * b + RO + a:PW * b + RO + a + 64 * n], T.tt[:, 4 * a + b:4 * a + 256 * n:4], T.ps[:, 2048 + 512 * b + a:2048 + 512 * b + a + 64 * n],
+           op.subtract, sig=x_rest)
+    x_kap, x_dec, x_mn, x_td, x_la = new(), new(), new(), new(), new()
+    on(S, x_h2, 256)
+    pick_s(T.la[:, :], T.lall[:, :], cu("offg"), x_la)
     on(S, x_m)
-    pick_s(T.m16[:, :], T.p16[:, 16:32], T.offp[:, 0:16], x_m16)
-    on(V, x_rs)
-    tt(T.rs[:, 32:48], T.rs[:, 16:32], jm, op.add, sig="step")
-    on(V, x_ut[0])
-    rest(0)
-    on(V, x_er2)
-    pw()
-    tt(T.oh2[:, :], T.rs[:, 32:48].indirect(T.offp[:, 0:16]), T.n256[:, :], op.is_equal)
-    on(S, x_rest)
-    act(T.tbd[:, 0:P], T.ps[:, 2048:2048 + P], sig=x_td[0])
-    on(S, x_r16b)
-    lin(T.dec[:, :], T.r16[:, 0:128], -4.0, 4.0 - 1.0 / 32, sig=x_dec)
+    pick_s(T.m16[:, :], T.p16[:, 16:32], cu("offp"), x_m16)
+    on(S, x_m4a)
+    pick_s(T.m4[:, :], T.m4a[:, :], cu("offp"), x_m4)
+    lin(fc("q1"), gs0, fc("pm"), 1.0 / P)
+    lin(fc("q4"), fc("p31"), 8.5 / 8, -17.0 / 64)
+    act(T.ct[:, NT - 3:NT:2], zeros(2), sig=x_c2)
+    lin(ct("offz"), p7, 15.0, 8.0, sig=x_c2)
+    sw()
+    lin(fc("q2"), fc("pm"), fc("q4"), 17.0 / 128)
+    lin(ct("psel", 0, 1), fc("isr"), fc("q1"), 4.0 + 4 * r, sig=x_c2)
+    lin(ct("offn"), p7, E - 1.0, -0.5, sig=x_c2)
+    lin(ct("offf"), p7, FW - 4.0 * E + 2, 2.0, sig=x_c2)
+    sw()
+    lin(ct("tl", 0, 1), fc("t1"), fc("p31"), fc("q2"), sig=x_c2)
+    on(V, x_ebd, 2)
+    for b in range(4):
+        tile(b)
     on(V, x_r16b)
     on(V, x_la)
     sums(T.lb[:, :], T.la[:, :], sig="step")
-    ts(T.ofx[:, 0:NM], T.rj[:, R0:R1], fc("u2"), op.min, 15.0, op.add, sig=x_ox)
-    vw()
+    rest(2)
     pw()
-    tt(T.lsm[:, :], T.lb[:, :].indirect(T.offs[:, 0:16]), T.oh2[:, :], op.mult, sig="step")
-    tile(3)
-    pw()
-    sums(T.lsz[:, :], T.lsm[:, :], sig="step")
-    ts(T.ofx[:, 16:16 + NM], T.rj[:, R0:R1], fc("u2"), op.max, 15.0, op.add, sig=x_ox)
-    pw()
-    x_offc = ts(T.offc[:, :], T.lsz[:, 15:256:16], 1.0 / UP, op.mult, -1.0 + LC * (2 * NR - 2 - r), op.add, sig=new())
-    cp(fc("u6"), ic("t4i"))
-    on(V, x_ut[1])
-    rest(1)
+    x_offc = new()
+    for k in range(4):
+        ts(T.offc[32 * k:32 * k + 32, :], T.lb[me32, 15:256:16], -1.0, op.mult, -1.0 + LC * (2 * NR - 2 - r), op.add, sig=x_offc)
+    on(V, x_lt)
+    on(V, x_rn)
+    tt(T.thr[:, :], T.lt[:, 0:16].indirect(cu("offp")), T.rel[:, :], op.subtract, sig=x_th)
+    rest(2)
+    rest(4)
     on(V, x_m16)
 
     x_cc, x_cs, x_s = [new(), new()], [new(), new()], [new(), new()]
-    on(V, "r_cod", 2 * ALL)
-    on(S, "r_pln", 2 * ALL)
+    on(V, "r_cod", WAVE)
+    on(S, "r_pln", PAIR)
     for q_ in (V, S):
-        on(q_, x_offc)
-        on(q_, x_wino, 32)
+        on(q_, x_offc, 4)
+        on(q_, x_wino)
     on(M, x_p8)
     on(M, x_p8s)
     for h in range(2):
@@ -487,251 +492,231 @@ def rank_program(g, core, T, topo):
         on(M, x_cc[h])
         on(M, x_cs[h])
         M.matmul_mx(T.ps[:, 512 * h:512 * h + 128], T.p8[:, :], T.p8s[:, :], T.cand[:, a], T.cands[:, a], True, True).then_inc(T.sem[x_s[h]], 1)
-    on(S, x_m4a)
-    pick_s(T.m4[:, 0:256], T.m4a[:, :], T.offp[:, 0:16], x_m4)
-    lin(fc("kap"), fc("pm"), -31.0, 2.0, sig=x_kap)
-    act(T.gs[:, 160:192], zeros(32), sig=x_r8)
-    lin(fc("kn"), fc("pm"), -30 * HI, 2 * HI, sig=x_mn)
-    x_rep, x_sz = new(), new()
-    on(V, x_s[0])
-    tt(T.sm[:, 0:128], T.ps[:, 0:128], T.m16[:, 0:128], op.mult, sig="step")
-    cp(T.offj[:, :], jm, sig=x_oj)
-    on(V, x_s[1])
-    x_sm = tt(T.sm[:, 128:256], T.ps[:, 512:640], T.m16[:, 128:256], op.mult, sig=new())
-    pw()
-    vw()
-    sums(T.sz[:, 0:128], T.sm[:, 0:128], sig=x_sz)
-    on(V, x_sm)
-    sums(T.sz[:, 128:256], T.sm[:, 128:256], sig=x_sz)
-    x_df = ts(dif, T.offc[:, :], -UP, op.mult, SHB - UP * (1 - LC * (2 * NR - 2 - r)), op.add, sig=new())
-    for q_ in (V, S):
-        on(q_, x_ox, 2)
-    on(S, x_sz, 2)
-    pick_s(T.rep[:, 0:16 * NM], T.sz[:, :], T.ofx[:, 16:16 + NM], x_rep)
-    on(V, x_sz, 2)
-    for c in list(range(R0)) + list(range(R1, C)):
-        me = T.sz[:, 16 * c + 15:16 * c + 16]
-        n = c + 1 if c else 0
-        if n:
-            ts(T.cm[:, 16 * c:16 * c + n], T.sz[:, 15:16 * n:16], me, op.is_ge)
-        if n < C:
-            ts(T.cm[:, 16 * c + n:16 * c + 16], T.sz[:, 16 * n + 15:256:16], me, op.is_le)
-    on(V, x_rep)
-    tt(T.cm[:, 16 * R0:16 * R1], T.sz[:, :].indirect(T.ofx[:, 0:NM]), T.rep[:, 0:16 * NM], op.is_ge)
-    on(V, x_df)
-    x_lts = tt(lts, T.lsz[:, 15:256:16], dif, op.add, sig=new())
-    x_rn, x_u3 = new(), new()
-    lin(fc("u3"), fc("u6"), 15.0, 16.0, sig=x_u3)
-    lin(fc("c6"), fc("pm"), -272.0, sig=x_u3)
-    act(T.m4[:, 256:272], T.m4a[:, :], sig=x_kap)
-    act(T.m4[:, 272:288], T.m4a[:, :], sig=x_kap)
-    on(S, x_m4)
-    lin(T.mn[:, :], T.m4[:, 0:128], 0.0, HI, sig=x_mn)
-    on(S, x_lts)
-    on(S, x_oj)
-    pick_s(T.rel[:, :], lts, T.offj[:, :], x_rn)
-    on(S, x_hn)
-    lin(fc("g4"), fc("hneg"), 0.25, -1.0 / 64, sig=x_r9)
-    lin(fc("g16"), fc("hneg"), -1.0, 1.0 / 16)
-    on(V, x_sg)
-    vw()
-    scan(T.rk[:, :], T.sg[:, :], T.cm[:, :], op.mult, op.add, sig="step")
-    x_k0 = fill(T.kmsg[:, :], 0, sig=new())
-    on(V, x_io2)
-    pw()
-    tt(T.oh[:, :], T.rk[:, :].indirect(T.offs[:, 0:8]), T.erow[:, 0:128], op.is_equal, sig="step")
-    on(V, x_u3, 2)
-    ts(offz, T.rj[:, 0:2], 0.0, op.mult, fc("u3"), op.add)
-    on(V, x_dec)
-    pw()
-    scan(T.lz[:, :], T.dec[:, :], T.oh[:, :], op.add, op.max, sig="step")
-    tt(T.ss[:, 0:64], T.sz[:, :].indirect(T.offs[:, 0:4]), T.oh[:, 0:64], op.mult)
-    pw()
-    x_offr, x_kc, x_ks = new(), new(), new()
-    ts(T.offr[:, 2 * odd:2 * odd + 8], T.lz[:, 15:128:16], 512.0, op.mult, fc("c6"), op.add, sig=x_offr)
-    tt(T.ss[:, 64:112], T.sz[:, :].indirect(T.offs[:, 4:7]), T.oh[:, 64:112], op.mult)
-    for q_ in (V, S):
-        on(q_, x_offr)
+    side = slice(128 - 112 * odd, 144 - 112 * odd)
     for h in range(2):
         on(V, x_cc[h])
         on(S, x_cs[h])
-    pick_v(T.pk[:, 0:144 + 16 * odd], T.cand[:, :], T.offr[:, 0:9 + odd], x_kc)
-    pick_s(T.pks[:, 0:144 + 16 * odd], T.cands[:, :], T.offr[:, 0:9 + odd], x_ks)
-    x_g = [new(), new()]
+    pick_s(T.pks[:, side], T.cands[:, :], cu("offp", 0, 1), x_pj)
+    x_rep, x_sz, x_u3, x_du = new(), new(), new(), new()
+    on(S, x_r16b)
+    lin(T.dec[:, :], T.r16[:, 0:128], -4.0, 4.0 - 1.0 / 32, sig=x_dec)
+    rest(2)
+    on(V, x_s[0])
+    tt(T.sm[:, 0:128], T.ps[:, 0:128], T.m16[:, 0:128], op.mult, sig="step")
+    pick_v(T.pk[:, side], T.cand[:, :], cu("offp", 0, 1), x_pj)
+    on(V, x_s[1])
+    x_sm = tt(T.sm[:, 128:256], T.ps[:, 512:640], T.m16[:, 128:256], op.mult, sig=new())
+    pw()
+    sums(T.sz[:, 0:128], T.sm[:, 0:128], sig=x_sz)
+    on(V, x_sm)
+    sums(T.sz[:, 128:256], T.sm[:, 128:256], sig=x_sz)
+    for h in range(2):
+        on(S, x_sz, h + 1)
+        pick_s(T.rep[:, 128 * h:128 * h + 112], T.sz[:, 128 * h:128 * h + 128], cu("offu", 8 * h, 8 * h + 7), x_rep)
+    on(V, x_sz, 2)
+    x_d, x_cm = new(), new()
+    for c in (0, C - 1):
+        ts(T.df[:, 16 * c:16 * c + 16], T.sz[:, 15:256:16], T.sz[:, 16 * c + 15:16 * c + 16], op.subtract, sig=x_d)
+    for h in range(2):
+        on(V, x_rep, h + 1)
+        tt(T.df[:, 16 + 112 * h:128 + 112 * h], T.sz[:, :].indirect(cu("offs", 0, 7)), T.rep[:, 128 * h:128 * h + 112], op.subtract, sig=x_d)
+    on(V, x_th)
+    for h in range(2):
+        a = slice(128 * h, 128 * h + 128)
+        on(V, x_d, h + 3)
+        tt(T.cm[:, a], T.df[:, a], T.thr[:, a], op.is_gt, sig=x_cm)
+    for h in range(2):
+        a = slice(128 * h, 128 * h + 128)
+        on(V, x_cm, h + 1)
+        sums(T.rk[:, a], T.cm[:, a], sig="step")
+    on(V, x_c2, 6)
+    cp(T.cu[:, N1:NT], T.ct[:, N1:NT])
+    lin(fc("c6"), fc("pm"), -272.0, sig=x_u3)
+    lin(fc("kap"), fc("pm"), -31.0, 2.0, sig=x_kap)
+    on(S, x_fb)
+    act(T.fb[:, FW - 3:FW:2], zeros(2), sig=x_r8)
+    on(S, x_m4)
+    lin(T.mn[:, :], T.m4[:, 0:128], 0.0, HI, sig=x_mn)
+    lin(fc("pm8"), fc("pm"), -DL * (8 + 32 * (SHB - SH + 30 * HI)), DL * (1 + 64 * HI), sig=x_du)
+    lin(fc("kn"), fc("pm"), -30 * HI, 2 * HI, sig=x_du)
+    lin(fc("knb"), fc("pm"), -30 * HI - SHB, 2 * HI, sig=x_du)
+    lin(fc("dmp"), fc("pm"), float(DUMP))
+    on(V, x_io2)
+    pw()
+    tt(T.oh[:, :], T.rk[:, :].indirect(cu("offs", 0, 8)), T.erow[:, 0:128], op.is_equal, sig="step")
+    on(V, x_u3)
+    on(V, x_dec)
+    pw()
+    scan(T.lz[:, :], T.dec[:, :], T.oh[:, :], op.add, op.max, sig="step")
+    tt(T.ss[:, 64:112], T.sz[:, :].indirect(cu("offs", 4, 7)), T.oh[:, 64:112], op.mult)
+    pw()
+    x_offr, x_kc, x_ks = new(), new(), new()
     best = slice(32 * odd, 32 * odd + 128)
+    ts(T.offr[:, :], T.lz[:, 15:128:16], 512.0, op.mult, fc("c6"), op.add, sig=x_offr)
+    for q_ in (V, S):
+        on(q_, x_offr)
+    pick_v(T.pk[:, best], T.cand[:, :], T.offr[:, :], x_kc)
+    tt(T.ss[:, 0:64], T.sz[:, :].indirect(cu("offs", 0, 4)), T.oh[:, 0:64], op.mult)
+    pick_s(T.pks[:, best], T.cands[:, :], T.offr[:, :], x_ks)
+    x_g = [new(), new()]
+    on(M, x_pj, 2)
     on(M, x_kc)
     on(M, x_ks)
     for t in range(2):
         a = slice(16 * (t + odd), 16 * (t + odd) + 128)
         M.matmul_mx(T.ps[:, 1024 + 512 * t:1152 + 512 * t], T.pk[:, a], T.pks[:, a], T.pk[:, best], T.pks[:, best], True, True).then_inc(T.sem[x_g[t]], 1)
-    half(2)
-    half(3)
     vw()
     x_so = sums(T.ssz[:, 0:112], T.ss[:, 0:112], sig=new())
-    ts(fc("u1"), fc("u6"), -1.0, op.mult, E - 1.0, op.add)
     x_nm = new()
     on(S, x_rn)
-    pick_s(T.nm[:, :], T.rel[:, :], T.offr[:, 2 * odd:2 * odd + 8], x_nm)
-    act(T.gs[:, 480:512], zeros(32), sig=x_r9)
-    on(S, x_io3)
-    s(S.activation(T.r8[:, 0:32], jm8, fn.Sign), x_r9)
-    on(S, x_vals)
+    lin(T.nm[:, :], T.rel[:, :].indirect(T.offr[:, :]), 0.0, 1.0 / TINY, sig=x_nm)
     sw()
-    lin(T.vald[:, :], T.vals[:, :], fc("g16"), sig=x_vald)
-    on(S, x_r9, 4)
-    lin(T.r8[:, 32:64], T.r8[:, 0:32], -4.0, 4.0 - 1.0 / 16, sig=x_d8)
+    lin(T.dumpc[:, :], T.rj[:, 0:4], fc("dmp"), sig=x_du)
+    lin(T.r8[:, :], r8, -4.0, 4.0 - 1.0 / 16, sig=x_d8)
 
     def start(b):
-        return 8 * b * (b - 1) + (32 if b > BA else 0)
+        return 8 * b * (b - 1) + 32 * (b // 2)
 
-    def pairs(b, sig=None):
+    x_pa, x_ke = new(), new()
+
+    def pairs(b):
         a = E - 1 - b
         t = a % 2
         h = (a + odd - t) // 2
         at = slice(32 * h, 32 * h + 32)
         ts(T.gb[me32, start(b):start(b) + 16 * b], T.ps[at, 1152 + 512 * t - 16 * b:1152 + 512 * t], T.ssz[at, 16 * a + 15:16 * a + 16], op.is_ge,
-           fc("kap", at), op.add, sig=sig)
+           fc("kap", at), op.add, sig=x_pa)
 
-    def keep(a, b, sig):
-        lo, hi = start(a), start(b) + 16 * b
-        scan(T.gs[me32, lo:hi], T.m4[me32, 0:hi - lo], T.gb[me32, lo:hi], op.add, op.max, sig=sig)
-    x_ga, x_gb, x_gc = new(), new(), new()
+    def part(k):
+        on(V, x_pa, (1, 4, 5, 7)[k])
+        lo, hi = start(max(1, 2 * k)), start(2 * k + 1) + 16 * (2 * k + 1)
+        scan(T.gs[me32, lo:hi], T.m4[me32, 0:hi - lo], T.gb[me32, lo:hi], op.add, op.max, sig=x_ke)
+
     on(V, x_so)
-    on(V, x_kap, 3)
+    on(V, x_kap)
     on(V, x_g[0])
-    pairs(1, "step")
-    pairs(3, "step")
-    on(V, x_g[1])
-    pairs(2, "step")
-    pairs(4, "step")
-    pairs(5, x_gc)
+    pairs(1)
+    pairs(3)
+    pairs(5)
     on(V, x_m4)
     on(V, x_r8, 2)
-    pw()
-    keep(1, BA, x_ga)
-    pairs(6, x_gc)
-    vw()
-    on(V, x_ga)
+    part(0)
+    on(V, x_g[1])
+    pairs(2)
+    pairs(4)
     for b in range(1, E):
         if b > 1:
             on(V, "prune", b - 1)
-        if b == BA + 1:
-            on(V, x_gb)
+        if b == 1 or b % 2 == 0:
+            on(V, x_ke, b // 2 + 1)
         e, n = FW - 4 * b, 2 * b + 3
         scan(T.fb[me32, e - n:e], T.fb[me32, e + 1:e + 1 + 2 * n:2], T.gs[me32, start(b) + 15:start(b) + 15 + 8 * n - 7:8], op.subtract, op.max, sig="prune", init=1.0)
         if b == 1:
-            pairs(7, x_gc)
-        if b in (2, 4):
-            a = slice(32 * b - 64, 32 * b)
-            on(V, x_nm)
-            on(V, x_mn, 2)
-            scan(T.nz[:, a], T.mn[:, a], T.nm[:, a], op.add, op.max)
+            part(1)
+            pairs(6)
+        if b == 2:
+            part(2)
         if b == 3:
-            on(V, x_gc, 3)
-            keep(BA + 1, E - 1, x_gb)
-            on(V, x_r9, 4)
-        if b == 5:
-            ts(offn, T.rj[:, 0:2], 0.0, op.mult, fc("u1"), op.add)
-        if b == 6:
-            vw(1)
-            ts(T.nz[:, 15:128:16], T.nz[:, 15:128:16], fc("kn"), op.add)
-        if b == 7:
-            ts(fc("pm8"), fc("pm"), DL, op.mult, -DL * (8 + 32 * (SHB - SH)), op.add)
+            pairs(7)
+        if b == 4:
+            part(3)
+        if b in (5, 6):
+            a = slice(64 * b - 320, 64 * b - 256)
+            on(V, x_nm)
+            on(V, x_mn)
+            scan(T.nz[:, a], T.mn[:, a], T.nm[:, a], op.add, op.max)
     x_pp = new()
+    on(S, x_h1)
     for b in range(1, E - 1):
         on(S, "prune", b)
-        s(S.activation(T.kc[me32, 32 + 8 * b:32 + 9 * b], T.fb[me32, FW - 4 * b - 1:FW - 4:4], fn.Identity, accum_out=T.pp[me32, b + 1:b + 2]), x_pp)
-    on(S, x_rest, 2)
-    act(T.tbd[:, P:2 * P], T.ps[:, 2560:2560 + P], sig=x_td[1])
+        s(S.activation(T.kc[me32, 80 + 8 * b:80 + 9 * b], T.fb[me32, FW - 4 * b - 1:FW - 4:4], fn.Identity, accum_out=T.kc[me32, 49 + b:50 + b]), x_pp)
+    rest()
     on(V, "prune", E - 1)
-    vw(1)
+    vw()
     tt(T.nz[me32, 15:112:16], T.nz[me32, 15:112:16], T.fb[me32, FW - 4 * E + 2:FW - 4:4], op.mult)
     on(V, x_pp, E - 2)
-    on(V, x_zw, 3)
-    tt(T.kh[:, :], T.pp[:, 0:8].indirect(offn), T.erow[:, 128:160], op.is_equal, sig="step")
-    ts(T.dumpc[:, :], T.rj[:, 0:4], fc("pm"), op.add, float(DUMP), op.add)
-    vw(1)
+    on(V, x_zw, 2)
+    on(V, x_h1)
+    on(V, x_im)
+    tt(T.kh[:, :], T.kc[:, 48:56].indirect(cu("offn")), T.erow[:, 128:160], op.is_equal, sig="step")
+    rest()
+    vw()
     pw()
-    tt(T.km[:, 0:32], T.nz[:, :].indirect(offz), T.kh[:, :], op.mult, sig="step")
-    ts(psel, fc("pm"), KP - 1.0, op.min, fc("g4"), op.add)
-    vw(1)
+    tt(T.km[:, 0:32], T.nz[:, :].indirect(cu("offz")), T.kh[:, :], op.mult, sig="step")
+    rest()
     pw()
-    scan(T.km[:, 32:64], T.r8[:, 0:32], T.km[:, 0:32], op.mult, op.add, sig="step")
-    ts(fc("u4"), fc("u6"), 4.0, op.mult, FW - 4.0 * E + 2, op.add)
+    scan(T.km[:, 32:64], r8, T.km[:, 0:32], op.mult, op.add, sig="step")
+    rest()
+    on(V, x_du, 4)
     pw()
     k1 = T.km[:, 39:64:8]
     x_zr, x_dz, x_dm = new(), new(), new()
     blk = [slice(32 * k, 32 * k + 32) for k in range(KP)]
 
     def bound(k):
-        ts(T.kd[blk[k], 0:1], T.km[me32, 39 + 8 * k:40 + 8 * k], T.dumpc[me32, k:k + 1], op.max)
-    ts(T.kl0[:, :], k1, float(SH - SHB), op.add, sig="step")
+        ts(T.kd[blk[k], 0:1], T.km[me32, 39 + 8 * k:40 + 8 * k], fc("kn", me32), op.add, T.dumpc[me32, k:k + 1], op.max)
+    ts(T.kl0[:, :], k1, fc("knb"), op.add, float(SH), op.add, sig="step")
     ts(T.dm[:, 0:4], k1, 32.0 * DL, op.mult, fc("pm8"), op.add, sig=x_dm)
     pw()
-    tt(T.zrow[:, :], T.zw[:, :].indirect(T.kl0[:, 0:4]), im64, op.add, sig=x_zr)
+    tt(T.zrow[:, :], T.zw[:, :].indirect(T.kl0[:, 0:4]), T.im64[:, :], op.add, sig=x_zr)
     bound(0)
     for q_ in (S, V):
         on(q_, x_dm)
         on(q_, x_zr)
     for k in range(KP):
         o = T.dz[blk[k], :]
-        if k < 2:
+        if k < 3:
             ts(o, T.zrow[me32, :], DL, op.mult, T.dm[me32, k:k + 1], op.subtract, sig="step")
         else:
             lin(o, T.zrow[me32, :], T.dm[me32, k:k + 1], -DL, sig=x_dz)
     bound(1)
-    bound(2)
     pw()
-    on(V, x_dz, 2)
+    on(V, x_dz)
     v(V.tensor_reduce(T.dm[:, 4:5], T.dz[:, :], X, op.min, apply_absolute_value=True), "step")
+    bound(2)
     bound(3)
-    vw(1)
+    vw(2)
     pw()
-    on(V, x_k0)
     x_km, x_kt = new(), new()
     for k in range(KP):
-        if k == KP - 1:
-            vw()
-        ts(T.kmsg[me32, k:k + 1], T.dm[blk[k], 4:5], T.dumpc[blk[k], k:k + 1], op.max, T.kd[blk[k], 0:1], op.min, sig=x_km)
-    for q_ in (g, Q):
-        on(q_, x_k0)
+        if k >= 2:
+            vw(3 - k)
+        ts(T.kk[me32, 40 + k:41 + k], T.dm[blk[k], 4:5], T.dumpc[blk[k], k:k + 1], op.max, T.kd[blk[k], 0:1], op.min, sig=x_km)
     on(g, x_km, KP)
-    tell(T.kmsg[:, :], lambda q: T.kland[:, 4 * r:4 * r + 4], "kept")
-    on(Q, x_km, KP)
-    load(Q, T.kland[:, 4 * r:4 * r + 4], T.kmsg[:, :], x_kown)
+    tell(kmsg, lambda q: T.kk[:, 28 - 4 * r:32 - 4 * r], "kept")
 
     x_y, x_ysb, x_yo, x_st, x_oy, x_oyd, x_kf, x_wq = new(), new(), new(), new(), new(), new(), new(), new()
     act(T.ky[:, 32:40], zeros(8), sig=x_kz)
     lin(fc("c7"), fc("pm"), -128.0, sig=x_kz)
     act(T.kf[:, :], zeros(32), sig=x_kf)
+    lin(fc("g16"), fc("hneg"), NR * A - 1.0, 1.0 / 16)
+    on(S, x_im)
+    sw()
+    lin(T.vald[:, :], T.im64[:, :], fc("g16"), -1.0, sig=x_vald)
     on(V, x_d8)
-    ts(T.of3[:, 4:6], T.rj[:, 0:2], 0.0, op.mult, fc("u4"), op.add, sig="step")
+    tt(T.km[:, 0:32], T.fb[:, :].indirect(cu("offf")), T.kh[:, :], op.mult, sig="step")
     on(V, x_w, 16)
     quant("wq", 0, 128, T.wt[:, :], x_wq)
     pw()
-    tt(T.km[:, 0:32], T.fb[:, :].indirect(T.of3[:, 4:6]), T.kh[:, :], op.mult, sig="step")
-    on(V, x_ut[2])
-    rest(2)
-    pw()
-    scan(T.ky[:, 0:32], T.r8[:, 32:64], T.km[:, 0:32], op.add, op.max, sig="step")
-    ts(ic("t1i"), ic("pi"), 1, op.bitwise_and)
-    ts(fc("v1"), ic("ogi"), -2.0, op.mult, 1.0, op.add)
+    scan(T.ky[:, 0:32], T.r8[:, :], T.km[:, 0:32], op.add, op.max, sig="step")
+    on(V, x_km, KP)
+    ts(T.kc[:, 32:36], kmsg, float(-DUMP), op.add)
     on(V, x_kz, 2)
     pw()
     ts(T.ofy[:, :], T.ky[:, 7:39:4], 256.0, op.mult, fc("c7"), op.add, sig=x_oy)
-    on(V, x_ut[3])
-    rest(3)
+    on(V, x_kf)
+    ts(T.kf[:, 0:4], k1, fc("knb"), op.add, -1.0, op.max)
+    rest(2)
     vw()
-    ts(fc("v3"), ic("t1i"), fc("v1"), op.mult, 272.0, op.mult)
+    v(V.transpose(T.kt[me32, :], T.kf[me32, :]), x_kt)
     on(Q, x_oy)
     for k in range(8):
         load(Q, T.oy[16 * k:16 * k + 16, :], T.ofy[16 * r:16 * r + 16, :], x_oyd)
     on(M, x_sz, 2)
-    on(M, x_gb)
-    on(M, x_ga)
+    on(M, x_ke, 4)
     on(M, x_ptown, 32)
-    on(M, "r_ptc", ALL)
-    on(M, "r_pts", ALL)
+    on(M, "r_ptc", TOLD)
+    on(M, "r_pts", TOLD)
     x_up = [new() for b in range(4)]
     for b in range(4):
         e = slice(128 * b, 128 * b + 128)
@@ -742,31 +727,28 @@ def rank_program(g, core, T, topo):
     on(M, x_un[0])
     on(M, x_wq)
     M.matmul_mx(T.ps[:, 0:128], T.wq[:, :], T.wqs[:, :], T.pk[:, best], T.pks[:, best], True, True).then_inc(T.sem[x_y], 1)
+    on(S, x_rest, 3)
+    for b in range(2):
+        act(T.tbd[:, P * b:P * b + P], T.ps[:, 2048 + 512 * b:2048 + 512 * b + P], sig=x_td)
     on(S, x_y)
     act(T.ysb[:, 16:144], T.ps[:, 0:128], sig=x_ysb)
     on(S, x_ysb, 2)
     on(S, x_oyd, 128)
     for i in range(KP):
         pick_s(T.yo[:, i:64:4], T.ysb[:, :], T.oy[:, 2 * i:2 * i + 1], x_yo)
-    on(Q, x_yo, KP)
-    load(Q, T.y[:, :], T.yo[:, :], x_st)
     on(Q, x_kt)
     load(Q, T.kp[:, :], T.kt[me32.start:me32.start + 4, 16 * odd:16 * odd + 16], x_st)
+    on(Q, x_yo, KP)
+    load(Q, T.y[:, :], T.yo[:, :], x_st)
 
     on(V, x_vald)
     on(V, x_cl)
-    on(V, x_kown, 16)
-    on(V, "r_kept", EV * len(others))
-    ts(klf, T.kland[:, :], float(-DUMP), op.add, sig="step")
-    ts(fc("v4"), ic("ogi"), 256.0, op.mult, fc("u2"), op.add)
+    on(V, "r_kept", TOLD)
+    ts(klf, kland, float(-DUMP), op.add, sig="step")
     pw()
-    cp(T.okl[:, :], klf.indirect(psel), sig="step")
-    on(V, x_kf)
-    ts(T.kf[:, 0:4], k1, float(-SHB), op.add, -1.0, op.max)
+    cp(T.okl[:, :], T.kc[:, 0:48].indirect(cu("psel", 0, 1)), sig="step")
     pw()
     cp(T.cl[:, :].indirect(T.okl[:, 0:KP]), T.vald[:, :], sig="claim")
-    vw(1)
-    ts(tl, fc("v3"), fc("v4"), op.add, 1.0 / 32, op.mult)
     on(V, "claim")
     v(V.transpose(T.ttc[:, 0:256], T.cl[:, c0:c0 + 256]), "step")
     v(V.transpose(T.ttc[:, 256:544], T.cl[:, c0 - 16:c0 + 272]), "step")
@@ -774,33 +756,36 @@ def rank_program(g, core, T, topo):
     tt(T.mx[0:64, 0:34], T.ttc[0:64, 0:544:16], T.ttc[64:128, 0:544:16], op.max); vw()
     tt(T.mx[0:32, 40:74], T.mx[0:32, 0:34], T.mx[32:64, 0:34], op.max); vw()
     for k in range(4):
-        tt(T.pp[32 * k:32 * k + 32, 16:33], T.mx[0:32, 40:74:2], T.mx[0:32, 41:74:2], op.max)
+        tt(T.ub[32 * k:32 * k + 32, 0:17], T.mx[0:32, 40:74:2], T.mx[0:32, 41:74:2], op.max)
     vw()
-    x_new, x_st2, x_gp = [new(), new()], new(), [new(), new()]
-    x_ptl = ts(T.ptl[:, :], ub.indirect(tl), -1.0, op.mult, float(NR * A), op.add, sig=new())
-    v(V.transpose(T.kt[me32, :], T.kf[me32, :]), x_kt)
+    x_new, x_st2, x_gp = new(), new(), new()
+    x_ptl = ts(T.ptl[:, :], ub.indirect(cu("tl", 0, 1)), -1.0, op.mult, float(NR * A), op.add, sig=new())
     for q_ in (V, S):
         on(q_, x_un[0])
         on(q_, x_un[1], 3)
-        on(q_, x_rest, 4)
-        on(q_, x_td[0])
-        on(q_, x_td[1])
+        on(q_, x_rest, done[1])
+        on(q_, x_td, 2)
         on(q_, x_ptl)
     for b in (2, 3):
-        pick_s(T.gp[:, P * b - 2 * P:P * b - P], T.ptd[:, PW * b:PW * b + PW], T.ptl[:, 0:16], x_gp[b - 2])
-    for b in range(4):
+        pick_s(T.gp[:, P * b - 2 * P:P * b - P], T.ptd[:, PW * b:PW * b + PW], T.ptl[:, 0:16], x_gp)
+    x_bb = new()
+    for b in range(3):
         o = T.bb[:, b:1024:4]
         if b < 2:
             tt(o, T.ptd[:, PW * b:PW * b + PW].indirect(T.ptl[:, 0:16]), T.tbd[:, P * b:P * b + P], op.add, sig="step")
         else:
-            on(V, x_gp[b - 2])
-            tt(o, T.gp[:, P * b - 2 * P:P * b - P], T.ps[:, 2048 + 512 * b:2048 + 512 * b + P], op.add, sig="step")
+            on(V, x_gp)
+            tt(o, T.gp[:, 0:P], T.ps[:, 3072:3072 + P], op.add, sig="step")
+    on(V, x_gp, 2)
+    for h in range(2):
+        tt(T.bb[:, 512 * h + 3:512 * h + 512:4], T.gp[:, P + 128 * h:P + 128 * h + 128], T.ps[:, 3584 + 128 * h:3712 + 128 * h], op.add, sig=x_bb)
     pw()
     for h in range(2):
-        quant("tn", 128 * h, 128 * h + 128, T.bb[:, 512 * h:512 * h + 512], x_new[h])
-        on(Q, x_new[h])
+        on(V, x_bb, h + 1)
+        quant("tn", 128 * h, 128 * h + 128, T.bb[:, 512 * h:512 * h + 512], x_new)
+        on(Q, x_new, h + 1)
         load(Q, T.oc[:, 512 * h:512 * h + 512], T.tn[:, 128 * h:128 * h + 128].bitcast(u8), x_st)
-        on(S, x_new[h])
+    on(S, x_new, 2)
     for k in range(4):
         load(S if k < 3 else Q, T.osc[4 * k:4 * k + 4, :], T.tns[32 * k:32 * k + 4, :], x_st2 if k < 3 else x_st)
     on(Q, x_st, 80)
@@ -808,4 +793,4 @@ def rank_program(g, core, T, topo):
     on(V, "v", vn[0])
     on(S, "s", sn_[0])
     for n in ROADS:
-        on(g, "l_" + n, 2 * ALL if n in ("cod", "pln") else ALL if n in ("ptc", "pts") else EV)
+        on(g, "l_" + n, {"cod": WAVE, "pln": PAIR, "ptc": 2 * EV}.get(n, EV))

@@ -17,12 +17,14 @@ PW = NR * A + P + 8
 NQ = 12
 TINY = 2.0 ** -90
 HI = 2048.0
+MARK = 0.125
+WHOLE = 3 * 2 ** 22
 BITS = 0x7C03
 ORDER = (1, 4, 2, 5, 3, 6, 7)
 WAVES = (slice(0, 4), slice(4, 7))
 
 TAB, NT = {}, 0
-for _n, _k in (("offp", 16), ("offs", 16), ("offg", 16), ("offj", 16), ("offu", 16), ("ofs", 2),
+for _n, _k in (("offp", 8), ("offs", 8), ("offg", 8), ("offj", 16), ("ofs", 2),
                ("offz", 2), ("offn", 2), ("offf", 2), ("psel", 2), ("tl", 2)):
     TAB[_n] = (NT, _k)
     NT += _k
@@ -30,17 +32,17 @@ N1 = TAB["offz"][0]
 
 F, B, I, U = "float32", "bfloat16", "int32", "uint16"
 SB = {
-    "cdi": (16, I), "offl": (16, U), "ones": (64, B), "pres": (4 * (S0 + NR * P), B), "r4": (2 * P, B), "orx": (4 * P, B),
-    "cnt": (P + 32, B), "ind": (2 * P, B), "junk": (P, B), "req": (3 * P, B), "rland": (32, B), "rt1": (64, B), "rt2": (64, B),
+    "cdi": (16, I), "offl": (16, U), "ones": (48, B), "pra": (3 * (S0 + NR * P), B), "prb": (3 * (S0 + NR * P), B), "ow": (16, F),
+    "cnt": (3 * P + 32, B), "ind": (2 * P, B), "junk": (P, B), "req": (3 * P, B), "rland": (32, B), "rt1": (64, B), "rt2": (64, B),
     "reql": (32, U), "rj": (32, F), "ct": (NT, F), "cu": (NT, U), "ic": (24, I),
     "jwb": (2, B), "dumpc": (4, F), "im64": (64, F), "r8": (32, F), "ofy": (8, U), "oy": (8, U),
-    "cf": (32, F), "m16": (256, B), "m4": (256, B), "m4a": (16, B),
+    "cf": (32, F), "m16": (128, B), "m4": (128, B), "m4a": (32, B), "ltr": (16, F), "tg": (32, B), "ohs": (32, B),
     "r16": (256, B), "zw": (ZW, F), "vald": (64, B), "erow": (160, F),
-    "lf": (32, F), "lt": (32, F), "thr": (256, B), "rel": (256, F), "mn": (128, B),
-    "offw": (16, U), "lw": (256, F), "lall": (256, F), "la": (256, F), "lb": (256, F), "offc": (16, U),
-    "sm": (256, F), "sz": (256, F), "rep": (256, F), "df": (256, B), "cm": (256, B), "rk": (256, B), "oh": (128, B), "dec": (128, B), "p16": (32, B),
-    "lz": (128, B), "offr": (8, U), "ss": (128, F), "ssz": (128, F), "nm": (128, F), "nz": (128, F), "gb": (576, B),
-    "gs": (576, B), "fb": (64, F), "ub": (24, F), "bo": (4, F), "kh": (32, F), "km": (64, F), "ky": (64, F),
+    "lf": (32, F), "lt": (32, F), "thr": (128, B), "rel": (256, F), "mn": (128, B),
+    "offw": (16, U), "lw": (256, F), "lall": (128, F), "la": (128, F), "lb": (128, F), "offc": (16, U), "offh": (8, U), "sall": (WOWN + P, F),
+    "sm": (128, F), "sz": (256, F), "df": (128, B), "cm": (128, B), "rk": (256, B), "oh": (128, B), "dec": (128, B), "p16": (32, B),
+    "lz": (128, B), "offr": (8, U), "ss": (32, F), "ssz": (32, F), "nm": (128, F), "nz": (128, F), "gb": (224, B),
+    "gs": (704, B), "fb": (64, F), "ub": (24, F), "bo": (8, F), "kh": (32, F), "km": (64, F), "ky": (64, F),
     "kf": (32, F), "kt": (32, F), "kd": (16, F), "kl0": (4, U), "zrow": (64, F), "dz": (64, F), "dm": (8, F),
     "kk": (48, U), "kc": (136, F), "okl": (16, U), "ysb": (144, F), "yo": (64, F), "mx": (80, F),
     "xz": (512, B), "wt": (512, B), "tt": (1024, B), "eb": (520, B), "cl": (CLW, B), "ttc": (544, B),
@@ -48,7 +50,8 @@ SB = {
 }
 CODES = {"p1": 128, "p8": 128, "wq": 128, "tq": 256, "win": 592, "tn": 256, "snd": 336, "cand": 256, "pk": 160, "eq": 512, "pt": 128}
 FCOL = {n: i for i, n in enumerate(["pm", "p31", "p7", "p7j", "t1", "u2", "pm8", "isr", "hneg", "kap", "c7", "g16", "dmp",
-                                    "sb1", "ac1", "nbase", "c6", "kn", "knb", "o32", "q1", "q2", "q3", "q4", "q5", "q6", "q7"])}
+                                    "sb1", "ac1", "nbase", "c6", "kn", "knb", "o32", "q1", "q2", "q3", "q4", "q5", "q6", "q7",
+                                    "q8", "rot", "q9", "g2", "u1"])}
 
 SCRATCH = {n: ("sbuf", [128, k], d) for n, (k, d) in SB.items()}
 SCRATCH["fc"] = ("sbuf", [128, len(FCOL)], F)
@@ -57,8 +60,8 @@ for _n, _k in CODES.items():
     SCRATCH[_n + "s"] = ("sbuf", [128, _k], "uint8")
 SCRATCH["ps"] = ("psum", [128, 4096], F)
 
-ROADS = ["ptc", "pts", "req", "cod", "pln", "kept"]
-XS = ["x%d" % i for i in range(132)]
+ROADS = ["ptc", "pts", "req", "cod", "co2", "pln", "kept"]
+XS = ["x%d" % i for i in range(130)]
 SEMAPHORES = ["v", "s", "step", "scat", "claim", "prune"] + ["r_" + n for n in ROADS] + ["l_" + n for n in ROADS] + XS
 
 
@@ -189,7 +192,7 @@ def rank_program(g, core, T, topo):
         tell(T.p1[:, 0:A].bitcast(u8), lambda q: T.pt[:, A * r:A * r + A].bitcast(u8), "ptc",
              [q for q in others if (topo.die(T.cores[q]) == topo.die(core)) == near])
 
-    WAVE = 4 * len(others)
+    WAVE = [4 * (w.stop - w.start) for w in WAVES]
     PAIR = 2 * len(others)
     TOLD = EV * len(others)
 
@@ -197,7 +200,7 @@ def rank_program(g, core, T, topo):
         return ORDER.index(a ^ b)
 
     def spot(q):
-        return LC * ((r - q - 1) % NR)
+        return LC * seat(q, r)
 
     row16, jm, r8 = T.rj[:, 0:16], T.rj[:, 16:32], T.r16[:, 0:64:2]
     kland, kmsg = T.kk[:, 0:32], T.kk[:, 40:44]
@@ -205,6 +208,9 @@ def rank_program(g, core, T, topo):
     gs0, p7 = T.bo[:, 0:1], T.fc[:, 2:4]
     odd = r % 2
     me32 = slice(32 * (r // 2), 32 * (r // 2) + 32)
+    lo, hi = slice(0, 64), slice(64, 128)
+    blk = [slice(32 * k, 32 * k + 32) for k in range(4)]
+    pres = (T.pra, T.prb)
 
     def zeros(n):
         return T.xz[:, 64:64 + n]
@@ -215,107 +221,108 @@ def rank_program(g, core, T, topo):
     load(Q, T.xz[:, 0:64], T.x[:, :], x_x)
     load(Q, T.tt[:, :], T.tb[:, :], x_tb)
 
-    x_pi, x_pj2, x_io1, x_io2, x_ebd, x_r4, x_jm, x_pr = [new() for k in range(8)]
+    x_pi, x_pj2, x_io1, x_io2, x_ebd, x_b6, x_jm, x_pr = [new() for k in range(8)]
     g.iota(T.ic[:, 0:4], [[1, 4]], 64 * 127, -64).then_inc(T.sem[x_pi], 1)
-    const(T.ones[:, :], 1, x_pr)
+
+    def place(w, k):
+        return pres[w][:, 3 * S0 + k:3 * S0 + 3 * P:3]
     for a, b, m in ((4, 5, 2048), (5, 6, 1024), (6, 8, 4096), (8, 9, 16384)):
         g.iota(T.ic[:, a:b], [[0, b - a]], 0, m).then_inc(T.sem[x_pj2], 1)
+    const(place(1, 2), -WHOLE, x_pr)
     iota(jm, [[1, 16]], 0, 0, x_jm)
     iota(row16, [[16, 16]], 0, 0, x_io1)
-    iota(T.r4[:, :], [[0, P // 2], [1, 4]], 0, 0, x_r4)
 
     x_m, x_zz, x_hn, x_gs, x_p1, x_pm = new(), new(), new(), new(), new(), new()
     fill(T.xz[:, 64:512], 0.0, sig=x_zz)
     on(V, x_pi)
     ts(T.ic[:, 12:16], T.ic[:, 0:4], BITS, op.bitwise_and)
-    fill(T.pres[:, 4 * S0:4 * S0 + 4 * P:4], 0.0, sig="step")
+    fill(place(0, 0), 0.5 - MARK / 2, sig="step")
     vw()
-    cp(T.bo[:, :], T.ic[:, 12:16], sig=x_gs)
+    cp(T.bo[:, 0:2], T.ic[:, 12:14], sig=x_gs)
+    fill(place(0, 1), 0.0, sig="step")
+    on(V, x_pj2, 4)
+    ts(T.ic[:, 16:21], T.ic[:, 4:9], BITS, op.bitwise_and)
     on(V, x_gs)
-    x_is = ts(fc("isr"), gs0, float(4 * S0 - 4 * P * r), op.is_equal, sig=new())
+    x_is = ts(fc("isr"), gs0, float(4 * S0 - 4 * P * r), op.is_equal, MARK, op.mult, sig=new())
+    ts(fc("g2"), gs0, -0.25, op.mult)
+    fill(place(0, 2), float(WHOLE), sig="step")
+    vw()
+    ts(T.bo[:, 4:6], T.bo[:, 0:2], fc("g2"), op.add, sig=x_b6)
+    ts(T.fc[:, 0:5], T.ic[:, 16:21], 1.0 / 2048, op.mult, sig=x_pm)
 
     x_cz, x_dd, x_b0, x_c1, x_c2 = new(), new(), new(), new(), new()
     x_r16b, x_r8, x_lz, x_h1, x_lf, x_rt = new(), new(), new(), new(), new(), new()
     on(S, x_zz)
-    for k in (1, 2):
-        act(T.pres[:, 4 * S0 + k:4 * S0 + 4 * P:4], zeros(P), sig=x_pr)
+    lin(T.ones[:, 0:16], zeros(16), 0.5 + MARK / 2, sig=x_pr)
+    lin(T.ones[:, 16:48], zeros(32), MARK, sig=x_pr)
+    act(place(1, 0), zeros(P), sig=x_pr)
     on(S, x_is)
-    lin(T.pres[:, 4 * S0 + 3:4 * S0 + 4 * P:4], zeros(P), fc("isr"), sig=x_pr)
-    lin(fc("q5"), gs0, 4.0 * S0 - 4 * P * r - 2 * P, -1.0, f=fn.Sign)
-    lin(fc("q6"), gs0, LC * NR / 2.0, LC / (4.0 * P))
-    lin(fc("hneg"), gs0, 16.0 - S0, 0.25, sig=x_hn)
-    act(T.lall[:, :], zeros(P), sig=x_lz)
-    sw()
-    lin(fc("nbase"), fc("q5"), fc("q6"), LC * NR / 2.0, sig=x_b0)
+    lin(place(1, 1), zeros(P), fc("isr"), sig=x_pr)
+    lin(fc("hneg"), gs0, 18.0 - 3 * S0, 0.75, sig=x_hn)
+    act(T.lall[:, :], zeros(128), sig=x_lz)
+    on(S, x_pm)
+    lin(fc("q6"), fc("pm"), 0.0, -1.0)
     on(S, x_jm)
     act(ct("offj"), jm, sig=x_c1)
-    on(S, x_b0)
-    lin(T.cnt[:, 0:16], zeros(16), fc("nbase"), sig=x_cz)
-    lin(T.cnt[:, P + 16:P + 32], zeros(16), fc("nbase"), sig=x_cz)
     on(S, x_io1)
-    lin(ct("offu", 0, 8), T.rj[:, 1:9], 15.0, sig=x_c1)
-    lin(ct("offu", 8, 16), T.rj[:, 0:8], 15.0, sig=x_c1)
-    on(S, x_pm)
+    sw()
+    lin(fc("q5"), fc("p31"), fc("q6"), 2.0)
     lin(T.jwb[:, :], T.rj[:, 0:4:2], fc("pm"), sig=x_dd)
     lin(fc("sb1"), fc("pm"), 16.5)
-    on(S, x_lf)
-    act(T.lf[:, 16:32], T.lf[:, 0:16], sig=x_lf)
-    lin(fc("u2"), fc("pm"), 0.0, 16.0)
-    lin(ct("offp"), zeros(16), fc("pm"))
+    lin(fc("u1"), fc("p7"), 0.0, 8.0 - 1.0 / 16)
+    lin(ct("offp"), zeros(8), fc("pm"), sig=x_c1)
     lin(fc("q3"), fc("p31"), 0.0, 4.0)
     lin(fc("q7"), fc("pm"), 66.0, 128.0)
     lin(T.cf[:, 0:16], jm, fc("pm"), -1.0, f=fn.Abs)
+    lin(fc("q8"), fc("p7"), 143.0, 16.0)
+    lin(fc("rot", lo), fc("pm", lo), 15.0, 16.0)
     sw()
-    lin(ct("offg"), jm, fc("u2"), sig=x_c1)
-    lin(ct("offs"), ct("offp"), 15.0, 16.0, sig=x_c1)
-    lin(fc("o32"), fc("pm"), fc("q3"), -1.0)
-
-    on(V, x_cd, 128)
+    lin(fc("u2"), fc("pm"), fc("u1"), 1.0 / 8)
     for k in range(4):
-        ts(T.offl[:, k:16:4], T.cdi[:, k:16:4], 4.0, op.mult, T.bo[:, k:k + 1], op.add, sig="step")
+        a, b = [LC * (seat(h, r) if h != r else NR - 1) for h in (2 * k, 2 * k + 1)]
+        lin(fc("nbase", blk[k]), fc("q5", blk[k]), -float(a), (a - b) / 16.0)
+    lin(fc("rot", hi), fc("pm", hi), fc("q8", hi), -16.0)
+    lin(fc("o32"), fc("pm"), fc("q3"), -1.0)
+    sw()
+    lin(T.cnt[:, 0:16], zeros(16), fc("nbase"), sig=x_cz)
+    lin(T.cnt[:, 3 * P + 16:3 * P + 32], zeros(16), fc("nbase"), sig=x_cz)
+    for n, a, b, c in (("ofs", T.rj[:, 0:2], "o32", 1.0), ("offs", zeros(8), "rot", 1.0), ("offg", T.rj[:, 16:24], "u2", 2.0)):
+        lin(ct(n), a, fc(b), c, sig=x_c1)
+    on(S, x_lf)
+    act(T.lf[:, 16:32], T.lf[:, 0:16], sig=x_lf)
+
+    on(V, x_b6)
+    on(V, x_cd, 128)
+    for k in range(2):
+        ts(T.offl[:, k:16:2], T.cdi[:, k:16:2], 3.0, op.mult, T.bo[:, 4 + k:5 + k], op.add, sig="step")
     x_p8, x_p8s, x_lt, x_k0 = new(), new(), new(), new()
     on(V, x_x, 16)
     on(V, x_zz)
     quant("p1", 0, 128, T.xz[:, :], x_p1)
     pw()
-    on(V, x_pr, 4)
-    for i in range(4):
-        if i:
-            on(V, "scat", i)
-        v(V.tensor_copy(T.pres[:, :].indirect(T.offl[:, 4 * i:4 * i + 4]), T.ones[:, :]), "scat")
-        if i == 0:
-            on(V, x_pj2, 4)
-            ts(T.ic[:, 16:21], T.ic[:, 4:9], BITS, op.bitwise_and)
-        if i == 1:
-            vw()
-            ts(T.fc[:, 0:5], T.ic[:, 16:21], 1.0 / 2048, op.mult, sig=x_pm)
-        if i == 2:
-            ts(T.lf[:, 0:16], T.cdi[:, :], float(SHB), op.add, TINY, op.mult, sig=x_lf)
-        if i == 3:
-            fill(T.kk[:, :], 0, sig=x_k0)
-    on(V, "scat", 4)
-    on(V, x_r4)
-    for k in range(2):
-        a = 2 * P * k
-        scan(T.orx[:, a:a + 2 * P], T.r4[:, :], T.pres[:, 4 * S0 + a:4 * S0 + a + 2 * P], op.min, op.max, sig="step")
-    on(V, x_lf, 2)
-    v(V.transpose(T.lt[:, :], T.lf[:, :]), x_lt)
-    pw()
-    x_cnt = scan(T.cnt[:, 16:P + 16], T.orx[:, 3:4 * P:4], T.orx[:, 3:4 * P:4], op.add, op.max, sig=new())
+    on(V, x_pr, 5)
+    for i in range(8):
+        if i > 1:
+            on(V, "scat", i - 1)
+        v(V.tensor_copy(pres[i % 2][:, :].indirect(T.offl[:, 2 * i:2 * i + 2]), T.ones[:, 16 * (i % 2):16 * (i % 2) + 32]), "scat")
+    ts(T.lf[:, 0:16], T.cdi[:, :], float(SHB), op.add, TINY, op.mult, sig=x_lf)
     on(V, x_hn)
-    x_ow = ts(T.offw[:, :], T.cdi[:, :], fc("hneg"), op.add, P + 16.0, op.min, sig=new())
+    ts(T.ow[:, :], T.cdi[:, :], 3.0, op.mult, fc("hneg"), op.add)
+    on(V, "scat", 8)
+    x_cnt = scan(T.cnt[:, 16:3 * P + 16], pres[0][:, 3 * S0:3 * S0 + 3 * P], pres[1][:, 3 * S0:3 * S0 + 3 * P], op.add, op.add, sig=new())
+    cnt = T.cnt[:, 18:3 * P + 13:3]
+    vw()
+    x_ow = ts(T.offw[:, :], T.ow[:, :], 3 * P + 16.0, op.min, sig=new())
 
     x_m16, x_acc, x_cl, x_op, x_rn, x_th, x_req, x_lv, x_h2, x_m4a = [new() for k in range(10)]
     on(S, x_cnt)
-    s(S.activation(T.junk[:, 0:P - 1], T.cnt[:, 16:P + 15], fn.Sign, bias=fc("sb1"), scale=-1.0, accum_out=fc("ac1")), x_acc)
-    sw()
-    lin(ct("ofs"), T.rj[:, 0:2], fc("o32"), sig=x_c1)
+    s(S.activation(T.junk[:, 0:P - 1], cnt, fn.Sign, bias=fc("sb1"), scale=-1.0, accum_out=fc("ac1")), x_acc)
+    lin(T.p16[:, 16:32], T.cf[:, 0:16], 1.0, -1.0, sig=x_m, f=fn.Relu)
     on(S, x_acc)
     lin(T.req[:, RQ + 1:RQ + 2], fc("ac1"), (P - 1) * 0.5, 0.5, sig=x_req)
     on(S, x_cz, 2)
     on(S, x_ow)
     lin(T.lw[:, :], T.cnt[:, :].indirect(T.offw[:, :]), fc("nbase"), -1.0, sig=x_lv)
-    lin(T.p16[:, 16:32], T.cf[:, 0:16], 1.0, -1.0, sig=x_m, f=fn.Relu)
     lin(T.cf[:, 16:32], jm, fc("q7"), -128.0, f=fn.Relu)
 
     def rows(q, a, b):
@@ -326,13 +333,13 @@ def rank_program(g, core, T, topo):
     on(S, x_lv)
     rows(S, NQ, 16)
     sw()
-    lin(T.m4a[:, :], T.cf[:, 16:32], 2.0, -1.0, sig=x_m4a)
+    lin(T.m4a[:, 0:16], T.cf[:, 16:32], 2.0, -1.0, sig=x_m4a)
 
     on(V, x_cnt)
     on(V, x_dd)
     x_i = new()
     for k in range(2):
-        ts(T.ind[:, P * k:P * k + P - 1], T.cnt[:, 16:P + 15], T.jwb[:, k:k + 1], op.is_le, sig=x_i)
+        ts(T.ind[:, P * k:P * k + P - 1], cnt, T.jwb[:, k:k + 1], op.is_le, sig=x_i)
     for k in range(2):
         on(V, x_i, k + 1)
         scan(T.req[:, 2 * k:RQ + 3:3], T.ind[:, P * k:P * k + P - 1], T.ind[:, P * k:P * k + P - 1], op.add, op.max, sig=x_req)
@@ -343,26 +350,26 @@ def rank_program(g, core, T, topo):
     points(True)
     on(g, x_zz)
     halves(0)
+    halves(1)
     on(g, x_req, 3)
     tell(T.req[:, RQ:RQ + 3], lambda q: T.rland[:, 3 * seat(q, r):3 * seat(q, r) + 3], "req")
     const(T.rt1[:, 0:16], 0, x_rt)
     const(T.rt1[:, 48:64], 0, x_rt)
-    halves(1)
     g.affine_select(T.r16[:, :], zeros(P), [[0, 16], [1, 16]], op.is_equal, 1.0, 0, 0).then_inc(T.sem[x_r16b], 1)
 
     x_tq, x_wino, x_rl, x_ptown, x_rz = new(), new(), new(), new(), new()
     x_zw, x_im, x_vald, x_pj, x_m4, x_eq = new(), new(), new(), new(), new(), [new(), new()]
+    on(V, x_lf, 2)
+    v(V.transpose(T.lt[:, :], T.lf[:, :]), x_lt)
+    on(V, x_c1, 5)
+    cp(T.cu[:, 0:N1], T.ct[:, 0:N1], sig=x_op)
+    fill(T.kk[:, :], 0, sig=x_k0)
     on(V, x_tb, 16)
     quant("tq", 0, P, T.tt[:, :], x_tq)
-    on(V, x_c1, 6)
-    cp(T.cu[:, 0:N1], T.ct[:, 0:N1], sig=x_op)
-    quant("win", WOWN, WOWN + P, T.tt[:, :], x_wino)
-
-    def tile(b):
+    on(V, x_ebd, 2)
+    for b in range(4):
         quant("eq", 128 * b, 128 * b + 128, T.eb[:, 3 - b:515 - b], x_eq[b // 2])
     on(V, x_op)
-    on(V, x_p1)
-    pick_v(T.p8[:, :], T.p1[:, :], cu("offp", 0, 8), x_p8)
     on(V, x_k0)
     on(V, x_rz, 16)
     on(V, "r_req", TOLD)
@@ -388,7 +395,7 @@ def rank_program(g, core, T, topo):
     on(Q, x_lv)
     on(Q, x_lz)
     rows(Q, 0, NQ)
-    on(Q, "l_cod", WAVE)
+    on(Q, "l_co2", WAVE[1])
     on(Q, x_p1)
     load(Q, T.pt[:, A * r:A * r + A].bitcast(u8), T.p1[:, 0:A].bitcast(u8), x_ptown)
     load(Q, T.pts[:, A * r:A * r + A], T.p1s[:, 0:A], x_ptown)
@@ -396,16 +403,23 @@ def rank_program(g, core, T, topo):
     x_d8, x_kz = new(), new()
     on(S, x_op)
     on(S, x_p1)
-    pick_s(T.p8s[:, :], T.p1s[:, :], cu("offp", 0, 8), x_p8s)
     on(S, x_lt)
-    pick_s(T.rel[:, :], T.lt[:, 0:16], cu("offj"), x_rn)
+    act(T.ltr[lo, :], T.lt[lo, 0:16])
+    act(T.ltr[hi, :], T.lt[hi, 8:24])
+    pick_s(T.p8s[:, :], T.p1s[:, :], cu("offp"), x_p8s)
+    sw()
+
+    def bounds(a):
+        for u in range(a, a + 4):
+            lin(T.thr[:, 16 * u:16 * u + 16], T.ltr[:, :], T.ltr[:, u:u + 1], -1.0, sig=x_th)
+    bounds(0)
 
     for q_ in (V, S):
         on(q_, x_tq)
         on(q_, x_rl)
 
     def codes(w):
-        send(lambda q: T.snd[:, LC * seat(r, q):LC * seat(r, q) + LC].bitcast(u8), lambda q: T.win[:, spot(q):spot(q) + LC].bitcast(u8), "cod", others[WAVES[w]], 4)
+        send(lambda q: T.snd[:, LC * seat(r, q):LC * seat(r, q) + LC].bitcast(u8), lambda q: T.win[:, spot(q):spot(q) + LC].bitcast(u8), ("cod", "co2")[w], others[WAVES[w]], 4)
     x_sndc, x_snds = new(), new()
     for w in range(2):
         c, d = WAVES[w].start, WAVES[w].stop
@@ -421,7 +435,9 @@ def rank_program(g, core, T, topo):
     c0 = KP * A + P * r
     iota(T.erow[:, 0:128], [[-1, 8], [0, 16]], E - 1, 0, x_io2)
     const(T.fb[:, :], 1, x_fb)
-    const(T.gs[:, 7:576:8], 0, x_r8)
+    const(T.gs[:, 7:704:8], 0, x_r8)
+    iota(T.m4a[:, 16:18], [[-1, 2]], 1, 0, x_r8)
+    const(T.gb[:, 208:210], 0, x_r8)
     const(T.kc[:, 36:64], 0, x_h1)
     iota(T.erow[:, 128:160], [[-1, 4], [-1, 8]], E - 1, 0, x_zw)
     iota(T.im64[:, :], [[0, 4], [1, 16]], 0, 0, x_im)
@@ -444,95 +460,92 @@ def rank_program(g, core, T, topo):
     x_kap, x_dec, x_mn, x_td, x_la = new(), new(), new(), new(), new()
     on(S, x_h2, 256)
     pick_s(T.la[:, :], T.lall[:, :], cu("offg"), x_la)
+    x_s, x_sa, x_oh = [new(), new(), new()], new(), new()
+    on(M, x_p8)
+    on(M, x_p8s)
+    M.matmul_mx(T.ps[:, 1024:1024 + P], T.p8[:, :], T.p8s[:, :], T.tq[:, :], T.tqs[:, :], True, True).then_inc(T.sem[x_s[2]], 1)
     on(S, x_m)
-    pick_s(T.m16[:, :], T.p16[:, 16:32], cu("offp"), x_m16)
+    pick_s(T.m16[:, :], T.p16[:, 16:32], cu("offp", 0, 8), x_m16)
     on(S, x_m4a)
-    pick_s(T.m4[:, :], T.m4a[:, :], cu("offp"), x_m4)
-    lin(fc("q1"), gs0, fc("pm"), 1.0 / P)
-    lin(fc("q4"), fc("p31"), 8.5 / 8, -17.0 / 64)
-    act(T.ct[:, NT - 3:NT:2], zeros(2), sig=x_c2)
-    lin(ct("offz"), p7, 15.0, 8.0, sig=x_c2)
-    sw()
-    lin(fc("q2"), fc("pm"), fc("q4"), 17.0 / 128)
-    lin(ct("psel", 0, 1), fc("isr"), fc("q1"), 4.0 + 4 * r, sig=x_c2)
-    lin(ct("offn"), p7, E - 1.0, -0.5, sig=x_c2)
-    lin(ct("offf"), p7, FW - 4.0 * E + 2, 2.0, sig=x_c2)
-    sw()
-    lin(ct("tl", 0, 1), fc("t1"), fc("p31"), fc("q2"), sig=x_c2)
-    on(V, x_ebd, 2)
-    for b in range(4):
-        tile(b)
+    pick_s(T.m4[:, :], T.m4a[:, 0:16], cu("offp", 0, 8), x_m4)
+    lin(fc("q9"), gs0, odd - 1.0, 1.0 / (4 * P))
+    on(S, x_s[2])
+    act(T.sall[:, WOWN:WOWN + P], T.ps[:, 1024:1024 + P], sig=x_sa)
+    on(V, x_p1)
+    pick_v(T.p8[:, :], T.p1[:, :], cu("offp"), x_p8)
+    quant("win", WOWN, WOWN + P, T.tt[:, :], x_wino)
+    side = slice(128 - 112 * odd, 144 - 112 * odd)
+    pick_v(T.pk[:, side], T.tq[:, :], cu("offp", 0, 1), x_pj)
+    pick_s(T.pks[:, side], T.tqs[:, :], cu("offp", 0, 1), x_pj)
     on(V, x_r16b)
     on(V, x_la)
-    sums(T.lb[:, :], T.la[:, :], sig="step")
+    scan(T.lb[:, :], T.r16[:, 0:256:2], T.la[:, :], op.mult, op.add, sig="step")
     rest(2)
     pw()
     x_offc = new()
     for k in range(4):
-        ts(T.offc[32 * k:32 * k + 32, :], T.lb[me32, 15:256:16], -1.0, op.mult, -1.0 + LC * (2 * NR - 2 - r), op.add, sig=x_offc)
-    on(V, x_lt)
-    on(V, x_rn)
-    tt(T.thr[:, :], T.lt[:, 0:16].indirect(cu("offp")), T.rel[:, :], op.subtract, sig=x_th)
+        ts(T.offc[32 * k:32 * k + 32, :], T.lb[me32, 7:128:8], -1.0, op.mult, -1.0, op.add, sig=x_offc)
     rest(2)
-    rest(4)
+    on(V, x_offc, 4)
+    cp(T.offh[lo, :], T.offc[lo, 0:8], sig=x_oh)
+    cp(T.offh[hi, :], T.offc[hi, 8:16], sig=x_oh)
     on(V, x_m16)
 
-    x_cc, x_cs, x_s = [new(), new()], [new(), new()], [new(), new()]
-    on(V, "r_cod", WAVE)
+    x_cc, x_cs = new(), new()
+    bounds(4)
+    on(M, "r_pln", PAIR)
+    for w in range(2):
+        on(M, "r_" + ("cod", "co2")[w], WAVE[w])
+        a = slice(LC * WAVES[w].start, LC * WAVES[w].stop)
+        M.matmul_mx(T.ps[:, 512 * w:512 * w + a.stop - a.start], T.p8[:, :], T.p8s[:, :], T.win[:, a], T.wins[:, a], True, True).then_inc(T.sem[x_s[w]], 1)
+        on((V, S)[w], x_s[w])
+        if w == 0:
+            cp(T.sall[:, a], T.ps[:, 0:a.stop], sig=x_sa)
+        else:
+            act(T.sall[:, a], T.ps[:, 512:512 + a.stop - a.start], sig=x_sa)
     on(S, "r_pln", PAIR)
-    for q_ in (V, S):
-        on(q_, x_offc, 4)
-        on(q_, x_wino)
-    on(M, x_p8)
-    on(M, x_p8s)
-    for h in range(2):
-        a = slice(128 * h, 128 * h + 128)
-        pick_v(T.cand[:, a], T.win[:, :], T.offc[:, 8 * h:8 * h + 8], x_cc[h])
-        pick_s(T.cands[:, a], T.wins[:, :], T.offc[:, 8 * h:8 * h + 8], x_cs[h])
-        on(M, x_cc[h])
-        on(M, x_cs[h])
-        M.matmul_mx(T.ps[:, 512 * h:512 * h + 128], T.p8[:, :], T.p8s[:, :], T.cand[:, a], T.cands[:, a], True, True).then_inc(T.sem[x_s[h]], 1)
-    side = slice(128 - 112 * odd, 144 - 112 * odd)
-    for h in range(2):
-        on(V, x_cc[h])
-        on(S, x_cs[h])
-    pick_s(T.pks[:, side], T.cands[:, :], cu("offp", 0, 1), x_pj)
-    x_rep, x_sz, x_u3, x_du = new(), new(), new(), new()
-    on(S, x_r16b)
-    lin(T.dec[:, :], T.r16[:, 0:128], -4.0, 4.0 - 1.0 / 32, sig=x_dec)
-    rest(2)
-    on(V, x_s[0])
-    tt(T.sm[:, 0:128], T.ps[:, 0:128], T.m16[:, 0:128], op.mult, sig="step")
-    pick_v(T.pk[:, side], T.cand[:, :], cu("offp", 0, 1), x_pj)
-    on(V, x_s[1])
-    x_sm = tt(T.sm[:, 128:256], T.ps[:, 512:640], T.m16[:, 128:256], op.mult, sig=new())
+    on(S, x_offc, 4)
+    on(S, x_wino)
+    pick_s(T.cands[:, :], T.wins[:, :], T.offc[:, :], x_cs)
+    on(V, "r_co2", WAVE[1])
+    on(V, x_wino)
+    pick_v(T.cand[:, :], T.win[:, :], T.offc[:, :], x_cc)
+    x_sz, x_u3, x_du, x_tg = new(), new(), new(), new()
+    sw()
+    on(V, x_sa, 3)
+    on(V, x_oh, 2)
+    tt(T.sm[:, :], T.sall[:, :].indirect(T.offh[:, :]), T.m16[:, :], op.mult, sig="step")
+    ts(T.dec[:, :], T.r16[:, 0:128], 4.0 - 1.0 / 32, op.mult, -4.0, op.add, sig=x_dec)
     pw()
-    sums(T.sz[:, 0:128], T.sm[:, 0:128], sig=x_sz)
-    on(V, x_sm)
-    sums(T.sz[:, 128:256], T.sm[:, 128:256], sig=x_sz)
+    sums(T.sz[:, 0:128], T.sm[:, :], sig="step")
+    pw()
+    cp(T.sz[hi, 143:256:16], T.sz[lo, 15:128:16], sig=x_sz)
+    cp(T.sz[lo, 143:256:16], T.sz[hi, 15:128:16], sig=x_sz)
+    x_d, x_d2, x_cm = new(), new(), new()
+    for q_ in (V, S):
+        on(q_, x_sz, 2)
+    for u in range(8):
+        o, su = T.df[:, 16 * u:16 * u + 16], T.sz[:, 16 * u + 15:16 * u + 16]
+        if u < 5:
+            ts(o, T.sz[:, 15:256:16], su, op.subtract, -1.0, op.mult, sig=x_d)
+        else:
+            lin(o, T.sz[:, 15:256:16], su, -1.0, sig=x_d2)
+    on(V, x_th, 8)
     for h in range(2):
-        on(S, x_sz, h + 1)
-        pick_s(T.rep[:, 128 * h:128 * h + 112], T.sz[:, 128 * h:128 * h + 128], cu("offu", 8 * h, 8 * h + 7), x_rep)
-    on(V, x_sz, 2)
-    x_d, x_cm = new(), new()
-    for c in (0, C - 1):
-        ts(T.df[:, 16 * c:16 * c + 16], T.sz[:, 15:256:16], T.sz[:, 16 * c + 15:16 * c + 16], op.subtract, sig=x_d)
-    for h in range(2):
-        on(V, x_rep, h + 1)
-        tt(T.df[:, 16 + 112 * h:128 + 112 * h], T.sz[:, :].indirect(cu("offs", 0, 7)), T.rep[:, 128 * h:128 * h + 112], op.subtract, sig=x_d)
-    on(V, x_th)
-    for h in range(2):
-        a = slice(128 * h, 128 * h + 128)
-        on(V, x_d, h + 3)
-        tt(T.cm[:, a], T.df[:, a], T.thr[:, a], op.is_gt, sig=x_cm)
-    for h in range(2):
-        a = slice(128 * h, 128 * h + 128)
-        on(V, x_cm, h + 1)
-        sums(T.rk[:, a], T.cm[:, a], sig="step")
-    on(V, x_c2, 6)
-    cp(T.cu[:, N1:NT], T.ct[:, N1:NT])
+        a = slice(64 * h, 64 * h + 64)
+        on(V, x_d, h + 4)
+        if h:
+            on(V, x_d2, 3)
+        tt(T.cm[:, a], T.df[:, a], T.thr[:, a], op.is_lt, sig=x_cm)
+    on(V, x_cm, 2)
+    sums(T.rk[:, 0:128], T.cm[:, :], sig="step")
+    for a, b in ((lo, hi), (hi, lo)):
+        scan(T.rk[b, 128:256], T.r16[a, 0:128], T.cm[a, :], op.mult, op.add, sig="step")
     lin(fc("c6"), fc("pm"), -272.0, sig=x_u3)
     lin(fc("kap"), fc("pm"), -31.0, 2.0, sig=x_kap)
+    on(S, x_io2)
+    lin(T.tg[:, :], T.erow[:, 96:128], fc("q9"), sig=x_tg)
+    pick_s(T.rel[:, :], T.lt[:, 0:16], cu("offj"), x_rn)
     on(S, x_fb)
     act(T.fb[:, FW - 3:FW:2], zeros(2), sig=x_r8)
     on(S, x_m4)
@@ -544,19 +557,25 @@ def rank_program(g, core, T, topo):
     on(V, x_io2)
     pw()
     tt(T.oh[:, :], T.rk[:, :].indirect(cu("offs", 0, 8)), T.erow[:, 0:128], op.is_equal, sig="step")
+    on(V, x_tg)
+    x_os = tt(T.ohs[:, :], T.rk[:, :].indirect(cu("offs", 0, 2)), T.tg[:, :], op.is_equal, sig=new())
     on(V, x_u3)
     on(V, x_dec)
     pw()
     scan(T.lz[:, :], T.dec[:, :], T.oh[:, :], op.add, op.max, sig="step")
-    tt(T.ss[:, 64:112], T.sz[:, :].indirect(cu("offs", 4, 7)), T.oh[:, 64:112], op.mult)
+    on(V, x_os)
+    tt(T.ss[:, :], T.sz[:, :].indirect(cu("offs", 0, 2)), T.ohs[:, :], op.mult)
     pw()
     x_offr, x_kc, x_ks = new(), new(), new()
     best = slice(32 * odd, 32 * odd + 128)
     ts(T.offr[:, :], T.lz[:, 15:128:16], 512.0, op.mult, fc("c6"), op.add, sig=x_offr)
+    vw()
+    x_so = sums(T.ssz[:, :], T.ss[:, :], sig=new())
     for q_ in (V, S):
         on(q_, x_offr)
+    on(V, x_cc)
+    on(S, x_cs)
     pick_v(T.pk[:, best], T.cand[:, :], T.offr[:, :], x_kc)
-    tt(T.ss[:, 0:64], T.sz[:, :].indirect(cu("offs", 0, 4)), T.oh[:, 0:64], op.mult)
     pick_s(T.pks[:, best], T.cands[:, :], T.offr[:, :], x_ks)
     x_g = [new(), new()]
     on(M, x_pj, 2)
@@ -565,75 +584,78 @@ def rank_program(g, core, T, topo):
     for t in range(2):
         a = slice(16 * (t + odd), 16 * (t + odd) + 128)
         M.matmul_mx(T.ps[:, 1024 + 512 * t:1152 + 512 * t], T.pk[:, a], T.pks[:, a], T.pk[:, best], T.pks[:, best], True, True).then_inc(T.sem[x_g[t]], 1)
-    vw()
-    x_so = sums(T.ssz[:, 0:112], T.ss[:, 0:112], sig=new())
-    x_nm = new()
+    rest(2)
+    x_nm, x_f1 = new(), new()
     on(S, x_rn)
     lin(T.nm[:, :], T.rel[:, :].indirect(T.offr[:, :]), 0.0, 1.0 / TINY, sig=x_nm)
     sw()
     lin(T.dumpc[:, :], T.rj[:, 0:4], fc("dmp"), sig=x_du)
+    on(S, x_r16b)
     lin(T.r8[:, :], r8, -4.0, 4.0 - 1.0 / 16, sig=x_d8)
+    lin(fc("q1"), gs0, fc("pm"), 1.0 / P)
+    lin(fc("q4"), fc("p31"), 8.5 / 8, -17.0 / 64)
+    act(T.ct[:, NT - 3:NT:2], zeros(2), sig=x_c2)
+    lin(ct("offz"), p7, 15.0, 8.0, sig=x_c2)
+    lin(ct("offn"), p7, E - 1.0, -0.5, sig=x_c2)
+    lin(ct("offf"), p7, FW - 4.0 * E + 2, 2.0, sig=x_c2)
+    sw()
+    lin(fc("q2"), fc("pm"), fc("q4"), 17.0 / 128)
+    lin(ct("psel", 0, 1), fc("isr"), fc("q1"), (4.0 + 4 * r) / MARK, sig=x_c2)
+    sw()
+    lin(ct("tl", 0, 1), fc("t1"), fc("p31"), fc("q2"), sig=x_c2)
 
     def start(b):
-        return 8 * b * (b - 1) + 32 * (b // 2)
+        return 8 * b * (b - 1) + 32 * b
 
     x_pa, x_ke = new(), new()
-
-    def pairs(b):
-        a = E - 1 - b
-        t = a % 2
-        h = (a + odd - t) // 2
-        at = slice(32 * h, 32 * h + 32)
-        ts(T.gb[me32, start(b):start(b) + 16 * b], T.ps[at, 1152 + 512 * t - 16 * b:1152 + 512 * t], T.ssz[at, 16 * a + 15:16 * a + 16], op.is_ge,
-           fc("kap", at), op.add, sig=x_pa)
-
-    def part(k):
-        on(V, x_pa, (1, 4, 5, 7)[k])
-        lo, hi = start(max(1, 2 * k)), start(2 * k + 1) + 16 * (2 * k + 1)
-        scan(T.gs[me32, lo:hi], T.m4[me32, 0:hi - lo], T.gb[me32, lo:hi], op.add, op.max, sig=x_ke)
-
     on(V, x_so)
     on(V, x_kap)
-    on(V, x_g[0])
-    pairs(1)
-    pairs(3)
-    pairs(5)
+    for t in range(2):
+        on(V, x_g[t])
+        ts(T.gb[:, 96 - 96 * t:208 - 112 * t], T.ps[:, 1040 + 528 * t:1152 + 512 * t], T.ssz[:, 16 * t + 15:16 * t + 16], op.is_ge, fc("kap"), op.add, sig=x_pa)
+
+    def part(b):
+        h, t = divmod(E - 1 - b, 2)
+        at, e = slice(32 * h, 32 * h + 32), 208 - 112 * t
+        scan(T.gs[me32, start(b):start(b) + 16 * b], T.m4[at, 0:16 * b], T.gb[at, e - 16 * b:e], op.add, op.max, sig=x_ke)
+
+    def order(k):
+        a = slice(64 * k, 64 * k + 64)
+        on(V, x_nm)
+        on(V, x_mn)
+        scan(T.nz[:, a], T.mn[:, a], T.nm[:, a], op.add, op.max)
+
     on(V, x_m4)
-    on(V, x_r8, 2)
-    part(0)
-    on(V, x_g[1])
-    pairs(2)
-    pairs(4)
-    for b in range(1, E):
-        if b > 1:
-            on(V, "prune", b - 1)
-        if b == 1 or b % 2 == 0:
-            on(V, x_ke, b // 2 + 1)
+    on(V, x_r8, 4)
+    on(V, x_pa)
+    scan(T.fb[me32, FW - 39:FW - 4:2], T.m4a[96:128, 0:18], T.gb[96:128, 192:210], op.add, op.max, sig="prune")
+    order(0)
+    on(V, x_pa, 2)
+    part(2)
+    part(3)
+    for b in range(2, E):
+        on(V, "prune", b - 1)
+        on(V, x_ke, b - 1)
         e, n = FW - 4 * b, 2 * b + 3
         scan(T.fb[me32, e - n:e], T.fb[me32, e + 1:e + 1 + 2 * n:2], T.gs[me32, start(b) + 15:start(b) + 15 + 8 * n - 7:8], op.subtract, op.max, sig="prune", init=1.0)
-        if b == 1:
-            part(1)
-            pairs(6)
-        if b == 2:
-            part(2)
-        if b == 3:
-            pairs(7)
-        if b == 4:
-            part(3)
-        if b in (5, 6):
-            a = slice(64 * b - 320, 64 * b - 256)
-            on(V, x_nm)
-            on(V, x_mn)
-            scan(T.nz[:, a], T.mn[:, a], T.nm[:, a], op.add, op.max)
+        if b < E - 2:
+            part(b + 2)
+        if b == E - 2:
+            order(1)
     x_pp = new()
     on(S, x_h1)
     for b in range(1, E - 1):
         on(S, "prune", b)
+        if b == 1:
+            lin(T.fb[me32, FW - 6:FW - 5], T.fb[me32, FW - 5:FW - 4], 1.0, -1.0, sig=x_f1)
         s(S.activation(T.kc[me32, 80 + 8 * b:80 + 9 * b], T.fb[me32, FW - 4 * b - 1:FW - 4:4], fn.Identity, accum_out=T.kc[me32, 49 + b:50 + b]), x_pp)
-    rest()
+    on(V, x_c2, 6)
+    x_cu = cp(T.cu[:, N1:NT], T.ct[:, N1:NT], sig=new())
+    on(V, x_f1)
     on(V, "prune", E - 1)
     vw()
     tt(T.nz[me32, 15:112:16], T.nz[me32, 15:112:16], T.fb[me32, FW - 4 * E + 2:FW - 4:4], op.mult)
+    on(V, x_cu)
     on(V, x_pp, E - 2)
     on(V, x_zw, 2)
     on(V, x_h1)
@@ -651,7 +673,6 @@ def rank_program(g, core, T, topo):
     pw()
     k1 = T.km[:, 39:64:8]
     x_zr, x_dz, x_dm = new(), new(), new()
-    blk = [slice(32 * k, 32 * k + 32) for k in range(KP)]
 
     def bound(k):
         ts(T.kd[blk[k], 0:1], T.km[me32, 39 + 8 * k:40 + 8 * k], fc("kn", me32), op.add, T.dumpc[me32, k:k + 1], op.max)
@@ -665,13 +686,13 @@ def rank_program(g, core, T, topo):
         on(q_, x_zr)
     for k in range(KP):
         o = T.dz[blk[k], :]
-        if k < 3:
+        if k < 2:
             ts(o, T.zrow[me32, :], DL, op.mult, T.dm[me32, k:k + 1], op.subtract, sig="step")
         else:
             lin(o, T.zrow[me32, :], T.dm[me32, k:k + 1], -DL, sig=x_dz)
     bound(1)
     pw()
-    on(V, x_dz)
+    on(V, x_dz, 2)
     v(V.tensor_reduce(T.dm[:, 4:5], T.dz[:, :], X, op.min, apply_absolute_value=True), "step")
     bound(2)
     bound(3)
@@ -689,7 +710,7 @@ def rank_program(g, core, T, topo):
     act(T.ky[:, 32:40], zeros(8), sig=x_kz)
     lin(fc("c7"), fc("pm"), -128.0, sig=x_kz)
     act(T.kf[:, :], zeros(32), sig=x_kf)
-    lin(fc("g16"), fc("hneg"), NR * A - 1.0, 1.0 / 16)
+    lin(fc("g16"), gs0, NR * A - S0 / 16, 1.0 / 64)
     on(S, x_im)
     sw()
     lin(T.vald[:, :], T.im64[:, :], fc("g16"), -1.0, sig=x_vald)
@@ -706,14 +727,15 @@ def rank_program(g, core, T, topo):
     ts(T.ofy[:, :], T.ky[:, 7:39:4], 256.0, op.mult, fc("c7"), op.add, sig=x_oy)
     on(V, x_kf)
     ts(T.kf[:, 0:4], k1, fc("knb"), op.add, -1.0, op.max)
-    rest(2)
+    rest(3)
     vw()
     v(V.transpose(T.kt[me32, :], T.kf[me32, :]), x_kt)
+    rest(4)
     on(Q, x_oy)
     for k in range(8):
         load(Q, T.oy[16 * k:16 * k + 16, :], T.ofy[16 * r:16 * r + 16, :], x_oyd)
     on(M, x_sz, 2)
-    on(M, x_ke, 4)
+    on(M, x_pa, 2)
     on(M, x_ptown, 32)
     on(M, "r_ptc", TOLD)
     on(M, "r_pts", TOLD)
@@ -727,7 +749,7 @@ def rank_program(g, core, T, topo):
     on(M, x_un[0])
     on(M, x_wq)
     M.matmul_mx(T.ps[:, 0:128], T.wq[:, :], T.wqs[:, :], T.pk[:, best], T.pks[:, best], True, True).then_inc(T.sem[x_y], 1)
-    on(S, x_rest, 3)
+    on(S, x_rest, 5)
     for b in range(2):
         act(T.tbd[:, P * b:P * b + P], T.ps[:, 2048 + 512 * b:2048 + 512 * b + P], sig=x_td)
     on(S, x_y)
@@ -793,4 +815,4 @@ def rank_program(g, core, T, topo):
     on(V, "v", vn[0])
     on(S, "s", sn_[0])
     for n in ROADS:
-        on(g, "l_" + n, {"cod": WAVE, "pln": PAIR, "ptc": 2 * EV}.get(n, EV))
+        on(g, "l_" + n, {"cod": WAVE[0], "co2": WAVE[1], "pln": PAIR, "ptc": 2 * EV}.get(n, EV))

@@ -5,7 +5,7 @@ NR, P, A, C, E, KP, LC = 8, 256, 16, 16, 8, 4, 48
 WOWN = (NR - 1) * LC
 SH = 16
 ZW = NR * P + SH
-DL = 4096.0
+DL = 2.0 ** 17
 DUMP = 7 * 4096
 SHB = DUMP + KP * A
 CLW = KP * A + NR * P + 16
@@ -20,7 +20,6 @@ HI = 2048.0
 MARK = 0.125
 WHOLE = 3 * 2 ** 22
 BITS = 0x7C03
-ORDER = (1, 4, 2, 5, 3, 6, 7)
 WAVES = (slice(0, 4), slice(4, 7))
 
 TAB, NT = {}, 0
@@ -28,7 +27,7 @@ for _n, _k in (("offp", 8), ("offs", 8), ("offg", 8), ("offj", 16), ("ofs", 2),
                ("offz", 2), ("offn", 2), ("offf", 2), ("psel", 2), ("tl", 2)):
     TAB[_n] = (NT, _k)
     NT += _k
-N1 = TAB["offz"][0]
+N1, N2 = TAB["offz"][0], TAB["psel"][0]
 
 F, B, I, U = "float32", "bfloat16", "int32", "uint16"
 SB = {
@@ -37,14 +36,14 @@ SB = {
     "reql": (32, U), "rj": (32, F), "ct": (NT, F), "cu": (NT, U), "ic": (24, I),
     "jwb": (2, B), "dumpc": (4, F), "im64": (64, F), "r8": (32, F), "ofy": (8, U), "oy": (8, U),
     "cf": (32, F), "m16": (128, B), "m4": (128, B), "m4a": (32, B), "ltr": (16, F), "tg": (32, B), "ohs": (32, B),
-    "r16": (256, B), "zw": (ZW, F), "vald": (64, B), "erow": (160, F),
+    "r16": (256, B), "zw": (ZW, F), "vald": (64, B), "erow": (192, F), "hz": (32, F),
     "lf": (32, F), "lt": (32, F), "thr": (128, B), "rel": (256, F), "mn": (128, B),
     "offw": (16, U), "lw": (256, F), "lall": (128, F), "la": (128, F), "lb": (128, F), "offc": (16, U), "offh": (8, U), "sall": (WOWN + P, F),
     "sm": (128, F), "sz": (256, F), "df": (128, B), "cm": (128, B), "rk": (256, B), "oh": (128, B), "dec": (128, B), "p16": (32, B),
     "lz": (128, B), "offr": (8, U), "ss": (32, F), "ssz": (32, F), "nm": (128, F), "nz": (128, F), "gb": (224, B),
-    "gs": (704, B), "fb": (64, F), "ub": (24, F), "bo": (8, F), "kh": (32, F), "km": (64, F), "ky": (64, F),
-    "kf": (32, F), "kt": (32, F), "kd": (16, F), "kl0": (4, U), "zrow": (64, F), "dz": (64, F), "dm": (8, F),
-    "kk": (48, U), "kc": (136, F), "okl": (16, U), "ysb": (144, F), "yo": (64, F), "mx": (80, F),
+    "gs": (704, B), "fb": (64, F), "ub": (136, B), "bo": (8, F), "kh": (32, F), "km": (64, F), "ky": (64, F),
+    "kf": (32, F), "kt": (32, F), "kd": (16, F), "kl0": (4, U), "two": (65, F), "dz": (65, F), "dm": (65, F), "bit": (16, F),
+    "kk": (48, U), "kc": (136, F), "okl": (16, U), "ysb": (144, F), "yo": (64, F), "mx": (136, B), "rs": (136, B),
     "xz": (512, B), "wt": (512, B), "tt": (1024, B), "eb": (520, B), "cl": (CLW, B), "ttc": (544, B),
     "ptd": (4 * PW, F), "tbd": (2 * P, B), "gp": (2 * P, F), "ptl": (16, U), "bb": (1024, B),
 }
@@ -60,8 +59,8 @@ for _n, _k in CODES.items():
     SCRATCH[_n + "s"] = ("sbuf", [128, _k], "uint8")
 SCRATCH["ps"] = ("psum", [128, 4096], F)
 
-ROADS = ["ptc", "pts", "req", "cod", "co2", "pln", "kept"]
-XS = ["x%d" % i for i in range(130)]
+ROADS = ["ptc", "pts", "req", "cod", "co2", "kept"]
+XS = ["x%d" % i for i in range(132)]
 SEMAPHORES = ["v", "s", "step", "scat", "claim", "prune"] + ["r_" + n for n in ROADS] + ["l_" + n for n in ROADS] + XS
 
 
@@ -71,6 +70,9 @@ def rank_program(g, core, T, topo):
         return
     V, S, Q, M = g.vector, g.scalar, g.sync, g.tensor
     op, X, fn = AluOpType, AxisListType.X, ActivationFunctionType
+    home = [m for m in range(1, NR) if topo.die(T.cores[r ^ m]) == topo.die(core)]
+    away = [m for m in range(1, NR) if m not in home]
+    ORDER = [m for pair in zip(home, away) for m in pair] + away[len(home):]
     others = [r ^ m for m in ORDER]
     u8, u32 = dt.uint8, dt.uint32
 
@@ -159,21 +161,12 @@ def rank_program(g, core, T, topo):
     def load(q, o, a, sig):
         q.dma_start(o, a).then_inc(T.sem[sig], 16)
 
-    def masks(dests, n):
-        near = [q for q in dests if topo.die(T.cores[q]) == topo.die(core)]
-        far = [q for q in dests if q not in near]
-        places = {0: [k for k in range(16 // n) if k % 2 == 0], 1: [k for k in range(16 // n) if k % 2 == 1]}
-        out = {}
-        for side, grp in ((0, near), (1, far)):
-            for q in grp:
-                k = (places[side] or places[1 - side]).pop(0)
-                e = topo.engines(core, T.cores[q])
-                out[q] = sum(1 << e[j] for j in range(k, len(e), len(e) // n))
-        return out
+    def shares(dests, parts):
+        return {q: sum(1 << e for e in topo.engines(core, T.cores[q])[k::n]) for q, (k, n) in zip(dests, parts)}
 
-    def send(src, dst, road, dests, n):
-        tr, mk = [], masks(dests, n)
-        for q in dests:
+    def send(src, dst, road, mk):
+        tr = []
+        for q in mk:
             rid, pid = topo.addr(T.cores[q])[:2]
             tr.append(RemoteDMATransfer(dst_ids=[DstId(rid=rid, pnc=pid)], dma_engine_mask=mk[q], remote_sem=T.sem["r_" + road], src=src(q), dst=dst(q)))
         g.remote_dma_fused(tr, local_sem=T.sem["l_" + road])
@@ -192,8 +185,7 @@ def rank_program(g, core, T, topo):
         tell(T.p1[:, 0:A].bitcast(u8), lambda q: T.pt[:, A * r:A * r + A].bitcast(u8), "ptc",
              [q for q in others if (topo.die(T.cores[q]) == topo.die(core)) == near])
 
-    WAVE = [4 * (w.stop - w.start) for w in WAVES]
-    PAIR = 2 * len(others)
+    WAVE = 2 * EV
     TOLD = EV * len(others)
 
     def seat(a, b):
@@ -204,7 +196,7 @@ def rank_program(g, core, T, topo):
 
     row16, jm, r8 = T.rj[:, 0:16], T.rj[:, 16:32], T.r16[:, 0:64:2]
     kland, kmsg = T.kk[:, 0:32], T.kk[:, 40:44]
-    klf, ub = T.kc[:, 0:32], T.ub[:, 0:17]
+    klf, ub = T.kc[:, 0:32], T.ub[:, :]
     gs0, p7 = T.bo[:, 0:1], T.fc[:, 2:4]
     odd = r % 2
     me32 = slice(32 * (r // 2), 32 * (r // 2) + 32)
@@ -250,7 +242,7 @@ def rank_program(g, core, T, topo):
     ts(T.bo[:, 4:6], T.bo[:, 0:2], fc("g2"), op.add, sig=x_b6)
     ts(T.fc[:, 0:5], T.ic[:, 16:21], 1.0 / 2048, op.mult, sig=x_pm)
 
-    x_cz, x_dd, x_b0, x_c1, x_c2 = new(), new(), new(), new(), new()
+    x_cz, x_dd, x_c1, x_c2 = new(), new(), new(), new()
     x_r16b, x_r8, x_lz, x_h1, x_lf, x_rt = new(), new(), new(), new(), new(), new()
     on(S, x_zz)
     lin(T.ones[:, 0:16], zeros(16), 0.5 + MARK / 2, sig=x_pr)
@@ -339,10 +331,11 @@ def rank_program(g, core, T, topo):
     on(V, x_dd)
     x_i = new()
     for k in range(2):
-        ts(T.ind[:, P * k:P * k + P - 1], cnt, T.jwb[:, k:k + 1], op.is_le, sig=x_i)
+        ts(T.ind[:, P * k + 32 * k:P * k + P - 1], cnt[:, 32 * k:P - 1], T.jwb[:, k:k + 1], op.is_le, sig=x_i)
     for k in range(2):
         on(V, x_i, k + 1)
-        scan(T.req[:, 2 * k:RQ + 3:3], T.ind[:, P * k:P * k + P - 1], T.ind[:, P * k:P * k + P - 1], op.add, op.max, sig=x_req)
+        a = T.ind[:, P * k + 32 * k:P * k + P - 1]
+        scan(T.req[:, 98 * k:RQ + 3:3], a, a, op.add, op.max, sig=x_req, init=32.0 * k)
 
     def halves(k):
         g.affine_select(T.eb[:, 258 * k:258 * k + 258], zeros(258), [[1, 258]], op.not_equal, 0.5, 258 * k - 3, -4).then_inc(T.sem[x_ebd], 1)
@@ -356,6 +349,11 @@ def rank_program(g, core, T, topo):
     const(T.rt1[:, 0:16], 0, x_rt)
     const(T.rt1[:, 48:64], 0, x_rt)
     g.affine_select(T.r16[:, :], zeros(P), [[0, 16], [1, 16]], op.is_equal, 1.0, 0, 0).then_inc(T.sem[x_r16b], 1)
+    x_two = new()
+    const(T.dm[:, 0:64], 2, x_two)
+    const(T.two[:, 64:65], -int(DL), x_two)
+    on(g, x_two, 2)
+    g.affine_select(T.two[:, 0:64], T.dm[:, 0:64], [[0, 4], [1, 16]], op.not_equal, 2.0 ** -15, 0, 0).then_inc(T.sem[x_two], 1)
 
     x_tq, x_wino, x_rl, x_ptown, x_rz = new(), new(), new(), new(), new()
     x_zw, x_im, x_vald, x_pj, x_m4, x_eq = new(), new(), new(), new(), new(), [new(), new()]
@@ -395,7 +393,10 @@ def rank_program(g, core, T, topo):
     on(Q, x_lv)
     on(Q, x_lz)
     rows(Q, 0, NQ)
-    on(Q, "l_co2", WAVE[1])
+    on(Q, x_tq)
+    load(Q, T.win[:, WOWN:WOWN + P].bitcast(u8), T.tq[:, :].bitcast(u8), x_wino)
+    load(Q, T.wins[:, WOWN:WOWN + P], T.tqs[:, :], x_wino)
+    on(Q, "l_co2", WAVE)
     on(Q, x_p1)
     load(Q, T.pt[:, A * r:A * r + A].bitcast(u8), T.p1[:, 0:A].bitcast(u8), x_ptown)
     load(Q, T.pts[:, A * r:A * r + A], T.p1s[:, 0:A], x_ptown)
@@ -418,19 +419,24 @@ def rank_program(g, core, T, topo):
         on(q_, x_tq)
         on(q_, x_rl)
 
-    def codes(w):
-        send(lambda q: T.snd[:, LC * seat(r, q):LC * seat(r, q) + LC].bitcast(u8), lambda q: T.win[:, spot(q):spot(q) + LC].bitcast(u8), ("cod", "co2")[w], others[WAVES[w]], 4)
+    def codes(road, mk):
+        send(lambda q: T.snd[:, LC * seat(r, q):LC * seat(r, q) + LC].bitcast(u8), lambda q: T.win[:, spot(q):spot(q) + LC].bitcast(u8), road, mk)
+
+    def planes(road, mk):
+        send(lambda q: T.snds[:, LC * seat(r, q):LC * seat(r, q) + LC], lambda q: T.wins[:, spot(q):spot(q) + LC], road, mk)
     x_sndc, x_snds = new(), new()
     for w in range(2):
         c, d = WAVES[w].start, WAVES[w].stop
         pick_v(T.snd[:, LC * c:LC * d], T.tq[:, :], T.reql[:, 3 * c:3 * d], x_sndc)
         pick_s(T.snds[:, LC * c:LC * d], T.tqs[:, :], T.reql[:, 3 * c:3 * d], x_snds)
     on(g, x_sndc)
-    codes(0)
+    codes("cod", shares(others[0:4], ((0, 4), (1, 4), (2, 4), (3, 4))))
+    on(g, x_snds)
+    planes("cod", shares(others[0:4], ((0, 4), (1, 4), (2, 4), (3, 4))))
     on(g, x_snds, 2)
-    send(lambda q: T.snds[:, LC * seat(r, q):LC * seat(r, q) + LC], lambda q: T.wins[:, spot(q):spot(q) + LC], "pln", others, 2)
+    planes("co2", shares(others[4:7], ((0, 4), (2, 4), (1, 2))))
     on(g, x_sndc, 2)
-    codes(1)
+    codes("co2", shares(others[4:7], ((0, 2), (1, 4), (3, 4))))
     x_fb = new()
     c0 = KP * A + P * r
     iota(T.erow[:, 0:128], [[-1, 8], [0, 16]], E - 1, 0, x_io2)
@@ -439,11 +445,18 @@ def rank_program(g, core, T, topo):
     iota(T.m4a[:, 16:18], [[-1, 2]], 1, 0, x_r8)
     const(T.gb[:, 208:210], 0, x_r8)
     const(T.kc[:, 36:64], 0, x_h1)
-    iota(T.erow[:, 128:160], [[-1, 4], [-1, 8]], E - 1, 0, x_zw)
+    x_e2 = new()
+    iota(T.erow[:, 128:160], [[-1, 4], [-1, 8]], E - 1, 0, x_e2)
     iota(T.im64[:, :], [[0, 4], [1, 16]], 0, 0, x_im)
-    iota(T.zw[:, :], [[32, ZW]], 0, 0, x_zw)
+    x_hz = new()
+    g.affine_select(T.hz[:, :], zeros(32), [[0, 4], [-1, 8]], op.is_gt, 1.0, 2, 0).then_inc(T.sem[x_hz], 1)
+    on(g, x_e2)
+    g.affine_select(T.erow[:, 160:192], T.erow[:, 128:160], [[0, 4], [1, 8]], op.not_equal, 0.0, 0, 0).then_inc(T.sem[x_zw], 1)
+    iota(T.zw[:, :], [[1, ZW]], SHB - SH, 0, x_zw)
     points(False)
     tell(T.p1s[:, 0:A], lambda q: T.pts[:, A * r:A * r + A], "pts")
+    x_rs = new()
+    g.affine_select(T.rs[:, :], zeros(136), [[0, 17], [1, 8]], op.not_equal, -1024.0, 0, 0).then_inc(T.sem[x_rs], 1)
     iota(T.cl[:, c0 - 16:c0 + 272], [[-1, 288]], 15, 0, x_cl)
 
     x_un, x_rest = [new(), new()], new()
@@ -457,7 +470,7 @@ def rank_program(g, core, T, topo):
         done[1] += 1
         tt(T.ptd[:, PW * b + RO + a:PW * b + RO + a + 64 * n], T.tt[:, 4 * a + b:4 * a + 256 * n:4], T.ps[:, 2048 + 512 * b + a:2048 + 512 * b + a + 64 * n],
            op.subtract, sig=x_rest)
-    x_kap, x_dec, x_mn, x_td, x_la = new(), new(), new(), new(), new()
+    x_dec, x_mn, x_td, x_la = new(), new(), new(), new()
     on(S, x_h2, 256)
     pick_s(T.la[:, :], T.lall[:, :], cu("offg"), x_la)
     x_s, x_sa, x_oh = [new(), new(), new()], new(), new()
@@ -466,14 +479,12 @@ def rank_program(g, core, T, topo):
     M.matmul_mx(T.ps[:, 1024:1024 + P], T.p8[:, :], T.p8s[:, :], T.tq[:, :], T.tqs[:, :], True, True).then_inc(T.sem[x_s[2]], 1)
     on(S, x_m)
     pick_s(T.m16[:, :], T.p16[:, 16:32], cu("offp", 0, 8), x_m16)
-    on(S, x_m4a)
-    pick_s(T.m4[:, :], T.m4a[:, 0:16], cu("offp", 0, 8), x_m4)
     lin(fc("q9"), gs0, odd - 1.0, 1.0 / (4 * P))
+    x_own, x_bit = new(), new()
     on(S, x_s[2])
     act(T.sall[:, WOWN:WOWN + P], T.ps[:, 1024:1024 + P], sig=x_sa)
     on(V, x_p1)
     pick_v(T.p8[:, :], T.p1[:, :], cu("offp"), x_p8)
-    quant("win", WOWN, WOWN + P, T.tt[:, :], x_wino)
     side = slice(128 - 112 * odd, 144 - 112 * odd)
     pick_v(T.pk[:, side], T.tq[:, :], cu("offp", 0, 1), x_pj)
     pick_s(T.pks[:, side], T.tqs[:, :], cu("offp", 0, 1), x_pj)
@@ -489,13 +500,15 @@ def rank_program(g, core, T, topo):
     on(V, x_offc, 4)
     cp(T.offh[lo, :], T.offc[lo, 0:8], sig=x_oh)
     cp(T.offh[hi, :], T.offc[hi, 8:16], sig=x_oh)
+    on(V, x_two, 3)
+    on(V, x_m)
+    scan(T.bit[:, :], T.two[:, 0:16], T.p16[:, 16:32], op.mult, op.add, sig=x_own)
     on(V, x_m16)
 
     x_cc, x_cs = new(), new()
     bounds(4)
-    on(M, "r_pln", PAIR)
     for w in range(2):
-        on(M, "r_" + ("cod", "co2")[w], WAVE[w])
+        on(M, "r_" + ("cod", "co2")[w], WAVE)
         a = slice(LC * WAVES[w].start, LC * WAVES[w].stop)
         M.matmul_mx(T.ps[:, 512 * w:512 * w + a.stop - a.start], T.p8[:, :], T.p8s[:, :], T.win[:, a], T.wins[:, a], True, True).then_inc(T.sem[x_s[w]], 1)
         on((V, S)[w], x_s[w])
@@ -503,12 +516,12 @@ def rank_program(g, core, T, topo):
             cp(T.sall[:, a], T.ps[:, 0:a.stop], sig=x_sa)
         else:
             act(T.sall[:, a], T.ps[:, 512:512 + a.stop - a.start], sig=x_sa)
-    on(S, "r_pln", PAIR)
+    on(S, x_s[0])
     on(S, x_offc, 4)
-    on(S, x_wino)
+    on(S, x_wino, 32)
     pick_s(T.cands[:, :], T.wins[:, :], T.offc[:, :], x_cs)
-    on(V, "r_co2", WAVE[1])
-    on(V, x_wino)
+    on(V, "r_co2", WAVE)
+    on(V, x_wino, 32)
     pick_v(T.cand[:, :], T.win[:, :], T.offc[:, :], x_cc)
     x_sz, x_u3, x_du, x_tg = new(), new(), new(), new()
     sw()
@@ -519,8 +532,9 @@ def rank_program(g, core, T, topo):
     pw()
     sums(T.sz[:, 0:128], T.sm[:, :], sig="step")
     pw()
+    on(S, "step", pn[0])
     cp(T.sz[hi, 143:256:16], T.sz[lo, 15:128:16], sig=x_sz)
-    cp(T.sz[lo, 143:256:16], T.sz[hi, 15:128:16], sig=x_sz)
+    act(T.sz[lo, 143:256:16], T.sz[hi, 15:128:16], sig=x_sz)
     x_d, x_d2, x_cm = new(), new(), new()
     for q_ in (V, S):
         on(q_, x_sz, 2)
@@ -542,24 +556,25 @@ def rank_program(g, core, T, topo):
     for a, b in ((lo, hi), (hi, lo)):
         scan(T.rk[b, 128:256], T.r16[a, 0:128], T.cm[a, :], op.mult, op.add, sig="step")
     lin(fc("c6"), fc("pm"), -272.0, sig=x_u3)
-    lin(fc("kap"), fc("pm"), -31.0, 2.0, sig=x_kap)
+    lin(fc("kap"), fc("pm"), -31.0, 2.0, sig=x_u3)
     on(S, x_io2)
     lin(T.tg[:, :], T.erow[:, 96:128], fc("q9"), sig=x_tg)
+    on(S, x_m4a)
+    pick_s(T.m4[:, :], T.m4a[:, 0:16], cu("offp", 0, 8), x_m4)
     pick_s(T.rel[:, :], T.lt[:, 0:16], cu("offj"), x_rn)
     on(S, x_fb)
     act(T.fb[:, FW - 3:FW:2], zeros(2), sig=x_r8)
     on(S, x_m4)
     lin(T.mn[:, :], T.m4[:, 0:128], 0.0, HI, sig=x_mn)
-    lin(fc("pm8"), fc("pm"), -DL * (8 + 32 * (SHB - SH + 30 * HI)), DL * (1 + 64 * HI), sig=x_du)
-    lin(fc("kn"), fc("pm"), -30 * HI, 2 * HI, sig=x_du)
-    lin(fc("knb"), fc("pm"), -30 * HI - SHB, 2 * HI, sig=x_du)
-    lin(fc("dmp"), fc("pm"), float(DUMP))
+    lin(ct("offz"), p7, 15.0, 8.0, sig=x_c2)
+    lin(ct("offn"), p7, E - 1.0, -0.5, sig=x_c2)
+    lin(ct("offf"), p7, FW - 4.0 * E + 2, 2.0, sig=x_c2)
     on(V, x_io2)
     pw()
     tt(T.oh[:, :], T.rk[:, :].indirect(cu("offs", 0, 8)), T.erow[:, 0:128], op.is_equal, sig="step")
     on(V, x_tg)
     x_os = tt(T.ohs[:, :], T.rk[:, :].indirect(cu("offs", 0, 2)), T.tg[:, :], op.is_equal, sig=new())
-    on(V, x_u3)
+    on(V, x_u3, 2)
     on(V, x_dec)
     pw()
     scan(T.lz[:, :], T.dec[:, :], T.oh[:, :], op.add, op.max, sig="step")
@@ -588,28 +603,23 @@ def rank_program(g, core, T, topo):
     x_nm, x_f1 = new(), new()
     on(S, x_rn)
     lin(T.nm[:, :], T.rel[:, :].indirect(T.offr[:, :]), 0.0, 1.0 / TINY, sig=x_nm)
-    sw()
-    lin(T.dumpc[:, :], T.rj[:, 0:4], fc("dmp"), sig=x_du)
+    lin(fc("dmp"), fc("pm"), float(DUMP))
+    lin(fc("kn"), fc("pm"), -30 * HI, 2 * HI, sig=x_du)
+    lin(fc("knb"), fc("pm"), -30 * HI - SHB, 2 * HI, sig=x_du)
+    on(S, x_own)
+    lin(T.dz[:, 64:65], T.bit[:, 15:16], -DL / 2, 2 * DL, sig=x_bit)
     on(S, x_r16b)
     lin(T.r8[:, :], r8, -4.0, 4.0 - 1.0 / 16, sig=x_d8)
-    lin(fc("q1"), gs0, fc("pm"), 1.0 / P)
-    lin(fc("q4"), fc("p31"), 8.5 / 8, -17.0 / 64)
-    act(T.ct[:, NT - 3:NT:2], zeros(2), sig=x_c2)
-    lin(ct("offz"), p7, 15.0, 8.0, sig=x_c2)
-    lin(ct("offn"), p7, E - 1.0, -0.5, sig=x_c2)
-    lin(ct("offf"), p7, FW - 4.0 * E + 2, 2.0, sig=x_c2)
     sw()
-    lin(fc("q2"), fc("pm"), fc("q4"), 17.0 / 128)
-    lin(ct("psel", 0, 1), fc("isr"), fc("q1"), (4.0 + 4 * r) / MARK, sig=x_c2)
-    sw()
-    lin(ct("tl", 0, 1), fc("t1"), fc("p31"), fc("q2"), sig=x_c2)
+    lin(T.dumpc[:, :], T.rj[:, 0:4], fc("dmp"), sig=x_du)
 
     def start(b):
         return 8 * b * (b - 1) + 32 * b
 
-    x_pa, x_ke = new(), new()
+    x_pa, x_ke, x_pp = new(), new(), new()
+    on(V, x_c2, 3)
+    x_cu = cp(T.cu[:, N1:N2], T.ct[:, N1:N2], sig=new())
     on(V, x_so)
-    on(V, x_kap)
     for t in range(2):
         on(V, x_g[t])
         ts(T.gb[:, 96 - 96 * t:208 - 112 * t], T.ps[:, 1040 + 528 * t:1152 + 512 * t], T.ssz[:, 16 * t + 15:16 * t + 16], op.is_ge, fc("kap"), op.add, sig=x_pa)
@@ -642,79 +652,76 @@ def rank_program(g, core, T, topo):
             part(b + 2)
         if b == E - 2:
             order(1)
-    x_pp = new()
+    on(V, x_cu)
+    on(V, x_pp, E - 3)
+    on(V, x_zw, 2)
+    on(V, x_h1)
+    on(V, x_im)
+    tt(T.kh[:, :], T.kc[:, 48:56].indirect(cu("offn")), T.erow[:, 160:192], op.is_equal, sig="step")
     on(S, x_h1)
     for b in range(1, E - 1):
         on(S, "prune", b)
         if b == 1:
             lin(T.fb[me32, FW - 6:FW - 5], T.fb[me32, FW - 5:FW - 4], 1.0, -1.0, sig=x_f1)
-        s(S.activation(T.kc[me32, 80 + 8 * b:80 + 9 * b], T.fb[me32, FW - 4 * b - 1:FW - 4:4], fn.Identity, accum_out=T.kc[me32, 49 + b:50 + b]), x_pp)
-    on(V, x_c2, 6)
-    x_cu = cp(T.cu[:, N1:NT], T.ct[:, N1:NT], sig=new())
+        s(S.activation(T.kc[me32, 80 + 8 * b:80 + 9 * b], T.fb[me32, FW - 4 * b - 1:FW - 4:4], fn.Identity, accum_out=T.kc[me32, 49 + b + b // 6:50 + b + b // 6]), x_pp)
+    x_c3 = new()
+    lin(fc("q1"), gs0, fc("pm"), 1.0 / P)
+    lin(fc("q4"), fc("p31"), 68.0 / 8, -17.0 / 8)
+    act(T.ct[:, NT - 3:NT:2], zeros(2), sig=x_c3)
+    sw()
+    lin(fc("q2"), fc("pm"), fc("q4"), 17.0 / 16)
+    lin(fc("q3"), fc("p31"), 0.0, 8.0)
+    lin(ct("psel", 0, 1), fc("isr"), fc("q1"), (4.0 + 4 * r) / MARK, sig=x_c3)
     on(V, x_f1)
-    on(V, "prune", E - 1)
     vw()
-    tt(T.nz[me32, 15:112:16], T.nz[me32, 15:112:16], T.fb[me32, FW - 4 * E + 2:FW - 4:4], op.mult)
-    on(V, x_cu)
-    on(V, x_pp, E - 2)
-    on(V, x_zw, 2)
-    on(V, x_h1)
-    on(V, x_im)
-    tt(T.kh[:, :], T.kc[:, 48:56].indirect(cu("offn")), T.erow[:, 128:160], op.is_equal, sig="step")
+    tt(T.nz[me32, 31:112:16], T.nz[me32, 31:112:16], T.fb[me32, FW - 4 * E + 6:FW - 4:4], op.mult, sig="step")
     rest()
-    vw()
     pw()
     tt(T.km[:, 0:32], T.nz[:, :].indirect(cu("offz")), T.kh[:, :], op.mult, sig="step")
+    on(V, "prune", E - 1)
+    on(V, x_pp, E - 2)
+    on(V, x_hz)
+    ts(T.hz[me32, 1:32:8], T.erow[me32, 128:160:8], T.kc[me32, 56:57], op.is_equal, T.fb[me32, FW - 4 * E + 2:FW - 4 * E + 3], op.mult, sig="step")
     rest()
     pw()
-    scan(T.km[:, 32:64], r8, T.km[:, 0:32], op.mult, op.add, sig="step")
+    x_k1 = scan(T.km[:, 32:64], T.hz[:, :], T.km[:, 0:32], op.mult, op.add, sig=new())
     rest()
-    on(V, x_du, 4)
-    pw()
+    on(V, x_du, 3)
+    on(V, x_k1)
+    on(S, x_du, 3)
     k1 = T.km[:, 39:64:8]
-    x_zr, x_dz, x_dm = new(), new(), new()
-
-    def bound(k):
-        ts(T.kd[blk[k], 0:1], T.km[me32, 39 + 8 * k:40 + 8 * k], fc("kn", me32), op.add, T.dumpc[me32, k:k + 1], op.max)
-    ts(T.kl0[:, :], k1, fc("knb"), op.add, float(SH), op.add, sig="step")
-    ts(T.dm[:, 0:4], k1, 32.0 * DL, op.mult, fc("pm8"), op.add, sig=x_dm)
-    pw()
-    tt(T.zrow[:, :], T.zw[:, :].indirect(T.kl0[:, 0:4]), T.im64[:, :], op.add, sig=x_zr)
-    bound(0)
-    for q_ in (S, V):
-        on(q_, x_dm)
-        on(q_, x_zr)
+    x_dz = new()
+    on(S, x_k1)
     for k in range(KP):
-        o = T.dz[blk[k], :]
-        if k < 2:
-            ts(o, T.zrow[me32, :], DL, op.mult, T.dm[me32, k:k + 1], op.subtract, sig="step")
-        else:
-            lin(o, T.zrow[me32, :], T.dm[me32, k:k + 1], -DL, sig=x_dz)
-    bound(1)
+        ts(T.kl0[blk[k], :], T.km[me32, 39:64:8], fc("knb", me32), op.add, float(SH), op.add, sig="step")
+        lin(T.kd[blk[k], 0:1], T.km[me32, 39 + 8 * k:40 + 8 * k], fc("kn", me32), sig=x_dz)
     pw()
-    on(V, x_dz, 2)
-    v(V.tensor_reduce(T.dm[:, 4:5], T.dz[:, :], X, op.min, apply_absolute_value=True), "step")
-    bound(2)
-    bound(3)
-    vw(2)
+    on(V, x_dz, KP)
+    ts(T.dz[:, 0:64], T.zw[:, :].indirect(T.kl0[:, 0:4]), T.kd[:, 0:1], op.is_equal, sig="step")
+    on(V, x_bit)
+    pw()
+    scan(T.dm[:, :], T.two[:, :], T.dz[:, :], op.mult, op.add, sig="step")
     pw()
     x_km, x_kt = new(), new()
     for k in range(KP):
-        if k >= 2:
-            vw(3 - k)
-        ts(T.kk[me32, 40 + k:41 + k], T.dm[blk[k], 4:5], T.dumpc[blk[k], k:k + 1], op.max, T.kd[blk[k], 0:1], op.min, sig=x_km)
+        ts(T.kk[me32, 40 + k:41 + k], T.dm[blk[k], 64:65], T.kd[blk[k], 0:1], op.min, T.dumpc[blk[k], k:k + 1], op.max, sig=x_km)
     on(g, x_km, KP)
     tell(kmsg, lambda q: T.kk[:, 28 - 4 * r:32 - 4 * r], "kept")
 
     x_y, x_ysb, x_yo, x_st, x_oy, x_oyd, x_kf, x_wq = new(), new(), new(), new(), new(), new(), new(), new()
+    x_kh = act(T.kh[me32, 0:32:8], T.hz[me32, 1:32:8], sig=new())
+    sw()
+    lin(fc("q4"), fc("t1"), fc("q3"), fc("q2"))
     act(T.ky[:, 32:40], zeros(8), sig=x_kz)
     lin(fc("c7"), fc("pm"), -128.0, sig=x_kz)
     act(T.kf[:, :], zeros(32), sig=x_kf)
     lin(fc("g16"), gs0, NR * A - S0 / 16, 1.0 / 64)
     on(S, x_im)
     sw()
+    lin(ct("tl", 0, 1), fc("q4"), 7.0, sig=x_c3)
     lin(T.vald[:, :], T.im64[:, :], fc("g16"), -1.0, sig=x_vald)
     on(V, x_d8)
+    on(V, x_kh)
     tt(T.km[:, 0:32], T.fb[:, :].indirect(cu("offf")), T.kh[:, :], op.mult, sig="step")
     on(V, x_w, 16)
     quant("wq", 0, 128, T.wt[:, :], x_wq)
@@ -727,6 +734,8 @@ def rank_program(g, core, T, topo):
     ts(T.ofy[:, :], T.ky[:, 7:39:4], 256.0, op.mult, fc("c7"), op.add, sig=x_oy)
     on(V, x_kf)
     ts(T.kf[:, 0:4], k1, fc("knb"), op.add, -1.0, op.max)
+    on(V, x_c3, 3)
+    cp(T.cu[:, N2:NT], T.ct[:, N2:NT])
     rest(3)
     vw()
     v(V.transpose(T.kt[me32, :], T.kf[me32, :]), x_kt)
@@ -775,10 +784,14 @@ def rank_program(g, core, T, topo):
     v(V.transpose(T.ttc[:, 0:256], T.cl[:, c0:c0 + 256]), "step")
     v(V.transpose(T.ttc[:, 256:544], T.cl[:, c0 - 16:c0 + 272]), "step")
     pw()
-    tt(T.mx[0:64, 0:34], T.ttc[0:64, 0:544:16], T.ttc[64:128, 0:544:16], op.max); vw()
-    tt(T.mx[0:32, 40:74], T.mx[0:32, 0:34], T.mx[32:64, 0:34], op.max); vw()
-    for k in range(4):
-        tt(T.ub[32 * k:32 * k + 32, 0:17], T.mx[0:32, 40:74:2], T.mx[0:32, 41:74:2], op.max)
+    on(S, "step", pn[0])
+    x_mx = new()
+    for j, (o, a, k) in enumerate(((lo, lo, 0), (lo, hi, 1), (blk[0], blk[1], 2), (blk[1], blk[0], 2), (blk[0], blk[3], 3), (blk[1], blk[2], 3))):
+        (cp, cp, act)[j % 3](T.mx[o, k:136:4], T.ttc[a, 0:544:16], sig=x_mx)
+    on(V, x_mx, 6)
+    on(V, x_rs)
+    for o in (lo, hi):
+        scan(T.ub[o, :], T.rs[lo, :], T.mx[lo, :], op.add, op.max)
     vw()
     x_new, x_st2, x_gp = new(), new(), new()
     x_ptl = ts(T.ptl[:, :], ub.indirect(cu("tl", 0, 1)), -1.0, op.mult, float(NR * A), op.add, sig=new())
@@ -815,4 +828,4 @@ def rank_program(g, core, T, topo):
     on(V, "v", vn[0])
     on(S, "s", sn_[0])
     for n in ROADS:
-        on(g, "l_" + n, {"cod": WAVE[0], "co2": WAVE[1], "pln": PAIR, "ptc": 2 * EV}.get(n, EV))
+        on(g, "l_" + n, {"cod": WAVE, "co2": WAVE, "ptc": 2 * EV}.get(n, EV))

from concourse.bass import DstId, RemoteDMATransfer
from concourse.mybir import dt, AluOpType, AxisListType, ActivationFunctionType

NR, P, A, C, E, KP, LC = 8, 256, 16, 16, 8, 4, 48
WOWN = (NR - 1) * LC
SH = 16
ZW = NR * P + SH
DL = 2.0 ** 17
DUMP = 7 * 4096
SHB = DUMP + KP * A
CLW = KP * A + NR * P + 16
RQ = 3 * (P - 2)
S0 = P * (NR - 1)
FW = 48
RO = NR * A + 1
PW = NR * A + P + 8
NQ = 12
TINY = 2.0 ** -90
HI = 2048.0
MARK = 0.125
WHOLE = 3 * 2 ** 22
BITS = 0x7C03
WAVES = (slice(0, 4), slice(4, 7))

TAB, NT = {}, 0
for _n, _k in (("offp", 8), ("offs", 8), ("offg", 8), ("offj", 16), ("ofs", 2),
               ("offz", 2), ("offn", 2), ("offf", 2), ("psel", 2), ("tl", 2)):
    TAB[_n] = (NT, _k)
    NT += _k
N1, N2 = TAB["offz"][0], TAB["psel"][0]

F, B, I, U = "float32", "bfloat16", "int32", "uint16"
SB = {
    "cdi": (16, I), "offl": (16, U), "ones": (48, B), "pra": (3 * (S0 + NR * P), B), "prb": (3 * (S0 + NR * P), B), "ow": (16, F),
    "cnt": (3 * P + 32, B), "ind": (2 * P, B), "junk": (P, B), "req": (3 * P, B), "rland": (32, B), "rt1": (64, B), "rt2": (64, B),
    "reql": (32, U), "rj": (32, F), "ct": (NT, F), "cu": (NT, U), "ic": (24, I),
    "jwb": (2, B), "dumpc": (4, F), "im64": (64, F), "r8": (32, F), "ofy": (8, U), "oy": (8, U),
    "cf": (32, F), "m16": (128, B), "m4": (128, B), "m4a": (32, B), "ltr": (16, F), "tg": (32, B), "ohs": (32, B),
    "r16": (256, B), "zw": (ZW, F), "vald": (64, B), "erow": (192, F), "hz": (32, F),
    "lf": (32, F), "lt": (32, F), "thr": (128, B), "rel": (256, F), "mn": (128, B),
    "offw": (16, U), "lw": (256, F), "lall": (128, F), "la": (128, F), "lb": (128, F), "offc": (16, U), "offh": (8, U), "sall": (WOWN + P, F),
    "sm": (128, F), "sz": (256, F), "df": (128, B), "cm": (128, B), "rk": (256, B), "oh": (128, B), "dec": (128, B), "p16": (32, B),
    "lz": (128, B), "offr": (8, U), "ss": (32, F), "ssz": (32, F), "nm": (128, F), "nz": (128, F), "gb": (224, B),
    "gs": (704, B), "fb": (64, F), "ub": (136, B), "bo": (8, F), "kh": (32, F), "km": (64, F), "ky": (64, F),
    "kf": (32, F), "kt": (32, F), "kd": (16, F), "kl0": (4, U), "two": (65, F), "dz": (65, F), "dm": (65, F), "bit": (16, F),
    "kk": (48, U), "kc": (136, F), "okl": (16, U), "ysb": (144, F), "yo": (64, F), "mx": (136, B), "rs": (136, B),
    "xz": (512, B), "wt": (512, B), "tt": (1024, B), "eb": (520, B), "cl": (CLW, B), "ttc": (544, B),
    "ptd": (4 * PW, F), "tbd": (2 * P, B), "gp": (2 * P, F), "ptl": (16, U), "bb": (1024, B),
}
CODES = {"p1": 128, "p8": 128, "wq": 128, "tq": 256, "win": 592, "tn": 256, "snd": 336, "cand": 256, "pk": 160, "eq": 512, "pt": 128}
FCOL = {n: i for i, n in enumerate(["pm", "p31", "p7", "p7j", "t1", "u2", "pm8", "isr", "hneg", "kap", "c7", "g16", "dmp",
                                    "sb1", "ac1", "nbase", "c6", "kn", "knb", "o32", "q1", "q2", "q3", "q4", "q5", "q6", "q7",
                                    "q8", "rot", "q9", "g2", "u1"])}

SCRATCH = {n: ("sbuf", [128, k], d) for n, (k, d) in SB.items()}
SCRATCH["fc"] = ("sbuf", [128, len(FCOL)], F)
for _n, _k in CODES.items():
    SCRATCH[_n] = ("sbuf", [128, _k], "float8_e4m3fn_x4")
    SCRATCH[_n + "s"] = ("sbuf", [128, _k], "uint8")
SCRATCH["ps"] = ("psum", [128, 4096], F)

ROADS = ["ptc", "pts", "req", "cod", "co2", "kept"]
XS = ["x%d" % i for i in range(132)]
SEMAPHORES = ["v", "s", "step", "scat", "claim", "prune"] + ["r_" + n for n in ROADS] + ["l_" + n for n in ROADS] + XS


def rank_program(g, core, T, topo):
    r = T.rank_of(core)
    if r is None:
        return
    V, S, Q, M = g.vector, g.scalar, g.sync, g.tensor
    op, X, fn = AluOpType, AxisListType.X, ActivationFunctionType
    home = [m for m in range(1, NR) if topo.die(T.cores[r ^ m]) == topo.die(core)]
    away = [m for m in range(1, NR) if m not in home]
    ORDER = [m for pair in zip(home, away) for m in pair] + away[len(home):]
    others = [r ^ m for m in ORDER]
    u8, u32 = dt.uint8, dt.uint32

    free = list(XS)
    vn, sn_, pn = [0], [0], [0]

    def new():
        return free.pop(0)

    def v(inst, sig=None):
        inst.then_inc(T.sem[sig or "v"], 1)
        if sig is None:
            vn[0] += 1
        if sig == "step":
            pn[0] += 1
        return sig

    def vw(skip=0):
        V.wait_ge(T.sem["v"], vn[0] - skip)

    def pw():
        V.wait_ge(T.sem["step"], pn[0])

    def s(inst, sig=None):
        inst.then_inc(T.sem[sig or "s"], 1)
        if sig is None:
            sn_[0] += 1
        return sig

    def sw():
        S.wait_ge(T.sem["s"], sn_[0])

    def on(q, sig, n=1):
        q.wait_ge(T.sem[sig], n)

    def fc(n, at=slice(0, 128)):
        return T.fc[at, FCOL[n]:FCOL[n] + 1]

    def ct(n, a=0, b=None):
        return T.ct[:, TAB[n][0] + a:TAB[n][0] + (TAB[n][1] if b is None else b)]

    def cu(n, a=0, b=None):
        return T.cu[:, TAB[n][0] + a:TAB[n][0] + (TAB[n][1] if b is None else b)]

    def ts(o, a, s1, op0, s2=None, op1=None, sig=None):
        if op1 is None:
            return v(V.tensor_scalar(o, a, s1, None, op0), sig)
        return v(V.tensor_scalar(o, a, s1, s2, op0, op1), sig)

    def tt(o, a, b, o_, sig=None):
        return v(V.tensor_tensor(o, a, b, o_), sig)

    def cp(o, a, sig=None):
        return v(V.tensor_copy(o, a), sig)

    def fill(o, c, sig=None):
        return v(V.memset(o, c), sig)

    def scan(o, a, b, o0, o1, sig=None, init=0.0):
        return v(V.tensor_tensor_scan(o, a, b, init, o0, o1), sig)

    def sums(o, a, sig=None):
        return scan(o, T.r16[:, 0:o.shape[1]], a, op.mult, op.add, sig)

    def act(o, a, sig=None):
        return s(S.activation(o, a, fn.Copy), sig)

    def lin(o, a, bias, scale=1.0, sig=None, f=fn.Identity):
        return s(S.activation(o, a, f, bias=bias, scale=scale), sig)

    def pick_v(o, src, off, sig):
        V.tensor_copy(o.bitcast(u32), src.bitcast(u32).indirect(off)).then_inc(T.sem[sig], 1)

    def pick_s(o, src, off, sig):
        S.activation(o, src.indirect(off), fn.Copy).then_inc(T.sem[sig], 1)

    def quant(o, a, b, src, sig):
        v(V.quantize_mx(T[o][:, a:b], T[o + "s"][:, a:b], src), sig)

    def iota(o, pat, base, cm, sig):
        g.iota(o, pat, base, cm, allow_small_or_imprecise_dtypes=True).then_inc(T.sem[sig], 1)

    def const(o, c, sig):
        iota(o, [[0, o.shape[1]]], c, 0, sig)

    def load(q, o, a, sig):
        q.dma_start(o, a).then_inc(T.sem[sig], 16)

    def shares(dests, parts):
        return {q: sum(1 << e for e in topo.engines(core, T.cores[q])[k::n]) for q, (k, n) in zip(dests, parts)}

    def send(src, dst, road, mk):
        tr = []
        for q in mk:
            rid, pid = topo.addr(T.cores[q])[:2]
            tr.append(RemoteDMATransfer(dst_ids=[DstId(rid=rid, pnc=pid)], dma_engine_mask=mk[q], remote_sem=T.sem["r_" + road], src=src(q), dst=dst(q)))
        g.remote_dma_fused(tr, local_sem=T.sem["l_" + road])

    every = topo.mask(core, T.cores[others[0]])
    for q in others:
        every &= topo.mask(core, T.cores[q])
    EV = bin(every).count("1")

    def tell(src, dst, road, dests=others):
        ids = [DstId(rid=topo.addr(T.cores[q])[0], pnc=topo.addr(T.cores[q])[1]) for q in dests]
        g.remote_dma_fused([RemoteDMATransfer(dst_ids=ids, dma_engine_mask=every, remote_sem=T.sem["r_" + road], srcs=[src],
                                              dsts=[dst(q) for q in dests])], local_sem=T.sem["l_" + road])

    def points(near):
        tell(T.p1[:, 0:A].bitcast(u8), lambda q: T.pt[:, A * r:A * r + A].bitcast(u8), "ptc",
             [q for q in others if (topo.die(T.cores[q]) == topo.die(core)) == near])

    WAVE = 2 * EV
    TOLD = EV * len(others)

    def seat(a, b):
        return ORDER.index(a ^ b)

    def spot(q):
        return LC * seat(q, r)

    row16, jm, r8 = T.rj[:, 0:16], T.rj[:, 16:32], T.r16[:, 0:64:2]
    kland, kmsg = T.kk[:, 0:32], T.kk[:, 40:44]
    klf, ub = T.kc[:, 0:32], T.ub[:, :]
    gs0, p7 = T.bo[:, 0:1], T.fc[:, 2:4]
    odd = r % 2
    me32 = slice(32 * (r // 2), 32 * (r // 2) + 32)
    lo, hi = slice(0, 64), slice(64, 128)
    blk = [slice(32 * k, 32 * k + 32) for k in range(4)]
    pres = (T.pra, T.prb)

    def zeros(n):
        return T.xz[:, 64:64 + n]

    x_cd, x_x, x_tb, x_w = new(), new(), new(), new()
    for k in range(8):
        load(Q if k < 4 else S, T.cdi[16 * k:16 * k + 16, :], T.cd[:, :], x_cd)
    load(Q, T.xz[:, 0:64], T.x[:, :], x_x)
    load(Q, T.tt[:, :], T.tb[:, :], x_tb)

    x_pi, x_pj2, x_io1, x_io2, x_ebd, x_b6, x_jm, x_pr = [new() for k in range(8)]
    g.iota(T.ic[:, 0:4], [[1, 4]], 64 * 127, -64).then_inc(T.sem[x_pi], 1)

    def place(w, k):
        return pres[w][:, 3 * S0 + k:3 * S0 + 3 * P:3]
    for a, b, m in ((4, 5, 2048), (5, 6, 1024), (6, 8, 4096), (8, 9, 16384)):
        g.iota(T.ic[:, a:b], [[0, b - a]], 0, m).then_inc(T.sem[x_pj2], 1)
    const(place(1, 2), -WHOLE, x_pr)
    iota(jm, [[1, 16]], 0, 0, x_jm)
    iota(row16, [[16, 16]], 0, 0, x_io1)

    x_m, x_zz, x_hn, x_gs, x_p1, x_pm = new(), new(), new(), new(), new(), new()
    fill(T.xz[:, 64:512], 0.0, sig=x_zz)
    on(V, x_pi)
    ts(T.ic[:, 12:16], T.ic[:, 0:4], BITS, op.bitwise_and)
    fill(place(0, 0), 0.5 - MARK / 2, sig="step")
    vw()
    cp(T.bo[:, 0:2], T.ic[:, 12:14], sig=x_gs)
    fill(place(0, 1), 0.0, sig="step")
    on(V, x_pj2, 4)
    ts(T.ic[:, 16:21], T.ic[:, 4:9], BITS, op.bitwise_and)
    on(V, x_gs)
    x_is = ts(fc("isr"), gs0, float(4 * S0 - 4 * P * r), op.is_equal, MARK, op.mult, sig=new())
    ts(fc("g2"), gs0, -0.25, op.mult)
    fill(place(0, 2), float(WHOLE), sig="step")
    vw()
    ts(T.bo[:, 4:6], T.bo[:, 0:2], fc("g2"), op.add, sig=x_b6)
    ts(T.fc[:, 0:5], T.ic[:, 16:21], 1.0 / 2048, op.mult, sig=x_pm)

    x_cz, x_dd, x_c1, x_c2 = new(), new(), new(), new()
    x_r16b, x_r8, x_lz, x_h1, x_lf, x_rt = new(), new(), new(), new(), new(), new()
    on(S, x_zz)
    lin(T.ones[:, 0:16], zeros(16), 0.5 + MARK / 2, sig=x_pr)
    lin(T.ones[:, 16:48], zeros(32), MARK, sig=x_pr)
    act(place(1, 0), zeros(P), sig=x_pr)
    on(S, x_is)
    lin(place(1, 1), zeros(P), fc("isr"), sig=x_pr)
    lin(fc("hneg"), gs0, 18.0 - 3 * S0, 0.75, sig=x_hn)
    act(T.lall[:, :], zeros(128), sig=x_lz)
    on(S, x_pm)
    lin(fc("q6"), fc("pm"), 0.0, -1.0)
    on(S, x_jm)
    act(ct("offj"), jm, sig=x_c1)
    on(S, x_io1)
    sw()
    lin(fc("q5"), fc("p31"), fc("q6"), 2.0)
    lin(T.jwb[:, :], T.rj[:, 0:4:2], fc("pm"), sig=x_dd)
    lin(fc("sb1"), fc("pm"), 16.5)
    lin(fc("u1"), fc("p7"), 0.0, 8.0 - 1.0 / 16)
    lin(ct("offp"), zeros(8), fc("pm"), sig=x_c1)
    lin(fc("q3"), fc("p31"), 0.0, 4.0)
    lin(fc("q7"), fc("pm"), 66.0, 128.0)
    lin(T.cf[:, 0:16], jm, fc("pm"), -1.0, f=fn.Abs)
    lin(fc("q8"), fc("p7"), 143.0, 16.0)
    lin(fc("rot", lo), fc("pm", lo), 15.0, 16.0)
    sw()
    lin(fc("u2"), fc("pm"), fc("u1"), 1.0 / 8)
    for k in range(4):
        a, b = [LC * (seat(h, r) if h != r else NR - 1) for h in (2 * k, 2 * k + 1)]
        lin(fc("nbase", blk[k]), fc("q5", blk[k]), -float(a), (a - b) / 16.0)
    lin(fc("rot", hi), fc("pm", hi), fc("q8", hi), -16.0)
    lin(fc("o32"), fc("pm"), fc("q3"), -1.0)
    sw()
    lin(T.cnt[:, 0:16], zeros(16), fc("nbase"), sig=x_cz)
    lin(T.cnt[:, 3 * P + 16:3 * P + 32], zeros(16), fc("nbase"), sig=x_cz)
    for n, a, b, c in (("ofs", T.rj[:, 0:2], "o32", 1.0), ("offs", zeros(8), "rot", 1.0), ("offg", T.rj[:, 16:24], "u2", 2.0)):
        lin(ct(n), a, fc(b), c, sig=x_c1)
    on(S, x_lf)
    act(T.lf[:, 16:32], T.lf[:, 0:16], sig=x_lf)

    on(V, x_b6)
    on(V, x_cd, 128)
    for k in range(2):
        ts(T.offl[:, k:16:2], T.cdi[:, k:16:2], 3.0, op.mult, T.bo[:, 4 + k:5 + k], op.add, sig="step")
    x_p8, x_p8s, x_lt, x_k0 = new(), new(), new(), new()
    on(V, x_x, 16)
    on(V, x_zz)
    quant("p1", 0, 128, T.xz[:, :], x_p1)
    pw()
    on(V, x_pr, 5)
    for i in range(8):
        if i > 1:
            on(V, "scat", i - 1)
        v(V.tensor_copy(pres[i % 2][:, :].indirect(T.offl[:, 2 * i:2 * i + 2]), T.ones[:, 16 * (i % 2):16 * (i % 2) + 32]), "scat")
    ts(T.lf[:, 0:16], T.cdi[:, :], float(SHB), op.add, TINY, op.mult, sig=x_lf)
    on(V, x_hn)
    ts(T.ow[:, :], T.cdi[:, :], 3.0, op.mult, fc("hneg"), op.add)
    on(V, "scat", 8)
    x_cnt = scan(T.cnt[:, 16:3 * P + 16], pres[0][:, 3 * S0:3 * S0 + 3 * P], pres[1][:, 3 * S0:3 * S0 + 3 * P], op.add, op.add, sig=new())
    cnt = T.cnt[:, 18:3 * P + 13:3]
    vw()
    x_ow = ts(T.offw[:, :], T.ow[:, :], 3 * P + 16.0, op.min, sig=new())

    x_m16, x_acc, x_cl, x_op, x_rn, x_th, x_req, x_lv, x_h2, x_m4a = [new() for k in range(10)]
    on(S, x_cnt)
    s(S.activation(T.junk[:, 0:P - 1], cnt, fn.Sign, bias=fc("sb1"), scale=-1.0, accum_out=fc("ac1")), x_acc)
    lin(T.p16[:, 16:32], T.cf[:, 0:16], 1.0, -1.0, sig=x_m, f=fn.Relu)
    on(S, x_acc)
    lin(T.req[:, RQ + 1:RQ + 2], fc("ac1"), (P - 1) * 0.5, 0.5, sig=x_req)
    on(S, x_cz, 2)
    on(S, x_ow)
    lin(T.lw[:, :], T.cnt[:, :].indirect(T.offw[:, :]), fc("nbase"), -1.0, sig=x_lv)
    lin(T.cf[:, 16:32], jm, fc("q7"), -128.0, f=fn.Relu)

    def rows(q, a, b):
        for j in range(a, b):
            k, at = j // 2, me32.start + 16 * (j % 2)
            load(q, T.lall[at:at + 16, 16 * k:16 * k + 16], T.lw[16 * k:16 * k + 1, :], x_h2)
    on(S, x_lz)
    on(S, x_lv)
    rows(S, NQ, 16)
    sw()
    lin(T.m4a[:, 0:16], T.cf[:, 16:32], 2.0, -1.0, sig=x_m4a)

    on(V, x_cnt)
    on(V, x_dd)
    x_i = new()
    for k in range(2):
        ts(T.ind[:, P * k + 32 * k:P * k + P - 1], cnt[:, 32 * k:P - 1], T.jwb[:, k:k + 1], op.is_le, sig=x_i)
    for k in range(2):
        on(V, x_i, k + 1)
        a = T.ind[:, P * k + 32 * k:P * k + P - 1]
        scan(T.req[:, 98 * k:RQ + 3:3], a, a, op.add, op.max, sig=x_req, init=32.0 * k)

    def halves(k):
        g.affine_select(T.eb[:, 258 * k:258 * k + 258], zeros(258), [[1, 258]], op.not_equal, 0.5, 258 * k - 3, -4).then_inc(T.sem[x_ebd], 1)
    on(g, x_p1)
    points(True)
    on(g, x_zz)
    halves(0)
    halves(1)
    on(g, x_req, 3)
    tell(T.req[:, RQ:RQ + 3], lambda q: T.rland[:, 3 * seat(q, r):3 * seat(q, r) + 3], "req")
    const(T.rt1[:, 0:16], 0, x_rt)
    const(T.rt1[:, 48:64], 0, x_rt)
    g.affine_select(T.r16[:, :], zeros(P), [[0, 16], [1, 16]], op.is_equal, 1.0, 0, 0).then_inc(T.sem[x_r16b], 1)
    x_two = new()
    const(T.dm[:, 0:64], 2, x_two)
    const(T.two[:, 64:65], -int(DL), x_two)
    on(g, x_two, 2)
    g.affine_select(T.two[:, 0:64], T.dm[:, 0:64], [[0, 4], [1, 16]], op.not_equal, 2.0 ** -15, 0, 0).then_inc(T.sem[x_two], 1)

    x_tq, x_wino, x_rl, x_ptown, x_rz = new(), new(), new(), new(), new()
    x_zw, x_im, x_vald, x_pj, x_m4, x_eq = new(), new(), new(), new(), new(), [new(), new()]
    on(V, x_lf, 2)
    v(V.transpose(T.lt[:, :], T.lf[:, :]), x_lt)
    on(V, x_c1, 5)
    cp(T.cu[:, 0:N1], T.ct[:, 0:N1], sig=x_op)
    fill(T.kk[:, :], 0, sig=x_k0)
    on(V, x_tb, 16)
    quant("tq", 0, P, T.tt[:, :], x_tq)
    on(V, x_ebd, 2)
    for b in range(4):
        quant("eq", 128 * b, 128 * b + 128, T.eb[:, 3 - b:515 - b], x_eq[b // 2])
    on(V, x_op)
    on(V, x_k0)
    on(V, x_rz, 16)
    on(V, "r_req", TOLD)
    for k in range(4):
        v(V.transpose(T.rt1[32 * k:32 * k + 32, 16:48], T.rland[me32, :]), "step")
    on(V, x_rt, 2)
    pw()
    for k in range(2):
        a = 16 * (odd + 1 - k)
        v(V.transpose(T.rt2[:, 32 * k:32 * k + 32], T.rt1[:, a:a + 32]), "step")
    pw()
    cp(T.reql[:, :], T.rt2[:, :].indirect(cu("ofs")), sig=x_rl)

    x_ut = [new() for b in range(4)]
    on(M, x_tq)
    for b in range(4):
        e = slice(128 * b, 128 * b + 128)
        on(M, x_eq[b // 2], 2)
        M.matmul_mx(T.ps[:, 2048 + 512 * b:2048 + 512 * b + P], T.eq[:, e], T.eqs[:, e], T.tq[:, :], T.tqs[:, :], True, True).then_inc(T.sem[x_ut[b]], 1)

    on(Q, x_zz)
    load(Q, T.rland[:, 21:32], zeros(11), x_rz)
    on(Q, x_lv)
    on(Q, x_lz)
    rows(Q, 0, NQ)
    on(Q, x_tq)
    load(Q, T.win[:, WOWN:WOWN + P].bitcast(u8), T.tq[:, :].bitcast(u8), x_wino)
    load(Q, T.wins[:, WOWN:WOWN + P], T.tqs[:, :], x_wino)
    on(Q, "l_co2", WAVE)
    on(Q, x_p1)
    load(Q, T.pt[:, A * r:A * r + A].bitcast(u8), T.p1[:, 0:A].bitcast(u8), x_ptown)
    load(Q, T.pts[:, A * r:A * r + A], T.p1s[:, 0:A], x_ptown)
    load(Q, T.wt[:, :], T.w[:, :], x_w)
    x_d8, x_kz = new(), new()
    on(S, x_op)
    on(S, x_p1)
    on(S, x_lt)
    act(T.ltr[lo, :], T.lt[lo, 0:16])
    act(T.ltr[hi, :], T.lt[hi, 8:24])
    pick_s(T.p8s[:, :], T.p1s[:, :], cu("offp"), x_p8s)
    sw()

    def bounds(a):
        for u in range(a, a + 4):
            lin(T.thr[:, 16 * u:16 * u + 16], T.ltr[:, :], T.ltr[:, u:u + 1], -1.0, sig=x_th)
    bounds(0)

    for q_ in (V, S):
        on(q_, x_tq)
        on(q_, x_rl)

    def codes(road, mk):
        send(lambda q: T.snd[:, LC * seat(r, q):LC * seat(r, q) + LC].bitcast(u8), lambda q: T.win[:, spot(q):spot(q) + LC].bitcast(u8), road, mk)

    def planes(road, mk):
        send(lambda q: T.snds[:, LC * seat(r, q):LC * seat(r, q) + LC], lambda q: T.wins[:, spot(q):spot(q) + LC], road, mk)
    x_sndc, x_snds = new(), new()
    for w in range(2):
        c, d = WAVES[w].start, WAVES[w].stop
        pick_v(T.snd[:, LC * c:LC * d], T.tq[:, :], T.reql[:, 3 * c:3 * d], x_sndc)
        pick_s(T.snds[:, LC * c:LC * d], T.tqs[:, :], T.reql[:, 3 * c:3 * d], x_snds)
    on(g, x_sndc)
    codes("cod", shares(others[0:4], ((0, 4), (1, 4), (2, 4), (3, 4))))
    on(g, x_snds)
    planes("cod", shares(others[0:4], ((0, 4), (1, 4), (2, 4), (3, 4))))
    on(g, x_snds, 2)
    planes("co2", shares(others[4:7], ((0, 4), (2, 4), (1, 2))))
    on(g, x_sndc, 2)
    codes("co2", shares(others[4:7], ((0, 2), (1, 4), (3, 4))))
    x_fb = new()
    c0 = KP * A + P * r
    iota(T.erow[:, 0:128], [[-1, 8], [0, 16]], E - 1, 0, x_io2)
    const(T.fb[:, :], 1, x_fb)
    const(T.gs[:, 7:704:8], 0, x_r8)
    iota(T.m4a[:, 16:18], [[-1, 2]], 1, 0, x_r8)
    const(T.gb[:, 208:210], 0, x_r8)
    const(T.kc[:, 36:64], 0, x_h1)
    x_e2 = new()
    iota(T.erow[:, 128:160], [[-1, 4], [-1, 8]], E - 1, 0, x_e2)
    iota(T.im64[:, :], [[0, 4], [1, 16]], 0, 0, x_im)
    x_hz = new()
    g.affine_select(T.hz[:, :], zeros(32), [[0, 4], [-1, 8]], op.is_gt, 1.0, 2, 0).then_inc(T.sem[x_hz], 1)
    on(g, x_e2)
    g.affine_select(T.erow[:, 160:192], T.erow[:, 128:160], [[0, 4], [1, 8]], op.not_equal, 0.0, 0, 0).then_inc(T.sem[x_zw], 1)
    iota(T.zw[:, :], [[1, ZW]], SHB - SH, 0, x_zw)
    points(False)
    tell(T.p1s[:, 0:A], lambda q: T.pts[:, A * r:A * r + A], "pts")
    x_rs = new()
    g.affine_select(T.rs[:, :], zeros(136), [[0, 17], [1, 8]], op.not_equal, -1024.0, 0, 0).then_inc(T.sem[x_rs], 1)
    iota(T.cl[:, c0 - 16:c0 + 272], [[-1, 288]], 15, 0, x_cl)

    x_un, x_rest = [new(), new()], new()
    done = [0, 0]

    def rest(n=1):
        b, a = divmod(64 * done[0], P)
        if a == 0:
            on(V, x_ut[b])
        done[0] += n
        done[1] += 1
        tt(T.ptd[:, PW * b + RO + a:PW * b + RO + a + 64 * n], T.tt[:, 4 * a + b:4 * a + 256 * n:4], T.ps[:, 2048 + 512 * b + a:2048 + 512 * b + a + 64 * n],
           op.subtract, sig=x_rest)
    x_dec, x_mn, x_td, x_la = new(), new(), new(), new()
    on(S, x_h2, 256)
    pick_s(T.la[:, :], T.lall[:, :], cu("offg"), x_la)
    x_s, x_sa, x_oh = [new(), new(), new()], new(), new()
    on(M, x_p8)
    on(M, x_p8s)
    M.matmul_mx(T.ps[:, 1024:1024 + P], T.p8[:, :], T.p8s[:, :], T.tq[:, :], T.tqs[:, :], True, True).then_inc(T.sem[x_s[2]], 1)
    on(S, x_m)
    pick_s(T.m16[:, :], T.p16[:, 16:32], cu("offp", 0, 8), x_m16)
    lin(fc("q9"), gs0, odd - 1.0, 1.0 / (4 * P))
    x_own, x_bit = new(), new()
    on(S, x_s[2])
    act(T.sall[:, WOWN:WOWN + P], T.ps[:, 1024:1024 + P], sig=x_sa)
    on(V, x_p1)
    pick_v(T.p8[:, :], T.p1[:, :], cu("offp"), x_p8)
    side = slice(128 - 112 * odd, 144 - 112 * odd)
    pick_v(T.pk[:, side], T.tq[:, :], cu("offp", 0, 1), x_pj)
    pick_s(T.pks[:, side], T.tqs[:, :], cu("offp", 0, 1), x_pj)
    on(V, x_r16b)
    on(V, x_la)
    scan(T.lb[:, :], T.r16[:, 0:256:2], T.la[:, :], op.mult, op.add, sig="step")
    rest(2)
    pw()
    x_offc = new()
    for k in range(4):
        ts(T.offc[32 * k:32 * k + 32, :], T.lb[me32, 7:128:8], -1.0, op.mult, -1.0, op.add, sig=x_offc)
    rest(2)
    on(V, x_offc, 4)
    cp(T.offh[lo, :], T.offc[lo, 0:8], sig=x_oh)
    cp(T.offh[hi, :], T.offc[hi, 8:16], sig=x_oh)
    on(V, x_two, 3)
    on(V, x_m)
    scan(T.bit[:, :], T.two[:, 0:16], T.p16[:, 16:32], op.mult, op.add, sig=x_own)
    on(V, x_m16)

    x_cc, x_cs = new(), new()
    bounds(4)
    for w in range(2):
        on(M, "r_" + ("cod", "co2")[w], WAVE)
        a = slice(LC * WAVES[w].start, LC * WAVES[w].stop)
        M.matmul_mx(T.ps[:, 512 * w:512 * w + a.stop - a.start], T.p8[:, :], T.p8s[:, :], T.win[:, a], T.wins[:, a], True, True).then_inc(T.sem[x_s[w]], 1)
        on((V, S)[w], x_s[w])
        if w == 0:
            cp(T.sall[:, a], T.ps[:, 0:a.stop], sig=x_sa)
        else:
            act(T.sall[:, a], T.ps[:, 512:512 + a.stop - a.start], sig=x_sa)
    on(S, x_s[0])
    on(S, x_offc, 4)
    on(S, x_wino, 32)
    pick_s(T.cands[:, :], T.wins[:, :], T.offc[:, :], x_cs)
    on(V, "r_co2", WAVE)
    on(V, x_wino, 32)
    pick_v(T.cand[:, :], T.win[:, :], T.offc[:, :], x_cc)
    x_sz, x_u3, x_du, x_tg = new(), new(), new(), new()
    sw()
    on(V, x_sa, 3)
    on(V, x_oh, 2)
    tt(T.sm[:, :], T.sall[:, :].indirect(T.offh[:, :]), T.m16[:, :], op.mult, sig="step")
    ts(T.dec[:, :], T.r16[:, 0:128], 4.0 - 1.0 / 32, op.mult, -4.0, op.add, sig=x_dec)
    pw()
    sums(T.sz[:, 0:128], T.sm[:, :], sig="step")
    pw()
    on(S, "step", pn[0])
    cp(T.sz[hi, 143:256:16], T.sz[lo, 15:128:16], sig=x_sz)
    act(T.sz[lo, 143:256:16], T.sz[hi, 15:128:16], sig=x_sz)
    x_d, x_d2, x_cm = new(), new(), new()
    for q_ in (V, S):
        on(q_, x_sz, 2)
    for u in range(8):
        o, su = T.df[:, 16 * u:16 * u + 16], T.sz[:, 16 * u + 15:16 * u + 16]
        if u < 5:
            ts(o, T.sz[:, 15:256:16], su, op.subtract, -1.0, op.mult, sig=x_d)
        else:
            lin(o, T.sz[:, 15:256:16], su, -1.0, sig=x_d2)
    on(V, x_th, 8)
    for h in range(2):
        a = slice(64 * h, 64 * h + 64)
        on(V, x_d, h + 4)
        if h:
            on(V, x_d2, 3)
        tt(T.cm[:, a], T.df[:, a], T.thr[:, a], op.is_lt, sig=x_cm)
    on(V, x_cm, 2)
    sums(T.rk[:, 0:128], T.cm[:, :], sig="step")
    for a, b in ((lo, hi), (hi, lo)):
        scan(T.rk[b, 128:256], T.r16[a, 0:128], T.cm[a, :], op.mult, op.add, sig="step")
    lin(fc("c6"), fc("pm"), -272.0, sig=x_u3)
    lin(fc("kap"), fc("pm"), -31.0, 2.0, sig=x_u3)
    on(S, x_io2)
    lin(T.tg[:, :], T.erow[:, 96:128], fc("q9"), sig=x_tg)
    on(S, x_m4a)
    pick_s(T.m4[:, :], T.m4a[:, 0:16], cu("offp", 0, 8), x_m4)
    pick_s(T.rel[:, :], T.lt[:, 0:16], cu("offj"), x_rn)
    on(S, x_fb)
    act(T.fb[:, FW - 3:FW:2], zeros(2), sig=x_r8)
    on(S, x_m4)
    lin(T.mn[:, :], T.m4[:, 0:128], 0.0, HI, sig=x_mn)
    lin(ct("offz"), p7, 15.0, 8.0, sig=x_c2)
    lin(ct("offn"), p7, E - 1.0, -0.5, sig=x_c2)
    lin(ct("offf"), p7, FW - 4.0 * E + 2, 2.0, sig=x_c2)
    on(V, x_io2)
    pw()
    tt(T.oh[:, :], T.rk[:, :].indirect(cu("offs", 0, 8)), T.erow[:, 0:128], op.is_equal, sig="step")
    on(V, x_tg)
    x_os = tt(T.ohs[:, :], T.rk[:, :].indirect(cu("offs", 0, 2)), T.tg[:, :], op.is_equal, sig=new())
    on(V, x_u3, 2)
    on(V, x_dec)
    pw()
    scan(T.lz[:, :], T.dec[:, :], T.oh[:, :], op.add, op.max, sig="step")
    on(V, x_os)
    tt(T.ss[:, :], T.sz[:, :].indirect(cu("offs", 0, 2)), T.ohs[:, :], op.mult)
    pw()
    x_offr, x_kc, x_ks = new(), new(), new()
    best = slice(32 * odd, 32 * odd + 128)
    ts(T.offr[:, :], T.lz[:, 15:128:16], 512.0, op.mult, fc("c6"), op.add, sig=x_offr)
    vw()
    x_so = sums(T.ssz[:, :], T.ss[:, :], sig=new())
    for q_ in (V, S):
        on(q_, x_offr)
    on(V, x_cc)
    on(S, x_cs)
    pick_v(T.pk[:, best], T.cand[:, :], T.offr[:, :], x_kc)
    pick_s(T.pks[:, best], T.cands[:, :], T.offr[:, :], x_ks)
    x_g = [new(), new()]
    on(M, x_pj, 2)
    on(M, x_kc)
    on(M, x_ks)
    for t in range(2):
        a = slice(16 * (t + odd), 16 * (t + odd) + 128)
        M.matmul_mx(T.ps[:, 1024 + 512 * t:1152 + 512 * t], T.pk[:, a], T.pks[:, a], T.pk[:, best], T.pks[:, best], True, True).then_inc(T.sem[x_g[t]], 1)
    rest(2)
    x_nm, x_f1 = new(), new()
    on(S, x_rn)
    lin(T.nm[:, :], T.rel[:, :].indirect(T.offr[:, :]), 0.0, 1.0 / TINY, sig=x_nm)
    lin(fc("dmp"), fc("pm"), float(DUMP))
    lin(fc("kn"), fc("pm"), -30 * HI, 2 * HI, sig=x_du)
    lin(fc("knb"), fc("pm"), -30 * HI - SHB, 2 * HI, sig=x_du)
    on(S, x_own)
    lin(T.dz[:, 64:65], T.bit[:, 15:16], -DL / 2, 2 * DL, sig=x_bit)
    on(S, x_r16b)
    lin(T.r8[:, :], r8, -4.0, 4.0 - 1.0 / 16, sig=x_d8)
    sw()
    lin(T.dumpc[:, :], T.rj[:, 0:4], fc("dmp"), sig=x_du)

    def start(b):
        return 8 * b * (b - 1) + 32 * b

    x_pa, x_ke, x_pp = new(), new(), new()
    on(V, x_c2, 3)
    x_cu = cp(T.cu[:, N1:N2], T.ct[:, N1:N2], sig=new())
    on(V, x_so)
    for t in range(2):
        on(V, x_g[t])
        ts(T.gb[:, 96 - 96 * t:208 - 112 * t], T.ps[:, 1040 + 528 * t:1152 + 512 * t], T.ssz[:, 16 * t + 15:16 * t + 16], op.is_ge, fc("kap"), op.add, sig=x_pa)

    def part(b):
        h, t = divmod(E - 1 - b, 2)
        at, e = slice(32 * h, 32 * h + 32), 208 - 112 * t
        scan(T.gs[me32, start(b):start(b) + 16 * b], T.m4[at, 0:16 * b], T.gb[at, e - 16 * b:e], op.add, op.max, sig=x_ke)

    def order(k):
        a = slice(64 * k, 64 * k + 64)
        on(V, x_nm)
        on(V, x_mn)
        scan(T.nz[:, a], T.mn[:, a], T.nm[:, a], op.add, op.max)

    on(V, x_m4)
    on(V, x_r8, 4)
    on(V, x_pa)
    scan(T.fb[me32, FW - 39:FW - 4:2], T.m4a[96:128, 0:18], T.gb[96:128, 192:210], op.add, op.max, sig="prune")
    order(0)
    on(V, x_pa, 2)
    part(2)
    part(3)
    for b in range(2, E):
        on(V, "prune", b - 1)
        on(V, x_ke, b - 1)
        e, n = FW - 4 * b, 2 * b + 3
        scan(T.fb[me32, e - n:e], T.fb[me32, e + 1:e + 1 + 2 * n:2], T.gs[me32, start(b) + 15:start(b) + 15 + 8 * n - 7:8], op.subtract, op.max, sig="prune", init=1.0)
        if b < E - 2:
            part(b + 2)
        if b == E - 2:
            order(1)
    on(V, x_cu)
    on(V, x_pp, E - 3)
    on(V, x_zw, 2)
    on(V, x_h1)
    on(V, x_im)
    tt(T.kh[:, :], T.kc[:, 48:56].indirect(cu("offn")), T.erow[:, 160:192], op.is_equal, sig="step")
    on(S, x_h1)
    for b in range(1, E - 1):
        on(S, "prune", b)
        if b == 1:
            lin(T.fb[me32, FW - 6:FW - 5], T.fb[me32, FW - 5:FW - 4], 1.0, -1.0, sig=x_f1)
        s(S.activation(T.kc[me32, 80 + 8 * b:80 + 9 * b], T.fb[me32, FW - 4 * b - 1:FW - 4:4], fn.Identity, accum_out=T.kc[me32, 49 + b + b // 6:50 + b + b // 6]), x_pp)
    x_c3 = new()
    lin(fc("q1"), gs0, fc("pm"), 1.0 / P)
    lin(fc("q4"), fc("p31"), 68.0 / 8, -17.0 / 8)
    act(T.ct[:, NT - 3:NT:2], zeros(2), sig=x_c3)
    sw()
    lin(fc("q2"), fc("pm"), fc("q4"), 17.0 / 16)
    lin(fc("q3"), fc("p31"), 0.0, 8.0)
    lin(ct("psel", 0, 1), fc("isr"), fc("q1"), (4.0 + 4 * r) / MARK, sig=x_c3)
    on(V, x_f1)
    vw()
    tt(T.nz[me32, 31:112:16], T.nz[me32, 31:112:16], T.fb[me32, FW - 4 * E + 6:FW - 4:4], op.mult, sig="step")
    rest()
    pw()
    tt(T.km[:, 0:32], T.nz[:, :].indirect(cu("offz")), T.kh[:, :], op.mult, sig="step")
    on(V, "prune", E - 1)
    on(V, x_pp, E - 2)
    on(V, x_hz)
    ts(T.hz[me32, 1:32:8], T.erow[me32, 128:160:8], T.kc[me32, 56:57], op.is_equal, T.fb[me32, FW - 4 * E + 2:FW - 4 * E + 3], op.mult, sig="step")
    rest()
    pw()
    x_k1 = scan(T.km[:, 32:64], T.hz[:, :], T.km[:, 0:32], op.mult, op.add, sig=new())
    rest()
    on(V, x_du, 3)
    on(V, x_k1)
    on(S, x_du, 3)
    k1 = T.km[:, 39:64:8]
    x_dz = new()
    on(S, x_k1)
    for k in range(KP):
        ts(T.kl0[blk[k], :], T.km[me32, 39:64:8], fc("knb", me32), op.add, float(SH), op.add, sig="step")
        lin(T.kd[blk[k], 0:1], T.km[me32, 39 + 8 * k:40 + 8 * k], fc("kn", me32), sig=x_dz)
    pw()
    on(V, x_dz, KP)
    ts(T.dz[:, 0:64], T.zw[:, :].indirect(T.kl0[:, 0:4]), T.kd[:, 0:1], op.is_equal, sig="step")
    on(V, x_bit)
    pw()
    scan(T.dm[:, :], T.two[:, :], T.dz[:, :], op.mult, op.add, sig="step")
    pw()
    x_km, x_kt = new(), new()
    for k in range(KP):
        ts(T.kk[me32, 40 + k:41 + k], T.dm[blk[k], 64:65], T.kd[blk[k], 0:1], op.min, T.dumpc[blk[k], k:k + 1], op.max, sig=x_km)
    on(g, x_km, KP)
    tell(kmsg, lambda q: T.kk[:, 28 - 4 * r:32 - 4 * r], "kept")

    x_y, x_ysb, x_yo, x_st, x_oy, x_oyd, x_kf, x_wq = new(), new(), new(), new(), new(), new(), new(), new()
    x_kh = act(T.kh[me32, 0:32:8], T.hz[me32, 1:32:8], sig=new())
    sw()
    lin(fc("q4"), fc("t1"), fc("q3"), fc("q2"))
    act(T.ky[:, 32:40], zeros(8), sig=x_kz)
    lin(fc("c7"), fc("pm"), -128.0, sig=x_kz)
    act(T.kf[:, :], zeros(32), sig=x_kf)
    lin(fc("g16"), gs0, NR * A - S0 / 16, 1.0 / 64)
    on(S, x_im)
    sw()
    lin(ct("tl", 0, 1), fc("q4"), 7.0, sig=x_c3)
    lin(T.vald[:, :], T.im64[:, :], fc("g16"), -1.0, sig=x_vald)
    on(V, x_d8)
    on(V, x_kh)
    tt(T.km[:, 0:32], T.fb[:, :].indirect(cu("offf")), T.kh[:, :], op.mult, sig="step")
    on(V, x_w, 16)
    quant("wq", 0, 128, T.wt[:, :], x_wq)
    pw()
    scan(T.ky[:, 0:32], T.r8[:, :], T.km[:, 0:32], op.add, op.max, sig="step")
    on(V, x_km, KP)
    ts(T.kc[:, 32:36], kmsg, float(-DUMP), op.add)
    on(V, x_kz, 2)
    pw()
    ts(T.ofy[:, :], T.ky[:, 7:39:4], 256.0, op.mult, fc("c7"), op.add, sig=x_oy)
    on(V, x_kf)
    ts(T.kf[:, 0:4], k1, fc("knb"), op.add, -1.0, op.max)
    on(V, x_c3, 3)
    cp(T.cu[:, N2:NT], T.ct[:, N2:NT])
    rest(3)
    vw()
    v(V.transpose(T.kt[me32, :], T.kf[me32, :]), x_kt)
    rest(4)
    on(Q, x_oy)
    for k in range(8):
        load(Q, T.oy[16 * k:16 * k + 16, :], T.ofy[16 * r:16 * r + 16, :], x_oyd)
    on(M, x_sz, 2)
    on(M, x_pa, 2)
    on(M, x_ptown, 32)
    on(M, "r_ptc", TOLD)
    on(M, "r_pts", TOLD)
    x_up = [new() for b in range(4)]
    for b in range(4):
        e = slice(128 * b, 128 * b + 128)
        M.matmul_mx(T.ps[:, 512 * b:512 * b + 128], T.eq[:, e], T.eqs[:, e], T.pt[:, :], T.pts[:, :], True, True).then_inc(T.sem[x_up[b]], 1)
        on(S, x_up[b])
        act(T.ptd[:, PW * b:PW * b + NR * A], T.ps[:, 512 * b:512 * b + 128], sig=x_un[min(b, 1)])
    act(T.ysb[:, 0:16], zeros(16), sig=x_ysb)
    on(M, x_un[0])
    on(M, x_wq)
    M.matmul_mx(T.ps[:, 0:128], T.wq[:, :], T.wqs[:, :], T.pk[:, best], T.pks[:, best], True, True).then_inc(T.sem[x_y], 1)
    on(S, x_rest, 5)
    for b in range(2):
        act(T.tbd[:, P * b:P * b + P], T.ps[:, 2048 + 512 * b:2048 + 512 * b + P], sig=x_td)
    on(S, x_y)
    act(T.ysb[:, 16:144], T.ps[:, 0:128], sig=x_ysb)
    on(S, x_ysb, 2)
    on(S, x_oyd, 128)
    for i in range(KP):
        pick_s(T.yo[:, i:64:4], T.ysb[:, :], T.oy[:, 2 * i:2 * i + 1], x_yo)
    on(Q, x_kt)
    load(Q, T.kp[:, :], T.kt[me32.start:me32.start + 4, 16 * odd:16 * odd + 16], x_st)
    on(Q, x_yo, KP)
    load(Q, T.y[:, :], T.yo[:, :], x_st)

    on(V, x_vald)
    on(V, x_cl)
    on(V, "r_kept", TOLD)
    ts(klf, kland, float(-DUMP), op.add, sig="step")
    pw()
    cp(T.okl[:, :], T.kc[:, 0:48].indirect(cu("psel", 0, 1)), sig="step")
    pw()
    cp(T.cl[:, :].indirect(T.okl[:, 0:KP]), T.vald[:, :], sig="claim")
    on(V, "claim")
    v(V.transpose(T.ttc[:, 0:256], T.cl[:, c0:c0 + 256]), "step")
    v(V.transpose(T.ttc[:, 256:544], T.cl[:, c0 - 16:c0 + 272]), "step")
    pw()
    on(S, "step", pn[0])
    x_mx = new()
    for j, (o, a, k) in enumerate(((lo, lo, 0), (lo, hi, 1), (blk[0], blk[1], 2), (blk[1], blk[0], 2), (blk[0], blk[3], 3), (blk[1], blk[2], 3))):
        (cp, cp, act)[j % 3](T.mx[o, k:136:4], T.ttc[a, 0:544:16], sig=x_mx)
    on(V, x_mx, 6)
    on(V, x_rs)
    for o in (lo, hi):
        scan(T.ub[o, :], T.rs[lo, :], T.mx[lo, :], op.add, op.max)
    vw()
    x_new, x_st2, x_gp = new(), new(), new()
    x_ptl = ts(T.ptl[:, :], ub.indirect(cu("tl", 0, 1)), -1.0, op.mult, float(NR * A), op.add, sig=new())
    for q_ in (V, S):
        on(q_, x_un[0])
        on(q_, x_un[1], 3)
        on(q_, x_rest, done[1])
        on(q_, x_td, 2)
        on(q_, x_ptl)
    for b in (2, 3):
        pick_s(T.gp[:, P * b - 2 * P:P * b - P], T.ptd[:, PW * b:PW * b + PW], T.ptl[:, 0:16], x_gp)
    x_bb = new()
    for b in range(3):
        o = T.bb[:, b:1024:4]
        if b < 2:
            tt(o, T.ptd[:, PW * b:PW * b + PW].indirect(T.ptl[:, 0:16]), T.tbd[:, P * b:P * b + P], op.add, sig="step")
        else:
            on(V, x_gp)
            tt(o, T.gp[:, 0:P], T.ps[:, 3072:3072 + P], op.add, sig="step")
    on(V, x_gp, 2)
    for h in range(2):
        tt(T.bb[:, 512 * h + 3:512 * h + 512:4], T.gp[:, P + 128 * h:P + 128 * h + 128], T.ps[:, 3584 + 128 * h:3712 + 128 * h], op.add, sig=x_bb)
    pw()
    for h in range(2):
        on(V, x_bb, h + 1)
        quant("tn", 128 * h, 128 * h + 128, T.bb[:, 512 * h:512 * h + 512], x_new)
        on(Q, x_new, h + 1)
        load(Q, T.oc[:, 512 * h:512 * h + 512], T.tn[:, 128 * h:128 * h + 128].bitcast(u8), x_st)
    on(S, x_new, 2)
    for k in range(4):
        load(S if k < 3 else Q, T.osc[4 * k:4 * k + 4, :], T.tns[32 * k:32 * k + 4, :], x_st2 if k < 3 else x_st)
    on(Q, x_st, 80)
    on(S, x_st2, 48)
    on(V, "v", vn[0])
    on(S, "s", sn_[0])
    for n in ROADS:
        on(g, "l_" + n, {"cod": WAVE, "co2": WAVE, "ptc": 2 * EV}.get(n, EV))
